import numpy as np
import ml_dtypes


def mxq(x, axis, fmt="e4m3"):
    dtype, down = {"e4m3": (ml_dtypes.float8_e4m3fn, 7), "e5m2": (ml_dtypes.float8_e5m2, 14)}[fmt]
    v = np.moveaxis(np.asarray(x, np.float32).astype(ml_dtypes.bfloat16).astype(np.float64), axis, -1)
    blocks = v.reshape(v.shape[:-1] + (-1, 32))
    amax = np.abs(blocks).max(-1, keepdims=True)
    byte = np.maximum(np.where(amax > 0, np.frexp(amax)[1] - 1 + 127, 0) - down, 1)
    scale = np.exp2(byte - 127.0)
    codes = (blocks / scale).astype(np.float32).astype(dtype).astype(np.float64)
    return np.moveaxis((codes * scale).reshape(v.shape), -1, axis)


WIDE = False


def mx_kscale(k):
    if not WIDE:
        return np.ones(k)
    levels = np.array([10, -10, 5, -5, 0])
    if k % 512:
        return np.exp2(np.random.permutation(np.resize(levels, k // 32))).repeat(32)
    a = np.empty((k // 512, 16))
    for p in range(k // 512):
        a[p, :8] = np.random.permutation(np.resize(levels, 8))
        for g in range(8):
            far = levels[np.abs(levels - a[p, g]) >= 10]
            a[p, g + 8] = far[np.random.randint(len(far))]
    return np.exp2(a.ravel()).repeat(32)


def f64(x):
    return np.asarray(x).astype(np.float64)


def striped(idx):
    return np.tile(idx.reshape(-1, 16).T, (8, 1)).astype(np.uint16)


def unstriped(offs):
    return offs[:16].T.reshape(-1).astype(np.int64)


E2M1 = np.array([0.0, 0.5, 1.0, 1.5, 2.0, 3.0, 4.0, 6.0, -0.0, -0.5, -1.0, -1.5, -2.0, -3.0, -4.0, -6.0])


def pack_weight(w, fmt):
    k, n = w.shape
    w = f64(np.asarray(w, np.float32).astype(ml_dtypes.bfloat16)).reshape(k // 32, 32, n)
    amax = np.abs(w).max(1)
    if fmt == "e4m3":
        byte = np.frexp(amax)[1] - 1 + 127 - 7
    else:
        mant, ex = np.frexp(amax / 6.0)
        byte = np.where(mant > 0.5, ex, ex - 1) + 127
    byte = np.clip(np.where(amax > 0, byte, 1), 1, 254)
    scaled = (w * np.exp2(127.0 - byte)[:, None, :]).reshape(k, n).astype(np.float32)
    by_word = np.ascontiguousarray(scaled.reshape(k // 512, 128, 4, n).transpose(0, 1, 3, 2))
    if fmt == "e4m3":
        words = by_word.astype(ml_dtypes.float8_e4m3fn).view(np.uint8)
    else:
        c = by_word.astype(ml_dtypes.float4_e2m1fn).view(np.uint8) & 0xF
        words = (c[..., 0::2] | (c[..., 1::2] << 4)).reshape(k // 512, 128, 2 * n)
    return np.ascontiguousarray(words), np.ascontiguousarray(byte.astype(np.uint8).reshape(k // 512, 16, n))


def unpack_weight(words, scales, fmt):
    g, _, n = scales.shape
    words = np.ascontiguousarray(words).reshape(g, 128, n, -1)
    if fmt == "e4m3":
        vals = words.view(ml_dtypes.float8_e4m3fn).astype(np.float64)
    else:
        nib = np.empty((g, 128, n, 4), np.uint8)
        nib[..., 0::2] = words & 0xF
        nib[..., 1::2] = words >> 4
        vals = E2M1[nib]
    vals = vals * np.repeat(np.exp2(scales.astype(np.float64) - 127.0), 8, axis=1)[..., None]
    return vals.transpose(0, 1, 3, 2).reshape(g * 512, n)


def gelu(v):
    return 0.5 * v * (1.0 + np.tanh(np.sqrt(2.0 / np.pi) * (v + 0.044715 * v**3)))


def often(T, S):
    return np.random.permutation(T)[(T * np.random.uniform(0, 1, S) ** 4).astype(np.int64)]


K, K2, T, T2, S, P, H, N = 1024, 512, 2048, 1024, 1024, 512, 1024, 512

def setup_inputs():
    n = np.random.standard_normal
    s = mx_kscale(K)[:, None]
    s2 = mx_kscale(K2)[:, None]
    u = mx_kscale(H)[:, None]
    tab_words, tab_scales = pack_weight(n((K, T)) * s, "e4m3")
    tab2_words, tab2_scales = pack_weight(n((K2, T2)) * s2, "e4m3")
    wang_words, wang_scales = pack_weight(0.4 * n((K, H)) / np.sqrt(K) / s, "e2m1")
    wsub2_words, wsub2_scales = pack_weight(n((K2, H)) / np.sqrt(K2) / s2 * u.T, "e4m3")
    return {
        "tab_words": tab_words, "tab_scales": tab_scales,
        "offs": striped(np.random.permutation(T)[:S]),
        "pos1": striped(often(S, P)),
        "tab2_words": tab2_words, "tab2_scales": tab2_scales,
        "offs2": striped(np.random.permutation(T2)[:P]),
        "wang_words": wang_words, "wang_scales": wang_scales,
        "bang": np.random.uniform(-0.5, 0.5, H).astype(np.float32),
        "wsub1": (n((K2, H)) / np.sqrt(K2) / s2 * u.T).astype(np.float32),
        "wsub2_words": wsub2_words, "wsub2_scales": wsub2_scales,
        "wspin": (n((H, N)) / np.sqrt(H) / u).astype(np.float32),
    }

def reference(tab_words, tab_scales, offs, pos1, tab2_words, tab2_scales, offs2, wang_words, wang_scales, bang, wsub1, wsub2_words, wsub2_scales, wspin):
    v = unpack_weight(tab_words, tab_scales, "e4m3")[:, unstriped(offs)]
    v2 = unpack_weight(tab2_words, tab2_scales, "e4m3")[:, unstriped(offs2)]
    wang = unpack_weight(wang_words, wang_scales, "e2m1")
    wsub2 = unpack_weight(wsub2_words, wsub2_scales, "e4m3")
    th = (wang.T @ v) + f64(bang)[:, None]
    ang = th[:, unstriped(pos1)]
    b1 = mxq(f64(wsub1), 0, "e4m3").T @ v2
    b2 = wsub2.T @ v2
    h = np.cos(ang) * b1 + np.sin(ang) * b2
    hq = mxq(h, 0, "e4m3")
    return mxq(f64(wspin), 0, "e4m3").T @ hq

@@ -1,0 +1,338 @@
+import math
+from contextlib import ExitStack
+
+import concourse.mybir as mybir
+from concourse.masks import make_identity
+
+K, K2, T, T2, S, P, H, N = 1024, 512, 2048, 1024, 1024, 512, 1024, 512
+FLOPS = 2 * K * H * S + 2 * 2 * K2 * H * P + 2 * H * N * P
+
+F32 = mybir.dt.float32
+BF16 = mybir.dt.bfloat16
+I32 = mybir.dt.int32
+U32 = mybir.dt.uint32
+U16 = mybir.dt.uint16
+U8 = mybir.dt.uint8
+FP8X4 = mybir.dt.float8_e4m3fn_x4
+FP4X4 = mybir.dt.float4_e2m1fn_x4
+ACT = mybir.ActivationFunctionType
+ALU = mybir.AluOpType
+
+PART = 128
+CH = 256
+ADD_ENG = "gggv"
+CAST1_ENG = "gg"
+CASTS_ENG = "gg"
+
+
+def tile_list_halo_spin_orientation_kernel(
+    tc, tab_words, tab_scales, offs, pos1, tab2_words, tab2_scales, offs2, wang_words, wang_scales,
+    bang, wsub1, wsub2_words, wsub2_scales, wspin, out,
+):
+    nc = tc.nc
+
+    def cast(eng, dst, src):
+        if eng == "s":
+            nc.scalar.copy(out=dst, in_=src)
+        elif eng == "v":
+            nc.vector.tensor_copy(out=dst, in_=src)
+        else:
+            nc.gpsimd.tensor_scalar(out=dst, in0=src, scalar1=1.0, scalar2=0.0, op0=ALU.mult, op1=ALU.add)
+
+    with ExitStack() as ctx:
+        lists = ctx.enter_context(tc.tile_pool(name="lists", bufs=1))
+        keep = ctx.enter_context(tc.tile_pool(name="keep", bufs=1))
+        ring = ctx.enter_context(tc.tile_pool(name="ring", bufs=3))
+        acc = ctx.enter_context(tc.psum_pool(name="acc", bufs=4))
+        proj = ctx.enter_context(tc.psum_pool(name="proj", bufs=4))
+
+        def kept(name, shape, dtype):
+            return keep.tile(shape, dtype, name=name, align_bytes=64)
+
+        offs_t = lists.tile([PART, S // 16], U16, name="offs_t")
+        pos_t = lists.tile([PART, P // 16], U16, name="pos_t")
+        offs2_t = lists.tile([PART, P // 16], U16, name="offs2_t")
+
+        tab_s = kept("tab_s", [PART, T], U8)
+        w_s = kept("w_s", [PART, 3, H], U8)
+        tab2_s = kept("tab2_s", [PART, T2], U8)
+        v_s = [kept("v_s%d" % k, [PART, S], U8) for k in range(2)]
+        bias_rows = kept("bias_rows", [PART, PART], F32)
+        ident = kept("ident", [PART, PART], F32)
+        for q in range(4):
+            nc.vector.memset(tab_s[32 * q : 32 * q + 24, :].bitcast(I32), 0)
+        nc.vector.memset(w_s[:].rearrange("p a c -> p (a c)").bitcast(I32), 0)
+        nc.vector.memset(bias_rows[:], 0.0)
+        for k in range(2):
+            nc.vector.memset(v_s[k][:].bitcast(I32), 0)
+        nc.vector.memset(tab2_s[:].bitcast(I32), 0)
+        make_identity(nc, ident[:])
+
+        tab_w = [kept("tab_w%d" % a, [PART, T], I32) for a in range(2)]
+        wang_raw = kept("wang_raw", [PART, 2, H // 2], I32)
+        tab2_w = kept("tab2_w", [PART, T2], I32)
+        wsub2_raw = kept("wsub2_raw", [PART, H], I32)
+        wsub1_raw = [kept("wsub1_raw%d" % a, [PART, 4, 512], F32) for a in range(2)]
+        wspin_raw = [kept("wspin_raw%d" % a, [PART, 4, N], F32) for a in range(2)]
+
+        wsub1_v = wsub1.rearrange("(p j) c -> p j c", j=4)
+        nc.sync.dma_start(offs_t[:], offs)
+        for q in range(4):
+            nc.sync.dma_start(tab_s[32 * q + 24 : 32 * q + 32, :].bitcast(I32), tab_scales[:, 4 * q : 4 * q + 4, :].bitcast(I32))
+        nc.sync.dma_start(wang_raw[:], wang_words.rearrange("a p c -> p a c").bitcast(I32))
+        nc.sync.dma_start(tab_w[0][:], tab_words[0].rearrange("p t i -> p (t i)").bitcast(I32))
+        nc.sync.dma_start(tab_w[1][:], tab_words[1].rearrange("p t i -> p (t i)").bitcast(I32))
+        for q in range(4):
+            nc.sync.dma_start(
+                w_s[32 * q : 32 * q + 4, 0:2, :].bitcast(I32),
+                wang_scales[:, 4 * q : 4 * q + 4, :].rearrange("a r c -> r a c").bitcast(I32),
+            )
+        for a in range(2):
+            nc.gpsimd.dma_start(
+                bias_rows[4 * a : 4 * a + 4, :].rearrange("t (q i) -> t q i", i=8),
+                bang[512 * a : 512 * (a + 1)].rearrange("(q t i) -> t q i", t=4, i=8),
+            )
+        nc.sync.dma_start(pos_t[:], pos1)
+        nc.sync.dma_start(offs2_t[:], offs2)
+        nc.sync.dma_start(wsub1_raw[0][:], wsub1_v[:, :, 0:512])
+        nc.sync.dma_start(tab2_w[:], tab2_words[0].rearrange("p t i -> p (t i)").bitcast(I32))
+        for q in range(4):
+            nc.sync.dma_start(w_s[32 * q : 32 * q + 4, 2, :].bitcast(I32), wsub2_scales[0, 4 * q : 4 * q + 4, :].bitcast(I32))
+        nc.sync.dma_start(wsub2_raw[:], wsub2_words[0].rearrange("p t i -> p (t i)").bitcast(I32))
+        nc.sync.dma_start(wsub1_raw[1][:], wsub1_v[:, :, 512:1024])
+        wspin_v = wspin.rearrange("(a q t i) n -> a t q i n", a=2, t=4, i=8)
+        for a in range(2):
+            for t in range(4):
+                nc.sync.dma_start(wspin_raw[a][:, t, :], wspin_v[a, t])
+
+        bias_ps = acc.tile([PART, 512], F32, name="bank", tag="bank")
+        nc.tensor.transpose(bias_ps[:, 0:PART], bias_rows[:], ident[:])
+        bias = kept("bias", [PART, 8], F32)
+        nc.scalar.activation(bias[:], bias_ps[:, 0:8], ACT.Identity)
+
+        v_sg = kept("v_sg", [PART, S], U8)
+        nc.vector.tensor_copy(v_sg[:], tab_s[:].indirect(offs_t[:]))
+        for k in range(2):
+            nc.gpsimd.dma_start(v_s[k][0:100, :].bitcast(I32), v_sg[24 + 4 * k : 124 + 4 * k, :].bitcast(I32))
+        for q in range(4):
+            nc.gpsimd.dma_start(tab2_s[32 * q : 32 * q + 4, :].bitcast(I32), tab2_scales[0, 4 * q : 4 * q + 4, :].bitcast(I32))
+        wang_w = kept("wang_w", [PART, 2, H // 2], I32)
+        nc.vector.tensor_copy(
+            wang_w[:].rearrange("p k (a t q w) -> p (k a) t q w", a=2, t=4, w=4),
+            wang_raw[:].rearrange("p k (a q t w) -> p (k a) t q w", a=2, t=4, w=4),
+        )
+        v_w = [[kept("v_w%d%d" % (a, h), [PART, 512], U32) for h in range(2)] for a in range(2)]
+
+        def gather_v(a, h):
+            nc.vector.tensor_copy(v_w[a][h][:], tab_w[a][:].bitcast(U32).indirect(offs_t[:, 32 * h : 32 * (h + 1)]))
+
+        gather_v(0, 0)
+        gather_v(0, 1)
+        wang_s = kept("wang_s", [PART, 2, H // 4], I32)
+        nc.vector.tensor_copy(
+            wang_s[:].rearrange("p k (a t q w) -> p (k a) t q w", a=2, t=4, w=2),
+            w_s[:, 0:2, :].bitcast(I32).rearrange("p k (a q t w) -> p (k a) t q w", a=2, t=4, w=2),
+        )
+        gather_v(1, 0)
+        gather_v(1, 1)
+
+        th = [None] * 8
+
+        def angles(j, h):
+            if th[j] is None:
+                th[j] = ring.tile([PART, S], F32, name="th", tag="th")
+            bank = acc.tile([PART, 512], F32, name="bank", tag="bank")
+            for k in range(2):
+                nc.tensor.matmul_mx(
+                    out=bank[:],
+                    lhsT=wang_w[:, k, 64 * j : 64 * (j + 1)].bitcast(FP4X4),
+                    lhsT_scale=wang_s[:, k, 32 * j : 32 * (j + 1)].bitcast(U8),
+                    rhs=v_w[k][h][:].bitcast(FP8X4),
+                    rhs_scale=v_s[k][:, 512 * h : 512 * (h + 1)],
+                    start=(k == 0),
+                    stop=(k == 1),
+                )
+            nc.scalar.activation(th[j][:, 512 * h : 512 * (h + 1)], bank[:], ACT.Identity, bias=bias[:, j : j + 1])
+
+        v2_w = kept("v2_w", [PART, P], U32)
+        v2_s = kept("v2_s", [PART, P], U8)
+        wsub2_w = kept("wsub2_w", [PART, H], I32)
+        wsub2_s = kept("wsub2_s", [PART, H // 4], I32)
+        wsub1_b = [kept("wsub1_b%d" % a, [PART, 512, 4], BF16) for a in range(2)]
+        wsub1_w = [kept("wsub1_w%d" % a, [PART, 512], U32) for a in range(2)]
+        wsub1_s = [kept("wsub1_s%d" % a, [PART, 512], U8) for a in range(2)]
+        wspin_b = [kept("wspin_b%d" % a, [PART, N, 4], BF16) for a in range(2)]
+        wspin_w = [kept("wspin_w%d" % a, [PART, N], U32) for a in range(2)]
+        wspin_s = [kept("wspin_s%d" % a, [PART, N], U8) for a in range(2)]
+
+        def second_table():
+            nc.vector.tensor_copy(v2_s[:], tab2_s[:].indirect(offs2_t[:]))
+            nc.vector.tensor_copy(v2_w[:], tab2_w[:].bitcast(U32).indirect(offs2_t[:]))
+            nc.vector.tensor_copy(
+                wsub2_s[:].rearrange("p (a t q w) -> p a t q w", a=2, t=4, w=2),
+                w_s[:, 2, :].bitcast(I32).rearrange("p (a q t w) -> p a t q w", a=2, t=4, w=2),
+            )
+            nc.vector.tensor_copy(
+                wsub2_w[:].rearrange("p (a t q w) -> p a t q w", a=2, t=4, w=8),
+                wsub2_raw[:].rearrange("p (a q t w) -> p a t q w", a=2, t=4, w=8),
+            )
+
+        def cast_wsub1(a):
+            for t in range(4):
+                dst = wsub1_b[a][:, 128 * t : 128 * (t + 1), :]
+                src = wsub1_raw[a][:].rearrange("p j (q t i) -> p t q i j", t=4, i=8)[:, t]
+                if CAST1_ENG[a] == "g":
+                    cast("g", dst.rearrange("p (q i) j -> p q i j", i=8), src)
+                else:
+                    cast(
+                        CAST1_ENG[a],
+                        dst.rearrange("p (q u i) j -> p q u j i", u=2, i=4),
+                        src.rearrange("p q (u i) j -> p q u j i", u=2),
+                    )
+
+        def cast_wspin(a):
+            for c in range(4):
+                dst = wspin_b[a][:, 128 * c : 128 * (c + 1), :]
+                src = wspin_raw[a][:, :, 128 * c : 128 * (c + 1)]
+                if CASTS_ENG[a] == "g":
+                    cast("g", dst, src.rearrange("p t n -> p n t"))
+                else:
+                    cast(CASTS_ENG[a], dst.rearrange("p (u i) t -> p u t i", i=4), src.rearrange("p t (u i) -> p u t i", i=4))
+
+        def quantize(codes, scales, values):
+            nc.vector.quantize_mx(out=codes[:].bitcast(FP8X4), scales=scales[:], in_=values[:].rearrange("p c j -> p (c j)"))
+
+        cos_t = [kept("cos%d" % u, [PART, 2, P], F32) for u in range(4)]
+        sin_t = [kept("sin%d" % u, [PART, 2, P], F32) for u in range(4)]
+        t1 = [[kept("t1_%d%d" % (a, c), [PART, 4, CH], F32) for c in range(2)] for a in range(2)]
+        t2 = [[kept("t2_%d%d" % (a, c), [PART, 4, CH], F32) for c in range(2)] for a in range(2)]
+        h_b = [[kept("h_b%d%d" % (a, c), [PART, CH, 4], BF16) for c in range(2)] for a in range(2)]
+        h_w = [[kept("h_w%d%d" % (a, c), [PART, CH], U32) for c in range(2)] for a in range(2)]
+        h_s = [[kept("h_s%d%d" % (a, c), [PART, CH], U8) for c in range(2)] for a in range(2)]
+
+        def trig(j):
+            ang = ring.tile([PART, P], F32, name="ang", tag="ang")
+            nc.vector.tensor_copy(ang[:], th[j][:].indirect(pos_t[:]))
+            cos_j = cos_t[j // 2][:, j % 2, :]
+            nc.scalar.activation(cos_j, ang[:], ACT.Abs)
+            nc.scalar.activation(sin_t[j // 2][:, j % 2, :], ang[:], ACT.Sin)
+            nc.scalar.activation(cos_j, cos_j, ACT.Sin, bias=math.pi / 2, scale=-1.0)
+
+        def products(u, c):
+            a, e = divmod(u, 2)
+            cols = slice(CH * c, CH * (c + 1))
+            for w_codes, w_scales, factor, dst in (
+                (wsub1_w[a][:], wsub1_s[a][:], cos_t[u], t1[a][c]),
+                (wsub2_w[:, 512 * a : 512 * (a + 1)], wsub2_s[:, 128 * a : 128 * (a + 1)].bitcast(U8), sin_t[u], t2[a][c]),
+            ):
+                bank = proj.tile([PART, 2, CH], F32, name="b", tag="b")
+                for d in range(2):
+                    t = 2 * e + d
+                    nc.tensor.matmul_mx(
+                        out=bank[:, d, :],
+                        lhsT=w_codes[:, 128 * t : 128 * (t + 1)].bitcast(FP8X4),
+                        lhsT_scale=w_scales[:, 128 * t : 128 * (t + 1)],
+                        rhs=v2_w[:, cols].bitcast(FP8X4),
+                        rhs_scale=v2_s[:, cols],
+                        start=True,
+                        stop=True,
+                    )
+                nc.vector.tensor_tensor(dst[:, 2 * e : 2 * e + 2, :], bank[:], factor[:, :, cols], ALU.mult)
+
+        def mix(a, c):
+            if ADD_ENG[2 * a + c] == "g":
+                nc.gpsimd.tensor_tensor(
+                    h_b[a][c][:], t1[a][c][:].rearrange("p t m -> p m t"), t2[a][c][:].rearrange("p t m -> p m t"), ALU.add
+                )
+            else:
+                nc.vector.tensor_tensor(
+                    h_b[a][c][:].rearrange("p (u i) t -> p u t i", i=4),
+                    t1[a][c][:].rearrange("p t (u i) -> p u t i", i=4),
+                    t2[a][c][:].rearrange("p t (u i) -> p u t i", i=4),
+                    ALU.add,
+                )
+
+        out_banks = {}
+
+        def spin(a, c):
+            for g in range(2):
+                if a == 0:
+                    out_banks[c, g] = acc.tile([PART, 2, CH], F32, name="bank", tag="bank")
+                for d in range(2):
+                    n = 2 * g + d
+                    nc.tensor.matmul_mx(
+                        out=out_banks[c, g][:, d, :],
+                        lhsT=wspin_w[a][:, 128 * n : 128 * (n + 1)].bitcast(FP8X4),
+                        lhsT_scale=wspin_s[a][:, 128 * n : 128 * (n + 1)],
+                        rhs=h_w[a][c][:].bitcast(FP8X4),
+                        rhs_scale=h_s[a][c][:],
+                        start=(a == 0 and d == 0),
+                        stop=(a == 1 and d == 1),
+                    )
+
+        out_v = out.rearrange("(n p) m -> p n m", p=PART)
+
+        def store(c):
+            for g in range(2):
+                res = kept("res%d%d" % (c, g), [PART, 2, CH], F32)
+                if g == 0 or c == 0:
+                    nc.scalar.copy(res[:], out_banks[c, g][:])
+                else:
+                    nc.vector.tensor_copy(res[:], out_banks[c, g][:])
+                nc.sync.dma_start(out_v[:, 2 * g : 2 * g + 2, CH * c : CH * (c + 1)], res[:])
+
+        cast_wsub1(0)
+        angles(0, 0)
+        angles(1, 0)
+        angles(0, 1)
+        angles(1, 1)
+        second_table()
+        trig(0)
+        quantize(wsub1_w[0], wsub1_s[0], wsub1_b[0])
+        for h in range(2):
+            angles(2, h)
+        trig(1)
+        for h in range(2):
+            angles(3, h)
+        cast_wsub1(1)
+        trig(2)
+        products(0, 0)
+        for h in range(2):
+            angles(4, h)
+        trig(3)
+        products(0, 1)
+        quantize(wsub1_w[1], wsub1_s[1], wsub1_b[1])
+        for h in range(2):
+            angles(5, h)
+        cast_wspin(0)
+        trig(4)
+        products(1, 0)
+        for h in range(2):
+            angles(6, h)
+        mix(0, 0)
+        trig(5)
+        products(1, 1)
+        for h in range(2):
+            angles(7, h)
+        quantize(h_w[0][0], h_s[0][0], h_b[0][0])
+        mix(0, 1)
+        cast_wspin(1)
+        trig(6)
+        quantize(wspin_w[0], wspin_s[0], wspin_b[0])
+        products(2, 0)
+        quantize(h_w[0][1], h_s[0][1], h_b[0][1])
+        trig(7)
+        products(2, 1)
+        quantize(wspin_w[1], wspin_s[1], wspin_b[1])
+        spin(0, 0)
+        spin(0, 1)
+        products(3, 0)
+        mix(1, 0)
+        products(3, 1)
+        quantize(h_w[1][0], h_s[1][0], h_b[1][0])
+        mix(1, 1)
+        spin(1, 0)
+        store(0)
+        quantize(h_w[1][1], h_s[1][1], h_b[1][1])
+        spin(1, 1)
+        store(1)

@@ -20,9 +20,8 @@ ALU = mybir.AluOpType
 
 PART = 128
 CH = 256
-ADD_ENG = "gggv"
-CAST1_ENG = "gg"
-CASTS_ENG = "gg"
+CAST1_ENG = "vvvvssss"
+CASTS_ENG = "ssssssss"
 
 
 def tile_list_halo_spin_orientation_kernel(
@@ -34,105 +33,115 @@ def tile_list_halo_spin_orientation_kernel(
     def cast(eng, dst, src):
         if eng == "s":
             nc.scalar.copy(out=dst, in_=src)
-        elif eng == "v":
-            nc.vector.tensor_copy(out=dst, in_=src)
         else:
-            nc.gpsimd.tensor_scalar(out=dst, in0=src, scalar1=1.0, scalar2=0.0, op0=ALU.mult, op1=ALU.add)
+            nc.vector.tensor_copy(out=dst, in_=src)
 
     with ExitStack() as ctx:
         lists = ctx.enter_context(tc.tile_pool(name="lists", bufs=1))
         keep = ctx.enter_context(tc.tile_pool(name="keep", bufs=1))
+        stage = ctx.enter_context(tc.tile_pool(name="stage", bufs=1))
         ring = ctx.enter_context(tc.tile_pool(name="ring", bufs=3))
         acc = ctx.enter_context(tc.psum_pool(name="acc", bufs=4))
         proj = ctx.enter_context(tc.psum_pool(name="proj", bufs=4))
 
-        def kept(name, shape, dtype):
-            return keep.tile(shape, dtype, name=name, align_bytes=64)
+        def kept(name, shape, dtype, tag=None):
+            return keep.tile(shape, dtype, name=name, tag=tag or name, align_bytes=64)
+
+        def staged(name, shape, dtype, offset):
+            return stage.tile(shape, dtype, name=name, offset=offset, align_bytes=64)
 
         offs_t = lists.tile([PART, S // 16], U16, name="offs_t")
         pos_t = lists.tile([PART, P // 16], U16, name="pos_t")
         offs2_t = lists.tile([PART, P // 16], U16, name="offs2_t")
 
         tab_s = kept("tab_s", [PART, T], U8)
-        w_s = kept("w_s", [PART, 3, H], U8)
-        tab2_s = kept("tab2_s", [PART, T2], U8)
+        w_s = kept("w_s", [PART, H // 2], I32)
+        v_sg = kept("v_sg", [PART, S], U8)
         v_s = [kept("v_s%d" % k, [PART, S], U8) for k in range(2)]
         bias_rows = kept("bias_rows", [PART, PART], F32)
         ident = kept("ident", [PART, PART], F32)
         for q in range(4):
             nc.vector.memset(tab_s[32 * q : 32 * q + 24, :].bitcast(I32), 0)
-        nc.vector.memset(w_s[:].rearrange("p a c -> p (a c)").bitcast(I32), 0)
-        nc.vector.memset(bias_rows[:], 0.0)
-        for k in range(2):
-            nc.vector.memset(v_s[k][:].bitcast(I32), 0)
-        nc.vector.memset(tab2_s[:].bitcast(I32), 0)
+        nc.gpsimd.memset(w_s[:], 0)
+        nc.gpsimd.memset(bias_rows[0:96, :], 0.0)
+        nc.gpsimd.memset(bias_rows[96:120, :], 0.0)
         make_identity(nc, ident[:])
+        warm = kept("warm", [PART, 16], F32)
+        nc.scalar.activation(warm[0:96, 0:1], bias_rows[0:96, 0:1], ACT.Sin)
 
-        tab_w = [kept("tab_w%d" % a, [PART, T], I32) for a in range(2)]
-        wang_raw = kept("wang_raw", [PART, 2, H // 2], I32)
-        tab2_w = kept("tab2_w", [PART, T2], I32)
-        wsub2_raw = kept("wsub2_raw", [PART, H], I32)
-        wsub1_raw = [kept("wsub1_raw%d" % a, [PART, 4, 512], F32) for a in range(2)]
-        wspin_raw = [kept("wspin_raw%d" % a, [PART, 4, N], F32) for a in range(2)]
+        tab_w = [kept("tab_w0", [PART, T], I32, tag="big0"), staged("tab_w1", [PART, T], I32, 0)]
+        wang_raw = kept("wang_raw", [PART, 2, H // 2], I32, tag="mid")
 
-        wsub1_v = wsub1.rearrange("(p j) c -> p j c", j=4)
         nc.sync.dma_start(offs_t[:], offs)
         for q in range(4):
             nc.sync.dma_start(tab_s[32 * q + 24 : 32 * q + 32, :].bitcast(I32), tab_scales[:, 4 * q : 4 * q + 4, :].bitcast(I32))
-        nc.sync.dma_start(wang_raw[:], wang_words.rearrange("a p c -> p a c").bitcast(I32))
         nc.sync.dma_start(tab_w[0][:], tab_words[0].rearrange("p t i -> p (t i)").bitcast(I32))
-        nc.sync.dma_start(tab_w[1][:], tab_words[1].rearrange("p t i -> p (t i)").bitcast(I32))
+        nc.sync.dma_start(wang_raw[:], wang_words.rearrange("a p c -> p a c").bitcast(I32))
+        nc.sync.dma_start(offs2_t[:], offs2)
         for q in range(4):
             nc.sync.dma_start(
-                w_s[32 * q : 32 * q + 4, 0:2, :].bitcast(I32),
+                w_s[32 * q : 32 * q + 4, :].rearrange("r (a c) -> r a c", a=2),
                 wang_scales[:, 4 * q : 4 * q + 4, :].rearrange("a r c -> r a c").bitcast(I32),
             )
+        nc.sync.dma_start(tab_w[1][:], tab_words[1].rearrange("p t i -> p (t i)").bitcast(I32))
+        nc.sync.dma_start(pos_t[:], pos1)
         for a in range(2):
-            nc.gpsimd.dma_start(
-                bias_rows[4 * a : 4 * a + 4, :].rearrange("t (q i) -> t q i", i=8),
+            nc.sync.dma_start(
+                bias_rows[120 + 4 * a : 124 + 4 * a, :].rearrange("t (q i) -> t q i", i=8),
                 bang[512 * a : 512 * (a + 1)].rearrange("(q t i) -> t q i", t=4, i=8),
             )
-        nc.sync.dma_start(pos_t[:], pos1)
-        nc.sync.dma_start(offs2_t[:], offs2)
-        nc.sync.dma_start(wsub1_raw[0][:], wsub1_v[:, :, 0:512])
-        nc.sync.dma_start(tab2_w[:], tab2_words[0].rearrange("p t i -> p (t i)").bitcast(I32))
+        nc.vector.tensor_copy(v_sg[:], tab_s[:].indirect(offs_t[:]))
+        for k in range(2):
+            nc.sync.dma_start(v_s[k][0:100, :].bitcast(I32), v_sg[24 + 4 * k : 124 + 4 * k, :].bitcast(I32))
+        tab2_s = kept("tab2_s", [PART, T2], U8, tag="tab_s")
+        nc.vector.memset(tab2_s[:].bitcast(I32), 0)
         for q in range(4):
-            nc.sync.dma_start(w_s[32 * q : 32 * q + 4, 2, :].bitcast(I32), wsub2_scales[0, 4 * q : 4 * q + 4, :].bitcast(I32))
-        nc.sync.dma_start(wsub2_raw[:], wsub2_words[0].rearrange("p t i -> p (t i)").bitcast(I32))
-        nc.sync.dma_start(wsub1_raw[1][:], wsub1_v[:, :, 512:1024])
-        wspin_v = wspin.rearrange("(a q t i) n -> a t q i n", a=2, t=4, i=8)
-        for a in range(2):
-            for t in range(4):
-                nc.sync.dma_start(wspin_raw[a][:, t, :], wspin_v[a, t])
+            nc.sync.dma_start(tab2_s[32 * q : 32 * q + 4, :].bitcast(I32), tab2_scales[0, 4 * q : 4 * q + 4, :].bitcast(I32))
 
         bias_ps = acc.tile([PART, 512], F32, name="bank", tag="bank")
         nc.tensor.transpose(bias_ps[:, 0:PART], bias_rows[:], ident[:])
         bias = kept("bias", [PART, 8], F32)
-        nc.scalar.activation(bias[:], bias_ps[:, 0:8], ACT.Identity)
+        nc.scalar.copy(bias[:], bias_ps[:, 120:128])
 
-        v_sg = kept("v_sg", [PART, S], U8)
-        nc.vector.tensor_copy(v_sg[:], tab_s[:].indirect(offs_t[:]))
-        for k in range(2):
-            nc.gpsimd.dma_start(v_s[k][0:100, :].bitcast(I32), v_sg[24 + 4 * k : 124 + 4 * k, :].bitcast(I32))
-        for q in range(4):
-            nc.gpsimd.dma_start(tab2_s[32 * q : 32 * q + 4, :].bitcast(I32), tab2_scales[0, 4 * q : 4 * q + 4, :].bitcast(I32))
+        v_w = [[kept("v_w%d%d" % (k, h), [PART, 512], U32) for h in range(2)] for k in range(2)]
+
+        def gather_v(k, h):
+            nc.vector.tensor_copy(v_w[k][h][:], tab_w[k][:].bitcast(U32).indirect(offs_t[:, 32 * h : 32 * (h + 1)]))
+
+        wsub1_v = wsub1.rearrange("(p j) c -> p j c", j=4)
+        wsub1_raw = []
+
+        def load_wsub1(a):
+            wsub1_raw.append(kept("wsub1_raw%d" % a, [PART, 4, 512], F32, tag=("mid", "v_sg")[a]))
+            nc.sync.dma_start(wsub1_raw[a][:], wsub1_v[:, :, 512 * a : 512 * (a + 1)])
+
+        wspin_v = wspin.rearrange("(a q t i) n -> a t q i n", a=2, t=4, i=8)
+        wspin_raw = []
+
+        def load_wspin(a):
+            wspin_raw.append(kept("wspin_raw%d" % a, [PART, 4, N], F32, tag=("mid", "big0")[a]))
+            for t in range(4):
+                nc.sync.dma_start(wspin_raw[a][:, t, :], wspin_v[a, t])
+
+        gather_v(0, 0)
         wang_w = kept("wang_w", [PART, 2, H // 2], I32)
         nc.vector.tensor_copy(
             wang_w[:].rearrange("p k (a t q w) -> p (k a) t q w", a=2, t=4, w=4),
             wang_raw[:].rearrange("p k (a q t w) -> p (k a) t q w", a=2, t=4, w=4),
         )
-        v_w = [[kept("v_w%d%d" % (a, h), [PART, 512], U32) for h in range(2)] for a in range(2)]
-
-        def gather_v(a, h):
-            nc.vector.tensor_copy(v_w[a][h][:], tab_w[a][:].bitcast(U32).indirect(offs_t[:, 32 * h : 32 * (h + 1)]))
-
-        gather_v(0, 0)
+        load_wsub1(0)
         gather_v(0, 1)
+        tab2_w = kept("tab2_w", [PART, T2], I32, tag="big0")
+        nc.sync.dma_start(tab2_w[:], tab2_words[0].rearrange("p t i -> p (t i)").bitcast(I32))
+        wsub2_raw = kept("wsub2_raw", [PART, H], I32, tag="v_sg")
+        nc.sync.dma_start(wsub2_raw[:], wsub2_words[0].rearrange("p t i -> p (t i)").bitcast(I32))
         wang_s = kept("wang_s", [PART, 2, H // 4], I32)
         nc.vector.tensor_copy(
             wang_s[:].rearrange("p k (a t q w) -> p (k a) t q w", a=2, t=4, w=2),
-            w_s[:, 0:2, :].bitcast(I32).rearrange("p k (a q t w) -> p (k a) t q w", a=2, t=4, w=2),
+            w_s[:].rearrange("p (k q t w) -> p k t q w", k=4, t=4, w=2),
         )
+        for q in range(4):
+            nc.sync.dma_start(w_s[32 * q : 32 * q + 4, 0 : H // 4], wsub2_scales[0, 4 * q : 4 * q + 4, :].bitcast(I32))
         gather_v(1, 0)
         gather_v(1, 1)
 
@@ -154,11 +163,11 @@ def tile_list_halo_spin_orientation_kernel(
                 )
             nc.scalar.activation(th[j][:, 512 * h : 512 * (h + 1)], bank[:], ACT.Identity, bias=bias[:, j : j + 1])
 
-        v2_w = kept("v2_w", [PART, P], U32)
-        v2_s = kept("v2_s", [PART, P], U8)
-        wsub2_w = kept("wsub2_w", [PART, H], I32)
-        wsub2_s = kept("wsub2_s", [PART, H // 4], I32)
-        wsub1_b = [kept("wsub1_b%d" % a, [PART, 512, 4], BF16) for a in range(2)]
+        v2_w = staged("v2_w", [PART, P], U32, 4096)
+        v2_s = staged("v2_s", [PART, P], U8, 6144)
+        wsub2_w = staged("wsub2_w", [PART, H], I32, 7680)
+        wsub2_s = staged("wsub2_s", [PART, H // 4], I32, 6656)
+        wsub1_b = [staged("wsub1_b0", [PART, 512, 4], BF16, 0), kept("wsub1_b1", [PART, 512, 4], BF16)]
         wsub1_w = [kept("wsub1_w%d" % a, [PART, 512], U32) for a in range(2)]
         wsub1_s = [kept("wsub1_s%d" % a, [PART, 512], U8) for a in range(2)]
         wspin_b = [kept("wspin_b%d" % a, [PART, N, 4], BF16) for a in range(2)]
@@ -166,46 +175,40 @@ def tile_list_halo_spin_orientation_kernel(
         wspin_s = [kept("wspin_s%d" % a, [PART, N], U8) for a in range(2)]
 
         def second_table():
-            nc.vector.tensor_copy(v2_s[:], tab2_s[:].indirect(offs2_t[:]))
             nc.vector.tensor_copy(v2_w[:], tab2_w[:].bitcast(U32).indirect(offs2_t[:]))
-            nc.vector.tensor_copy(
-                wsub2_s[:].rearrange("p (a t q w) -> p a t q w", a=2, t=4, w=2),
-                w_s[:, 2, :].bitcast(I32).rearrange("p (a q t w) -> p a t q w", a=2, t=4, w=2),
-            )
+            nc.vector.tensor_copy(v2_s[:], tab2_s[:].indirect(offs2_t[:]))
             nc.vector.tensor_copy(
                 wsub2_w[:].rearrange("p (a t q w) -> p a t q w", a=2, t=4, w=8),
                 wsub2_raw[:].rearrange("p (a q t w) -> p a t q w", a=2, t=4, w=8),
+            )
+            nc.vector.tensor_copy(
+                wsub2_s[:].rearrange("p (a t q w) -> p a t q w", a=2, t=4, w=2),
+                w_s[:, 0 : H // 4].rearrange("p (a q t w) -> p a t q w", a=2, t=4, w=2),
             )
 
         def cast_wsub1(a):
             for t in range(4):
                 dst = wsub1_b[a][:, 128 * t : 128 * (t + 1), :]
                 src = wsub1_raw[a][:].rearrange("p j (q t i) -> p t q i j", t=4, i=8)[:, t]
-                if CAST1_ENG[a] == "g":
-                    cast("g", dst.rearrange("p (q i) j -> p q i j", i=8), src)
-                else:
-                    cast(
-                        CAST1_ENG[a],
-                        dst.rearrange("p (q u i) j -> p q u j i", u=2, i=4),
-                        src.rearrange("p q (u i) j -> p q u j i", u=2),
-                    )
+                cast(
+                    CAST1_ENG[4 * a + t],
+                    dst.rearrange("p (q u i) j -> p q u j i", u=2, i=4),
+                    src.rearrange("p q (u i) j -> p q u j i", u=2),
+                )
 
         def cast_wspin(a):
             for c in range(4):
                 dst = wspin_b[a][:, 128 * c : 128 * (c + 1), :]
                 src = wspin_raw[a][:, :, 128 * c : 128 * (c + 1)]
-                if CASTS_ENG[a] == "g":
-                    cast("g", dst, src.rearrange("p t n -> p n t"))
-                else:
-                    cast(CASTS_ENG[a], dst.rearrange("p (u i) t -> p u t i", i=4), src.rearrange("p t (u i) -> p u t i", i=4))
+                cast(CASTS_ENG[4 * a + c], dst.rearrange("p (u i) t -> p u t i", i=4), src.rearrange("p t (u i) -> p u t i", i=4))
 
         def quantize(codes, scales, values):
             nc.vector.quantize_mx(out=codes[:].bitcast(FP8X4), scales=scales[:], in_=values[:].rearrange("p c j -> p (c j)"))
 
-        cos_t = [kept("cos%d" % u, [PART, 2, P], F32) for u in range(4)]
-        sin_t = [kept("sin%d" % u, [PART, 2, P], F32) for u in range(4)]
-        t1 = [[kept("t1_%d%d" % (a, c), [PART, 4, CH], F32) for c in range(2)] for a in range(2)]
-        t2 = [[kept("t2_%d%d" % (a, c), [PART, 4, CH], F32) for c in range(2)] for a in range(2)]
+        cos_t = [kept("cos%d" % j, [PART, P], F32) for j in range(8)]
+        sin_t = [kept("sin%d" % j, [PART, P], F32) for j in range(8)]
+        t1 = [kept("t1_%d" % a, [PART, 4, P], F32) for a in range(2)]
+        t2 = [kept("t2_%d" % a, [PART, 4, P], F32) for a in range(2)]
         h_b = [[kept("h_b%d%d" % (a, c), [PART, CH, 4], BF16) for c in range(2)] for a in range(2)]
         h_w = [[kept("h_w%d%d" % (a, c), [PART, CH], U32) for c in range(2)] for a in range(2)]
         h_s = [[kept("h_s%d%d" % (a, c), [PART, CH], U8) for c in range(2)] for a in range(2)]
@@ -213,44 +216,39 @@ def tile_list_halo_spin_orientation_kernel(
         def trig(j):
             ang = ring.tile([PART, P], F32, name="ang", tag="ang")
             nc.vector.tensor_copy(ang[:], th[j][:].indirect(pos_t[:]))
-            cos_j = cos_t[j // 2][:, j % 2, :]
-            nc.scalar.activation(cos_j, ang[:], ACT.Abs)
-            nc.scalar.activation(sin_t[j // 2][:, j % 2, :], ang[:], ACT.Sin)
-            nc.scalar.activation(cos_j, cos_j, ACT.Sin, bias=math.pi / 2, scale=-1.0)
+            nc.scalar.activation(cos_t[j][:], ang[:], ACT.Abs)
+            nc.scalar.activation(sin_t[j][:], ang[:], ACT.Sin)
+            nc.scalar.activation(cos_t[j][:], cos_t[j][:], ACT.Sin, bias=math.pi / 2, scale=-1.0)
 
-        def products(u, c):
-            a, e = divmod(u, 2)
-            cols = slice(CH * c, CH * (c + 1))
+        def products(j):
+            a, t = divmod(j, 4)
             for w_codes, w_scales, factor, dst in (
-                (wsub1_w[a][:], wsub1_s[a][:], cos_t[u], t1[a][c]),
-                (wsub2_w[:, 512 * a : 512 * (a + 1)], wsub2_s[:, 128 * a : 128 * (a + 1)].bitcast(U8), sin_t[u], t2[a][c]),
+                (wsub2_w[:, 512 * a : 512 * (a + 1)], wsub2_s[:, 128 * a : 128 * (a + 1)].bitcast(U8), sin_t[j], t2[a]),
+                (wsub1_w[a][:], wsub1_s[a][:], cos_t[j], t1[a]),
             ):
-                bank = proj.tile([PART, 2, CH], F32, name="b", tag="b")
-                for d in range(2):
-                    t = 2 * e + d
-                    nc.tensor.matmul_mx(
-                        out=bank[:, d, :],
-                        lhsT=w_codes[:, 128 * t : 128 * (t + 1)].bitcast(FP8X4),
-                        lhsT_scale=w_scales[:, 128 * t : 128 * (t + 1)],
-                        rhs=v2_w[:, cols].bitcast(FP8X4),
-                        rhs_scale=v2_s[:, cols],
-                        start=True,
-                        stop=True,
-                    )
-                nc.vector.tensor_tensor(dst[:, 2 * e : 2 * e + 2, :], bank[:], factor[:, :, cols], ALU.mult)
+                bank = proj.tile([PART, P], F32, name="b", tag="b")
+                nc.tensor.matmul_mx(
+                    out=bank[:],
+                    lhsT=w_codes[:, 128 * t : 128 * (t + 1)].bitcast(FP8X4),
+                    lhsT_scale=w_scales[:, 128 * t : 128 * (t + 1)],
+                    rhs=v2_w[:].bitcast(FP8X4),
+                    rhs_scale=v2_s[:],
+                    start=True,
+                    stop=True,
+                )
+                nc.vector.tensor_tensor(dst[:, t, :], bank[:], factor[:], ALU.mult)
 
         def mix(a, c):
-            if ADD_ENG[2 * a + c] == "g":
-                nc.gpsimd.tensor_tensor(
-                    h_b[a][c][:], t1[a][c][:].rearrange("p t m -> p m t"), t2[a][c][:].rearrange("p t m -> p m t"), ALU.add
-                )
-            else:
-                nc.vector.tensor_tensor(
-                    h_b[a][c][:].rearrange("p (u i) t -> p u t i", i=4),
-                    t1[a][c][:].rearrange("p t (u i) -> p u t i", i=4),
-                    t2[a][c][:].rearrange("p t (u i) -> p u t i", i=4),
-                    ALU.add,
-                )
+            cols = slice(CH * c, CH * (c + 1))
+            nc.vector.tensor_tensor(
+                h_b[a][c][:].rearrange("p (u i) t -> p u t i", i=4),
+                t1[a][:, :, cols].rearrange("p t (u i) -> p u t i", i=4),
+                t2[a][:, :, cols].rearrange("p t (u i) -> p u t i", i=4),
+                ALU.add,
+            )
+
+        def quantize_h(a, c):
+            quantize(h_w[a][c], h_s[a][c], h_b[a][c])
 
         out_banks = {}
 
@@ -281,58 +279,46 @@ def tile_list_halo_spin_orientation_kernel(
                     nc.vector.tensor_copy(res[:], out_banks[c, g][:])
                 nc.sync.dma_start(out_v[:, 2 * g : 2 * g + 2, CH * c : CH * (c + 1)], res[:])
 
-        cast_wsub1(0)
         angles(0, 0)
         angles(1, 0)
         angles(0, 1)
         angles(1, 1)
-        second_table()
+        cast_wsub1(0)
+        load_wspin(0)
         trig(0)
         quantize(wsub1_w[0], wsub1_s[0], wsub1_b[0])
-        for h in range(2):
-            angles(2, h)
-        trig(1)
-        for h in range(2):
-            angles(3, h)
-        cast_wsub1(1)
-        trig(2)
-        products(0, 0)
-        for h in range(2):
-            angles(4, h)
-        trig(3)
-        products(0, 1)
-        quantize(wsub1_w[1], wsub1_s[1], wsub1_b[1])
-        for h in range(2):
-            angles(5, h)
-        cast_wspin(0)
-        trig(4)
-        products(1, 0)
-        for h in range(2):
-            angles(6, h)
-        mix(0, 0)
-        trig(5)
-        products(1, 1)
-        for h in range(2):
-            angles(7, h)
-        quantize(h_w[0][0], h_s[0][0], h_b[0][0])
-        mix(0, 1)
-        cast_wspin(1)
-        trig(6)
-        quantize(wspin_w[0], wspin_s[0], wspin_b[0])
-        products(2, 0)
-        quantize(h_w[0][1], h_s[0][1], h_b[0][1])
+        second_table()
+        load_wsub1(1)
+        load_wspin(1)
+        for j in range(1, 7):
+            angles(j + 1, 0)
+            angles(j + 1, 1)
+            trig(j)
+            products(j - 1)
+            if j == 2:
+                cast_wsub1(1)
+            if j == 3:
+                quantize(wsub1_w[1], wsub1_s[1], wsub1_b[1])
+                cast_wspin(0)
+            if j == 4:
+                mix(0, 0)
+                mix(0, 1)
+            if j == 5:
+                quantize_h(0, 0)
+                quantize_h(0, 1)
+                quantize(wspin_w[0], wspin_s[0], wspin_b[0])
         trig(7)
-        products(2, 1)
-        quantize(wspin_w[1], wspin_s[1], wspin_b[1])
+        cast_wspin(1)
+        products(6)
         spin(0, 0)
         spin(0, 1)
-        products(3, 0)
+        products(7)
         mix(1, 0)
-        products(3, 1)
-        quantize(h_w[1][0], h_s[1][0], h_b[1][0])
+        quantize(wspin_w[1], wspin_s[1], wspin_b[1])
+        quantize_h(1, 0)
         mix(1, 1)
         spin(1, 0)
         store(0)
-        quantize(h_w[1][1], h_s[1][1], h_b[1][1])
+        quantize_h(1, 1)
         spin(1, 1)
         store(1)

@@ -19,9 +19,16 @@ ACT = mybir.ActivationFunctionType
 ALU = mybir.AluOpType
 
 PART = 128
-CH = 256
-CAST1_ENG = "vvvvssss"
-CASTS_ENG = "ssssssss"
+BANK = 512
+QUADS = 4
+ROW_TILES = H // PART
+TAB_ROW = 24
+PLANE_ROWS = 100
+BIAS_ROW = PART - ROW_TILES
+VECTOR_CAST_TILES = 3
+PIECES = ([(0, 256), (256, 256)], [(0, 256), (256, 128), (384, 128)])
+TILES_PER_BANK = (2, 4, 2)
+AT_WSUB1, AT_V2_WORDS, AT_V2_SCALES, AT_WSUB2_SCALES, AT_WSUB2_WORDS = 0, 4096, 6144, 6656, 7680
 
 
 def tile_list_halo_spin_orientation_kernel(
@@ -30,16 +37,10 @@ def tile_list_halo_spin_orientation_kernel(
 ):
     nc = tc.nc
 
-    def cast(eng, dst, src):
-        if eng == "s":
-            nc.scalar.copy(out=dst, in_=src)
-        else:
-            nc.vector.tensor_copy(out=dst, in_=src)
-
     with ExitStack() as ctx:
         lists = ctx.enter_context(tc.tile_pool(name="lists", bufs=1))
         keep = ctx.enter_context(tc.tile_pool(name="keep", bufs=1))
-        stage = ctx.enter_context(tc.tile_pool(name="stage", bufs=1))
+        reuse = ctx.enter_context(tc.tile_pool(name="reuse", bufs=1))
         ring = ctx.enter_context(tc.tile_pool(name="ring", bufs=3))
         acc = ctx.enter_context(tc.psum_pool(name="acc", bufs=4))
         proj = ctx.enter_context(tc.psum_pool(name="proj", bufs=4))
@@ -47,8 +48,21 @@ def tile_list_halo_spin_orientation_kernel(
         def kept(name, shape, dtype, tag=None):
             return keep.tile(shape, dtype, name=name, tag=tag or name, align_bytes=64)
 
-        def staged(name, shape, dtype, offset):
-            return stage.tile(shape, dtype, name=name, offset=offset, align_bytes=64)
+        def reused(name, shape, dtype, offset):
+            return reuse.tile(shape, dtype, name=name, offset=offset, align_bytes=64)
+
+        def words(packed):
+            return packed.rearrange("p c i -> p (c i)").bitcast(I32)
+
+        def load_plane(dst, scales):
+            for quad in range(QUADS):
+                nc.sync.dma_start(dst[32 * quad : 32 * quad + 4, :], scales[4 * quad : 4 * quad + 4, :].bitcast(I32))
+
+        def order_columns(dst, src, run):
+            nc.vector.tensor_copy(
+                dst.rearrange("p (a t q w) -> p a t q w", t=4, q=16, w=run),
+                src.rearrange("p (a q t w) -> p a t q w", t=4, q=16, w=run),
+            )
 
         offs_t = lists.tile([PART, S // 16], U16, name="offs_t")
         pos_t = lists.tile([PART, P // 16], U16, name="pos_t")
@@ -57,119 +71,117 @@ def tile_list_halo_spin_orientation_kernel(
         tab_s = kept("tab_s", [PART, T], U8)
         w_s = kept("w_s", [PART, H // 2], I32)
         v_sg = kept("v_sg", [PART, S], U8)
-        v_s = [kept("v_s%d" % k, [PART, S], U8) for k in range(2)]
+        v_s = [kept("v_s%d" % g, [PART, S], U8) for g in range(2)]
         bias_rows = kept("bias_rows", [PART, PART], F32)
         ident = kept("ident", [PART, PART], F32)
-        for q in range(4):
-            nc.vector.memset(tab_s[32 * q : 32 * q + 24, :].bitcast(I32), 0)
+        for quad in range(QUADS):
+            nc.vector.memset(tab_s[32 * quad : 32 * quad + TAB_ROW, :].bitcast(I32), 0)
         nc.gpsimd.memset(w_s[:], 0)
         nc.gpsimd.memset(bias_rows[0:96, :], 0.0)
-        nc.gpsimd.memset(bias_rows[96:120, :], 0.0)
+        nc.gpsimd.memset(bias_rows[96:BIAS_ROW, :], 0.0)
         make_identity(nc, ident[:])
         warm = kept("warm", [PART, 16], F32)
         nc.scalar.activation(warm[0:96, 0:1], bias_rows[0:96, 0:1], ACT.Sin)
 
-        tab_w = [kept("tab_w0", [PART, T], I32, tag="big0"), staged("tab_w1", [PART, T], I32, 0)]
-        wang_raw = kept("wang_raw", [PART, 2, H // 2], I32, tag="mid")
-
+        tab_w = [kept("tab_w0", [PART, T], I32, tag="stage_a"), reused("tab_w1", [PART, T], I32, 0)]
+        wang_raw = kept("wang_raw", [PART, 2, H // 2], I32, tag="stage_b")
         nc.sync.dma_start(offs_t[:], offs)
-        for q in range(4):
-            nc.sync.dma_start(tab_s[32 * q + 24 : 32 * q + 32, :].bitcast(I32), tab_scales[:, 4 * q : 4 * q + 4, :].bitcast(I32))
-        nc.sync.dma_start(tab_w[0][:], tab_words[0].rearrange("p t i -> p (t i)").bitcast(I32))
-        nc.sync.dma_start(wang_raw[:], wang_words.rearrange("a p c -> p a c").bitcast(I32))
-        nc.sync.dma_start(offs2_t[:], offs2)
-        for q in range(4):
+        for quad in range(QUADS):
             nc.sync.dma_start(
-                w_s[32 * q : 32 * q + 4, :].rearrange("r (a c) -> r a c", a=2),
-                wang_scales[:, 4 * q : 4 * q + 4, :].rearrange("a r c -> r a c").bitcast(I32),
+                tab_s[32 * quad + TAB_ROW : 32 * quad + 32, :].bitcast(I32),
+                tab_scales[:, 4 * quad : 4 * quad + 4, :].bitcast(I32),
             )
-        nc.sync.dma_start(tab_w[1][:], tab_words[1].rearrange("p t i -> p (t i)").bitcast(I32))
+        nc.sync.dma_start(tab_w[0][:], words(tab_words[0]))
+        nc.sync.dma_start(wang_raw[:], wang_words.rearrange("g p c -> p g c").bitcast(I32))
+        nc.sync.dma_start(offs2_t[:], offs2)
+        for quad in range(QUADS):
+            nc.sync.dma_start(
+                w_s[32 * quad : 32 * quad + 4, :].rearrange("s (g c) -> s g c", g=2),
+                wang_scales[:, 4 * quad : 4 * quad + 4, :].rearrange("g s c -> s g c").bitcast(I32),
+            )
+        nc.sync.dma_start(tab_w[1][:], words(tab_words[1]))
         nc.sync.dma_start(pos_t[:], pos1)
         for a in range(2):
             nc.sync.dma_start(
-                bias_rows[120 + 4 * a : 124 + 4 * a, :].rearrange("t (q i) -> t q i", i=8),
-                bang[512 * a : 512 * (a + 1)].rearrange("(q t i) -> t q i", t=4, i=8),
+                bias_rows[BIAS_ROW + 4 * a : BIAS_ROW + 4 * a + 4, :].rearrange("t (q i) -> t q i", i=8),
+                bang[BANK * a : BANK * (a + 1)].rearrange("(q t i) -> t q i", t=4, i=8),
             )
+
         nc.vector.tensor_copy(v_sg[:], tab_s[:].indirect(offs_t[:]))
-        for k in range(2):
-            nc.sync.dma_start(v_s[k][0:100, :].bitcast(I32), v_sg[24 + 4 * k : 124 + 4 * k, :].bitcast(I32))
+        for g in range(2):
+            first = TAB_ROW + 4 * g
+            nc.sync.dma_start(v_s[g][0:PLANE_ROWS, :].bitcast(I32), v_sg[first : first + PLANE_ROWS, :].bitcast(I32))
         tab2_s = kept("tab2_s", [PART, T2], U8, tag="tab_s")
         nc.vector.memset(tab2_s[:].bitcast(I32), 0)
-        for q in range(4):
-            nc.sync.dma_start(tab2_s[32 * q : 32 * q + 4, :].bitcast(I32), tab2_scales[0, 4 * q : 4 * q + 4, :].bitcast(I32))
+        load_plane(tab2_s[:].bitcast(I32), tab2_scales[0])
 
-        bias_ps = acc.tile([PART, 512], F32, name="bank", tag="bank")
+        bias_ps = acc.tile([PART, BANK], F32, name="bank", tag="bank")
         nc.tensor.transpose(bias_ps[:, 0:PART], bias_rows[:], ident[:])
-        bias = kept("bias", [PART, 8], F32)
-        nc.scalar.copy(bias[:], bias_ps[:, 120:128])
+        bias = kept("bias", [PART, ROW_TILES], F32)
+        nc.scalar.copy(bias[:], bias_ps[:, BIAS_ROW:PART])
 
-        v_w = [[kept("v_w%d%d" % (k, h), [PART, 512], U32) for h in range(2)] for k in range(2)]
+        v_w = [[kept("v_w%d%d" % (g, half), [PART, BANK], U32) for half in range(2)] for g in range(2)]
 
-        def gather_v(k, h):
-            nc.vector.tensor_copy(v_w[k][h][:], tab_w[k][:].bitcast(U32).indirect(offs_t[:, 32 * h : 32 * (h + 1)]))
+        def gather_v(g, half):
+            picks = offs_t[:, 32 * half : 32 * (half + 1)]
+            nc.vector.tensor_copy(v_w[g][half][:], tab_w[g][:].bitcast(U32).indirect(picks))
 
         wsub1_v = wsub1.rearrange("(p j) c -> p j c", j=4)
         wsub1_raw = []
 
         def load_wsub1(a):
-            wsub1_raw.append(kept("wsub1_raw%d" % a, [PART, 4, 512], F32, tag=("mid", "v_sg")[a]))
-            nc.sync.dma_start(wsub1_raw[a][:], wsub1_v[:, :, 512 * a : 512 * (a + 1)])
+            wsub1_raw.append(kept("wsub1_raw%d" % a, [PART, 4, BANK], F32, tag=("stage_b", "v_sg")[a]))
+            nc.sync.dma_start(wsub1_raw[a][:], wsub1_v[:, :, BANK * a : BANK * (a + 1)])
 
         wspin_v = wspin.rearrange("(a q t i) n -> a t q i n", a=2, t=4, i=8)
         wspin_raw = []
 
         def load_wspin(a):
-            wspin_raw.append(kept("wspin_raw%d" % a, [PART, 4, N], F32, tag=("mid", "big0")[a]))
+            wspin_raw.append(kept("wspin_raw%d" % a, [PART, 4, N], F32, tag=("stage_b", "stage_a")[a]))
             for t in range(4):
                 nc.sync.dma_start(wspin_raw[a][:, t, :], wspin_v[a, t])
 
         gather_v(0, 0)
         wang_w = kept("wang_w", [PART, 2, H // 2], I32)
-        nc.vector.tensor_copy(
-            wang_w[:].rearrange("p k (a t q w) -> p (k a) t q w", a=2, t=4, w=4),
-            wang_raw[:].rearrange("p k (a q t w) -> p (k a) t q w", a=2, t=4, w=4),
-        )
+        order_columns(wang_w[:].rearrange("p g c -> p (g c)"), wang_raw[:].rearrange("p g c -> p (g c)"), 4)
         load_wsub1(0)
         gather_v(0, 1)
-        tab2_w = kept("tab2_w", [PART, T2], I32, tag="big0")
-        nc.sync.dma_start(tab2_w[:], tab2_words[0].rearrange("p t i -> p (t i)").bitcast(I32))
+        tab2_w = kept("tab2_w", [PART, T2], I32, tag="stage_a")
+        nc.sync.dma_start(tab2_w[:], words(tab2_words[0]))
         wsub2_raw = kept("wsub2_raw", [PART, H], I32, tag="v_sg")
-        nc.sync.dma_start(wsub2_raw[:], wsub2_words[0].rearrange("p t i -> p (t i)").bitcast(I32))
+        nc.sync.dma_start(wsub2_raw[:], words(wsub2_words[0]))
         wang_s = kept("wang_s", [PART, 2, H // 4], I32)
-        nc.vector.tensor_copy(
-            wang_s[:].rearrange("p k (a t q w) -> p (k a) t q w", a=2, t=4, w=2),
-            w_s[:].rearrange("p (k q t w) -> p k t q w", k=4, t=4, w=2),
-        )
-        for q in range(4):
-            nc.sync.dma_start(w_s[32 * q : 32 * q + 4, 0 : H // 4], wsub2_scales[0, 4 * q : 4 * q + 4, :].bitcast(I32))
+        order_columns(wang_s[:].rearrange("p g c -> p (g c)"), w_s[:], 2)
+        load_plane(w_s[:, 0 : H // 4], wsub2_scales[0])
         gather_v(1, 0)
         gather_v(1, 1)
 
-        th = [None] * 8
+        th = [None] * ROW_TILES
 
-        def angles(j, h):
+        def angles(j, half):
             if th[j] is None:
                 th[j] = ring.tile([PART, S], F32, name="th", tag="th")
-            bank = acc.tile([PART, 512], F32, name="bank", tag="bank")
-            for k in range(2):
+            cols = slice(BANK * half, BANK * (half + 1))
+            bank = acc.tile([PART, BANK], F32, name="bank", tag="bank")
+            for g in range(2):
                 nc.tensor.matmul_mx(
                     out=bank[:],
-                    lhsT=wang_w[:, k, 64 * j : 64 * (j + 1)].bitcast(FP4X4),
-                    lhsT_scale=wang_s[:, k, 32 * j : 32 * (j + 1)].bitcast(U8),
-                    rhs=v_w[k][h][:].bitcast(FP8X4),
-                    rhs_scale=v_s[k][:, 512 * h : 512 * (h + 1)],
-                    start=(k == 0),
-                    stop=(k == 1),
+                    lhsT=wang_w[:, g, 64 * j : 64 * (j + 1)].bitcast(FP4X4),
+                    lhsT_scale=wang_s[:, g, 32 * j : 32 * (j + 1)].bitcast(U8),
+                    rhs=v_w[g][half][:].bitcast(FP8X4),
+                    rhs_scale=v_s[g][:, cols],
+                    start=(g == 0),
+                    stop=(g == 1),
                 )
-            nc.scalar.activation(th[j][:, 512 * h : 512 * (h + 1)], bank[:], ACT.Identity, bias=bias[:, j : j + 1])
+            nc.scalar.activation(th[j][:, cols], bank[:], ACT.Identity, bias=bias[:, j : j + 1])
 
-        v2_w = staged("v2_w", [PART, P], U32, 4096)
-        v2_s = staged("v2_s", [PART, P], U8, 6144)
-        wsub2_w = staged("wsub2_w", [PART, H], I32, 7680)
-        wsub2_s = staged("wsub2_s", [PART, H // 4], I32, 6656)
-        wsub1_b = [staged("wsub1_b0", [PART, 512, 4], BF16, 0), kept("wsub1_b1", [PART, 512, 4], BF16)]
-        wsub1_w = [kept("wsub1_w%d" % a, [PART, 512], U32) for a in range(2)]
-        wsub1_s = [kept("wsub1_s%d" % a, [PART, 512], U8) for a in range(2)]
+        v2_w = reused("v2_w", [PART, P], U32, AT_V2_WORDS)
+        v2_s = reused("v2_s", [PART, P], U8, AT_V2_SCALES)
+        wsub2_w = reused("wsub2_w", [PART, H], I32, AT_WSUB2_WORDS)
+        wsub2_s = reused("wsub2_s", [PART, H // 4], I32, AT_WSUB2_SCALES)
+        wsub1_b = [reused("wsub1_b0", [PART, BANK, 4], BF16, AT_WSUB1), kept("wsub1_b1", [PART, BANK, 4], BF16)]
+        wsub1_w = [kept("wsub1_w%d" % a, [PART, BANK], U32) for a in range(2)]
+        wsub1_s = [kept("wsub1_s%d" % a, [PART, BANK], U8) for a in range(2)]
         wspin_b = [kept("wspin_b%d" % a, [PART, N, 4], BF16) for a in range(2)]
         wspin_w = [kept("wspin_w%d" % a, [PART, N], U32) for a in range(2)]
         wspin_s = [kept("wspin_s%d" % a, [PART, N], U8) for a in range(2)]
@@ -177,41 +189,42 @@ def tile_list_halo_spin_orientation_kernel(
         def second_table():
             nc.vector.tensor_copy(v2_w[:], tab2_w[:].bitcast(U32).indirect(offs2_t[:]))
             nc.vector.tensor_copy(v2_s[:], tab2_s[:].indirect(offs2_t[:]))
-            nc.vector.tensor_copy(
-                wsub2_w[:].rearrange("p (a t q w) -> p a t q w", a=2, t=4, w=8),
-                wsub2_raw[:].rearrange("p (a q t w) -> p a t q w", a=2, t=4, w=8),
-            )
-            nc.vector.tensor_copy(
-                wsub2_s[:].rearrange("p (a t q w) -> p a t q w", a=2, t=4, w=2),
-                w_s[:, 0 : H // 4].rearrange("p (a q t w) -> p a t q w", a=2, t=4, w=2),
-            )
+            order_columns(wsub2_w[:], wsub2_raw[:], 8)
+            order_columns(wsub2_s[:], w_s[:, 0 : H // 4], 2)
 
         def cast_wsub1(a):
             for t in range(4):
-                dst = wsub1_b[a][:, 128 * t : 128 * (t + 1), :]
-                src = wsub1_raw[a][:].rearrange("p j (q t i) -> p t q i j", t=4, i=8)[:, t]
-                cast(
-                    CAST1_ENG[4 * a + t],
-                    dst.rearrange("p (q u i) j -> p q u j i", u=2, i=4),
-                    src.rearrange("p q (u i) j -> p q u j i", u=2),
-                )
+                dst = wsub1_b[a][:, PART * t : PART * (t + 1), :].rearrange("p (q u e) j -> p q u j e", u=2, e=4)
+                src = wsub1_raw[a][:].rearrange("p j (q t u e) -> p t q u j e", t=4, u=2, e=4)[:, t]
+                if a == 0 and t < VECTOR_CAST_TILES:
+                    nc.vector.tensor_copy(out=dst, in_=src)
+                else:
+                    nc.scalar.copy(out=dst, in_=src)
 
         def cast_wspin(a):
-            for c in range(4):
-                dst = wspin_b[a][:, 128 * c : 128 * (c + 1), :]
-                src = wspin_raw[a][:, :, 128 * c : 128 * (c + 1)]
-                cast(CASTS_ENG[4 * a + c], dst.rearrange("p (u i) t -> p u t i", i=4), src.rearrange("p t (u i) -> p u t i", i=4))
+            for n in range(4):
+                cols = slice(PART * n, PART * (n + 1))
+                nc.scalar.copy(
+                    out=wspin_b[a][:, cols, :].rearrange("p (u e) t -> p u t e", e=4),
+                    in_=wspin_raw[a][:, :, cols].rearrange("p t (u e) -> p u t e", e=4),
+                )
 
         def quantize(codes, scales, values):
             nc.vector.quantize_mx(out=codes[:].bitcast(FP8X4), scales=scales[:], in_=values[:].rearrange("p c j -> p (c j)"))
 
-        cos_t = [kept("cos%d" % j, [PART, P], F32) for j in range(8)]
-        sin_t = [kept("sin%d" % j, [PART, P], F32) for j in range(8)]
-        t1 = [kept("t1_%d" % a, [PART, 4, P], F32) for a in range(2)]
-        t2 = [kept("t2_%d" % a, [PART, 4, P], F32) for a in range(2)]
-        h_b = [[kept("h_b%d%d" % (a, c), [PART, CH, 4], BF16) for c in range(2)] for a in range(2)]
-        h_w = [[kept("h_w%d%d" % (a, c), [PART, CH], U32) for c in range(2)] for a in range(2)]
-        h_s = [[kept("h_s%d%d" % (a, c), [PART, CH], U8) for c in range(2)] for a in range(2)]
+        def quantize_wsub1(a):
+            quantize(wsub1_w[a], wsub1_s[a], wsub1_b[a])
+
+        def quantize_wspin(a):
+            quantize(wspin_w[a], wspin_s[a], wspin_b[a])
+
+        cos_t = [kept("cos%d" % j, [PART, P], F32) for j in range(ROW_TILES)]
+        sin_t = [kept("sin%d" % j, [PART, P], F32) for j in range(ROW_TILES)]
+        cos_b1 = [kept("cos_b1_%d" % a, [PART, 4, P], F32) for a in range(2)]
+        sin_b2 = [kept("sin_b2_%d" % a, [PART, 4, P], F32) for a in range(2)]
+        h_b = [[kept("h_b%d%d" % (a, c), [PART, w, 4], BF16) for c, (m0, w) in enumerate(PIECES[a])] for a in range(2)]
+        h_w = [[kept("h_w%d%d" % (a, c), [PART, w], U32) for c, (m0, w) in enumerate(PIECES[a])] for a in range(2)]
+        h_s = [[kept("h_s%d%d" % (a, c), [PART, w], U8) for c, (m0, w) in enumerate(PIECES[a])] for a in range(2)]
 
         def trig(j):
             ang = ring.tile([PART, P], F32, name="ang", tag="ang")
@@ -223,14 +236,14 @@ def tile_list_halo_spin_orientation_kernel(
         def products(j):
             a, t = divmod(j, 4)
             for w_codes, w_scales, factor, dst in (
-                (wsub2_w[:, 512 * a : 512 * (a + 1)], wsub2_s[:, 128 * a : 128 * (a + 1)].bitcast(U8), sin_t[j], t2[a]),
-                (wsub1_w[a][:], wsub1_s[a][:], cos_t[j], t1[a]),
+                (wsub2_w[:, BANK * a : BANK * (a + 1)], wsub2_s[:, PART * a : PART * (a + 1)].bitcast(U8), sin_t[j], sin_b2[a]),
+                (wsub1_w[a][:], wsub1_s[a][:], cos_t[j], cos_b1[a]),
             ):
                 bank = proj.tile([PART, P], F32, name="b", tag="b")
                 nc.tensor.matmul_mx(
                     out=bank[:],
-                    lhsT=w_codes[:, 128 * t : 128 * (t + 1)].bitcast(FP8X4),
-                    lhsT_scale=w_scales[:, 128 * t : 128 * (t + 1)],
+                    lhsT=w_codes[:, PART * t : PART * (t + 1)].bitcast(FP8X4),
+                    lhsT_scale=w_scales[:, PART * t : PART * (t + 1)],
                     rhs=v2_w[:].bitcast(FP8X4),
                     rhs_scale=v2_s[:],
                     start=True,
@@ -239,11 +252,11 @@ def tile_list_halo_spin_orientation_kernel(
                 nc.vector.tensor_tensor(dst[:, t, :], bank[:], factor[:], ALU.mult)
 
         def mix(a, c):
-            cols = slice(CH * c, CH * (c + 1))
+            m0, w = PIECES[a][c]
             nc.vector.tensor_tensor(
-                h_b[a][c][:].rearrange("p (u i) t -> p u t i", i=4),
-                t1[a][:, :, cols].rearrange("p t (u i) -> p u t i", i=4),
-                t2[a][:, :, cols].rearrange("p t (u i) -> p u t i", i=4),
+                h_b[a][c][:].rearrange("p (u e) t -> p u t e", e=4),
+                cos_b1[a][:, :, m0 : m0 + w].rearrange("p t (u e) -> p u t e", e=4),
+                sin_b2[a][:, :, m0 : m0 + w].rearrange("p t (u e) -> p u t e", e=4),
                 ALU.add,
             )
 
@@ -251,74 +264,84 @@ def tile_list_halo_spin_orientation_kernel(
             quantize(h_w[a][c], h_s[a][c], h_b[a][c])
 
         out_banks = {}
+        last_piece = len(PIECES[1]) - 1
 
         def spin(a, c):
-            for g in range(2):
-                if a == 0:
-                    out_banks[c, g] = acc.tile([PART, 2, CH], F32, name="bank", tag="bank")
-                for d in range(2):
-                    n = 2 * g + d
+            m0, w = PIECES[1][c]
+            piece, off = (c, 0) if a == 1 else divmod(m0, PIECES[0][0][1])
+            tiles = TILES_PER_BANK[c]
+            for b in range(4 // tiles):
+                if a == 0 and c < last_piece:
+                    out_banks[c, b] = acc.tile([PART, tiles, w], F32, name="bank", tag="bank")
+                elif a == 0:
+                    out_banks[c, b] = proj.tile([PART, tiles, w], F32, name="b", tag="b")
+                for d in range(tiles):
+                    rows = slice(PART * (tiles * b + d), PART * (tiles * b + d + 1))
                     nc.tensor.matmul_mx(
-                        out=out_banks[c, g][:, d, :],
-                        lhsT=wspin_w[a][:, 128 * n : 128 * (n + 1)].bitcast(FP8X4),
-                        lhsT_scale=wspin_s[a][:, 128 * n : 128 * (n + 1)],
-                        rhs=h_w[a][c][:].bitcast(FP8X4),
-                        rhs_scale=h_s[a][c][:],
+                        out=out_banks[c, b][:, d, :],
+                        lhsT=wspin_w[a][:, rows].bitcast(FP8X4),
+                        lhsT_scale=wspin_s[a][:, rows],
+                        rhs=h_w[a][piece][:, off : off + w].bitcast(FP8X4),
+                        rhs_scale=h_s[a][piece][:, off : off + w],
                         start=(a == 0 and d == 0),
-                        stop=(a == 1 and d == 1),
+                        stop=(a == 1 and d == tiles - 1),
                     )
 
         out_v = out.rearrange("(n p) m -> p n m", p=PART)
 
         def store(c):
-            for g in range(2):
-                res = kept("res%d%d" % (c, g), [PART, 2, CH], F32)
-                if g == 0 or c == 0:
-                    nc.scalar.copy(res[:], out_banks[c, g][:])
+            m0, w = PIECES[1][c]
+            tiles = TILES_PER_BANK[c]
+            for b in range(4 // tiles):
+                res = kept("res%d%d" % (c, b), [PART, tiles, w], F32)
+                if b == 0 or c < last_piece:
+                    nc.scalar.copy(res[:], out_banks[c, b][:])
                 else:
-                    nc.vector.tensor_copy(res[:], out_banks[c, g][:])
-                nc.sync.dma_start(out_v[:, 2 * g : 2 * g + 2, CH * c : CH * (c + 1)], res[:])
+                    nc.vector.tensor_copy(res[:], out_banks[c, b][:])
+                nc.sync.dma_start(out_v[:, tiles * b : tiles * (b + 1), m0 : m0 + w], res[:])
 
-        angles(0, 0)
-        angles(1, 0)
-        angles(0, 1)
-        angles(1, 1)
+        for half in range(2):
+            angles(0, half)
+            angles(1, half)
         cast_wsub1(0)
         load_wspin(0)
         trig(0)
-        quantize(wsub1_w[0], wsub1_s[0], wsub1_b[0])
+        quantize_wsub1(0)
         second_table()
         load_wsub1(1)
         load_wspin(1)
-        for j in range(1, 7):
+
+        group_0 = range(len(PIECES[0]))
+        after_step = {
+            2: lambda: cast_wsub1(1),
+            3: lambda: (quantize_wsub1(1), cast_wspin(0)),
+            4: lambda: [mix(0, c) for c in group_0],
+            5: lambda: ([quantize_h(0, c) for c in group_0], quantize_wspin(0)),
+        }
+        last = ROW_TILES - 1
+        for j in range(1, last):
             angles(j + 1, 0)
             angles(j + 1, 1)
             trig(j)
             products(j - 1)
-            if j == 2:
-                cast_wsub1(1)
-            if j == 3:
-                quantize(wsub1_w[1], wsub1_s[1], wsub1_b[1])
-                cast_wspin(0)
-            if j == 4:
-                mix(0, 0)
-                mix(0, 1)
-            if j == 5:
-                quantize_h(0, 0)
-                quantize_h(0, 1)
-                quantize(wspin_w[0], wspin_s[0], wspin_b[0])
-        trig(7)
+            if j in after_step:
+                after_step[j]()
+
+        trig(last)
         cast_wspin(1)
-        products(6)
+        products(last - 1)
         spin(0, 0)
         spin(0, 1)
-        products(7)
+        products(last)
+        spin(0, last_piece)
         mix(1, 0)
-        quantize(wspin_w[1], wspin_s[1], wspin_b[1])
+        quantize_wspin(1)
         quantize_h(1, 0)
         mix(1, 1)
         spin(1, 0)
         store(0)
-        quantize_h(1, 1)
-        spin(1, 1)
-        store(1)
+        mix(1, 2)
+        for c in (1, 2):
+            quantize_h(1, c)
+            spin(1, c)
+            store(c)

@@ -25,10 +25,9 @@ ROW_TILES = H // PART
 TAB_ROW = 24
 PLANE_ROWS = 100
 BIAS_ROW = PART - ROW_TILES
-VECTOR_CAST_TILES = 3
-PIECES = ([(0, 256), (256, 256)], [(0, 256), (256, 128), (384, 128)])
+VECTOR_CAST_TILES = 4
+PIECES = ([(0, 512)], [(0, 256), (256, 128), (384, 128)])
 TILES_PER_BANK = (2, 4, 2)
-AT_WSUB1, AT_V2_WORDS, AT_V2_SCALES, AT_WSUB2_SCALES, AT_WSUB2_WORDS = 0, 4096, 6144, 6656, 7680
 
 
 def tile_list_halo_spin_orientation_kernel(
@@ -40,16 +39,12 @@ def tile_list_halo_spin_orientation_kernel(
     with ExitStack() as ctx:
         lists = ctx.enter_context(tc.tile_pool(name="lists", bufs=1))
         keep = ctx.enter_context(tc.tile_pool(name="keep", bufs=1))
-        reuse = ctx.enter_context(tc.tile_pool(name="reuse", bufs=1))
-        ring = ctx.enter_context(tc.tile_pool(name="ring", bufs=3))
+        ring = ctx.enter_context(tc.tile_pool(name="ring", bufs=4))
         acc = ctx.enter_context(tc.psum_pool(name="acc", bufs=4))
         proj = ctx.enter_context(tc.psum_pool(name="proj", bufs=4))
 
         def kept(name, shape, dtype, tag=None):
             return keep.tile(shape, dtype, name=name, tag=tag or name, align_bytes=64)
-
-        def reused(name, shape, dtype, offset):
-            return reuse.tile(shape, dtype, name=name, offset=offset, align_bytes=64)
 
         def words(packed):
             return packed.rearrange("p c i -> p (c i)").bitcast(I32)
@@ -69,22 +64,35 @@ def tile_list_halo_spin_orientation_kernel(
         offs2_t = lists.tile([PART, P // 16], U16, name="offs2_t")
 
         tab_s = kept("tab_s", [PART, T], U8)
-        w_s = kept("w_s", [PART, H // 2], I32)
+        wang_s_raw = kept("wang_s_raw", [PART, H // 2], I32)
+        tab2_s = kept("tab2_s", [PART, T2], U8)
+        wsub2_s_raw = kept("wsub2_s_raw", [PART, H // 4], I32)
         v_sg = kept("v_sg", [PART, S], U8)
         v_s = [kept("v_s%d" % g, [PART, S], U8) for g in range(2)]
         bias_rows = kept("bias_rows", [PART, PART], F32)
         ident = kept("ident", [PART, PART], F32)
+        nc.gpsimd.memset(wang_s_raw[:], 0)
+        make_identity(nc, ident[:])
         for quad in range(QUADS):
             nc.vector.memset(tab_s[32 * quad : 32 * quad + TAB_ROW, :].bitcast(I32), 0)
-        nc.gpsimd.memset(w_s[:], 0)
-        nc.gpsimd.memset(bias_rows[0:96, :], 0.0)
-        nc.gpsimd.memset(bias_rows[96:BIAS_ROW, :], 0.0)
-        make_identity(nc, ident[:])
+        nc.vector.memset(tab2_s[:].bitcast(I32), 0)
+        nc.vector.memset(wsub2_s_raw[:], 0)
+        for a in range(2):
+            nc.gpsimd.dma_start(
+                bias_rows[BIAS_ROW + 4 * a : BIAS_ROW + 4 * a + 4, :].rearrange("t (q i) -> t q i", i=8),
+                bang[BANK * a : BANK * (a + 1)].rearrange("(q t i) -> t q i", t=4, i=8),
+            )
+        nc.vector.memset(bias_rows[0:96, :], 0.0)
+        nc.vector.memset(bias_rows[96:BIAS_ROW, :], 0.0)
         warm = kept("warm", [PART, 16], F32)
         nc.scalar.activation(warm[0:96, 0:1], bias_rows[0:96, 0:1], ACT.Sin)
 
-        tab_w = [kept("tab_w0", [PART, T], I32, tag="stage_a"), reused("tab_w1", [PART, T], I32, 0)]
-        wang_raw = kept("wang_raw", [PART, 2, H // 2], I32, tag="stage_b")
+        tab_w = [kept("tab_w%d" % g, [PART, T], I32, tag="stage%d" % g) for g in range(2)]
+        wang_raw = kept("wang_raw", [PART, 2, H // 2], I32)
+        tab2_w = kept("tab2_w", [PART, T2], I32)
+        wsub2_raw = kept("wsub2_raw", [PART, H], I32)
+        wsub1_v = wsub1.rearrange("(p j) c -> p j c", j=4)
+        wsub1_raw = [kept("wsub1_raw%d" % a, [PART, 4, BANK], F32) for a in range(2)]
         nc.sync.dma_start(offs_t[:], offs)
         for quad in range(QUADS):
             nc.sync.dma_start(
@@ -93,29 +101,28 @@ def tile_list_halo_spin_orientation_kernel(
             )
         nc.sync.dma_start(tab_w[0][:], words(tab_words[0]))
         nc.sync.dma_start(wang_raw[:], wang_words.rearrange("g p c -> p g c").bitcast(I32))
-        nc.sync.dma_start(offs2_t[:], offs2)
         for quad in range(QUADS):
             nc.sync.dma_start(
-                w_s[32 * quad : 32 * quad + 4, :].rearrange("s (g c) -> s g c", g=2),
+                wang_s_raw[32 * quad : 32 * quad + 4, :].rearrange("s (g c) -> s g c", g=2),
                 wang_scales[:, 4 * quad : 4 * quad + 4, :].rearrange("g s c -> s g c").bitcast(I32),
             )
         nc.sync.dma_start(tab_w[1][:], words(tab_words[1]))
-        nc.sync.dma_start(pos_t[:], pos1)
-        for a in range(2):
-            nc.sync.dma_start(
-                bias_rows[BIAS_ROW + 4 * a : BIAS_ROW + 4 * a + 4, :].rearrange("t (q i) -> t q i", i=8),
-                bang[BANK * a : BANK * (a + 1)].rearrange("(q t i) -> t q i", t=4, i=8),
-            )
+        nc.sync.dma_start(offs2_t[:], offs2)
 
         nc.vector.tensor_copy(v_sg[:], tab_s[:].indirect(offs_t[:]))
         for g in range(2):
             first = TAB_ROW + 4 * g
-            nc.sync.dma_start(v_s[g][0:PLANE_ROWS, :].bitcast(I32), v_sg[first : first + PLANE_ROWS, :].bitcast(I32))
-        tab2_s = kept("tab2_s", [PART, T2], U8, tag="tab_s")
-        nc.vector.memset(tab2_s[:].bitcast(I32), 0)
-        load_plane(tab2_s[:].bitcast(I32), tab2_scales[0])
+            nc.scalar.dma_start(v_s[g][0:PLANE_ROWS, :].bitcast(I32), v_sg[first : first + PLANE_ROWS, :].bitcast(I32))
 
-        bias_ps = acc.tile([PART, BANK], F32, name="bank", tag="bank")
+        nc.sync.dma_start(tab2_w[:], words(tab2_words[0]))
+        load_plane(tab2_s[:].bitcast(I32), tab2_scales[0])
+        nc.sync.dma_start(wsub1_raw[0][:], wsub1_v[:, :, 0:BANK])
+        nc.sync.dma_start(pos_t[:], pos1)
+        nc.sync.dma_start(wsub2_raw[:], words(wsub2_words[0]))
+        load_plane(wsub2_s_raw[:], wsub2_scales[0])
+        nc.sync.dma_start(wsub1_raw[1][:], wsub1_v[:, :, BANK : 2 * BANK])
+
+        bias_ps = proj.tile([PART, BANK], F32, name="b", tag="b")
         nc.tensor.transpose(bias_ps[:, 0:PART], bias_rows[:], ident[:])
         bias = kept("bias", [PART, ROW_TILES], F32)
         nc.scalar.copy(bias[:], bias_ps[:, BIAS_ROW:PART])
@@ -126,88 +133,77 @@ def tile_list_halo_spin_orientation_kernel(
             picks = offs_t[:, 32 * half : 32 * (half + 1)]
             nc.vector.tensor_copy(v_w[g][half][:], tab_w[g][:].bitcast(U32).indirect(picks))
 
-        wsub1_v = wsub1.rearrange("(p j) c -> p j c", j=4)
-        wsub1_raw = []
-
-        def load_wsub1(a):
-            wsub1_raw.append(kept("wsub1_raw%d" % a, [PART, 4, BANK], F32, tag=("stage_b", "v_sg")[a]))
-            nc.sync.dma_start(wsub1_raw[a][:], wsub1_v[:, :, BANK * a : BANK * (a + 1)])
-
-        wspin_v = wspin.rearrange("(a q t i) n -> a t q i n", a=2, t=4, i=8)
-        wspin_raw = []
-
-        def load_wspin(a):
-            wspin_raw.append(kept("wspin_raw%d" % a, [PART, 4, N], F32, tag=("stage_b", "stage_a")[a]))
-            for t in range(4):
-                nc.sync.dma_start(wspin_raw[a][:, t, :], wspin_v[a, t])
-
-        gather_v(0, 0)
         wang_w = kept("wang_w", [PART, 2, H // 2], I32)
-        order_columns(wang_w[:].rearrange("p g c -> p (g c)"), wang_raw[:].rearrange("p g c -> p (g c)"), 4)
-        load_wsub1(0)
-        gather_v(0, 1)
-        tab2_w = kept("tab2_w", [PART, T2], I32, tag="stage_a")
-        nc.sync.dma_start(tab2_w[:], words(tab2_words[0]))
-        wsub2_raw = kept("wsub2_raw", [PART, H], I32, tag="v_sg")
-        nc.sync.dma_start(wsub2_raw[:], words(wsub2_words[0]))
         wang_s = kept("wang_s", [PART, 2, H // 4], I32)
-        order_columns(wang_s[:].rearrange("p g c -> p (g c)"), w_s[:], 2)
-        load_plane(w_s[:, 0 : H // 4], wsub2_scales[0])
+        gather_v(0, 0)
+        gather_v(0, 1)
+        order_columns(wang_w[:].rearrange("p g c -> p (g c)"), wang_raw[:].rearrange("p g c -> p (g c)"), 4)
+        order_columns(wang_s[:].rearrange("p g c -> p (g c)"), wang_s_raw[:], 2)
         gather_v(1, 0)
         gather_v(1, 1)
+
+        wspin_v = wspin.rearrange("(a q t i) n -> a t q i n", a=2, t=4, i=8)
+        wspin_raw = [kept("wspin_raw%d" % a, [PART, 4, N], F32, tag="stage%d" % a) for a in range(2)]
+        for a in range(2):
+            for t in range(4):
+                nc.sync.dma_start(wspin_raw[a][:, t, :], wspin_v[a, t])
 
         th = [None] * ROW_TILES
 
         def angles(j, half):
             if th[j] is None:
-                th[j] = ring.tile([PART, S], F32, name="th", tag="th")
+                th[j] = kept("th%d" % j, [PART, S], F32, tag="th%d" % (j % 8))
             cols = slice(BANK * half, BANK * (half + 1))
             bank = acc.tile([PART, BANK], F32, name="bank", tag="bank")
-            for g in range(2):
+            for g in (1, 0):
                 nc.tensor.matmul_mx(
                     out=bank[:],
                     lhsT=wang_w[:, g, 64 * j : 64 * (j + 1)].bitcast(FP4X4),
                     lhsT_scale=wang_s[:, g, 32 * j : 32 * (j + 1)].bitcast(U8),
                     rhs=v_w[g][half][:].bitcast(FP8X4),
                     rhs_scale=v_s[g][:, cols],
-                    start=(g == 0),
-                    stop=(g == 1),
+                    start=(g == 1),
+                    stop=(g == 0),
                 )
             nc.scalar.activation(th[j][:, cols], bank[:], ACT.Identity, bias=bias[:, j : j + 1])
 
-        v2_w = reused("v2_w", [PART, P], U32, AT_V2_WORDS)
-        v2_s = reused("v2_s", [PART, P], U8, AT_V2_SCALES)
-        wsub2_w = reused("wsub2_w", [PART, H], I32, AT_WSUB2_WORDS)
-        wsub2_s = reused("wsub2_s", [PART, H // 4], I32, AT_WSUB2_SCALES)
-        wsub1_b = [reused("wsub1_b0", [PART, BANK, 4], BF16, AT_WSUB1), kept("wsub1_b1", [PART, BANK, 4], BF16)]
+        def both(j):
+            angles(j, 0)
+            angles(j, 1)
+
+        v2_w = kept("v2_w", [PART, P], U32)
+        v2_s = kept("v2_s", [PART, P], U8)
+        wsub2_w = kept("wsub2_w", [PART, H], I32)
+        wsub2_s = kept("wsub2_s", [PART, H // 4], I32)
+        wsub1_b = [kept("wsub1_b%d" % a, [PART, BANK, 4], BF16) for a in range(2)]
         wsub1_w = [kept("wsub1_w%d" % a, [PART, BANK], U32) for a in range(2)]
         wsub1_s = [kept("wsub1_s%d" % a, [PART, BANK], U8) for a in range(2)]
-        wspin_b = [kept("wspin_b%d" % a, [PART, N, 4], BF16) for a in range(2)]
+        wspin_b = [None, None]
         wspin_w = [kept("wspin_w%d" % a, [PART, N], U32) for a in range(2)]
         wspin_s = [kept("wspin_s%d" % a, [PART, N], U8) for a in range(2)]
 
-        def second_table():
+        def second_gathers():
             nc.vector.tensor_copy(v2_w[:], tab2_w[:].bitcast(U32).indirect(offs2_t[:]))
             nc.vector.tensor_copy(v2_s[:], tab2_s[:].indirect(offs2_t[:]))
+
+        def second_weights():
             order_columns(wsub2_w[:], wsub2_raw[:], 8)
-            order_columns(wsub2_s[:], w_s[:, 0 : H // 4], 2)
+            order_columns(wsub2_s[:], wsub2_s_raw[:], 2)
 
-        def cast_wsub1(a):
-            for t in range(4):
-                dst = wsub1_b[a][:, PART * t : PART * (t + 1), :].rearrange("p (q u e) j -> p q u j e", u=2, e=4)
-                src = wsub1_raw[a][:].rearrange("p j (q t u e) -> p t q u j e", t=4, u=2, e=4)[:, t]
-                if a == 0 and t < VECTOR_CAST_TILES:
-                    nc.vector.tensor_copy(out=dst, in_=src)
-                else:
-                    nc.scalar.copy(out=dst, in_=src)
+        def cast_wsub1(a, first, count, engine):
+            engine(
+                out=wsub1_b[a][:].rearrange("p (t q i) j -> p t q j i", t=4, i=8)[:, first : first + count],
+                in_=wsub1_raw[a][:].rearrange("p j (q t i) -> p t q j i", t=4, i=8)[:, first : first + count],
+            )
 
-        def cast_wspin(a):
-            for n in range(4):
-                cols = slice(PART * n, PART * (n + 1))
-                nc.scalar.copy(
-                    out=wspin_b[a][:, cols, :].rearrange("p (u e) t -> p u t e", e=4),
-                    in_=wspin_raw[a][:, :, cols].rearrange("p t (u e) -> p u t e", e=4),
-                )
+        def cast_wspin(a, first, count, engine):
+            if wspin_b[a] is None:
+                wspin_b[a] = kept("wspin_b%d" % a, [PART, N, 4], BF16, tag="th%d" % ((ROW_TILES - 2 + a) % 8))
+            cols = slice(first, first + count)
+            engine(
+                out=wspin_b[a][:, cols, :].rearrange("p (u e) t -> p u t e", e=4),
+                in_=wspin_raw[a][:, :, cols].rearrange("p t (u e) -> p u t e", e=4),
+            )
 
         def quantize(codes, scales, values):
             nc.vector.quantize_mx(out=codes[:].bitcast(FP8X4), scales=scales[:], in_=values[:].rearrange("p c j -> p (c j)"))
@@ -218,19 +214,24 @@ def tile_list_halo_spin_orientation_kernel(
         def quantize_wspin(a):
             quantize(wspin_w[a], wspin_s[a], wspin_b[a])
 
-        cos_t = [kept("cos%d" % j, [PART, P], F32) for j in range(ROW_TILES)]
-        sin_t = [kept("sin%d" % j, [PART, P], F32) for j in range(ROW_TILES)]
+        angs = [None] * ROW_TILES
+        cos_t = [None] * ROW_TILES
+        sin_t = [None] * ROW_TILES
         cos_b1 = [kept("cos_b1_%d" % a, [PART, 4, P], F32) for a in range(2)]
         sin_b2 = [kept("sin_b2_%d" % a, [PART, 4, P], F32) for a in range(2)]
         h_b = [[kept("h_b%d%d" % (a, c), [PART, w, 4], BF16) for c, (m0, w) in enumerate(PIECES[a])] for a in range(2)]
         h_w = [[kept("h_w%d%d" % (a, c), [PART, w], U32) for c, (m0, w) in enumerate(PIECES[a])] for a in range(2)]
         h_s = [[kept("h_s%d%d" % (a, c), [PART, w], U8) for c, (m0, w) in enumerate(PIECES[a])] for a in range(2)]
 
+        def pick(j):
+            angs[j] = kept("ang%d" % j, [PART, P], F32)
+            nc.vector.tensor_copy(angs[j][:], th[j][:].indirect(pos_t[:]))
+
         def trig(j):
-            ang = ring.tile([PART, P], F32, name="ang", tag="ang")
-            nc.vector.tensor_copy(ang[:], th[j][:].indirect(pos_t[:]))
-            nc.scalar.activation(cos_t[j][:], ang[:], ACT.Abs)
-            nc.scalar.activation(sin_t[j][:], ang[:], ACT.Sin)
+            cos_t[j] = ring.tile([PART, P], F32, name="cos", tag="cos")
+            sin_t[j] = ring.tile([PART, P], F32, name="sin", tag="sin")
+            nc.scalar.activation(sin_t[j][:], angs[j][:], ACT.Sin)
+            nc.scalar.activation(cos_t[j][:], angs[j][:], ACT.Abs)
             nc.scalar.activation(cos_t[j][:], cos_t[j][:], ACT.Sin, bias=math.pi / 2, scale=-1.0)
 
         def products(j):
@@ -300,44 +301,58 @@ def tile_list_halo_spin_orientation_kernel(
                     nc.vector.tensor_copy(res[:], out_banks[c, b][:])
                 nc.sync.dma_start(out_v[:, tiles * b : tiles * (b + 1), m0 : m0 + w], res[:])
 
+        on_vector, on_scalar = nc.vector.tensor_copy, nc.scalar.copy
         for half in range(2):
             angles(0, half)
             angles(1, half)
-        cast_wsub1(0)
-        load_wspin(0)
+        second_gathers()
+        pick(0)
+        both(2)
+        cast_wsub1(0, 0, 4, on_vector)
+        both(3)
         trig(0)
+        pick(1)
+        second_weights()
+        pick(2)
         quantize_wsub1(0)
-        second_table()
-        load_wsub1(1)
-        load_wspin(1)
-
-        group_0 = range(len(PIECES[0]))
-        after_step = {
-            2: lambda: cast_wsub1(1),
-            3: lambda: (quantize_wsub1(1), cast_wspin(0)),
-            4: lambda: [mix(0, c) for c in group_0],
-            5: lambda: ([quantize_h(0, c) for c in group_0], quantize_wspin(0)),
-        }
-        last = ROW_TILES - 1
-        for j in range(1, last):
-            angles(j + 1, 0)
-            angles(j + 1, 1)
-            trig(j)
-            products(j - 1)
-            if j in after_step:
-                after_step[j]()
-
-        trig(last)
-        cast_wspin(1)
-        products(last - 1)
+        both(4)
+        trig(1)
+        pick(3)
+        products(0)
+        both(5)
+        trig(2)
+        pick(4)
+        products(1)
+        both(6)
+        trig(3)
+        pick(5)
+        products(2)
+        both(7)
+        cast_wsub1(1, 0, 4, on_scalar)
+        trig(4)
+        pick(6)
+        products(3)
+        quantize_wsub1(1)
+        trig(5)
+        pick(7)
+        products(4)
+        trig(6)
+        mix(0, 0)
+        trig(7)
+        cast_wspin(0, 0, 512, on_scalar)
+        cast_wspin(1, 0, 512, on_scalar)
+        products(5)
+        quantize_h(0, 0)
+        products(6)
+        quantize_wspin(0)
+        products(7)
         spin(0, 0)
         spin(0, 1)
-        products(last)
         spin(0, last_piece)
         mix(1, 0)
         quantize_wspin(1)
-        quantize_h(1, 0)
         mix(1, 1)
+        quantize_h(1, 0)
         spin(1, 0)
         store(0)
         mix(1, 2)

@@ -26,8 +26,9 @@ TAB_ROW = 24
 PLANE_ROWS = 100
 BIAS_ROW = PART - ROW_TILES
 VECTOR_CAST_TILES = 4
-PIECES = ([(0, 512)], [(0, 256), (256, 128), (384, 128)])
+PIECES = ([(0, 384), (384, 128)], [(0, 256), (256, 128), (384, 128)])
 TILES_PER_BANK = (2, 4, 2)
+UNITS = ((0, 1), (2, 3), (4, 5), (6,), (7,))
 
 
 def tile_list_halo_spin_orientation_kernel(
@@ -40,6 +41,7 @@ def tile_list_halo_spin_orientation_kernel(
         lists = ctx.enter_context(tc.tile_pool(name="lists", bufs=1))
         keep = ctx.enter_context(tc.tile_pool(name="keep", bufs=1))
         ring = ctx.enter_context(tc.tile_pool(name="ring", bufs=4))
+        reuse = ctx.enter_context(tc.tile_pool(name="reuse", bufs=1))
         acc = ctx.enter_context(tc.psum_pool(name="acc", bufs=4))
         proj = ctx.enter_context(tc.psum_pool(name="proj", bufs=4))
 
@@ -66,7 +68,7 @@ def tile_list_halo_spin_orientation_kernel(
         tab_s = kept("tab_s", [PART, T], U8)
         wang_s_raw = kept("wang_s_raw", [PART, H // 2], I32)
         tab2_s = kept("tab2_s", [PART, T2], U8)
-        wsub2_s_raw = kept("wsub2_s_raw", [PART, H // 4], I32)
+        wsub2_s_raw = reuse.tile([PART, H // 4], I32, name="wsub2_s_raw", offset=4096, align_bytes=64)
         v_sg = kept("v_sg", [PART, S], U8)
         v_s = [kept("v_s%d" % g, [PART, S], U8) for g in range(2)]
         bias_rows = kept("bias_rows", [PART, PART], F32)
@@ -115,9 +117,9 @@ def tile_list_halo_spin_orientation_kernel(
             nc.scalar.dma_start(v_s[g][0:PLANE_ROWS, :].bitcast(I32), v_sg[first : first + PLANE_ROWS, :].bitcast(I32))
 
         nc.sync.dma_start(tab2_w[:], words(tab2_words[0]))
-        load_plane(tab2_s[:].bitcast(I32), tab2_scales[0])
-        nc.sync.dma_start(wsub1_raw[0][:], wsub1_v[:, :, 0:BANK])
         nc.sync.dma_start(pos_t[:], pos1)
+        nc.sync.dma_start(wsub1_raw[0][:], wsub1_v[:, :, 0:BANK])
+        load_plane(tab2_s[:].bitcast(I32), tab2_scales[0])
         nc.sync.dma_start(wsub2_raw[:], words(wsub2_words[0]))
         load_plane(wsub2_s_raw[:], wsub2_scales[0])
         nc.sync.dma_start(wsub1_raw[1][:], wsub1_v[:, :, BANK : 2 * BANK])
@@ -152,7 +154,10 @@ def tile_list_halo_spin_orientation_kernel(
 
         def angles(j, half):
             if th[j] is None:
-                th[j] = kept("th%d" % j, [PART, S], F32, tag="th%d" % (j % 8))
+                if j == 3:
+                    th[j] = reuse.tile([PART, S], F32, name="th3", offset=0, align_bytes=64)
+                else:
+                    th[j] = kept("th%d" % j, [PART, S], F32)
             cols = slice(BANK * half, BANK * (half + 1))
             bank = acc.tile([PART, BANK], F32, name="bank", tag="bank")
             for g in (1, 0):
@@ -175,9 +180,10 @@ def tile_list_halo_spin_orientation_kernel(
         v2_s = kept("v2_s", [PART, P], U8)
         wsub2_w = kept("wsub2_w", [PART, H], I32)
         wsub2_s = kept("wsub2_s", [PART, H // 4], I32)
-        wsub1_b = [kept("wsub1_b%d" % a, [PART, BANK, 4], BF16) for a in range(2)]
-        wsub1_w = [kept("wsub1_w%d" % a, [PART, BANK], U32) for a in range(2)]
-        wsub1_s = [kept("wsub1_s%d" % a, [PART, BANK], U8) for a in range(2)]
+        wsub1_b0 = reuse.tile([PART, BANK, 4], BF16, name="wsub1_b0", offset=5120, align_bytes=64)
+        wsub1_b1 = [None, None]
+        wsub1_w = [kept("wsub1_w0", [PART, BANK], U32), None, None]
+        wsub1_s = [kept("wsub1_s0", [PART, BANK], U8), None, None]
         wspin_b = [None, None]
         wspin_w = [kept("wspin_w%d" % a, [PART, N], U32) for a in range(2)]
         wspin_s = [kept("wspin_s%d" % a, [PART, N], U8) for a in range(2)]
@@ -190,15 +196,32 @@ def tile_list_halo_spin_orientation_kernel(
             order_columns(wsub2_w[:], wsub2_raw[:], 8)
             order_columns(wsub2_s[:], wsub2_s_raw[:], 2)
 
-        def cast_wsub1(a, first, count, engine):
-            engine(
-                out=wsub1_b[a][:].rearrange("p (t q i) j -> p t q j i", t=4, i=8)[:, first : first + count],
-                in_=wsub1_raw[a][:].rearrange("p j (q t i) -> p t q j i", t=4, i=8)[:, first : first + count],
+        def cast_wsub1_first():
+            nc.vector.tensor_copy(
+                wsub1_b0[:].rearrange("p (t q i) j -> p t q j i", t=4, i=8),
+                wsub1_raw[0][:].rearrange("p j (q t i) -> p t q j i", t=4, i=8),
             )
+
+        def cast_wsub1_second(half):
+            if half == 0:
+                wsub1_b1[0] = reuse.tile([PART, 256, 4], BF16, name="wsub1_b10", offset=4096 - 512, align_bytes=64)
+            else:
+                wsub1_b1[1] = kept("wsub1_b11", [PART, 256, 4], BF16, tag="th5")
+            for d in range(2):
+                nc.gpsimd.tensor_scalar(
+                    wsub1_b1[half][:, PART * d : PART * (d + 1), :].rearrange("p (q i) j -> p q i j", i=8),
+                    wsub1_raw[1][:].rearrange("p j (q t i) -> p t q i j", t=4, i=8)[:, 2 * half + d],
+                    1.0, 0.0, ALU.mult, ALU.add,
+                )
+
+        def quantize_wsub1_second(half):
+            wsub1_w[1 + half] = kept("wsub1_w1%d" % half, [PART, 256], U32, tag="cos%d" % (2 * half))
+            wsub1_s[1 + half] = kept("wsub1_s1%d" % half, [PART, 256], U8)
+            quantize(wsub1_w[1 + half], wsub1_s[1 + half], wsub1_b1[half])
 
         def cast_wspin(a, first, count, engine):
             if wspin_b[a] is None:
-                wspin_b[a] = kept("wspin_b%d" % a, [PART, N, 4], BF16, tag="th%d" % ((ROW_TILES - 2 + a) % 8))
+                wspin_b[a] = kept("wspin_b%d" % a, [PART, N, 4], BF16, tag=("th6", "ang7")[a])
             cols = slice(first, first + count)
             engine(
                 out=wspin_b[a][:, cols, :].rearrange("p (u e) t -> p u t e", e=4),
@@ -208,60 +231,66 @@ def tile_list_halo_spin_orientation_kernel(
         def quantize(codes, scales, values):
             nc.vector.quantize_mx(out=codes[:].bitcast(FP8X4), scales=scales[:], in_=values[:].rearrange("p c j -> p (c j)"))
 
-        def quantize_wsub1(a):
-            quantize(wsub1_w[a], wsub1_s[a], wsub1_b[a])
+        def quantize_wsub1_first():
+            quantize(wsub1_w[0], wsub1_s[0], wsub1_b0)
 
         def quantize_wspin(a):
             quantize(wspin_w[a], wspin_s[a], wspin_b[a])
 
-        angs = [None] * ROW_TILES
-        cos_t = [None] * ROW_TILES
-        sin_t = [None] * ROW_TILES
         cos_b1 = [kept("cos_b1_%d" % a, [PART, 4, P], F32) for a in range(2)]
         sin_b2 = [kept("sin_b2_%d" % a, [PART, 4, P], F32) for a in range(2)]
-        h_b = [[kept("h_b%d%d" % (a, c), [PART, w, 4], BF16) for c, (m0, w) in enumerate(PIECES[a])] for a in range(2)]
-        h_w = [[kept("h_w%d%d" % (a, c), [PART, w], U32) for c, (m0, w) in enumerate(PIECES[a])] for a in range(2)]
+        h_b = [[None] * len(PIECES[a]) for a in range(2)]
+        h_w = [[None] * len(PIECES[a]) for a in range(2)]
         h_s = [[kept("h_s%d%d" % (a, c), [PART, w], U8) for c, (m0, w) in enumerate(PIECES[a])] for a in range(2)]
+        units = {j: unit for unit in UNITS for j in unit}
+        ang, cos, sin = {}, {}, {}
 
         def pick(j):
-            angs[j] = kept("ang%d" % j, [PART, P], F32)
-            nc.vector.tensor_copy(angs[j][:], th[j][:].indirect(pos_t[:]))
+            unit = units[j]
+            if unit not in ang:
+                ang[unit] = kept("ang%d" % unit[0], [PART, len(unit), P], F32)
+            nc.vector.tensor_copy(ang[unit][:, j - unit[0], :], th[j][:].indirect(pos_t[:]))
 
-        def trig(j):
-            cos_t[j] = ring.tile([PART, P], F32, name="cos", tag="cos")
-            sin_t[j] = ring.tile([PART, P], F32, name="sin", tag="sin")
-            nc.scalar.activation(sin_t[j][:], angs[j][:], ACT.Sin)
-            nc.scalar.activation(cos_t[j][:], angs[j][:], ACT.Abs)
-            nc.scalar.activation(cos_t[j][:], cos_t[j][:], ACT.Sin, bias=math.pi / 2, scale=-1.0)
+        def trig(unit):
+            cos[unit] = kept("cos%d" % unit[0], [PART, len(unit), P], F32)
+            sin[unit] = kept("sin%d" % unit[0], [PART, len(unit), P], F32, tag="wsub1_raw0" if unit[0] == 0 else None)
+            nc.scalar.activation(sin[unit][:], ang[unit][:], ACT.Sin)
+            nc.scalar.activation(cos[unit][:], ang[unit][:], ACT.Abs)
+            nc.scalar.activation(cos[unit][:], cos[unit][:], ACT.Sin, bias=math.pi / 2, scale=-1.0)
 
-        def products(j):
-            a, t = divmod(j, 4)
-            for w_codes, w_scales, factor, dst in (
-                (wsub2_w[:, BANK * a : BANK * (a + 1)], wsub2_s[:, PART * a : PART * (a + 1)].bitcast(U8), sin_t[j], sin_b2[a]),
-                (wsub1_w[a][:], wsub1_s[a][:], cos_t[j], cos_b1[a]),
-            ):
-                bank = proj.tile([PART, P], F32, name="b", tag="b")
-                nc.tensor.matmul_mx(
-                    out=bank[:],
-                    lhsT=w_codes[:, PART * t : PART * (t + 1)].bitcast(FP8X4),
-                    lhsT_scale=w_scales[:, PART * t : PART * (t + 1)],
-                    rhs=v2_w[:].bitcast(FP8X4),
-                    rhs_scale=v2_s[:],
-                    start=True,
-                    stop=True,
-                )
-                nc.vector.tensor_tensor(dst[:, t, :], bank[:], factor[:], ALU.mult)
+        def product(j, w_codes, w_scales, factor, dst):
+            bank = proj.tile([PART, P], F32, name="b", tag="b")
+            nc.tensor.matmul_mx(
+                out=bank[:],
+                lhsT=w_codes.bitcast(FP8X4),
+                lhsT_scale=w_scales,
+                rhs=v2_w[:].bitcast(FP8X4),
+                rhs_scale=v2_s[:],
+                start=True,
+                stop=True,
+            )
+            nc.vector.tensor_tensor(dst[j // 4][:, j % 4, :], bank[:], factor[units[j]][:, j - units[j][0], :], ALU.mult)
 
-        def mix(a, c):
+        def products(unit):
+            for j in unit:
+                product(j, wsub2_w[:, PART * j : PART * (j + 1)], wsub2_s[:, 32 * j : 32 * (j + 1)].bitcast(U8), sin, sin_b2)
+            for j in unit:
+                part, t = (0, j) if j < 4 else (1 + (j - 4) // 2, j % 2)
+                cols = slice(PART * t, PART * (t + 1))
+                product(j, wsub1_w[part][:, cols], wsub1_s[part][:, cols], cos, cos_b1)
+
+        def mix(a, c, engine, tag=None):
             m0, w = PIECES[a][c]
-            nc.vector.tensor_tensor(
+            h_b[a][c] = kept("h_b%d%d" % (a, c), [PART, w, 4], BF16, tag=tag)
+            engine.tensor_tensor(
                 h_b[a][c][:].rearrange("p (u e) t -> p u t e", e=4),
                 cos_b1[a][:, :, m0 : m0 + w].rearrange("p t (u e) -> p u t e", e=4),
                 sin_b2[a][:, :, m0 : m0 + w].rearrange("p t (u e) -> p u t e", e=4),
                 ALU.add,
             )
 
-        def quantize_h(a, c):
+        def quantize_h(a, c, tag=None):
+            h_w[a][c] = kept("h_w%d%d" % (a, c), [PART, PIECES[a][c][1]], U32, tag=tag)
             quantize(h_w[a][c], h_s[a][c], h_b[a][c])
 
         out_banks = {}
@@ -301,61 +330,55 @@ def tile_list_halo_spin_orientation_kernel(
                     nc.vector.tensor_copy(res[:], out_banks[c, b][:])
                 nc.sync.dma_start(out_v[:, tiles * b : tiles * (b + 1), m0 : m0 + w], res[:])
 
-        on_vector, on_scalar = nc.vector.tensor_copy, nc.scalar.copy
-        for half in range(2):
-            angles(0, half)
-            angles(1, half)
-        second_gathers()
+        on_scalar = nc.scalar.copy
+        both(0)
+        both(1)
         pick(0)
-        both(2)
-        cast_wsub1(0, 0, 4, on_vector)
-        both(3)
-        trig(0)
         pick(1)
-        second_weights()
+        second_gathers()
+        both(2)
+        both(3)
+        cast_wsub1_first()
         pick(2)
-        quantize_wsub1(0)
-        both(4)
-        trig(1)
+        second_weights()
+        quantize_wsub1_first()
         pick(3)
-        products(0)
+        cast_wsub1_second(0)
+        trig(UNITS[0])
+        products(UNITS[0])
+        both(4)
         both(5)
-        trig(2)
+        quantize_wsub1_second(0)
         pick(4)
-        products(1)
-        both(6)
-        trig(3)
         pick(5)
-        products(2)
+        cast_wsub1_second(1)
+        trig(UNITS[1])
+        products(UNITS[1])
+        both(6)
         both(7)
-        cast_wsub1(1, 0, 4, on_scalar)
-        trig(4)
+        quantize_wsub1_second(1)
+        mix(0, 1, nc.vector)
         pick(6)
-        products(3)
-        quantize_wsub1(1)
-        trig(5)
+        quantize_h(0, 1)
         pick(7)
-        products(4)
-        trig(6)
-        mix(0, 0)
-        trig(7)
+        mix(0, 0, nc.gpsimd, tag="th7")
+        for unit in UNITS[2:]:
+            trig(unit)
+            products(unit)
         cast_wspin(0, 0, 512, on_scalar)
         cast_wspin(1, 0, 512, on_scalar)
-        products(5)
-        quantize_h(0, 0)
-        products(6)
+        mix(1, 0, nc.vector)
+        quantize_h(0, 0, tag="cos7")
+        mix(1, 1, nc.vector)
         quantize_wspin(0)
-        products(7)
         spin(0, 0)
         spin(0, 1)
         spin(0, last_piece)
-        mix(1, 0)
-        quantize_wspin(1)
-        mix(1, 1)
         quantize_h(1, 0)
+        mix(1, 2, nc.vector)
+        quantize_wspin(1)
         spin(1, 0)
         store(0)
-        mix(1, 2)
         for c in (1, 2):
             quantize_h(1, c)
             spin(1, c)

@@ -26,7 +26,7 @@ TAB_ROW = 24
 PLANE_ROWS = 100
 BIAS_ROW = PART - ROW_TILES
 VECTOR_CAST_TILES = 4
-PIECES = ([(0, 384), (384, 128)], [(0, 256), (256, 128), (384, 128)])
+PIECES = ([(0, 512)], [(0, 256), (256, 128), (384, 128)])
 TILES_PER_BANK = (2, 4, 2)
 UNITS = ((0, 1), (2, 3), (4, 5), (6,), (7,))
 
@@ -41,7 +41,6 @@ def tile_list_halo_spin_orientation_kernel(
         lists = ctx.enter_context(tc.tile_pool(name="lists", bufs=1))
         keep = ctx.enter_context(tc.tile_pool(name="keep", bufs=1))
         ring = ctx.enter_context(tc.tile_pool(name="ring", bufs=4))
-        reuse = ctx.enter_context(tc.tile_pool(name="reuse", bufs=1))
         acc = ctx.enter_context(tc.psum_pool(name="acc", bufs=4))
         proj = ctx.enter_context(tc.psum_pool(name="proj", bufs=4))
 
@@ -68,7 +67,7 @@ def tile_list_halo_spin_orientation_kernel(
         tab_s = kept("tab_s", [PART, T], U8)
         wang_s_raw = kept("wang_s_raw", [PART, H // 2], I32)
         tab2_s = kept("tab2_s", [PART, T2], U8)
-        wsub2_s_raw = reuse.tile([PART, H // 4], I32, name="wsub2_s_raw", offset=4096, align_bytes=64)
+        wsub2_s_raw = kept("wsub2_s_raw", [PART, H // 4], I32)
         v_sg = kept("v_sg", [PART, S], U8)
         v_s = [kept("v_s%d" % g, [PART, S], U8) for g in range(2)]
         bias_rows = kept("bias_rows", [PART, PART], F32)
@@ -118,8 +117,8 @@ def tile_list_halo_spin_orientation_kernel(
 
         nc.sync.dma_start(tab2_w[:], words(tab2_words[0]))
         nc.sync.dma_start(pos_t[:], pos1)
-        nc.sync.dma_start(wsub1_raw[0][:], wsub1_v[:, :, 0:BANK])
         load_plane(tab2_s[:].bitcast(I32), tab2_scales[0])
+        nc.sync.dma_start(wsub1_raw[0][:], wsub1_v[:, :, 0:BANK])
         nc.sync.dma_start(wsub2_raw[:], words(wsub2_words[0]))
         load_plane(wsub2_s_raw[:], wsub2_scales[0])
         nc.sync.dma_start(wsub1_raw[1][:], wsub1_v[:, :, BANK : 2 * BANK])
@@ -154,10 +153,7 @@ def tile_list_halo_spin_orientation_kernel(
 
         def angles(j, half):
             if th[j] is None:
-                if j == 3:
-                    th[j] = reuse.tile([PART, S], F32, name="th3", offset=0, align_bytes=64)
-                else:
-                    th[j] = kept("th%d" % j, [PART, S], F32)
+                th[j] = kept("th%d" % j, [PART, S], F32)
             cols = slice(BANK * half, BANK * (half + 1))
             bank = acc.tile([PART, BANK], F32, name="bank", tag="bank")
             for g in (1, 0):
@@ -180,13 +176,14 @@ def tile_list_halo_spin_orientation_kernel(
         v2_s = kept("v2_s", [PART, P], U8)
         wsub2_w = kept("wsub2_w", [PART, H], I32)
         wsub2_s = kept("wsub2_s", [PART, H // 4], I32)
-        wsub1_b0 = reuse.tile([PART, BANK, 4], BF16, name="wsub1_b0", offset=5120, align_bytes=64)
-        wsub1_b1 = [None, None]
-        wsub1_w = [kept("wsub1_w0", [PART, BANK], U32), None, None]
-        wsub1_s = [kept("wsub1_s0", [PART, BANK], U8), None, None]
-        wspin_b = [None, None]
-        wspin_w = [kept("wspin_w%d" % a, [PART, N], U32) for a in range(2)]
-        wspin_s = [kept("wspin_s%d" % a, [PART, N], U8) for a in range(2)]
+        wsub1_b0 = kept("wsub1_b0", [PART, BANK, 4], BF16)
+        wsub1_w = [None]
+        wsub1_s = [kept("wsub1_s0", [PART, BANK], U8)]
+        both_b, both_w = [None], [None]
+        both_s = kept("both_s", [PART, 2 * BANK], U8)
+        wspin_b = [None]
+        wspin_w = kept("wspin_w", [PART, N], U32)
+        wspin_s = kept("wspin_s", [PART, N], U8)
 
         def second_gathers():
             nc.vector.tensor_copy(v2_w[:], tab2_w[:].bitcast(U32).indirect(offs2_t[:]))
@@ -202,40 +199,38 @@ def tile_list_halo_spin_orientation_kernel(
                 wsub1_raw[0][:].rearrange("p j (q t i) -> p t q j i", t=4, i=8),
             )
 
-        def cast_wsub1_second(half):
-            if half == 0:
-                wsub1_b1[0] = reuse.tile([PART, 256, 4], BF16, name="wsub1_b10", offset=4096 - 512, align_bytes=64)
-            else:
-                wsub1_b1[1] = kept("wsub1_b11", [PART, 256, 4], BF16, tag="th5")
-            for d in range(2):
+        def cast_on_gpsimd():
+            both_b[0] = kept("both_b", [PART, 2 * BANK, 4], BF16, tag="wsub1_b0")
+            for t in range(4):
                 nc.gpsimd.tensor_scalar(
-                    wsub1_b1[half][:, PART * d : PART * (d + 1), :].rearrange("p (q i) j -> p q i j", i=8),
-                    wsub1_raw[1][:].rearrange("p j (q t i) -> p t q i j", t=4, i=8)[:, 2 * half + d],
+                    both_b[0][:, PART * t : PART * (t + 1), :].rearrange("p (q i) j -> p q i j", i=8),
+                    wsub1_raw[1][:].rearrange("p j (q t i) -> p t q i j", t=4, i=8)[:, t],
                     1.0, 0.0, ALU.mult, ALU.add,
                 )
+            nc.gpsimd.tensor_scalar(
+                both_b[0][:, BANK : 2 * BANK, :], wspin_raw[0][:].rearrange("p t n -> p n t"), 1.0, 0.0, ALU.mult, ALU.add
+            )
 
-        def quantize_wsub1_second(half):
-            wsub1_w[1 + half] = kept("wsub1_w1%d" % half, [PART, 256], U32, tag="cos%d" % (2 * half))
-            wsub1_s[1 + half] = kept("wsub1_s1%d" % half, [PART, 256], U8)
-            quantize(wsub1_w[1 + half], wsub1_s[1 + half], wsub1_b1[half])
+        def quantize_both():
+            both_w[0] = kept("both_w", [PART, 2 * BANK], U32, tag="cos2")
+            quantize(both_w[0], both_s, both_b[0])
 
-        def cast_wspin(a, first, count, engine):
-            if wspin_b[a] is None:
-                wspin_b[a] = kept("wspin_b%d" % a, [PART, N, 4], BF16, tag=("th6", "ang7")[a])
-            cols = slice(first, first + count)
-            engine(
-                out=wspin_b[a][:, cols, :].rearrange("p (u e) t -> p u t e", e=4),
-                in_=wspin_raw[a][:, :, cols].rearrange("p t (u e) -> p u t e", e=4),
+        def cast_wspin_second():
+            wspin_b[0] = kept("wspin_b", [PART, N, 4], BF16, tag="ang7")
+            nc.scalar.copy(
+                wspin_b[0][:].rearrange("p (u e) t -> p u t e", e=4),
+                wspin_raw[1][:].rearrange("p t (u e) -> p u t e", e=4),
             )
 
         def quantize(codes, scales, values):
             nc.vector.quantize_mx(out=codes[:].bitcast(FP8X4), scales=scales[:], in_=values[:].rearrange("p c j -> p (c j)"))
 
         def quantize_wsub1_first():
+            wsub1_w[0] = kept("wsub1_w0", [PART, BANK], U32, tag="wsub2_s_raw")
             quantize(wsub1_w[0], wsub1_s[0], wsub1_b0)
 
-        def quantize_wspin(a):
-            quantize(wspin_w[a], wspin_s[a], wspin_b[a])
+        def quantize_wspin_second():
+            quantize(wspin_w, wspin_s, wspin_b[0])
 
         cos_b1 = [kept("cos_b1_%d" % a, [PART, 4, P], F32) for a in range(2)]
         sin_b2 = [kept("sin_b2_%d" % a, [PART, 4, P], F32) for a in range(2)]
@@ -254,8 +249,8 @@ def tile_list_halo_spin_orientation_kernel(
         def trig(unit):
             cos[unit] = kept("cos%d" % unit[0], [PART, len(unit), P], F32)
             sin[unit] = kept("sin%d" % unit[0], [PART, len(unit), P], F32, tag="wsub1_raw0" if unit[0] == 0 else None)
-            nc.scalar.activation(sin[unit][:], ang[unit][:], ACT.Sin)
             nc.scalar.activation(cos[unit][:], ang[unit][:], ACT.Abs)
+            nc.scalar.activation(sin[unit][:], ang[unit][:], ACT.Sin)
             nc.scalar.activation(cos[unit][:], cos[unit][:], ACT.Sin, bias=math.pi / 2, scale=-1.0)
 
         def product(j, w_codes, w_scales, factor, dst):
@@ -275,9 +270,9 @@ def tile_list_halo_spin_orientation_kernel(
             for j in unit:
                 product(j, wsub2_w[:, PART * j : PART * (j + 1)], wsub2_s[:, 32 * j : 32 * (j + 1)].bitcast(U8), sin, sin_b2)
             for j in unit:
-                part, t = (0, j) if j < 4 else (1 + (j - 4) // 2, j % 2)
+                codes, scales, t = (wsub1_w[0], wsub1_s[0], j) if j < 4 else (both_w[0], both_s, j - 4)
                 cols = slice(PART * t, PART * (t + 1))
-                product(j, wsub1_w[part][:, cols], wsub1_s[part][:, cols], cos, cos_b1)
+                product(j, codes[:, cols], scales[:, cols], cos, cos_b1)
 
         def mix(a, c, engine, tag=None):
             m0, w = PIECES[a][c]
@@ -306,11 +301,13 @@ def tile_list_halo_spin_orientation_kernel(
                 elif a == 0:
                     out_banks[c, b] = proj.tile([PART, tiles, w], F32, name="b", tag="b")
                 for d in range(tiles):
-                    rows = slice(PART * (tiles * b + d), PART * (tiles * b + d + 1))
+                    n = tiles * b + d
+                    codes, scales, at = (both_w[0], both_s, 4 + n) if a == 0 else (wspin_w, wspin_s, n)
+                    rows = slice(PART * at, PART * (at + 1))
                     nc.tensor.matmul_mx(
                         out=out_banks[c, b][:, d, :],
-                        lhsT=wspin_w[a][:, rows].bitcast(FP8X4),
-                        lhsT_scale=wspin_s[a][:, rows],
+                        lhsT=codes[:, rows].bitcast(FP8X4),
+                        lhsT_scale=scales[:, rows],
                         rhs=h_w[a][piece][:, off : off + w].bitcast(FP8X4),
                         rhs_scale=h_s[a][piece][:, off : off + w],
                         start=(a == 0 and d == 0),
@@ -330,55 +327,47 @@ def tile_list_halo_spin_orientation_kernel(
                     nc.vector.tensor_copy(res[:], out_banks[c, b][:])
                 nc.sync.dma_start(out_v[:, tiles * b : tiles * (b + 1), m0 : m0 + w], res[:])
 
-        on_scalar = nc.scalar.copy
         both(0)
         both(1)
+        second_gathers()
         pick(0)
         pick(1)
-        second_gathers()
         both(2)
         both(3)
         cast_wsub1_first()
         pick(2)
-        second_weights()
-        quantize_wsub1_first()
         pick(3)
-        cast_wsub1_second(0)
-        trig(UNITS[0])
-        products(UNITS[0])
         both(4)
         both(5)
-        quantize_wsub1_second(0)
         pick(4)
         pick(5)
-        cast_wsub1_second(1)
-        trig(UNITS[1])
-        products(UNITS[1])
+        second_weights()
+        quantize_wsub1_first()
+        cast_on_gpsimd()
+        for unit in UNITS[:2]:
+            trig(unit)
+            products(unit)
         both(6)
         both(7)
-        quantize_wsub1_second(1)
-        mix(0, 1, nc.vector)
+        quantize_both()
         pick(6)
-        quantize_h(0, 1)
         pick(7)
         mix(0, 0, nc.gpsimd, tag="th7")
         for unit in UNITS[2:]:
             trig(unit)
             products(unit)
-        cast_wspin(0, 0, 512, on_scalar)
-        cast_wspin(1, 0, 512, on_scalar)
-        mix(1, 0, nc.vector)
+        cast_wspin_second()
         quantize_h(0, 0, tag="cos7")
-        mix(1, 1, nc.vector)
-        quantize_wspin(0)
         spin(0, 0)
         spin(0, 1)
         spin(0, last_piece)
+        mix(1, 0, nc.vector)
+        quantize_wspin_second()
         quantize_h(1, 0)
-        mix(1, 2, nc.vector)
-        quantize_wspin(1)
         spin(1, 0)
         store(0)
+        mix(1, 1, nc.vector, tag="ang7")
+        mix(1, 2, nc.vector)
         for c in (1, 2):
             quantize_h(1, c)
             spin(1, c)

@@ -26,7 +26,8 @@ TAB_ROW = 24
 PLANE_ROWS = 100
 BIAS_ROW = PART - ROW_TILES
 VECTOR_CAST_TILES = 4
-PIECES = ([(0, 512)], [(0, 256), (256, 128), (384, 128)])
+GPSIMD_SPIN = 128
+PIECES = ([(0, 384), (384, 128)], [(0, 256), (256, 128), (384, 128)])
 TILES_PER_BANK = (2, 4, 2)
 UNITS = ((0, 1), (2, 3), (4, 5), (6,), (7,))
 
@@ -208,7 +209,15 @@ def tile_list_halo_spin_orientation_kernel(
                     1.0, 0.0, ALU.mult, ALU.add,
                 )
             nc.gpsimd.tensor_scalar(
-                both_b[0][:, BANK : 2 * BANK, :], wspin_raw[0][:].rearrange("p t n -> p n t"), 1.0, 0.0, ALU.mult, ALU.add
+                both_b[0][:, BANK : BANK + GPSIMD_SPIN, :],
+                wspin_raw[0][:, :, 0:GPSIMD_SPIN].rearrange("p t n -> p n t"),
+                1.0, 0.0, ALU.mult, ALU.add,
+            )
+
+        def cast_wspin_first():
+            nc.scalar.copy(
+                both_b[0][:, BANK + GPSIMD_SPIN : 2 * BANK, :].rearrange("p (u e) t -> p u t e", e=4),
+                wspin_raw[0][:, :, GPSIMD_SPIN:N].rearrange("p t (u e) -> p u t e", e=4),
             )
 
         def quantize_both():
@@ -347,10 +356,13 @@ def tile_list_halo_spin_orientation_kernel(
         for unit in UNITS[:2]:
             trig(unit)
             products(unit)
+        cast_wspin_first()
         both(6)
         both(7)
         quantize_both()
+        mix(0, 1, nc.vector)
         pick(6)
+        quantize_h(0, 1)
         pick(7)
         mix(0, 0, nc.gpsimd, tag="th7")
         for unit in UNITS[2:]:

@@ -22,10 +22,7 @@ PART = 128
 BANK = 512
 QUADS = 4
 ROW_TILES = H // PART
-TAB_ROW = 24
-PLANE_ROWS = 100
 BIAS_ROW = PART - ROW_TILES
-VECTOR_CAST_TILES = 4
 GPSIMD_SPIN = 128
 PIECES = ([(0, 384), (384, 128)], [(0, 256), (256, 128), (384, 128)])
 TILES_PER_BANK = (2, 4, 2)
@@ -68,22 +65,20 @@ def tile_list_halo_spin_orientation_kernel(
         tab_s = kept("tab_s", [PART, T], U8)
         wang_s_raw = kept("wang_s_raw", [PART, H // 2], I32)
         tab2_s = kept("tab2_s", [PART, T2], U8)
-        wsub2_s_raw = kept("wsub2_s_raw", [PART, H // 4], I32)
         v_sg = kept("v_sg", [PART, S], U8)
-        v_s = [kept("v_s%d" % g, [PART, S], U8) for g in range(2)]
+        v_s = kept("v_s", [PART, 2, S], U8)
         bias_rows = kept("bias_rows", [PART, PART], F32)
         ident = kept("ident", [PART, PART], F32)
         nc.gpsimd.memset(wang_s_raw[:], 0)
         make_identity(nc, ident[:])
-        for quad in range(QUADS):
-            nc.vector.memset(tab_s[32 * quad : 32 * quad + TAB_ROW, :].bitcast(I32), 0)
-        nc.vector.memset(tab2_s[:].bitcast(I32), 0)
-        nc.vector.memset(wsub2_s_raw[:], 0)
+        nc.vector.memset(tab_s[32:64, :].bitcast(I32), 0)
+        nc.vector.memset(tab_s[64:PART, :].bitcast(I32), 0)
         for a in range(2):
             nc.gpsimd.dma_start(
                 bias_rows[BIAS_ROW + 4 * a : BIAS_ROW + 4 * a + 4, :].rearrange("t (q i) -> t q i", i=8),
                 bang[BANK * a : BANK * (a + 1)].rearrange("(q t i) -> t q i", t=4, i=8),
             )
+        nc.vector.memset(tab2_s[:].bitcast(I32), 0)
         nc.vector.memset(bias_rows[0:96, :], 0.0)
         nc.vector.memset(bias_rows[96:BIAS_ROW, :], 0.0)
         warm = kept("warm", [PART, 16], F32)
@@ -92,37 +87,27 @@ def tile_list_halo_spin_orientation_kernel(
         tab_w = [kept("tab_w%d" % g, [PART, T], I32, tag="stage%d" % g) for g in range(2)]
         wang_raw = kept("wang_raw", [PART, 2, H // 2], I32)
         tab2_w = kept("tab2_w", [PART, T2], I32)
-        wsub2_raw = kept("wsub2_raw", [PART, H], I32)
         wsub1_v = wsub1.rearrange("(p j) c -> p j c", j=4)
-        wsub1_raw = [kept("wsub1_raw%d" % a, [PART, 4, BANK], F32) for a in range(2)]
         nc.sync.dma_start(offs_t[:], offs)
-        for quad in range(QUADS):
-            nc.sync.dma_start(
-                tab_s[32 * quad + TAB_ROW : 32 * quad + 32, :].bitcast(I32),
-                tab_scales[:, 4 * quad : 4 * quad + 4, :].bitcast(I32),
-            )
+        nc.sync.dma_start(tab_s[0:32, :].bitcast(I32), tab_scales.rearrange("g r c -> r g c").bitcast(I32))
         nc.sync.dma_start(tab_w[0][:], words(tab_words[0]))
-        nc.sync.dma_start(wang_raw[:], wang_words.rearrange("g p c -> p g c").bitcast(I32))
         for quad in range(QUADS):
             nc.sync.dma_start(
                 wang_s_raw[32 * quad : 32 * quad + 4, :].rearrange("s (g c) -> s g c", g=2),
                 wang_scales[:, 4 * quad : 4 * quad + 4, :].rearrange("g s c -> s g c").bitcast(I32),
             )
-        nc.sync.dma_start(tab_w[1][:], words(tab_words[1]))
+        nc.sync.dma_start(wang_raw[:], wang_words.rearrange("g p c -> p g c").bitcast(I32))
         nc.sync.dma_start(offs2_t[:], offs2)
-
+        nc.sync.dma_start(tab_w[1][:], words(tab_words[1]))
         nc.vector.tensor_copy(v_sg[:], tab_s[:].indirect(offs_t[:]))
-        for g in range(2):
-            first = TAB_ROW + 4 * g
-            nc.scalar.dma_start(v_s[g][0:PLANE_ROWS, :].bitcast(I32), v_sg[first : first + PLANE_ROWS, :].bitcast(I32))
+        for quad in range(QUADS):
+            nc.sync.dma_start(
+                v_s[32 * quad : 32 * quad + 4].bitcast(I32), v_sg[8 * quad : 8 * quad + 8, :].bitcast(I32)
+            )
 
         nc.sync.dma_start(tab2_w[:], words(tab2_words[0]))
         nc.sync.dma_start(pos_t[:], pos1)
         load_plane(tab2_s[:].bitcast(I32), tab2_scales[0])
-        nc.sync.dma_start(wsub1_raw[0][:], wsub1_v[:, :, 0:BANK])
-        nc.sync.dma_start(wsub2_raw[:], words(wsub2_words[0]))
-        load_plane(wsub2_s_raw[:], wsub2_scales[0])
-        nc.sync.dma_start(wsub1_raw[1][:], wsub1_v[:, :, BANK : 2 * BANK])
 
         bias_ps = proj.tile([PART, BANK], F32, name="b", tag="b")
         nc.tensor.transpose(bias_ps[:, 0:PART], bias_rows[:], ident[:])
@@ -139,14 +124,24 @@ def tile_list_halo_spin_orientation_kernel(
         wang_s = kept("wang_s", [PART, 2, H // 4], I32)
         gather_v(0, 0)
         gather_v(0, 1)
+        wsub1_raw = [kept("wsub1_raw0", [PART, 4, BANK], F32, tag="stage0")]
+        nc.sync.dma_start(wsub1_raw[0][:], wsub1_v[:, :, 0:BANK])
         order_columns(wang_w[:].rearrange("p g c -> p (g c)"), wang_raw[:].rearrange("p g c -> p (g c)"), 4)
+        wsub2_raw = kept("wsub2_raw", [PART, H], I32, tag="wang_raw")
+        nc.sync.dma_start(wsub2_raw[:], words(wsub2_words[0]))
         order_columns(wang_s[:].rearrange("p g c -> p (g c)"), wang_s_raw[:], 2)
+        wsub2_s_raw = wang_s_raw[:, 0 : H // 4]
+        load_plane(wsub2_s_raw, wsub2_scales[0])
         gather_v(1, 0)
         gather_v(1, 1)
+        wsub1_raw.append(kept("wsub1_raw1", [PART, 4, BANK], F32, tag="stage1"))
+        nc.sync.dma_start(wsub1_raw[1][:], wsub1_v[:, :, BANK : 2 * BANK])
 
         wspin_v = wspin.rearrange("(a q t i) n -> a t q i n", a=2, t=4, i=8)
-        wspin_raw = [kept("wspin_raw%d" % a, [PART, 4, N], F32, tag="stage%d" % a) for a in range(2)]
-        for a in range(2):
+        wspin_raw = []
+
+        def load_wspin(a, tag):
+            wspin_raw.append(kept("wspin_raw%d" % a, [PART, 4, N], F32, tag=tag))
             for t in range(4):
                 nc.sync.dma_start(wspin_raw[a][:, t, :], wspin_v[a, t])
 
@@ -163,7 +158,7 @@ def tile_list_halo_spin_orientation_kernel(
                     lhsT=wang_w[:, g, 64 * j : 64 * (j + 1)].bitcast(FP4X4),
                     lhsT_scale=wang_s[:, g, 32 * j : 32 * (j + 1)].bitcast(U8),
                     rhs=v_w[g][half][:].bitcast(FP8X4),
-                    rhs_scale=v_s[g][:, cols],
+                    rhs_scale=v_s[:, g, cols],
                     start=(g == 1),
                     stop=(g == 0),
                 )
@@ -188,11 +183,13 @@ def tile_list_halo_spin_orientation_kernel(
 
         def second_gathers():
             nc.vector.tensor_copy(v2_w[:], tab2_w[:].bitcast(U32).indirect(offs2_t[:]))
+            load_wspin(0, "tab2_w")
             nc.vector.tensor_copy(v2_s[:], tab2_s[:].indirect(offs2_t[:]))
+            load_wspin(1, "tab2_s")
 
         def second_weights():
             order_columns(wsub2_w[:], wsub2_raw[:], 8)
-            order_columns(wsub2_s[:], wsub2_s_raw[:], 2)
+            order_columns(wsub2_s[:], wsub2_s_raw, 2)
 
         def cast_wsub1_first():
             nc.vector.tensor_copy(
@@ -235,7 +232,7 @@ def tile_list_halo_spin_orientation_kernel(
             nc.vector.quantize_mx(out=codes[:].bitcast(FP8X4), scales=scales[:], in_=values[:].rearrange("p c j -> p (c j)"))
 
         def quantize_wsub1_first():
-            wsub1_w[0] = kept("wsub1_w0", [PART, BANK], U32, tag="wsub2_s_raw")
+            wsub1_w[0] = kept("wsub1_w0", [PART, BANK], U32, tag="wang_s_raw")
             quantize(wsub1_w[0], wsub1_s[0], wsub1_b0)
 
         def quantize_wspin_second():
@@ -257,7 +254,7 @@ def tile_list_halo_spin_orientation_kernel(
 
         def trig(unit):
             cos[unit] = kept("cos%d" % unit[0], [PART, len(unit), P], F32)
-            sin[unit] = kept("sin%d" % unit[0], [PART, len(unit), P], F32, tag="wsub1_raw0" if unit[0] == 0 else None)
+            sin[unit] = kept("sin%d" % unit[0], [PART, len(unit), P], F32, tag="stage0" if unit[0] == 0 else None)
             nc.scalar.activation(cos[unit][:], ang[unit][:], ACT.Abs)
             nc.scalar.activation(sin[unit][:], ang[unit][:], ACT.Sin)
             nc.scalar.activation(cos[unit][:], cos[unit][:], ACT.Sin, bias=math.pi / 2, scale=-1.0)

@@ -23,10 +23,9 @@ BANK = 512
 QUADS = 4
 ROW_TILES = H // PART
 BIAS_ROW = PART - ROW_TILES
+PIECES = ([(0, 256), (256, 256)], [(0, 256), (256, 128), (384, 128)])
+OUT_TILES_PER_BANK = (2, 4, 2)
 GPSIMD_SPIN = 128
-PIECES = ([(0, 384), (384, 128)], [(0, 256), (256, 128), (384, 128)])
-TILES_PER_BANK = (2, 4, 2)
-UNITS = ((0, 1), (2, 3), (4, 5), (6,), (7,))
 
 
 def tile_list_halo_spin_orientation_kernel(
@@ -38,12 +37,14 @@ def tile_list_halo_spin_orientation_kernel(
     with ExitStack() as ctx:
         lists = ctx.enter_context(tc.tile_pool(name="lists", bufs=1))
         keep = ctx.enter_context(tc.tile_pool(name="keep", bufs=1))
-        ring = ctx.enter_context(tc.tile_pool(name="ring", bufs=4))
-        acc = ctx.enter_context(tc.psum_pool(name="acc", bufs=4))
-        proj = ctx.enter_context(tc.psum_pool(name="proj", bufs=4))
+        shared = ctx.enter_context(tc.tile_pool(name="shared", bufs=1))
+        banks = ctx.enter_context(tc.psum_pool(name="banks", bufs=8))
 
         def kept(name, shape, dtype, tag=None):
             return keep.tile(shape, dtype, name=name, tag=tag or name, align_bytes=64)
+
+        def placed(name, shape, dtype, offset):
+            return shared.tile(shape, dtype, name=name, offset=offset, align_bytes=64)
 
         def words(packed):
             return packed.rearrange("p c i -> p (c i)").bitcast(I32)
@@ -52,24 +53,32 @@ def tile_list_halo_spin_orientation_kernel(
             for quad in range(QUADS):
                 nc.sync.dma_start(dst[32 * quad : 32 * quad + 4, :], scales[4 * quad : 4 * quad + 4, :].bitcast(I32))
 
-        def order_columns(dst, src, run):
-            nc.vector.tensor_copy(
+        def order_columns(dst, src, run, copy):
+            copy(
                 dst.rearrange("p (a t q w) -> p a t q w", t=4, q=16, w=run),
                 src.rearrange("p (a q t w) -> p a t q w", t=4, q=16, w=run),
             )
+
+        def scalar_move(dst, src):
+            nc.scalar.copy(dst.bitcast(U32), src.bitcast(U32))
+
+        def quantize(codes, scales, values):
+            nc.vector.quantize_mx(out=codes.bitcast(FP8X4), scales=scales, in_=values.rearrange("p c j -> p (c j)"))
 
         offs_t = lists.tile([PART, S // 16], U16, name="offs_t")
         pos_t = lists.tile([PART, P // 16], U16, name="pos_t")
         offs2_t = lists.tile([PART, P // 16], U16, name="offs2_t")
 
         tab_s = kept("tab_s", [PART, T], U8)
-        wang_s_raw = kept("wang_s_raw", [PART, H // 2], I32)
+        at_th_last, at_ang, at_cos_last = 2048, 8192, 18432
+        weight_s_raw = kept("weight_s_raw", [PART, H // 2], I32)
+        wsub2_s_raw = placed("wsub2_s_raw", [PART, H // 4], I32, at_ang + 4096)
         tab2_s = kept("tab2_s", [PART, T2], U8)
         v_sg = kept("v_sg", [PART, S], U8)
         v_s = kept("v_s", [PART, 2, S], U8)
         bias_rows = kept("bias_rows", [PART, PART], F32)
         ident = kept("ident", [PART, PART], F32)
-        nc.gpsimd.memset(wang_s_raw[:], 0)
+        nc.gpsimd.memset(weight_s_raw[:], 0)
         make_identity(nc, ident[:])
         nc.vector.memset(tab_s[32:64, :].bitcast(I32), 0)
         nc.vector.memset(tab_s[64:PART, :].bitcast(I32), 0)
@@ -79,24 +88,28 @@ def tile_list_halo_spin_orientation_kernel(
                 bang[BANK * a : BANK * (a + 1)].rearrange("(q t i) -> t q i", t=4, i=8),
             )
         nc.vector.memset(tab2_s[:].bitcast(I32), 0)
+        nc.vector.memset(wsub2_s_raw[:], 0)
         nc.vector.memset(bias_rows[0:96, :], 0.0)
         nc.vector.memset(bias_rows[96:BIAS_ROW, :], 0.0)
         warm = kept("warm", [PART, 16], F32)
         nc.scalar.activation(warm[0:96, 0:1], bias_rows[0:96, 0:1], ACT.Sin)
 
         tab_w = [kept("tab_w%d" % g, [PART, T], I32, tag="stage%d" % g) for g in range(2)]
-        wang_raw = kept("wang_raw", [PART, 2, H // 2], I32)
-        tab2_w = kept("tab2_w", [PART, T2], I32)
+        wang_raw = [kept("wang_raw%d" % a, [PART, 2, BANK // 2], I32) for a in range(2)]
+        wang_v = wang_words.rearrange("g p c -> p g c").bitcast(I32)
+        tab2_w = kept("tab2_w", [PART, T2], I32, tag="stage2")
+        wsub2_raw = kept("wsub2_raw", [PART, H], I32)
         wsub1_v = wsub1.rearrange("(p j) c -> p j c", j=4)
+        wsub1_raw = [kept("wsub1_raw0", [PART, 4, BANK], F32)]
         nc.sync.dma_start(offs_t[:], offs)
         nc.sync.dma_start(tab_s[0:32, :].bitcast(I32), tab_scales.rearrange("g r c -> r g c").bitcast(I32))
         nc.sync.dma_start(tab_w[0][:], words(tab_words[0]))
         for quad in range(QUADS):
             nc.sync.dma_start(
-                wang_s_raw[32 * quad : 32 * quad + 4, :].rearrange("s (g c) -> s g c", g=2),
+                weight_s_raw[32 * quad : 32 * quad + 4, :].rearrange("s (g c) -> s g c", g=2),
                 wang_scales[:, 4 * quad : 4 * quad + 4, :].rearrange("g s c -> s g c").bitcast(I32),
             )
-        nc.sync.dma_start(wang_raw[:], wang_words.rearrange("g p c -> p g c").bitcast(I32))
+        nc.sync.dma_start(wang_raw[0][:], wang_v[:, :, 0 : BANK // 2])
         nc.sync.dma_start(offs2_t[:], offs2)
         nc.sync.dma_start(tab_w[1][:], words(tab_words[1]))
         nc.vector.tensor_copy(v_sg[:], tab_s[:].indirect(offs_t[:]))
@@ -104,12 +117,15 @@ def tile_list_halo_spin_orientation_kernel(
             nc.sync.dma_start(
                 v_s[32 * quad : 32 * quad + 4].bitcast(I32), v_sg[8 * quad : 8 * quad + 8, :].bitcast(I32)
             )
-
+        nc.sync.dma_start(wang_raw[1][:], wang_v[:, :, BANK // 2 : BANK])
+        nc.sync.dma_start(wsub2_raw[:], words(wsub2_words[0]))
+        load_plane(tab2_s[:].bitcast(I32), tab2_scales[0])
         nc.sync.dma_start(tab2_w[:], words(tab2_words[0]))
         nc.sync.dma_start(pos_t[:], pos1)
-        load_plane(tab2_s[:].bitcast(I32), tab2_scales[0])
+        nc.sync.dma_start(wsub1_raw[0][:], wsub1_v[:, :, 0:BANK])
+        load_plane(wsub2_s_raw[:], wsub2_scales[0])
 
-        bias_ps = proj.tile([PART, BANK], F32, name="b", tag="b")
+        bias_ps = banks.tile([PART, BANK], F32, name="bank", tag="bank")
         nc.tensor.transpose(bias_ps[:, 0:PART], bias_rows[:], ident[:])
         bias = kept("bias", [PART, ROW_TILES], F32)
         nc.scalar.copy(bias[:], bias_ps[:, BIAS_ROW:PART])
@@ -120,202 +136,198 @@ def tile_list_halo_spin_orientation_kernel(
             picks = offs_t[:, 32 * half : 32 * (half + 1)]
             nc.vector.tensor_copy(v_w[g][half][:], tab_w[g][:].bitcast(U32).indirect(picks))
 
-        wang_w = kept("wang_w", [PART, 2, H // 2], I32)
+        wang_w = [kept("wang_w%d" % a, [PART, 2, BANK // 2], I32) for a in range(2)]
         wang_s = kept("wang_s", [PART, 2, H // 4], I32)
+        wsub2_w = kept("wsub2_w", [PART, H], I32)
+        wsub2_s = kept("wsub2_s", [PART, H // 4], I32)
+
+        def order_wang(a):
+            order_columns(wang_w[a][:].rearrange("p g c -> p (g c)"), wang_raw[a][:].rearrange("p g c -> p (g c)"), 4, scalar_move)
+
         gather_v(0, 0)
         gather_v(0, 1)
-        wsub1_raw = [kept("wsub1_raw0", [PART, 4, BANK], F32, tag="stage0")]
-        nc.sync.dma_start(wsub1_raw[0][:], wsub1_v[:, :, 0:BANK])
-        order_columns(wang_w[:].rearrange("p g c -> p (g c)"), wang_raw[:].rearrange("p g c -> p (g c)"), 4)
-        wsub2_raw = kept("wsub2_raw", [PART, H], I32, tag="wang_raw")
-        nc.sync.dma_start(wsub2_raw[:], words(wsub2_words[0]))
-        order_columns(wang_s[:].rearrange("p g c -> p (g c)"), wang_s_raw[:], 2)
-        wsub2_s_raw = wang_s_raw[:, 0 : H // 4]
-        load_plane(wsub2_s_raw, wsub2_scales[0])
+        order_wang(0)
+        order_columns(wang_s[:].rearrange("p g c -> p (g c)"), weight_s_raw[:], 2, scalar_move)
+        order_wang(1)
         gather_v(1, 0)
         gather_v(1, 1)
-        wsub1_raw.append(kept("wsub1_raw1", [PART, 4, BANK], F32, tag="stage1"))
+        order_columns(wsub2_w[:], wsub2_raw[:], 8, scalar_move)
+        wsub1_raw.append(kept("wsub1_raw1", [PART, 4, BANK], F32, tag="stage0"))
         nc.sync.dma_start(wsub1_raw[1][:], wsub1_v[:, :, BANK : 2 * BANK])
-
-        wspin_v = wspin.rearrange("(a q t i) n -> a t q i n", a=2, t=4, i=8)
-        wspin_raw = []
-
-        def load_wspin(a, tag):
-            wspin_raw.append(kept("wspin_raw%d" % a, [PART, 4, N], F32, tag=tag))
-            for t in range(4):
-                nc.sync.dma_start(wspin_raw[a][:, t, :], wspin_v[a, t])
-
-        th = [None] * ROW_TILES
-
-        def angles(j, half):
-            if th[j] is None:
-                th[j] = kept("th%d" % j, [PART, S], F32)
-            cols = slice(BANK * half, BANK * (half + 1))
-            bank = acc.tile([PART, BANK], F32, name="bank", tag="bank")
-            for g in (1, 0):
-                nc.tensor.matmul_mx(
-                    out=bank[:],
-                    lhsT=wang_w[:, g, 64 * j : 64 * (j + 1)].bitcast(FP4X4),
-                    lhsT_scale=wang_s[:, g, 32 * j : 32 * (j + 1)].bitcast(U8),
-                    rhs=v_w[g][half][:].bitcast(FP8X4),
-                    rhs_scale=v_s[:, g, cols],
-                    start=(g == 1),
-                    stop=(g == 0),
-                )
-            nc.scalar.activation(th[j][:, cols], bank[:], ACT.Identity, bias=bias[:, j : j + 1])
-
-        def both(j):
-            angles(j, 0)
-            angles(j, 1)
 
         v2_w = kept("v2_w", [PART, P], U32)
         v2_s = kept("v2_s", [PART, P], U8)
-        wsub2_w = kept("wsub2_w", [PART, H], I32)
-        wsub2_s = kept("wsub2_s", [PART, H // 4], I32)
-        wsub1_b0 = kept("wsub1_b0", [PART, BANK, 4], BF16)
-        wsub1_w = [None]
-        wsub1_s = [kept("wsub1_s0", [PART, BANK], U8)]
-        both_b, both_w = [None], [None]
-        both_s = kept("both_s", [PART, 2 * BANK], U8)
-        wspin_b = [None]
-        wspin_w = kept("wspin_w", [PART, N], U32)
-        wspin_s = kept("wspin_s", [PART, N], U8)
+        nc.vector.tensor_copy(v2_s[:], tab2_s[:].indirect(offs2_t[:]))
+        nc.vector.tensor_copy(v2_w[:], tab2_w[:].bitcast(U32).indirect(offs2_t[:]))
 
-        def second_gathers():
-            nc.vector.tensor_copy(v2_w[:], tab2_w[:].bitcast(U32).indirect(offs2_t[:]))
-            load_wspin(0, "tab2_w")
-            nc.vector.tensor_copy(v2_s[:], tab2_s[:].indirect(offs2_t[:]))
-            load_wspin(1, "tab2_s")
-
-        def second_weights():
-            order_columns(wsub2_w[:], wsub2_raw[:], 8)
-            order_columns(wsub2_s[:], wsub2_s_raw, 2)
-
-        def cast_wsub1_first():
-            nc.vector.tensor_copy(
-                wsub1_b0[:].rearrange("p (t q i) j -> p t q j i", t=4, i=8),
-                wsub1_raw[0][:].rearrange("p j (q t i) -> p t q j i", t=4, i=8),
-            )
-
-        def cast_on_gpsimd():
-            both_b[0] = kept("both_b", [PART, 2 * BANK, 4], BF16, tag="wsub1_b0")
+        wspin_v = wspin.rearrange("(a q t i) n -> a t q i n", a=2, t=4, i=8)
+        wspin_raw = [kept("wspin_raw%d" % a, [PART, 4, N], F32, tag="stage%d" % (a + 1)) for a in range(2)]
+        for a in range(2):
             for t in range(4):
-                nc.gpsimd.tensor_scalar(
-                    both_b[0][:, PART * t : PART * (t + 1), :].rearrange("p (q i) j -> p q i j", i=8),
-                    wsub1_raw[1][:].rearrange("p j (q t i) -> p t q i j", t=4, i=8)[:, t],
-                    1.0, 0.0, ALU.mult, ALU.add,
-                )
+                nc.sync.dma_start(wspin_raw[a][:, t, :], wspin_v[a, t])
+
+        th = [kept("th%d" % j, [PART, S], F32) for j in range(ROW_TILES - 1)]
+        th.append(placed("th7", [PART, S], F32, at_th_last))
+        ang = [kept("ang0", [PART, 4, P], F32)]
+
+        def angles(j):
+            for half in range(2):
+                cols = slice(BANK * half, BANK * (half + 1))
+                bank = banks.tile([PART, BANK], F32, name="bank", tag="bank")
+                for g in (1, 0):
+                    nc.tensor.matmul_mx(
+                        out=bank[:],
+                        lhsT=wang_w[j // 4][:, g, 64 * (j % 4) : 64 * (j % 4 + 1)].bitcast(FP4X4),
+                        lhsT_scale=wang_s[:, g, 32 * j : 32 * (j + 1)].bitcast(U8),
+                        rhs=v_w[g][half][:].bitcast(FP8X4),
+                        rhs_scale=v_s[:, g, cols],
+                        start=(g == 1),
+                        stop=(g == 0),
+                    )
+                nc.scalar.activation(th[j][:, cols], bank[:], ACT.Identity, bias=bias[:, j : j + 1])
+
+        def pick(j):
+            nc.vector.tensor_copy(ang[j // 4][:, j % 4, :], th[j][:].indirect(pos_t[:]))
+
+        wsub1_b0 = placed("wsub1_b0", [PART, BANK, 4], BF16, at_ang)
+        wsub1_w = [kept("wsub1_w0", [PART, BANK], U32)]
+        wsub1_s = [kept("wsub1_s%d" % a, [PART, BANK], U8) for a in range(2)]
+
+        for j in range(ROW_TILES):
+            angles(j)
+        pick(0)
+        pick(1)
+        for h in range(2):
+            nc.vector.tensor_copy(
+                wsub1_b0[:].rearrange("p (t q h e) j -> p h t q j e", t=4, h=2, e=4)[:, h],
+                wsub1_raw[0][:].rearrange("p j (q t h e) -> p h t q j e", t=4, h=2, e=4)[:, h],
+            )
+        pick(2)
+        order_columns(wsub2_s[:], wsub2_s_raw[:], 2, nc.vector.tensor_copy)
+        quantize(wsub1_w[0][:], wsub1_s[0][:], wsub1_b0[:])
+        pick(3)
+        ang.append(placed("ang1", [PART, 4, P], F32, at_ang))
+        for j in range(4, ROW_TILES):
+            pick(j)
+
+        wsub1_b1 = placed("wsub1_b1", [PART, BANK, 4], BF16, at_th_last)
+        for t in range(4):
             nc.gpsimd.tensor_scalar(
-                both_b[0][:, BANK : BANK + GPSIMD_SPIN, :],
-                wspin_raw[0][:, :, 0:GPSIMD_SPIN].rearrange("p t n -> p n t"),
+                wsub1_b1[:, PART * t : PART * (t + 1), :].rearrange("p (q i) j -> p q i j", i=8),
+                wsub1_raw[1][:].rearrange("p j (q t i) -> p t q i j", t=4, i=8)[:, t],
                 1.0, 0.0, ALU.mult, ALU.add,
             )
 
-        def cast_wspin_first():
-            nc.scalar.copy(
-                both_b[0][:, BANK + GPSIMD_SPIN : 2 * BANK, :].rearrange("p (u e) t -> p u t e", e=4),
-                wspin_raw[0][:, :, GPSIMD_SPIN:N].rearrange("p t (u e) -> p u t e", e=4),
-            )
+        cos, sin, cos_b1, sin_b2 = {}, {}, {}, {}
+        last = (1, len(PIECES[1]) - 1)
 
-        def quantize_both():
-            both_w[0] = kept("both_w", [PART, 2 * BANK], U32, tag="cos2")
-            quantize(both_w[0], both_s, both_b[0])
-
-        def cast_wspin_second():
-            wspin_b[0] = kept("wspin_b", [PART, N, 4], BF16, tag="ang7")
-            nc.scalar.copy(
-                wspin_b[0][:].rearrange("p (u e) t -> p u t e", e=4),
-                wspin_raw[1][:].rearrange("p t (u e) -> p u t e", e=4),
-            )
-
-        def quantize(codes, scales, values):
-            nc.vector.quantize_mx(out=codes[:].bitcast(FP8X4), scales=scales[:], in_=values[:].rearrange("p c j -> p (c j)"))
-
-        def quantize_wsub1_first():
-            wsub1_w[0] = kept("wsub1_w0", [PART, BANK], U32, tag="wang_s_raw")
-            quantize(wsub1_w[0], wsub1_s[0], wsub1_b0)
-
-        def quantize_wspin_second():
-            quantize(wspin_w, wspin_s, wspin_b[0])
-
-        cos_b1 = [kept("cos_b1_%d" % a, [PART, 4, P], F32) for a in range(2)]
-        sin_b2 = [kept("sin_b2_%d" % a, [PART, 4, P], F32) for a in range(2)]
-        h_b = [[None] * len(PIECES[a]) for a in range(2)]
-        h_w = [[None] * len(PIECES[a]) for a in range(2)]
-        h_s = [[kept("h_s%d%d" % (a, c), [PART, w], U8) for c, (m0, w) in enumerate(PIECES[a])] for a in range(2)]
-        units = {j: unit for unit in UNITS for j in unit}
-        ang, cos, sin = {}, {}, {}
-
-        def pick(j):
-            unit = units[j]
-            if unit not in ang:
-                ang[unit] = kept("ang%d" % unit[0], [PART, len(unit), P], F32)
-            nc.vector.tensor_copy(ang[unit][:, j - unit[0], :], th[j][:].indirect(pos_t[:]))
-
-        def trig(unit):
-            cos[unit] = kept("cos%d" % unit[0], [PART, len(unit), P], F32)
-            sin[unit] = kept("sin%d" % unit[0], [PART, len(unit), P], F32, tag="stage0" if unit[0] == 0 else None)
-            nc.scalar.activation(cos[unit][:], ang[unit][:], ACT.Abs)
-            nc.scalar.activation(sin[unit][:], ang[unit][:], ACT.Sin)
-            nc.scalar.activation(cos[unit][:], cos[unit][:], ACT.Sin, bias=math.pi / 2, scale=-1.0)
-
-        def product(j, w_codes, w_scales, factor, dst):
-            bank = proj.tile([PART, P], F32, name="b", tag="b")
-            nc.tensor.matmul_mx(
-                out=bank[:],
-                lhsT=w_codes.bitcast(FP8X4),
-                lhsT_scale=w_scales,
-                rhs=v2_w[:].bitcast(FP8X4),
-                rhs_scale=v2_s[:],
-                start=True,
-                stop=True,
-            )
-            nc.vector.tensor_tensor(dst[j // 4][:, j % 4, :], bank[:], factor[units[j]][:, j - units[j][0], :], ALU.mult)
-
-        def products(unit):
-            for j in unit:
-                product(j, wsub2_w[:, PART * j : PART * (j + 1)], wsub2_s[:, 32 * j : 32 * (j + 1)].bitcast(U8), sin, sin_b2)
-            for j in unit:
-                codes, scales, t = (wsub1_w[0], wsub1_s[0], j) if j < 4 else (both_w[0], both_s, j - 4)
-                cols = slice(PART * t, PART * (t + 1))
-                product(j, codes[:, cols], scales[:, cols], cos, cos_b1)
-
-        def mix(a, c, engine, tag=None):
+        def trig(a, c):
             m0, w = PIECES[a][c]
-            h_b[a][c] = kept("h_b%d%d" % (a, c), [PART, w, 4], BF16, tag=tag)
+            if (a, c) == last:
+                cos[a, c] = placed("cos_last", [PART, 4, w], F32, at_cos_last)
+            else:
+                cos[a, c] = kept("cos%d%d" % (a, c), [PART, 4, w], F32)
+            sin[a, c] = kept("sin%d%d" % (a, c), [PART, 4, w], F32)
+            picked = ang[a][:, :, m0 : m0 + w]
+            nc.scalar.activation(cos[a, c][:], picked, ACT.Abs)
+            nc.scalar.activation(sin[a, c][:], picked, ACT.Sin)
+            nc.scalar.activation(cos[a, c][:], cos[a, c][:], ACT.Sin, bias=math.pi / 2, scale=-1.0)
+
+        def products(a, c, name, codes, scales, factor, dst, at=None):
+            m0, w = PIECES[a][c]
+            tiles = BANK // w
+            if at is None:
+                dst[a, c] = kept("%s%d%d" % (name, a, c), [PART, w // 4, 4, 4], F32)
+            else:
+                dst[a, c] = placed("%s%d%d" % (name, a, c), [PART, w // 4, 4, 4], F32, at)
+            for t0 in range(0, 4, tiles):
+                bank = banks.tile([PART, tiles, w], F32, name="bank", tag="bank")
+                for d in range(tiles):
+                    cols = slice(PART * (t0 + d), PART * (t0 + d + 1))
+                    nc.tensor.matmul_mx(
+                        out=bank[:, d, :],
+                        lhsT=codes[:, cols].bitcast(FP8X4),
+                        lhsT_scale=scales[:, cols],
+                        rhs=v2_w[:, m0 : m0 + w].bitcast(FP8X4),
+                        rhs_scale=v2_s[:, m0 : m0 + w],
+                        start=True,
+                        stop=True,
+                    )
+                nc.vector.tensor_tensor(
+                    dst[a, c][:].rearrange("p u t e -> p t u e")[:, t0 : t0 + tiles],
+                    bank[:].rearrange("p t (u e) -> p t u e", e=4),
+                    factor[a, c][:, t0 : t0 + tiles, :].rearrange("p t (u e) -> p t u e", e=4),
+                    ALU.mult,
+                )
+
+        def sine_products(a, c):
+            cols = slice(BANK * a, BANK * (a + 1))
+            products(a, c, "sin_b2_", wsub2_w[:, cols], wsub2_s[:].bitcast(U8)[:, cols], sin, sin_b2)
+
+        def cosine_products(a, c, at=None):
+            products(a, c, "cos_b1_", wsub1_w[a][:], wsub1_s[a][:], cos, cos_b1, at)
+
+        def mix(a, c, engine, dst):
             engine.tensor_tensor(
-                h_b[a][c][:].rearrange("p (u e) t -> p u t e", e=4),
-                cos_b1[a][:, :, m0 : m0 + w].rearrange("p t (u e) -> p u t e", e=4),
-                sin_b2[a][:, :, m0 : m0 + w].rearrange("p t (u e) -> p u t e", e=4),
-                ALU.add,
+                dst.rearrange("p (u e) t -> p u t e", e=4), cos_b1[a, c][:], sin_b2[a, c][:], ALU.add
             )
 
-        def quantize_h(a, c, tag=None):
-            h_w[a][c] = kept("h_w%d%d" % (a, c), [PART, PIECES[a][c][1]], U32, tag=tag)
-            quantize(h_w[a][c], h_s[a][c], h_b[a][c])
+        trig(0, 0)
+        sine_products(0, 0)
+        cosine_products(0, 0)
+        trig(0, 1)
+        sine_products(0, 1)
+        wsub1_w.append(kept("wsub1_w1", [PART, BANK], U32, tag="cos00"))
+        quantize(wsub1_w[1][:], wsub1_s[1][:], wsub1_b1[:])
+        cosine_products(0, 1, at_th_last + 2048)
+        h0_b = placed("h0_b", [PART, P, 4], BF16, at_th_last - 2048)
+        for c, (m0, w) in enumerate(PIECES[0]):
+            mix(0, c, nc.gpsimd, h0_b[:, m0 : m0 + w, :])
+        head_b = kept("head_b", [PART, GPSIMD_SPIN, 4], BF16, tag="cos_b1_00")
+        nc.gpsimd.tensor_scalar(
+            head_b[:], wspin_raw[1][:, :, 0:GPSIMD_SPIN].rearrange("p t n -> p n t"), 1.0, 0.0, ALU.mult, ALU.add
+        )
+        for c in range(len(PIECES[1])):
+            trig(1, c)
+            sine_products(1, c)
+            cosine_products(1, c)
 
+        first = (0, GPSIMD_SPIN)
+        wspin_b = [placed("wspin_b%d" % a, [PART, N - first[a], 4], BF16, at_ang + 4096 * a) for a in range(2)]
+        wspin_w = [placed("wspin_w0", [PART, N], U32, at_cos_last), kept("wspin_w1", [PART, N], U32)]
+        wspin_s = [kept("wspin_s%d" % a, [PART, N], U8) for a in range(2)]
+        for a in range(2):
+            nc.scalar.copy(
+                wspin_b[a][:].rearrange("p (u e) t -> p u t e", e=4),
+                wspin_raw[a][:, :, first[a] : N].rearrange("p t (u e) -> p u t e", e=4),
+            )
+
+        h0_w = placed("h0_w", [PART, P], U32, at_ang)
+        h0_s = kept("h0_s", [PART, P], U8)
+        h1_b = [
+            placed("h1_b0", [PART, 256, 4], BF16, at_th_last - 2048),
+            placed("h1_b1", [PART, 128, 4], BF16, at_ang + 4096),
+            placed("h1_b2", [PART, 128, 4], BF16, at_th_last - 2048),
+        ]
+        h1_w = [kept("h1_w%d" % c, [PART, w], U32) for c, (m0, w) in enumerate(PIECES[1])]
+        h1_s = [kept("h1_s%d" % c, [PART, w], U8) for c, (m0, w) in enumerate(PIECES[1])]
         out_banks = {}
-        last_piece = len(PIECES[1]) - 1
 
         def spin(a, c):
             m0, w = PIECES[1][c]
-            piece, off = (c, 0) if a == 1 else divmod(m0, PIECES[0][0][1])
-            tiles = TILES_PER_BANK[c]
+            tiles = OUT_TILES_PER_BANK[c]
+            codes, scales = (h0_w[:, m0 : m0 + w], h0_s[:, m0 : m0 + w]) if a == 0 else (h1_w[c][:], h1_s[c][:])
             for b in range(4 // tiles):
-                if a == 0 and c < last_piece:
-                    out_banks[c, b] = acc.tile([PART, tiles, w], F32, name="bank", tag="bank")
-                elif a == 0:
-                    out_banks[c, b] = proj.tile([PART, tiles, w], F32, name="b", tag="b")
+                if a == 0:
+                    out_banks[c, b] = banks.tile([PART, tiles, w], F32, name="bank", tag="bank")
                 for d in range(tiles):
-                    n = tiles * b + d
-                    codes, scales, at = (both_w[0], both_s, 4 + n) if a == 0 else (wspin_w, wspin_s, n)
-                    rows = slice(PART * at, PART * (at + 1))
+                    rows = slice(PART * (tiles * b + d), PART * (tiles * b + d + 1))
                     nc.tensor.matmul_mx(
                         out=out_banks[c, b][:, d, :],
-                        lhsT=codes[:, rows].bitcast(FP8X4),
-                        lhsT_scale=scales[:, rows],
-                        rhs=h_w[a][piece][:, off : off + w].bitcast(FP8X4),
-                        rhs_scale=h_s[a][piece][:, off : off + w],
+                        lhsT=wspin_w[a][:, rows].bitcast(FP8X4),
+                        lhsT_scale=wspin_s[a][:, rows],
+                        rhs=codes.bitcast(FP8X4),
+                        rhs_scale=scales,
                         start=(a == 0 and d == 0),
                         stop=(a == 1 and d == tiles - 1),
                     )
@@ -324,60 +336,28 @@ def tile_list_halo_spin_orientation_kernel(
 
         def store(c):
             m0, w = PIECES[1][c]
-            tiles = TILES_PER_BANK[c]
+            tiles = OUT_TILES_PER_BANK[c]
             for b in range(4 // tiles):
                 res = kept("res%d%d" % (c, b), [PART, tiles, w], F32)
-                if b == 0 or c < last_piece:
+                if b == 0 or c < last[1]:
                     nc.scalar.copy(res[:], out_banks[c, b][:])
                 else:
                     nc.vector.tensor_copy(res[:], out_banks[c, b][:])
                 nc.sync.dma_start(out_v[:, tiles * b : tiles * (b + 1), m0 : m0 + w], res[:])
 
-        both(0)
-        both(1)
-        second_gathers()
-        pick(0)
-        pick(1)
-        both(2)
-        both(3)
-        cast_wsub1_first()
-        pick(2)
-        pick(3)
-        both(4)
-        both(5)
-        pick(4)
-        pick(5)
-        second_weights()
-        quantize_wsub1_first()
-        cast_on_gpsimd()
-        for unit in UNITS[:2]:
-            trig(unit)
-            products(unit)
-        cast_wspin_first()
-        both(6)
-        both(7)
-        quantize_both()
-        mix(0, 1, nc.vector)
-        pick(6)
-        quantize_h(0, 1)
-        pick(7)
-        mix(0, 0, nc.gpsimd, tag="th7")
-        for unit in UNITS[2:]:
-            trig(unit)
-            products(unit)
-        cast_wspin_second()
-        quantize_h(0, 0, tag="cos7")
-        spin(0, 0)
-        spin(0, 1)
-        spin(0, last_piece)
-        mix(1, 0, nc.vector)
-        quantize_wspin_second()
-        quantize_h(1, 0)
+        quantize(wspin_w[0][:], wspin_s[0][:], wspin_b[0][:])
+        quantize(h0_w[:], h0_s[:], h0_b[:])
+        for c in range(len(PIECES[1])):
+            spin(0, c)
+        quantize(wspin_w[1][:, 0:GPSIMD_SPIN], wspin_s[1][:, 0:GPSIMD_SPIN], head_b[:])
+        mix(1, 0, nc.vector, h1_b[0][:])
+        quantize(wspin_w[1][:, GPSIMD_SPIN:N], wspin_s[1][:, GPSIMD_SPIN:N], wspin_b[1][:])
+        quantize(h1_w[0][:], h1_s[0][:], h1_b[0][:])
         spin(1, 0)
         store(0)
-        mix(1, 1, nc.vector, tag="ang7")
-        mix(1, 2, nc.vector)
+        mix(1, 1, nc.vector, h1_b[1][:])
+        mix(1, 2, nc.vector, h1_b[2][:])
         for c in (1, 2):
-            quantize_h(1, c)
+            quantize(h1_w[c][:], h1_s[c][:], h1_b[c][:])
             spin(1, c)
             store(c)

@@ -25,7 +25,6 @@ ROW_TILES = H // PART
 BIAS_ROW = PART - ROW_TILES
 PIECES = ([(0, 256), (256, 256)], [(0, 256), (256, 128), (384, 128)])
 OUT_TILES_PER_BANK = (2, 4, 2)
-GPSIMD_SPIN = 128
 
 
 def tile_list_halo_spin_orientation_kernel(
@@ -78,8 +77,10 @@ def tile_list_halo_spin_orientation_kernel(
         v_s = kept("v_s", [PART, 2, S], U8)
         bias_rows = kept("bias_rows", [PART, PART], F32)
         ident = kept("ident", [PART, PART], F32)
-        nc.gpsimd.memset(weight_s_raw[:], 0)
+        nc.vector.memset(weight_s_raw[:], 0)
         make_identity(nc, ident[:])
+        nc.vector.memset(tab2_s[:].bitcast(I32), 0)
+        nc.gpsimd.dma_start(tab2_s[0:16, :].bitcast(I32), tab2_scales[0].bitcast(I32))
         nc.vector.memset(tab_s[32:64, :].bitcast(I32), 0)
         nc.vector.memset(tab_s[64:PART, :].bitcast(I32), 0)
         for a in range(2):
@@ -87,7 +88,6 @@ def tile_list_halo_spin_orientation_kernel(
                 bias_rows[BIAS_ROW + 4 * a : BIAS_ROW + 4 * a + 4, :].rearrange("t (q i) -> t q i", i=8),
                 bang[BANK * a : BANK * (a + 1)].rearrange("(q t i) -> t q i", t=4, i=8),
             )
-        nc.vector.memset(tab2_s[:].bitcast(I32), 0)
         nc.vector.memset(wsub2_s_raw[:], 0)
         nc.vector.memset(bias_rows[0:96, :], 0.0)
         nc.vector.memset(bias_rows[96:BIAS_ROW, :], 0.0)
@@ -117,11 +117,10 @@ def tile_list_halo_spin_orientation_kernel(
             nc.sync.dma_start(
                 v_s[32 * quad : 32 * quad + 4].bitcast(I32), v_sg[8 * quad : 8 * quad + 8, :].bitcast(I32)
             )
-        nc.sync.dma_start(wang_raw[1][:], wang_v[:, :, BANK // 2 : BANK])
         nc.sync.dma_start(wsub2_raw[:], words(wsub2_words[0]))
-        load_plane(tab2_s[:].bitcast(I32), tab2_scales[0])
         nc.sync.dma_start(tab2_w[:], words(tab2_words[0]))
         nc.sync.dma_start(pos_t[:], pos1)
+        nc.sync.dma_start(wang_raw[1][:], wang_v[:, :, BANK // 2 : BANK])
         nc.sync.dma_start(wsub1_raw[0][:], wsub1_v[:, :, 0:BANK])
         load_plane(wsub2_s_raw[:], wsub2_scales[0])
 
@@ -130,7 +129,8 @@ def tile_list_halo_spin_orientation_kernel(
         bias = kept("bias", [PART, ROW_TILES], F32)
         nc.scalar.copy(bias[:], bias_ps[:, BIAS_ROW:PART])
 
-        v_w = [[kept("v_w%d%d" % (g, half), [PART, BANK], U32) for half in range(2)] for g in range(2)]
+        later = {(0, 1): "cos00", (1, 1): "sin00"}
+        v_w = [[kept("v_w%d%d" % (g, half), [PART, BANK], U32, later.get((g, half))) for half in range(2)] for g in range(2)]
 
         def gather_v(g, half):
             picks = offs_t[:, 32 * half : 32 * (half + 1)]
@@ -141,14 +141,20 @@ def tile_list_halo_spin_orientation_kernel(
         wsub2_w = kept("wsub2_w", [PART, H], I32)
         wsub2_s = kept("wsub2_s", [PART, H // 4], I32)
 
-        def order_wang(a):
-            order_columns(wang_w[a][:].rearrange("p g c -> p (g c)"), wang_raw[a][:].rearrange("p g c -> p (g c)"), 4, scalar_move)
+        def order_wang(a, copy):
+            order_columns(wang_w[a][:].rearrange("p g c -> p (g c)"), wang_raw[a][:].rearrange("p g c -> p (g c)"), 4, copy)
 
         gather_v(0, 0)
         gather_v(0, 1)
-        order_wang(0)
+        v2_sg = kept("v2_sg", [PART, P], U8)
+        v2_s = kept("v2_s", [PART, P], U8)
+        nc.vector.tensor_copy(v2_sg[:], tab2_s[:].indirect(offs2_t[:]))
+        for quad in range(QUADS):
+            nc.sync.dma_start(
+                v2_s[32 * quad : 32 * quad + 4, :].bitcast(I32), v2_sg[4 * quad : 4 * quad + 4, :].bitcast(I32)
+            )
         order_columns(wang_s[:].rearrange("p g c -> p (g c)"), weight_s_raw[:], 2, scalar_move)
-        order_wang(1)
+        order_wang(0, scalar_move)
         gather_v(1, 0)
         gather_v(1, 1)
         order_columns(wsub2_w[:], wsub2_raw[:], 8, scalar_move)
@@ -156,8 +162,6 @@ def tile_list_halo_spin_orientation_kernel(
         nc.sync.dma_start(wsub1_raw[1][:], wsub1_v[:, :, BANK : 2 * BANK])
 
         v2_w = kept("v2_w", [PART, P], U32)
-        v2_s = kept("v2_s", [PART, P], U8)
-        nc.vector.tensor_copy(v2_s[:], tab2_s[:].indirect(offs2_t[:]))
         nc.vector.tensor_copy(v2_w[:], tab2_w[:].bitcast(U32).indirect(offs2_t[:]))
 
         wspin_v = wspin.rearrange("(a q t i) n -> a t q i n", a=2, t=4, i=8)
@@ -174,15 +178,15 @@ def tile_list_halo_spin_orientation_kernel(
             for half in range(2):
                 cols = slice(BANK * half, BANK * (half + 1))
                 bank = banks.tile([PART, BANK], F32, name="bank", tag="bank")
-                for g in (1, 0):
+                for g in range(2):
                     nc.tensor.matmul_mx(
                         out=bank[:],
                         lhsT=wang_w[j // 4][:, g, 64 * (j % 4) : 64 * (j % 4 + 1)].bitcast(FP4X4),
                         lhsT_scale=wang_s[:, g, 32 * j : 32 * (j + 1)].bitcast(U8),
                         rhs=v_w[g][half][:].bitcast(FP8X4),
                         rhs_scale=v_s[:, g, cols],
-                        start=(g == 1),
-                        stop=(g == 0),
+                        start=(g == 0),
+                        stop=(g == 1),
                     )
                 nc.scalar.activation(th[j][:, cols], bank[:], ACT.Identity, bias=bias[:, j : j + 1])
 
@@ -193,9 +197,12 @@ def tile_list_halo_spin_orientation_kernel(
         wsub1_w = [kept("wsub1_w0", [PART, BANK], U32)]
         wsub1_s = [kept("wsub1_s%d" % a, [PART, BANK], U8) for a in range(2)]
 
-        for j in range(ROW_TILES):
+        for j in range(4):
             angles(j)
         pick(0)
+        order_wang(1, nc.vector.tensor_copy)
+        for j in range(4, ROW_TILES):
+            angles(j)
         pick(1)
         for h in range(2):
             nc.vector.tensor_copy(
@@ -277,29 +284,24 @@ def tile_list_halo_spin_orientation_kernel(
         cosine_products(0, 0)
         trig(0, 1)
         sine_products(0, 1)
-        wsub1_w.append(kept("wsub1_w1", [PART, BANK], U32, tag="cos00"))
+        wsub1_w.append(kept("wsub1_w1", [PART, BANK], U32, tag="sin01"))
         quantize(wsub1_w[1][:], wsub1_s[1][:], wsub1_b1[:])
         cosine_products(0, 1, at_th_last + 2048)
         h0_b = placed("h0_b", [PART, P, 4], BF16, at_th_last - 2048)
         for c, (m0, w) in enumerate(PIECES[0]):
             mix(0, c, nc.gpsimd, h0_b[:, m0 : m0 + w, :])
-        head_b = kept("head_b", [PART, GPSIMD_SPIN, 4], BF16, tag="cos_b1_00")
-        nc.gpsimd.tensor_scalar(
-            head_b[:], wspin_raw[1][:, :, 0:GPSIMD_SPIN].rearrange("p t n -> p n t"), 1.0, 0.0, ALU.mult, ALU.add
-        )
         for c in range(len(PIECES[1])):
             trig(1, c)
             sine_products(1, c)
             cosine_products(1, c)
 
-        first = (0, GPSIMD_SPIN)
-        wspin_b = [placed("wspin_b%d" % a, [PART, N - first[a], 4], BF16, at_ang + 4096 * a) for a in range(2)]
-        wspin_w = [placed("wspin_w0", [PART, N], U32, at_cos_last), kept("wspin_w1", [PART, N], U32)]
+        wspin_b = [placed("wspin_b%d" % a, [PART, N, 4], BF16, at_ang + 4096 * a) for a in range(2)]
+        wspin_w = [placed("wspin_w0", [PART, N], U32, at_cos_last), placed("wspin_w1", [PART, N], U32, at_th_last)]
         wspin_s = [kept("wspin_s%d" % a, [PART, N], U8) for a in range(2)]
         for a in range(2):
             nc.scalar.copy(
                 wspin_b[a][:].rearrange("p (u e) t -> p u t e", e=4),
-                wspin_raw[a][:, :, first[a] : N].rearrange("p t (u e) -> p u t e", e=4),
+                wspin_raw[a][:].rearrange("p t (u e) -> p u t e", e=4),
             )
 
         h0_w = placed("h0_w", [PART, P], U32, at_ang)
@@ -349,9 +351,8 @@ def tile_list_halo_spin_orientation_kernel(
         quantize(h0_w[:], h0_s[:], h0_b[:])
         for c in range(len(PIECES[1])):
             spin(0, c)
-        quantize(wspin_w[1][:, 0:GPSIMD_SPIN], wspin_s[1][:, 0:GPSIMD_SPIN], head_b[:])
         mix(1, 0, nc.vector, h1_b[0][:])
-        quantize(wspin_w[1][:, GPSIMD_SPIN:N], wspin_s[1][:, GPSIMD_SPIN:N], wspin_b[1][:])
+        quantize(wspin_w[1][:], wspin_s[1][:], wspin_b[1][:])
         quantize(h1_w[0][:], h1_s[0][:], h1_b[0][:])
         spin(1, 0)
         store(0)

@@ -69,9 +69,10 @@ def tile_list_halo_spin_orientation_kernel(
         offs2_t = lists.tile([PART, P // 16], U16, name="offs2_t")
 
         tab_s = kept("tab_s", [PART, T], U8)
-        at_th_last, at_ang, at_cos_last = 2048, 8192, 18432
+        at_th_last, at_ang, at_cos_last = 2048, 11264, 19584
+        at_wsub1_b1, at_h0_b = 4096, 6144
         weight_s_raw = kept("weight_s_raw", [PART, H // 2], I32)
-        wsub2_s_raw = placed("wsub2_s_raw", [PART, H // 4], I32, at_ang + 4096)
+        wsub2_s_raw = kept("wsub2_s_raw", [PART, H // 4], I32)
         tab2_s = kept("tab2_s", [PART, T2], U8)
         v_sg = kept("v_sg", [PART, S], U8)
         v_s = kept("v_s", [PART, 2, S], U8)
@@ -139,7 +140,6 @@ def tile_list_halo_spin_orientation_kernel(
         wang_w = [kept("wang_w%d" % a, [PART, 2, BANK // 2], I32) for a in range(2)]
         wang_s = kept("wang_s", [PART, 2, H // 4], I32)
         wsub2_w = kept("wsub2_w", [PART, H], I32)
-        wsub2_s = kept("wsub2_s", [PART, H // 4], I32)
 
         def order_wang(a, copy):
             order_columns(wang_w[a][:].rearrange("p g c -> p (g c)"), wang_raw[a][:].rearrange("p g c -> p (g c)"), 4, copy)
@@ -158,17 +158,18 @@ def tile_list_halo_spin_orientation_kernel(
         gather_v(1, 0)
         gather_v(1, 1)
         order_columns(wsub2_w[:], wsub2_raw[:], 8, scalar_move)
-        wsub1_raw.append(kept("wsub1_raw1", [PART, 4, BANK], F32, tag="stage0"))
-        nc.sync.dma_start(wsub1_raw[1][:], wsub1_v[:, :, BANK : 2 * BANK])
 
         v2_w = kept("v2_w", [PART, P], U32)
         nc.vector.tensor_copy(v2_w[:], tab2_w[:].bitcast(U32).indirect(offs2_t[:]))
 
         wspin_v = wspin.rearrange("(a q t i) n -> a t q i n", a=2, t=4, i=8)
         wspin_raw = [kept("wspin_raw%d" % a, [PART, 4, N], F32, tag="stage%d" % (a + 1)) for a in range(2)]
+        wsub1_raw.append(kept("wsub1_raw1", [PART, 4, BANK], F32, tag="stage0"))
         for a in range(2):
             for t in range(4):
                 nc.sync.dma_start(wspin_raw[a][:, t, :], wspin_v[a, t])
+            if a == 0:
+                nc.sync.dma_start(wsub1_raw[1][:], wsub1_v[:, :, BANK : 2 * BANK])
 
         th = [kept("th%d" % j, [PART, S], F32) for j in range(ROW_TILES - 1)]
         th.append(placed("th7", [PART, S], F32, at_th_last))
@@ -193,8 +194,7 @@ def tile_list_halo_spin_orientation_kernel(
         def pick(j):
             nc.vector.tensor_copy(ang[j // 4][:, j % 4, :], th[j][:].indirect(pos_t[:]))
 
-        wsub1_b0 = placed("wsub1_b0", [PART, BANK, 4], BF16, at_ang)
-        wsub1_w = [kept("wsub1_w0", [PART, BANK], U32)]
+        wsub1_b0 = kept("wsub1_b0", [PART, BANK, 4], BF16)
         wsub1_s = [kept("wsub1_s%d" % a, [PART, BANK], U8) for a in range(2)]
 
         for j in range(4):
@@ -209,15 +209,31 @@ def tile_list_halo_spin_orientation_kernel(
                 wsub1_b0[:].rearrange("p (t q h e) j -> p h t q j e", t=4, h=2, e=4)[:, h],
                 wsub1_raw[0][:].rearrange("p j (q t h e) -> p h t q j e", t=4, h=2, e=4)[:, h],
             )
-        pick(2)
-        order_columns(wsub2_s[:], wsub2_s_raw[:], 2, nc.vector.tensor_copy)
-        quantize(wsub1_w[0][:], wsub1_s[0][:], wsub1_b0[:])
-        pick(3)
-        ang.append(placed("ang1", [PART, 4, P], F32, at_ang))
-        for j in range(4, ROW_TILES):
-            pick(j)
+        wspin_b = [placed("wspin_b0", [PART, N, 4], BF16, at_ang)]
+        wspin_w = [kept("wspin_w0", [PART, N], U32)]
+        wspin_s = [kept("wspin_s%d" % a, [PART, N], U8) for a in range(2)]
 
-        wsub1_b1 = placed("wsub1_b1", [PART, BANK, 4], BF16, at_th_last)
+        def round_wspin(a, copy):
+            copy(
+                wspin_b[a][:].rearrange("p (u e) t -> p u t e", e=4),
+                wspin_raw[a][:].rearrange("p t (u e) -> p u t e", e=4),
+            )
+
+        pick(2)
+        round_wspin(0, nc.vector.tensor_copy)
+        pick(3)
+        quantize(wspin_w[0][:], wspin_s[0][:], wspin_b[0][:])
+        ang.append(placed("ang1", [PART, 4, P], F32, at_ang))
+        pick(4)
+        pick(5)
+        wsub1_w = [kept("wsub1_w0", [PART, BANK], U32, tag="th4")]
+        quantize(wsub1_w[0][:], wsub1_s[0][:], wsub1_b0[:])
+        pick(6)
+        wsub2_s = kept("wsub2_s", [PART, H // 4], I32, tag="th5")
+        order_columns(wsub2_s[:], wsub2_s_raw[:], 2, nc.vector.tensor_copy)
+        pick(7)
+
+        wsub1_b1 = placed("wsub1_b1", [PART, BANK, 4], BF16, at_wsub1_b1)
         for t in range(4):
             nc.gpsimd.tensor_scalar(
                 wsub1_b1[:, PART * t : PART * (t + 1), :].rearrange("p (q i) j -> p q i j", i=8),
@@ -286,8 +302,8 @@ def tile_list_halo_spin_orientation_kernel(
         sine_products(0, 1)
         wsub1_w.append(kept("wsub1_w1", [PART, BANK], U32, tag="sin01"))
         quantize(wsub1_w[1][:], wsub1_s[1][:], wsub1_b1[:])
-        cosine_products(0, 1, at_th_last + 2048)
-        h0_b = placed("h0_b", [PART, P, 4], BF16, at_th_last - 2048)
+        cosine_products(0, 1, at_th_last)
+        h0_b = placed("h0_b", [PART, P, 4], BF16, at_h0_b)
         for c, (m0, w) in enumerate(PIECES[0]):
             mix(0, c, nc.gpsimd, h0_b[:, m0 : m0 + w, :])
         for c in range(len(PIECES[1])):
@@ -295,21 +311,16 @@ def tile_list_halo_spin_orientation_kernel(
             sine_products(1, c)
             cosine_products(1, c)
 
-        wspin_b = [placed("wspin_b%d" % a, [PART, N, 4], BF16, at_ang + 4096 * a) for a in range(2)]
-        wspin_w = [placed("wspin_w0", [PART, N], U32, at_cos_last), placed("wspin_w1", [PART, N], U32, at_th_last)]
-        wspin_s = [kept("wspin_s%d" % a, [PART, N], U8) for a in range(2)]
-        for a in range(2):
-            nc.scalar.copy(
-                wspin_b[a][:].rearrange("p (u e) t -> p u t e", e=4),
-                wspin_raw[a][:].rearrange("p t (u e) -> p u t e", e=4),
-            )
+        wspin_b.append(placed("wspin_b1", [PART, N, 4], BF16, at_ang))
+        wspin_w.append(placed("wspin_w1", [PART, N], U32, at_h0_b + 2048))
+        round_wspin(1, nc.scalar.copy)
 
-        h0_w = placed("h0_w", [PART, P], U32, at_ang)
+        h0_w = placed("h0_w", [PART, P], U32, at_cos_last)
         h0_s = kept("h0_s", [PART, P], U8)
         h1_b = [
-            placed("h1_b0", [PART, 256, 4], BF16, at_th_last - 2048),
-            placed("h1_b1", [PART, 128, 4], BF16, at_ang + 4096),
-            placed("h1_b2", [PART, 128, 4], BF16, at_th_last - 2048),
+            placed("h1_b0", [PART, 256, 4], BF16, at_h0_b),
+            placed("h1_b1", [PART, 128, 4], BF16, at_ang),
+            placed("h1_b2", [PART, 128, 4], BF16, at_h0_b),
         ]
         h1_w = [kept("h1_w%d" % c, [PART, w], U32) for c, (m0, w) in enumerate(PIECES[1])]
         h1_s = [kept("h1_s%d" % c, [PART, w], U8) for c, (m0, w) in enumerate(PIECES[1])]
@@ -347,7 +358,6 @@ def tile_list_halo_spin_orientation_kernel(
                     nc.vector.tensor_copy(res[:], out_banks[c, b][:])
                 nc.sync.dma_start(out_v[:, tiles * b : tiles * (b + 1), m0 : m0 + w], res[:])
 
-        quantize(wspin_w[0][:], wspin_s[0][:], wspin_b[0][:])
         quantize(h0_w[:], h0_s[:], h0_b[:])
         for c in range(len(PIECES[1])):
             spin(0, c)

@@ -24,7 +24,7 @@ QUADS = 4
 ROW_TILES = H // PART
 BIAS_ROW = PART - ROW_TILES
 PIECES = ([(0, 256), (256, 256)], [(0, 256), (256, 128), (384, 128)])
-OUT_TILES_PER_BANK = (2, 4, 2)
+OUT_TILES_PER_BANK = (2, 2, 2)
 
 
 def tile_list_halo_spin_orientation_kernel(
@@ -37,7 +37,8 @@ def tile_list_halo_spin_orientation_kernel(
         lists = ctx.enter_context(tc.tile_pool(name="lists", bufs=1))
         keep = ctx.enter_context(tc.tile_pool(name="keep", bufs=1))
         shared = ctx.enter_context(tc.tile_pool(name="shared", bufs=1))
-        banks = ctx.enter_context(tc.psum_pool(name="banks", bufs=8))
+        banks = ctx.enter_context(tc.psum_pool(name="banks", bufs=5))
+        proj = ctx.enter_context(tc.psum_pool(name="proj", bufs=3))
 
         def kept(name, shape, dtype, tag=None):
             return keep.tile(shape, dtype, name=name, tag=tag or name, align_bytes=64)
@@ -69,8 +70,7 @@ def tile_list_halo_spin_orientation_kernel(
         offs2_t = lists.tile([PART, P // 16], U16, name="offs2_t")
 
         tab_s = kept("tab_s", [PART, T], U8)
-        at_th_last, at_ang, at_cos_last = 2048, 11264, 19584
-        at_wsub1_b1, at_h0_b = 4096, 6144
+        at_th_last, at_h0_b, at_ang, at_cos_last = 0, 4096, 8192, 18432
         weight_s_raw = kept("weight_s_raw", [PART, H // 2], I32)
         wsub2_s_raw = kept("wsub2_s_raw", [PART, H // 4], I32)
         tab2_s = kept("tab2_s", [PART, T2], U8)
@@ -99,7 +99,7 @@ def tile_list_halo_spin_orientation_kernel(
         wang_raw = [kept("wang_raw%d" % a, [PART, 2, BANK // 2], I32) for a in range(2)]
         wang_v = wang_words.rearrange("g p c -> p g c").bitcast(I32)
         tab2_w = kept("tab2_w", [PART, T2], I32, tag="stage2")
-        wsub2_raw = kept("wsub2_raw", [PART, H], I32)
+        wsub2_raw = kept("wsub2_raw", [PART, H], I32, tag="wsub1_w1")
         wsub1_v = wsub1.rearrange("(p j) c -> p j c", j=4)
         wsub1_raw = [kept("wsub1_raw0", [PART, 4, BANK], F32)]
         nc.sync.dma_start(offs_t[:], offs)
@@ -112,18 +112,18 @@ def tile_list_halo_spin_orientation_kernel(
             )
         nc.sync.dma_start(wang_raw[0][:], wang_v[:, :, 0 : BANK // 2])
         nc.sync.dma_start(offs2_t[:], offs2)
-        nc.sync.dma_start(tab_w[1][:], words(tab_words[1]))
+        nc.sync.dma_start(tab_w[1][:, 0 : 3 * T // 4], words(tab_words[1])[:, 0 : 3 * T // 4])
         nc.vector.tensor_copy(v_sg[:], tab_s[:].indirect(offs_t[:]))
         for quad in range(QUADS):
             nc.sync.dma_start(
                 v_s[32 * quad : 32 * quad + 4].bitcast(I32), v_sg[8 * quad : 8 * quad + 8, :].bitcast(I32)
             )
-        nc.sync.dma_start(wsub2_raw[:], words(wsub2_words[0]))
+        nc.sync.dma_start(tab_w[1][:, 3 * T // 4 : T], words(tab_words[1])[:, 3 * T // 4 : T])
         nc.sync.dma_start(tab2_w[:], words(tab2_words[0]))
         nc.sync.dma_start(pos_t[:], pos1)
         nc.sync.dma_start(wang_raw[1][:], wang_v[:, :, BANK // 2 : BANK])
         nc.sync.dma_start(wsub1_raw[0][:], wsub1_v[:, :, 0:BANK])
-        load_plane(wsub2_s_raw[:], wsub2_scales[0])
+        nc.sync.dma_start(wsub2_raw[:], words(wsub2_words[0]))
 
         bias_ps = banks.tile([PART, BANK], F32, name="bank", tag="bank")
         nc.tensor.transpose(bias_ps[:, 0:PART], bias_rows[:], ident[:])
@@ -149,27 +149,26 @@ def tile_list_halo_spin_orientation_kernel(
         v2_sg = kept("v2_sg", [PART, P], U8)
         v2_s = kept("v2_s", [PART, P], U8)
         nc.vector.tensor_copy(v2_sg[:], tab2_s[:].indirect(offs2_t[:]))
-        for quad in range(QUADS):
-            nc.sync.dma_start(
-                v2_s[32 * quad : 32 * quad + 4, :].bitcast(I32), v2_sg[4 * quad : 4 * quad + 4, :].bitcast(I32)
-            )
         order_columns(wang_s[:].rearrange("p g c -> p (g c)"), weight_s_raw[:], 2, scalar_move)
         order_wang(0, scalar_move)
         gather_v(1, 0)
         gather_v(1, 1)
-        order_columns(wsub2_w[:], wsub2_raw[:], 8, scalar_move)
 
         v2_w = kept("v2_w", [PART, P], U32)
         nc.vector.tensor_copy(v2_w[:], tab2_w[:].bitcast(U32).indirect(offs2_t[:]))
 
         wspin_v = wspin.rearrange("(a q t i) n -> a t q i n", a=2, t=4, i=8)
-        wspin_raw = [kept("wspin_raw%d" % a, [PART, 4, N], F32, tag="stage%d" % (a + 1)) for a in range(2)]
         wsub1_raw.append(kept("wsub1_raw1", [PART, 4, BANK], F32, tag="stage0"))
+        nc.sync.dma_start(wsub1_raw[1][:], wsub1_v[:, :, BANK : 2 * BANK])
+        load_plane(wsub2_s_raw[:], wsub2_scales[0])
+        for quad in range(QUADS):
+            nc.sync.dma_start(
+                v2_s[32 * quad : 32 * quad + 4, :].bitcast(I32), v2_sg[4 * quad : 4 * quad + 4, :].bitcast(I32)
+            )
+        wspin_raw = [kept("wspin_raw%d" % a, [PART, 4, N], F32, tag="stage%d" % (a + 1)) for a in range(2)]
         for a in range(2):
             for t in range(4):
                 nc.sync.dma_start(wspin_raw[a][:, t, :], wspin_v[a, t])
-            if a == 0:
-                nc.sync.dma_start(wsub1_raw[1][:], wsub1_v[:, :, BANK : 2 * BANK])
 
         th = [kept("th%d" % j, [PART, S], F32) for j in range(ROW_TILES - 1)]
         th.append(placed("th7", [PART, S], F32, at_th_last))
@@ -194,7 +193,7 @@ def tile_list_halo_spin_orientation_kernel(
         def pick(j):
             nc.vector.tensor_copy(ang[j // 4][:, j % 4, :], th[j][:].indirect(pos_t[:]))
 
-        wsub1_b0 = kept("wsub1_b0", [PART, BANK, 4], BF16)
+        wsub1_b0 = placed("wsub1_b0", [PART, BANK, 4], BF16, at_ang)
         wsub1_s = [kept("wsub1_s%d" % a, [PART, BANK], U8) for a in range(2)]
 
         for j in range(4):
@@ -209,37 +208,32 @@ def tile_list_halo_spin_orientation_kernel(
                 wsub1_b0[:].rearrange("p (t q h e) j -> p h t q j e", t=4, h=2, e=4)[:, h],
                 wsub1_raw[0][:].rearrange("p j (q t h e) -> p h t q j e", t=4, h=2, e=4)[:, h],
             )
-        wspin_b = [placed("wspin_b0", [PART, N, 4], BF16, at_ang)]
-        wspin_w = [kept("wspin_w0", [PART, N], U32)]
+        wsub1_b1 = [kept("wsub1_b1%d" % half, [PART, 256, 4], BF16) for half in range(2)]
         wspin_s = [kept("wspin_s%d" % a, [PART, N], U8) for a in range(2)]
 
-        def round_wspin(a, copy):
-            copy(
-                wspin_b[a][:].rearrange("p (u e) t -> p u t e", e=4),
-                wspin_raw[a][:].rearrange("p t (u e) -> p u t e", e=4),
-            )
 
         pick(2)
-        round_wspin(0, nc.vector.tensor_copy)
+        order_columns(wsub2_w[:], wsub2_raw[:], 8, nc.vector.tensor_copy)
         pick(3)
-        quantize(wspin_w[0][:], wspin_s[0][:], wspin_b[0][:])
-        ang.append(placed("ang1", [PART, 4, P], F32, at_ang))
-        pick(4)
-        pick(5)
-        wsub1_w = [kept("wsub1_w0", [PART, BANK], U32, tag="th4")]
-        quantize(wsub1_w[0][:], wsub1_s[0][:], wsub1_b0[:])
-        pick(6)
-        wsub2_s = kept("wsub2_s", [PART, H // 4], I32, tag="th5")
-        order_columns(wsub2_s[:], wsub2_s_raw[:], 2, nc.vector.tensor_copy)
-        pick(7)
-
-        wsub1_b1 = placed("wsub1_b1", [PART, BANK, 4], BF16, at_wsub1_b1)
-        for t in range(4):
-            nc.gpsimd.tensor_scalar(
-                wsub1_b1[:, PART * t : PART * (t + 1), :].rearrange("p (q i) j -> p q i j", i=8),
-                wsub1_raw[1][:].rearrange("p j (q t i) -> p t q i j", t=4, i=8)[:, t],
-                1.0, 0.0, ALU.mult, ALU.add,
+        halves = [slice(256 * half, 256 * (half + 1)) for half in range(2)]
+        for half in range(2):
+            nc.vector.tensor_copy(
+                wsub1_b1[half][:].rearrange("p (t q i) j -> p t q j i", t=2, i=8),
+                wsub1_raw[1][:].rearrange("p j (q t i) -> p t q j i", t=4, i=8)[:, 2 * half : 2 * half + 2],
             )
+        late_w = kept("wsub1_w1", [PART, BANK], U32)
+        for half in range(2):
+            quantize(late_w[:, halves[half]], wsub1_s[1][:, halves[half]], wsub1_b1[half][:])
+        wsub1_w = [kept("wsub1_w0", [PART, BANK], U32, tag="wsub1_b10"), late_w]
+        quantize(wsub1_w[0][:], wsub1_s[0][:], wsub1_b0[:])
+        wsub2_s = kept("wsub2_s", [PART, H // 4], I32, tag="wsub1_b11")
+        order_columns(wsub2_s[:], wsub2_s_raw[:], 2, nc.vector.tensor_copy)
+        ang.append(placed("ang1", [PART, 4, P], F32, at_ang))
+        for j in range(4, ROW_TILES):
+            pick(j)
+
+        wspin_b0 = placed("wspin_b0", [PART, N, 4], BF16, at_th_last)
+        nc.gpsimd.tensor_scalar(wspin_b0[:], wspin_raw[0][:].rearrange("p t n -> p n t"), 1.0, 0.0, ALU.mult, ALU.add)
 
         cos, sin, cos_b1, sin_b2 = {}, {}, {}, {}
         last = (1, len(PIECES[1]) - 1)
@@ -256,15 +250,12 @@ def tile_list_halo_spin_orientation_kernel(
             nc.scalar.activation(sin[a, c][:], picked, ACT.Sin)
             nc.scalar.activation(cos[a, c][:], cos[a, c][:], ACT.Sin, bias=math.pi / 2, scale=-1.0)
 
-        def products(a, c, name, codes, scales, factor, dst, at=None):
+        def products(a, c, name, codes, scales, factor, dst):
             m0, w = PIECES[a][c]
             tiles = BANK // w
-            if at is None:
-                dst[a, c] = kept("%s%d%d" % (name, a, c), [PART, w // 4, 4, 4], F32)
-            else:
-                dst[a, c] = placed("%s%d%d" % (name, a, c), [PART, w // 4, 4, 4], F32, at)
+            dst[a, c] = kept("%s%d%d" % (name, a, c), [PART, w // 4, 4, 4], F32)
             for t0 in range(0, 4, tiles):
-                bank = banks.tile([PART, tiles, w], F32, name="bank", tag="bank")
+                bank = proj.tile([PART, tiles, w], F32, name="projection", tag="projection")
                 for d in range(tiles):
                     cols = slice(PART * (t0 + d), PART * (t0 + d + 1))
                     nc.tensor.matmul_mx(
@@ -287,8 +278,8 @@ def tile_list_halo_spin_orientation_kernel(
             cols = slice(BANK * a, BANK * (a + 1))
             products(a, c, "sin_b2_", wsub2_w[:, cols], wsub2_s[:].bitcast(U8)[:, cols], sin, sin_b2)
 
-        def cosine_products(a, c, at=None):
-            products(a, c, "cos_b1_", wsub1_w[a][:], wsub1_s[a][:], cos, cos_b1, at)
+        def cosine_products(a, c):
+            products(a, c, "cos_b1_", wsub1_w[a][:], wsub1_s[a][:], cos, cos_b1)
 
         def mix(a, c, engine, dst):
             engine.tensor_tensor(
@@ -300,23 +291,24 @@ def tile_list_halo_spin_orientation_kernel(
         cosine_products(0, 0)
         trig(0, 1)
         sine_products(0, 1)
-        wsub1_w.append(kept("wsub1_w1", [PART, BANK], U32, tag="sin01"))
-        quantize(wsub1_w[1][:], wsub1_s[1][:], wsub1_b1[:])
-        cosine_products(0, 1, at_th_last)
-        h0_b = placed("h0_b", [PART, P, 4], BF16, at_h0_b)
-        for c, (m0, w) in enumerate(PIECES[0]):
-            mix(0, c, nc.gpsimd, h0_b[:, m0 : m0 + w, :])
+        cosine_products(0, 1)
+        h0_b = [placed("h0_b%d" % c, [PART, 256, 4], BF16, at_h0_b + 2048 * c) for c in range(2)]
+        for c in range(2):
+            mix(0, c, nc.gpsimd, h0_b[c][:])
         for c in range(len(PIECES[1])):
             trig(1, c)
             sine_products(1, c)
             cosine_products(1, c)
 
-        wspin_b.append(placed("wspin_b1", [PART, N, 4], BF16, at_ang))
-        wspin_w.append(placed("wspin_w1", [PART, N], U32, at_h0_b + 2048))
-        round_wspin(1, nc.scalar.copy)
+        wspin_b1 = placed("wspin_b1", [PART, N, 4], BF16, at_ang)
+        nc.scalar.copy(
+            wspin_b1[:].rearrange("p (u e) t -> p u t e", e=4), wspin_raw[1][:].rearrange("p t (u e) -> p u t e", e=4)
+        )
 
-        h0_w = placed("h0_w", [PART, P], U32, at_cos_last)
+        wspin_w = [placed("wspin_w0", [PART, N], U32, at_cos_last - 1984)]
+        h0_w = placed("h0_w", [PART, P], U32, at_cos_last + 64)
         h0_s = kept("h0_s", [PART, P], U8)
+        wspin_w.append(placed("wspin_w1", [PART, N], U32, at_h0_b + 2048))
         h1_b = [
             placed("h1_b0", [PART, 256, 4], BF16, at_h0_b),
             placed("h1_b1", [PART, 128, 4], BF16, at_ang),
@@ -331,8 +323,10 @@ def tile_list_halo_spin_orientation_kernel(
             tiles = OUT_TILES_PER_BANK[c]
             codes, scales = (h0_w[:, m0 : m0 + w], h0_s[:, m0 : m0 + w]) if a == 0 else (h1_w[c][:], h1_s[c][:])
             for b in range(4 // tiles):
-                if a == 0:
+                if a == 0 and c < last[1]:
                     out_banks[c, b] = banks.tile([PART, tiles, w], F32, name="bank", tag="bank")
+                elif a == 0:
+                    out_banks[c, b] = proj.tile([PART, tiles, w], F32, name="projection", tag="projection")
                 for d in range(tiles):
                     rows = slice(PART * (tiles * b + d), PART * (tiles * b + d + 1))
                     nc.tensor.matmul_mx(
@@ -352,23 +346,28 @@ def tile_list_halo_spin_orientation_kernel(
             tiles = OUT_TILES_PER_BANK[c]
             for b in range(4 // tiles):
                 res = kept("res%d%d" % (c, b), [PART, tiles, w], F32)
-                if b == 0 or c < last[1]:
+                if b == 0 or c == 0:
                     nc.scalar.copy(res[:], out_banks[c, b][:])
                 else:
                     nc.vector.tensor_copy(res[:], out_banks[c, b][:])
-                nc.sync.dma_start(out_v[:, tiles * b : tiles * (b + 1), m0 : m0 + w], res[:])
+                queue = nc.scalar if (c, b) == (last[1], 0) else nc.sync
+                queue.dma_start(out_v[:, tiles * b : tiles * (b + 1), m0 : m0 + w], res[:])
 
-        quantize(h0_w[:], h0_s[:], h0_b[:])
-        for c in range(len(PIECES[1])):
-            spin(0, c)
+        quantize(wspin_w[0][:], wspin_s[0][:], wspin_b0[:])
+        for half in range(2):
+            quantize(h0_w[:, halves[half]], h0_s[:, halves[half]], h0_b[half][:])
+        spin(0, 0)
         mix(1, 0, nc.vector, h1_b[0][:])
-        quantize(wspin_w[1][:], wspin_s[1][:], wspin_b[1][:])
+        quantize(wspin_w[1][:], wspin_s[1][:], wspin_b1[:])
         quantize(h1_w[0][:], h1_s[0][:], h1_b[0][:])
         spin(1, 0)
+        spin(0, 1)
+        spin(0, 2)
         store(0)
         mix(1, 1, nc.vector, h1_b[1][:])
         mix(1, 2, nc.vector, h1_b[2][:])
         for c in (1, 2):
             quantize(h1_w[c][:], h1_s[c][:], h1_b[c][:])
             spin(1, c)
+        for c in (1, 2):
             store(c)

@@ -102,8 +102,8 @@ def tile_list_halo_spin_orientation_kernel(
         wsub2_raw = kept("wsub2_raw", [PART, H], I32, tag="wsub1_w1")
         wsub1_v = wsub1.rearrange("(p j) c -> p j c", j=4)
         wsub1_raw = [kept("wsub1_raw0", [PART, 4, BANK], F32)]
-        nc.sync.dma_start(offs_t[:], offs)
         nc.sync.dma_start(tab_s[0:32, :].bitcast(I32), tab_scales.rearrange("g r c -> r g c").bitcast(I32))
+        nc.sync.dma_start(offs_t[:], offs)
         nc.sync.dma_start(tab_w[0][:], words(tab_words[0]))
         for quad in range(QUADS):
             nc.sync.dma_start(
@@ -170,8 +170,8 @@ def tile_list_halo_spin_orientation_kernel(
             for t in range(4):
                 nc.sync.dma_start(wspin_raw[a][:, t, :], wspin_v[a, t])
 
-        th = [kept("th%d" % j, [PART, S], F32) for j in range(ROW_TILES - 1)]
-        th.append(placed("th7", [PART, S], F32, at_th_last))
+        th = [kept("th%d" % j, [PART, S], F32) for j in range(ROW_TILES - 2)]
+        th += [placed("th6", [PART, S], F32, at_th_last), kept("th7", [PART, S], F32)]
         ang = [kept("ang0", [PART, 4, P], F32)]
 
         def angles(j):

@@ -24,7 +24,6 @@ QUADS = 4
 ROW_TILES = H // PART
 BIAS_ROW = PART - ROW_TILES
 PIECES = ([(0, 256), (256, 256)], [(0, 256), (256, 128), (384, 128)])
-OUT_TILES_PER_BANK = (2, 2, 2)
 
 
 def tile_list_halo_spin_orientation_kernel(
@@ -49,10 +48,6 @@ def tile_list_halo_spin_orientation_kernel(
         def words(packed):
             return packed.rearrange("p c i -> p (c i)").bitcast(I32)
 
-        def load_plane(dst, scales):
-            for quad in range(QUADS):
-                nc.sync.dma_start(dst[32 * quad : 32 * quad + 4, :], scales[4 * quad : 4 * quad + 4, :].bitcast(I32))
-
         def order_columns(dst, src, run, copy):
             copy(
                 dst.rearrange("p (a t q w) -> p a t q w", t=4, q=16, w=run),
@@ -65,20 +60,19 @@ def tile_list_halo_spin_orientation_kernel(
         def quantize(codes, scales, values):
             nc.vector.quantize_mx(out=codes.bitcast(FP8X4), scales=scales, in_=values.rearrange("p c j -> p (c j)"))
 
+        at_th6, at_h0_b, at_ang1, at_cos_last = 0, 4096, 8192, 18432
+
         offs_t = lists.tile([PART, S // 16], U16, name="offs_t")
         pos_t = lists.tile([PART, P // 16], U16, name="pos_t")
         offs2_t = lists.tile([PART, P // 16], U16, name="offs2_t")
 
         tab_s = kept("tab_s", [PART, T], U8)
-        at_th_last, at_h0_b, at_ang, at_cos_last = 0, 4096, 8192, 18432
-        weight_s_raw = kept("weight_s_raw", [PART, H // 2], I32)
-        wsub2_s_raw = kept("wsub2_s_raw", [PART, H // 4], I32)
         tab2_s = kept("tab2_s", [PART, T2], U8)
-        v_sg = kept("v_sg", [PART, S], U8)
-        v_s = kept("v_s", [PART, 2, S], U8)
+        wang_s_raw = kept("wang_s_raw", [PART, H // 2], I32)
+        wsub2_s_raw = kept("wsub2_s_raw", [PART, H // 4], I32)
         bias_rows = kept("bias_rows", [PART, PART], F32)
         ident = kept("ident", [PART, PART], F32)
-        nc.vector.memset(weight_s_raw[:], 0)
+        nc.vector.memset(wang_s_raw[:], 0)
         make_identity(nc, ident[:])
         nc.vector.memset(tab2_s[:].bitcast(I32), 0)
         nc.gpsimd.dma_start(tab2_s[0:16, :].bitcast(I32), tab2_scales[0].bitcast(I32))
@@ -96,89 +90,94 @@ def tile_list_halo_spin_orientation_kernel(
         nc.scalar.activation(warm[0:96, 0:1], bias_rows[0:96, 0:1], ACT.Sin)
 
         tab_w = [kept("tab_w%d" % g, [PART, T], I32, tag="stage%d" % g) for g in range(2)]
+        tab2_w = kept("tab2_w", [PART, T2], I32, tag="stage2")
         wang_raw = [kept("wang_raw%d" % a, [PART, 2, BANK // 2], I32) for a in range(2)]
         wang_v = wang_words.rearrange("g p c -> p g c").bitcast(I32)
-        tab2_w = kept("tab2_w", [PART, T2], I32, tag="stage2")
-        wsub2_raw = kept("wsub2_raw", [PART, H], I32, tag="wsub1_w1")
+        wsub2_raw = [kept("wsub2_raw%d" % a, [PART, BANK], I32) for a in range(2)]
         wsub1_v = wsub1.rearrange("(p j) c -> p j c", j=4)
         wsub1_raw = [kept("wsub1_raw0", [PART, 4, BANK], F32)]
+        v_sg = kept("v_sg", [PART, S], U8, tag="picked_scales")
+        v_s = kept("v_s", [PART, 2, S], U8)
+
         nc.sync.dma_start(tab_s[0:32, :].bitcast(I32), tab_scales.rearrange("g r c -> r g c").bitcast(I32))
         nc.sync.dma_start(offs_t[:], offs)
         nc.sync.dma_start(tab_w[0][:], words(tab_words[0]))
         for quad in range(QUADS):
             nc.sync.dma_start(
-                weight_s_raw[32 * quad : 32 * quad + 4, :].rearrange("s (g c) -> s g c", g=2),
+                wang_s_raw[32 * quad : 32 * quad + 4, :].rearrange("s (g c) -> s g c", g=2),
                 wang_scales[:, 4 * quad : 4 * quad + 4, :].rearrange("g s c -> s g c").bitcast(I32),
             )
         nc.sync.dma_start(wang_raw[0][:], wang_v[:, :, 0 : BANK // 2])
+        nc.sync.dma_start(tab_w[1][:], words(tab_words[1]))
         nc.sync.dma_start(offs2_t[:], offs2)
-        nc.sync.dma_start(tab_w[1][:, 0 : 3 * T // 4], words(tab_words[1])[:, 0 : 3 * T // 4])
         nc.vector.tensor_copy(v_sg[:], tab_s[:].indirect(offs_t[:]))
         for quad in range(QUADS):
             nc.sync.dma_start(
                 v_s[32 * quad : 32 * quad + 4].bitcast(I32), v_sg[8 * quad : 8 * quad + 8, :].bitcast(I32)
             )
-        nc.sync.dma_start(tab_w[1][:, 3 * T // 4 : T], words(tab_words[1])[:, 3 * T // 4 : T])
+        for a in range(2):
+            nc.sync.dma_start(wsub2_raw[a][:], words(wsub2_words[0])[:, BANK * a : BANK * (a + 1)])
         nc.sync.dma_start(tab2_w[:], words(tab2_words[0]))
-        nc.sync.dma_start(pos_t[:], pos1)
         nc.sync.dma_start(wang_raw[1][:], wang_v[:, :, BANK // 2 : BANK])
+        nc.sync.dma_start(pos_t[:], pos1)
         nc.sync.dma_start(wsub1_raw[0][:], wsub1_v[:, :, 0:BANK])
-        nc.sync.dma_start(wsub2_raw[:], words(wsub2_words[0]))
+        for quad in range(QUADS):
+            nc.sync.dma_start(
+                wsub2_s_raw[32 * quad : 32 * quad + 4, :], wsub2_scales[0][4 * quad : 4 * quad + 4, :].bitcast(I32)
+            )
 
         bias_ps = banks.tile([PART, BANK], F32, name="bank", tag="bank")
         nc.tensor.transpose(bias_ps[:, 0:PART], bias_rows[:], ident[:])
         bias = kept("bias", [PART, ROW_TILES], F32)
         nc.scalar.copy(bias[:], bias_ps[:, BIAS_ROW:PART])
 
-        later = {(0, 1): "cos00", (1, 1): "sin00"}
-        v_w = [[kept("v_w%d%d" % (g, half), [PART, BANK], U32, later.get((g, half))) for half in range(2)] for g in range(2)]
-
-        def gather_v(g, half):
-            picks = offs_t[:, 32 * half : 32 * (half + 1)]
-            nc.vector.tensor_copy(v_w[g][half][:], tab_w[g][:].bitcast(U32).indirect(picks))
+        v_w = [[kept("v_w%d%d" % (g, half), [PART, BANK], U32) for half in range(2)] for g in range(2)]
+        for g in range(2):
+            for half in range(2):
+                picks = offs_t[:, 32 * half : 32 * (half + 1)]
+                nc.vector.tensor_copy(v_w[g][half][:], tab_w[g][:].bitcast(U32).indirect(picks))
+        v2_sg = kept("v2_sg", [PART, P], U8, tag="picked_scales")
+        v2_s = kept("v2_s", [PART, P], U8)
+        v2_w = kept("v2_w", [PART, P], U32)
+        nc.vector.tensor_copy(v2_sg[:], tab2_s[:].indirect(offs2_t[:]))
+        nc.vector.tensor_copy(v2_w[:], tab2_w[:].bitcast(U32).indirect(offs2_t[:]))
 
         wang_w = [kept("wang_w%d" % a, [PART, 2, BANK // 2], I32) for a in range(2)]
         wang_s = kept("wang_s", [PART, 2, H // 4], I32)
-        wsub2_w = kept("wsub2_w", [PART, H], I32)
+        wsub2_w = [kept("wsub2_w%d" % a, [PART, BANK], I32) for a in range(2)]
+        wsub2_s = kept("wsub2_s", [PART, H // 4], I32)
 
         def order_wang(a, copy):
             order_columns(wang_w[a][:].rearrange("p g c -> p (g c)"), wang_raw[a][:].rearrange("p g c -> p (g c)"), 4, copy)
 
-        gather_v(0, 0)
-        gather_v(0, 1)
-        v2_sg = kept("v2_sg", [PART, P], U8)
-        v2_s = kept("v2_s", [PART, P], U8)
-        nc.vector.tensor_copy(v2_sg[:], tab2_s[:].indirect(offs2_t[:]))
-        order_columns(wang_s[:].rearrange("p g c -> p (g c)"), weight_s_raw[:], 2, scalar_move)
+        order_columns(wang_s[:].rearrange("p g c -> p (g c)"), wang_s_raw[:], 2, scalar_move)
         order_wang(0, scalar_move)
-        gather_v(1, 0)
-        gather_v(1, 1)
-
-        v2_w = kept("v2_w", [PART, P], U32)
-        nc.vector.tensor_copy(v2_w[:], tab2_w[:].bitcast(U32).indirect(offs2_t[:]))
+        for a in range(2):
+            order_columns(wsub2_w[a][:], wsub2_raw[a][:], 8, scalar_move)
+        order_wang(1, nc.vector.tensor_copy)
 
         wspin_v = wspin.rearrange("(a q t i) n -> a t q i n", a=2, t=4, i=8)
         wsub1_raw.append(kept("wsub1_raw1", [PART, 4, BANK], F32, tag="stage0"))
         nc.sync.dma_start(wsub1_raw[1][:], wsub1_v[:, :, BANK : 2 * BANK])
-        load_plane(wsub2_s_raw[:], wsub2_scales[0])
+        wspin_raw = [kept("wspin_raw%d" % a, [PART, 4, N], F32, tag="stage%d" % (a + 1)) for a in range(2)]
+        for t in range(4):
+            nc.sync.dma_start(wspin_raw[0][:, t, :], wspin_v[0, t])
         for quad in range(QUADS):
             nc.sync.dma_start(
                 v2_s[32 * quad : 32 * quad + 4, :].bitcast(I32), v2_sg[4 * quad : 4 * quad + 4, :].bitcast(I32)
             )
-        wspin_raw = [kept("wspin_raw%d" % a, [PART, 4, N], F32, tag="stage%d" % (a + 1)) for a in range(2)]
-        for a in range(2):
-            for t in range(4):
-                nc.sync.dma_start(wspin_raw[a][:, t, :], wspin_v[a, t])
+        for t in range(4):
+            nc.sync.dma_start(wspin_raw[1][:, t, :], wspin_v[1, t])
 
         th = [kept("th%d" % j, [PART, S], F32) for j in range(ROW_TILES - 2)]
-        th += [placed("th6", [PART, S], F32, at_th_last), kept("th7", [PART, S], F32)]
-        ang = [kept("ang0", [PART, 4, P], F32)]
+        th += [placed("th6", [PART, S], F32, at_th6), kept("th7", [PART, S], F32)]
+        ang = [kept("ang0", [PART, 4, P], F32), placed("ang1", [PART, 4, P], F32, at_ang1)]
 
-        def angles(j):
-            for half in range(2):
-                cols = slice(BANK * half, BANK * (half + 1))
-                bank = banks.tile([PART, BANK], F32, name="bank", tag="bank")
-                for g in range(2):
+        def angles(tiles, half):
+            cols = slice(BANK * half, BANK * (half + 1))
+            sums = [banks.tile([PART, BANK], F32, name="bank", tag="bank") for j in tiles]
+            for g in range(2):
+                for j, bank in zip(tiles, sums):
                     nc.tensor.matmul_mx(
                         out=bank[:],
                         lhsT=wang_w[j // 4][:, g, 64 * (j % 4) : 64 * (j % 4 + 1)].bitcast(FP4X4),
@@ -188,51 +187,59 @@ def tile_list_halo_spin_orientation_kernel(
                         start=(g == 0),
                         stop=(g == 1),
                     )
+            for j, bank in zip(tiles, sums):
                 nc.scalar.activation(th[j][:, cols], bank[:], ACT.Identity, bias=bias[:, j : j + 1])
 
         def pick(j):
             nc.vector.tensor_copy(ang[j // 4][:, j % 4, :], th[j][:].indirect(pos_t[:]))
 
-        wsub1_b0 = placed("wsub1_b0", [PART, BANK, 4], BF16, at_ang)
-        wsub1_s = [kept("wsub1_s%d" % a, [PART, BANK], U8) for a in range(2)]
+        def round_wsub1(dst, a, t0, tiles, copy):
+            for t in range(tiles):
+                copy(
+                    dst[:, PART * t : PART * (t + 1), :].rearrange("p (q h e) j -> p q h j e", h=2, e=4),
+                    wsub1_raw[a][:].rearrange("p j (q t h e) -> p t q h j e", t=4, h=2, e=4)[:, t0 + t],
+                )
 
-        for j in range(4):
-            angles(j)
+        wsub1_b0 = kept("wsub1_b0", [PART, BANK, 4], BF16)
+        wsub1_b1 = [kept("wsub1_b1%d" % half, [PART, 256, 4], BF16) for half in range(2)]
+        wsub1_w = [kept("wsub1_w%d" % a, [PART, BANK], U32) for a in range(2)]
+        wsub1_s = [kept("wsub1_s%d" % a, [PART, BANK], U8) for a in range(2)]
+        halves = [slice(256 * half, 256 * (half + 1)) for half in range(2)]
+
+        angles([0, 1], 0)
+        angles([0], 1)
+        angles([1], 1)
+        for j in range(2, 6):
+            for half in range(2):
+                angles([j], half)
+        round_wsub1(wsub1_b1[1], 1, 2, 2, nc.scalar.copy)
+        for j in range(6, ROW_TILES):
+            for half in range(2):
+                angles([j], half)
+
         pick(0)
-        order_wang(1, nc.vector.tensor_copy)
-        for j in range(4, ROW_TILES):
-            angles(j)
         pick(1)
         for h in range(2):
             nc.vector.tensor_copy(
                 wsub1_b0[:].rearrange("p (t q h e) j -> p h t q j e", t=4, h=2, e=4)[:, h],
                 wsub1_raw[0][:].rearrange("p j (q t h e) -> p h t q j e", t=4, h=2, e=4)[:, h],
             )
-        wsub1_b1 = [kept("wsub1_b1%d" % half, [PART, 256, 4], BF16) for half in range(2)]
-        wspin_s = [kept("wspin_s%d" % a, [PART, N], U8) for a in range(2)]
-
-
         pick(2)
-        order_columns(wsub2_w[:], wsub2_raw[:], 8, nc.vector.tensor_copy)
-        pick(3)
-        halves = [slice(256 * half, 256 * (half + 1)) for half in range(2)]
-        for half in range(2):
-            nc.vector.tensor_copy(
-                wsub1_b1[half][:].rearrange("p (t q i) j -> p t q j i", t=2, i=8),
-                wsub1_raw[1][:].rearrange("p j (q t i) -> p t q j i", t=4, i=8)[:, 2 * half : 2 * half + 2],
-            )
-        late_w = kept("wsub1_w1", [PART, BANK], U32)
-        for half in range(2):
-            quantize(late_w[:, halves[half]], wsub1_s[1][:, halves[half]], wsub1_b1[half][:])
-        wsub1_w = [kept("wsub1_w0", [PART, BANK], U32, tag="wsub1_b10"), late_w]
         quantize(wsub1_w[0][:], wsub1_s[0][:], wsub1_b0[:])
-        wsub2_s = kept("wsub2_s", [PART, H // 4], I32, tag="wsub1_b11")
+        pick(3)
+        nc.vector.tensor_copy(
+            wsub1_b1[0][:].rearrange("p (t q i) j -> p t q j i", t=2, i=8),
+            wsub1_raw[1][:].rearrange("p j (q t i) -> p t q j i", t=4, i=8)[:, 0:2],
+        )
         order_columns(wsub2_s[:], wsub2_s_raw[:], 2, nc.vector.tensor_copy)
-        ang.append(placed("ang1", [PART, 4, P], F32, at_ang))
-        for j in range(4, ROW_TILES):
-            pick(j)
+        pick(4)
+        quantize(wsub1_w[1][:, halves[0]], wsub1_s[1][:, halves[0]], wsub1_b1[0][:])
+        pick(5)
+        quantize(wsub1_w[1][:, halves[1]], wsub1_s[1][:, halves[1]], wsub1_b1[1][:])
+        pick(6)
+        pick(7)
 
-        wspin_b0 = placed("wspin_b0", [PART, N, 4], BF16, at_th_last)
+        wspin_b0 = placed("wspin_b0", [PART, N, 4], BF16, at_th6)
         nc.gpsimd.tensor_scalar(wspin_b0[:], wspin_raw[0][:].rearrange("p t n -> p n t"), 1.0, 0.0, ALU.mult, ALU.add)
 
         cos, sin, cos_b1, sin_b2 = {}, {}, {}, {}
@@ -241,77 +248,68 @@ def tile_list_halo_spin_orientation_kernel(
         def trig(a, c):
             m0, w = PIECES[a][c]
             if (a, c) == last:
-                cos[a, c] = placed("cos_last", [PART, 4, w], F32, at_cos_last)
+                cos[a, c] = placed("cos_last", [PART, 2, w, 2], F32, at_cos_last)
             else:
-                cos[a, c] = kept("cos%d%d" % (a, c), [PART, 4, w], F32)
-            sin[a, c] = kept("sin%d%d" % (a, c), [PART, 4, w], F32)
-            picked = ang[a][:, :, m0 : m0 + w]
+                cos[a, c] = kept("cos%d%d" % (a, c), [PART, 2, w, 2], F32)
+            sin[a, c] = kept("sin%d%d" % (a, c), [PART, 2, w, 2], F32)
+            picked = ang[a][:, :, m0 : m0 + w].rearrange("p (y z) m -> p y m z", z=2)
             nc.scalar.activation(cos[a, c][:], picked, ACT.Abs)
             nc.scalar.activation(sin[a, c][:], picked, ACT.Sin)
             nc.scalar.activation(cos[a, c][:], cos[a, c][:], ACT.Sin, bias=math.pi / 2, scale=-1.0)
 
         def products(a, c, name, codes, scales, factor, dst):
             m0, w = PIECES[a][c]
-            tiles = BANK // w
-            dst[a, c] = kept("%s%d%d" % (name, a, c), [PART, w // 4, 4, 4], F32)
-            for t0 in range(0, 4, tiles):
-                bank = proj.tile([PART, tiles, w], F32, name="projection", tag="projection")
-                for d in range(tiles):
-                    cols = slice(PART * (t0 + d), PART * (t0 + d + 1))
+            dst[a, c] = kept("%s%d%d" % (name, a, c), [PART, w, 4], F32)
+            for u0 in range(0, w, PART):
+                bank = proj.tile([PART, 4, PART], F32, name="projection", tag="projection")
+                picked = slice(m0 + u0, m0 + u0 + PART)
+                for t in range(4):
+                    cols = slice(PART * t, PART * (t + 1))
                     nc.tensor.matmul_mx(
-                        out=bank[:, d, :],
+                        out=bank[:, t, :],
                         lhsT=codes[:, cols].bitcast(FP8X4),
                         lhsT_scale=scales[:, cols],
-                        rhs=v2_w[:, m0 : m0 + w].bitcast(FP8X4),
-                        rhs_scale=v2_s[:, m0 : m0 + w],
+                        rhs=v2_w[:, picked].bitcast(FP8X4),
+                        rhs_scale=v2_s[:, picked],
                         start=True,
                         stop=True,
                     )
                 nc.vector.tensor_tensor(
-                    dst[a, c][:].rearrange("p u t e -> p t u e")[:, t0 : t0 + tiles],
-                    bank[:].rearrange("p t (u e) -> p t u e", e=4),
-                    factor[a, c][:, t0 : t0 + tiles, :].rearrange("p t (u e) -> p t u e", e=4),
+                    dst[a, c][:, u0 : u0 + PART, :].rearrange("p m (y z) -> p m y z", z=2),
+                    bank[:].rearrange("p (y z) m -> p m y z", z=2),
+                    factor[a, c][:, :, u0 : u0 + PART, :].rearrange("p y m z -> p m y z"),
                     ALU.mult,
                 )
 
-        def sine_products(a, c):
-            cols = slice(BANK * a, BANK * (a + 1))
-            products(a, c, "sin_b2_", wsub2_w[:, cols], wsub2_s[:].bitcast(U8)[:, cols], sin, sin_b2)
+        def mix(a, c, engine, dst):
+            engine.tensor_tensor(dst, cos_b1[a, c][:], sin_b2[a, c][:], ALU.add)
 
-        def cosine_products(a, c):
+        def project(a, c):
+            trig(a, c)
+            products(a, c, "sin_b2_", wsub2_w[a][:], wsub2_s[:].bitcast(U8)[:, BANK * a : BANK * (a + 1)], sin, sin_b2)
             products(a, c, "cos_b1_", wsub1_w[a][:], wsub1_s[a][:], cos, cos_b1)
 
-        def mix(a, c, engine, dst):
-            engine.tensor_tensor(
-                dst.rearrange("p (u e) t -> p u t e", e=4), cos_b1[a, c][:], sin_b2[a, c][:], ALU.add
-            )
-
-        trig(0, 0)
-        sine_products(0, 0)
-        cosine_products(0, 0)
-        trig(0, 1)
-        sine_products(0, 1)
-        cosine_products(0, 1)
+        for c in range(2):
+            project(0, c)
         h0_b = [placed("h0_b%d" % c, [PART, 256, 4], BF16, at_h0_b + 2048 * c) for c in range(2)]
         for c in range(2):
             mix(0, c, nc.gpsimd, h0_b[c][:])
         for c in range(len(PIECES[1])):
-            trig(1, c)
-            sine_products(1, c)
-            cosine_products(1, c)
+            project(1, c)
 
-        wspin_b1 = placed("wspin_b1", [PART, N, 4], BF16, at_ang)
+        wspin_b1 = placed("wspin_b1", [PART, N, 4], BF16, at_ang1)
         nc.scalar.copy(
             wspin_b1[:].rearrange("p (u e) t -> p u t e", e=4), wspin_raw[1][:].rearrange("p t (u e) -> p u t e", e=4)
         )
 
+        wspin_s = [kept("wspin_s%d" % a, [PART, N], U8) for a in range(2)]
         wspin_w = [placed("wspin_w0", [PART, N], U32, at_cos_last - 1984)]
         h0_w = placed("h0_w", [PART, P], U32, at_cos_last + 64)
         h0_s = kept("h0_s", [PART, P], U8)
         wspin_w.append(placed("wspin_w1", [PART, N], U32, at_h0_b + 2048))
         h1_b = [
             placed("h1_b0", [PART, 256, 4], BF16, at_h0_b),
-            placed("h1_b1", [PART, 128, 4], BF16, at_ang),
+            placed("h1_b1", [PART, 128, 4], BF16, at_ang1),
             placed("h1_b2", [PART, 128, 4], BF16, at_h0_b),
         ]
         h1_w = [kept("h1_w%d" % c, [PART, w], U32) for c, (m0, w) in enumerate(PIECES[1])]
@@ -320,15 +318,14 @@ def tile_list_halo_spin_orientation_kernel(
 
         def spin(a, c):
             m0, w = PIECES[1][c]
-            tiles = OUT_TILES_PER_BANK[c]
             codes, scales = (h0_w[:, m0 : m0 + w], h0_s[:, m0 : m0 + w]) if a == 0 else (h1_w[c][:], h1_s[c][:])
-            for b in range(4 // tiles):
+            for b in range(2):
                 if a == 0 and c < last[1]:
-                    out_banks[c, b] = banks.tile([PART, tiles, w], F32, name="bank", tag="bank")
+                    out_banks[c, b] = banks.tile([PART, 2, w], F32, name="bank", tag="bank")
                 elif a == 0:
-                    out_banks[c, b] = proj.tile([PART, tiles, w], F32, name="projection", tag="projection")
-                for d in range(tiles):
-                    rows = slice(PART * (tiles * b + d), PART * (tiles * b + d + 1))
+                    out_banks[c, b] = proj.tile([PART, 2, w], F32, name="projection", tag="projection")
+                for d in range(2):
+                    rows = slice(PART * (2 * b + d), PART * (2 * b + d + 1))
                     nc.tensor.matmul_mx(
                         out=out_banks[c, b][:, d, :],
                         lhsT=wspin_w[a][:, rows].bitcast(FP8X4),
@@ -336,22 +333,21 @@ def tile_list_halo_spin_orientation_kernel(
                         rhs=codes.bitcast(FP8X4),
                         rhs_scale=scales,
                         start=(a == 0 and d == 0),
-                        stop=(a == 1 and d == tiles - 1),
+                        stop=(a == 1 and d == 1),
                     )
 
         out_v = out.rearrange("(n p) m -> p n m", p=PART)
 
         def store(c):
             m0, w = PIECES[1][c]
-            tiles = OUT_TILES_PER_BANK[c]
-            for b in range(4 // tiles):
-                res = kept("res%d%d" % (c, b), [PART, tiles, w], F32)
+            for b in range(2):
+                res = kept("res%d%d" % (c, b), [PART, 2, w], F32)
                 if b == 0 or c == 0:
                     nc.scalar.copy(res[:], out_banks[c, b][:])
                 else:
                     nc.vector.tensor_copy(res[:], out_banks[c, b][:])
                 queue = nc.scalar if (c, b) == (last[1], 0) else nc.sync
-                queue.dma_start(out_v[:, tiles * b : tiles * (b + 1), m0 : m0 + w], res[:])
+                queue.dma_start(out_v[:, 2 * b : 2 * (b + 1), m0 : m0 + w], res[:])
 
         quantize(wspin_w[0][:], wspin_s[0][:], wspin_b0[:])
         for half in range(2):

@@ -248,41 +248,43 @@ def tile_list_halo_spin_orientation_kernel(
         def trig(a, c):
             m0, w = PIECES[a][c]
             if (a, c) == last:
-                cos[a, c] = placed("cos_last", [PART, 2, w, 2], F32, at_cos_last)
+                cos[a, c] = placed("cos_last", [PART, 4, w], F32, at_cos_last)
             else:
-                cos[a, c] = kept("cos%d%d" % (a, c), [PART, 2, w, 2], F32)
-            sin[a, c] = kept("sin%d%d" % (a, c), [PART, 2, w, 2], F32)
-            picked = ang[a][:, :, m0 : m0 + w].rearrange("p (y z) m -> p y m z", z=2)
+                cos[a, c] = kept("cos%d%d" % (a, c), [PART, 4, w], F32)
+            sin[a, c] = kept("sin%d%d" % (a, c), [PART, 4, w], F32)
+            picked = ang[a][:, :, m0 : m0 + w]
             nc.scalar.activation(cos[a, c][:], picked, ACT.Abs)
             nc.scalar.activation(sin[a, c][:], picked, ACT.Sin)
             nc.scalar.activation(cos[a, c][:], cos[a, c][:], ACT.Sin, bias=math.pi / 2, scale=-1.0)
 
         def products(a, c, name, codes, scales, factor, dst):
             m0, w = PIECES[a][c]
-            dst[a, c] = kept("%s%d%d" % (name, a, c), [PART, w, 4], F32)
-            for u0 in range(0, w, PART):
-                bank = proj.tile([PART, 4, PART], F32, name="projection", tag="projection")
-                picked = slice(m0 + u0, m0 + u0 + PART)
-                for t in range(4):
-                    cols = slice(PART * t, PART * (t + 1))
+            tiles = BANK // w
+            dst[a, c] = kept("%s%d%d" % (name, a, c), [PART, w // 4, 4, 4], F32)
+            for t0 in range(0, 4, tiles):
+                bank = proj.tile([PART, tiles, w], F32, name="projection", tag="projection")
+                for d in range(tiles):
+                    cols = slice(PART * (t0 + d), PART * (t0 + d + 1))
                     nc.tensor.matmul_mx(
-                        out=bank[:, t, :],
+                        out=bank[:, d, :],
                         lhsT=codes[:, cols].bitcast(FP8X4),
                         lhsT_scale=scales[:, cols],
-                        rhs=v2_w[:, picked].bitcast(FP8X4),
-                        rhs_scale=v2_s[:, picked],
+                        rhs=v2_w[:, m0 : m0 + w].bitcast(FP8X4),
+                        rhs_scale=v2_s[:, m0 : m0 + w],
                         start=True,
                         stop=True,
                     )
                 nc.vector.tensor_tensor(
-                    dst[a, c][:, u0 : u0 + PART, :].rearrange("p m (y z) -> p m y z", z=2),
-                    bank[:].rearrange("p (y z) m -> p m y z", z=2),
-                    factor[a, c][:, :, u0 : u0 + PART, :].rearrange("p y m z -> p m y z"),
+                    dst[a, c][:].rearrange("p u t e -> p t u e")[:, t0 : t0 + tiles],
+                    bank[:].rearrange("p t (u e) -> p t u e", e=4),
+                    factor[a, c][:, t0 : t0 + tiles, :].rearrange("p t (u e) -> p t u e", e=4),
                     ALU.mult,
                 )
 
         def mix(a, c, engine, dst):
-            engine.tensor_tensor(dst, cos_b1[a, c][:], sin_b2[a, c][:], ALU.add)
+            engine.tensor_tensor(
+                dst.rearrange("p (u e) t -> p u t e", e=4), cos_b1[a, c][:], sin_b2[a, c][:], ALU.add
+            )
 
         def project(a, c):
             trig(a, c)

@@ -60,7 +60,7 @@ def tile_list_halo_spin_orientation_kernel(
         def quantize(codes, scales, values):
             nc.vector.quantize_mx(out=codes.bitcast(FP8X4), scales=scales, in_=values.rearrange("p c j -> p (c j)"))
 
-        at_th6, at_h0_b, at_ang1, at_cos_last = 0, 4096, 8192, 18432
+        at_th7, at_wspin_b0, at_late_b, at_h0_b, at_ang1, at_cos_last = 0, 2048, 4096, 6144, 10240, 20480
 
         offs_t = lists.tile([PART, S // 16], U16, name="offs_t")
         pos_t = lists.tile([PART, P // 16], U16, name="pos_t")
@@ -69,7 +69,7 @@ def tile_list_halo_spin_orientation_kernel(
         tab_s = kept("tab_s", [PART, T], U8)
         tab2_s = kept("tab2_s", [PART, T2], U8)
         wang_s_raw = kept("wang_s_raw", [PART, H // 2], I32)
-        wsub2_s_raw = kept("wsub2_s_raw", [PART, H // 4], I32)
+        wsub2_s_raw = placed("wsub2_s_raw", [PART, H // 4], I32, at_late_b)
         bias_rows = kept("bias_rows", [PART, PART], F32)
         ident = kept("ident", [PART, PART], F32)
         nc.vector.memset(wang_s_raw[:], 0)
@@ -169,8 +169,8 @@ def tile_list_halo_spin_orientation_kernel(
         for t in range(4):
             nc.sync.dma_start(wspin_raw[1][:, t, :], wspin_v[1, t])
 
-        th = [kept("th%d" % j, [PART, S], F32) for j in range(ROW_TILES - 2)]
-        th += [placed("th6", [PART, S], F32, at_th6), kept("th7", [PART, S], F32)]
+        th = [kept("th%d" % j, [PART, S], F32) for j in range(ROW_TILES - 1)]
+        th.append(placed("th7", [PART, S], F32, at_th7))
         ang = [kept("ang0", [PART, 4, P], F32), placed("ang1", [PART, 4, P], F32, at_ang1)]
 
         def angles(tiles, half):
@@ -201,8 +201,8 @@ def tile_list_halo_spin_orientation_kernel(
                 )
 
         wsub1_b0 = kept("wsub1_b0", [PART, BANK, 4], BF16)
-        wsub1_b1 = [kept("wsub1_b1%d" % half, [PART, 256, 4], BF16) for half in range(2)]
-        wsub1_w = [kept("wsub1_w%d" % a, [PART, BANK], U32) for a in range(2)]
+        wsub1_w = [kept("wsub1_w0", [PART, BANK], U32)]
+        late_by_scalar = kept("wsub1_b11", [PART, 256, 4], BF16)
         wsub1_s = [kept("wsub1_s%d" % a, [PART, BANK], U8) for a in range(2)]
         halves = [slice(256 * half, 256 * (half + 1)) for half in range(2)]
 
@@ -212,7 +212,7 @@ def tile_list_halo_spin_orientation_kernel(
         for j in range(2, 6):
             for half in range(2):
                 angles([j], half)
-        round_wsub1(wsub1_b1[1], 1, 2, 2, nc.scalar.copy)
+        round_wsub1(late_by_scalar, 1, 2, 2, nc.scalar.copy)
         for j in range(6, ROW_TILES):
             for half in range(2):
                 angles([j], half)
@@ -226,20 +226,22 @@ def tile_list_halo_spin_orientation_kernel(
             )
         pick(2)
         quantize(wsub1_w[0][:], wsub1_s[0][:], wsub1_b0[:])
+        order_columns(wsub2_s[:], wsub2_s_raw[:], 2, nc.vector.tensor_copy)
         pick(3)
+        wsub1_b1 = [placed("wsub1_b10", [PART, 256, 4], BF16, at_late_b), late_by_scalar]
         nc.vector.tensor_copy(
             wsub1_b1[0][:].rearrange("p (t q i) j -> p t q j i", t=2, i=8),
             wsub1_raw[1][:].rearrange("p j (q t i) -> p t q j i", t=4, i=8)[:, 0:2],
         )
-        order_columns(wsub2_s[:], wsub2_s_raw[:], 2, nc.vector.tensor_copy)
         pick(4)
+        wsub1_w.append(kept("wsub1_w1", [PART, BANK], U32, tag="wsub1_b0"))
         quantize(wsub1_w[1][:, halves[0]], wsub1_s[1][:, halves[0]], wsub1_b1[0][:])
         pick(5)
         quantize(wsub1_w[1][:, halves[1]], wsub1_s[1][:, halves[1]], wsub1_b1[1][:])
         pick(6)
         pick(7)
 
-        wspin_b0 = placed("wspin_b0", [PART, N, 4], BF16, at_th6)
+        wspin_b0 = placed("wspin_b0", [PART, N, 4], BF16, at_wspin_b0)
         nc.gpsimd.tensor_scalar(wspin_b0[:], wspin_raw[0][:].rearrange("p t n -> p n t"), 1.0, 0.0, ALU.mult, ALU.add)
 
         cos, sin, cos_b1, sin_b2 = {}, {}, {}, {}

@@ -20,7 +20,6 @@ ALU = mybir.AluOpType
 
 PART = 128
 BANK = 512
-QUADS = 4
 ROW_TILES = H // PART
 BIAS_ROW = PART - ROW_TILES
 PIECES = ([(0, 256), (256, 256)], [(0, 256), (256, 128), (384, 128)])
@@ -99,32 +98,31 @@ def tile_list_halo_spin_orientation_kernel(
         v_sg = kept("v_sg", [PART, S], U8, tag="picked_scales")
         v_s = kept("v_s", [PART, 2, S], U8)
 
-        nc.sync.dma_start(tab_s[0:32, :].bitcast(I32), tab_scales.rearrange("g r c -> r g c").bitcast(I32))
+        for g in range(2):
+            nc.sync.dma_start(
+                tab_s[g:32:2, :].bitcast(I32), tab_scales[g].rearrange("(q r) c -> r q c", r=4).bitcast(I32)
+            )
         nc.sync.dma_start(offs_t[:], offs)
         nc.sync.dma_start(tab_w[0][:], words(tab_words[0]))
-        for quad in range(QUADS):
+        for r in range(4):
             nc.sync.dma_start(
-                wang_s_raw[32 * quad : 32 * quad + 4, :].rearrange("s (g c) -> s g c", g=2),
-                wang_scales[:, 4 * quad : 4 * quad + 4, :].rearrange("g s c -> s g c").bitcast(I32),
+                wang_s_raw[r:PART:32, :].rearrange("q (g c) -> q g c", g=2),
+                wang_scales[:, r:16:4, :].rearrange("g q c -> q g c").bitcast(I32),
             )
         nc.sync.dma_start(wang_raw[0][:], wang_v[:, :, 0 : BANK // 2])
         nc.sync.dma_start(tab_w[1][:], words(tab_words[1]))
         nc.sync.dma_start(offs2_t[:], offs2)
         nc.vector.tensor_copy(v_sg[:], tab_s[:].indirect(offs_t[:]))
-        for quad in range(QUADS):
-            nc.sync.dma_start(
-                v_s[32 * quad : 32 * quad + 4].bitcast(I32), v_sg[8 * quad : 8 * quad + 8, :].bitcast(I32)
-            )
+        for r in range(4):
+            nc.sync.dma_start(v_s[r:PART:32].bitcast(I32), v_sg[8 * r : 8 * r + 8, :].bitcast(I32))
         for a in range(2):
             nc.sync.dma_start(wsub2_raw[a][:], words(wsub2_words[0])[:, BANK * a : BANK * (a + 1)])
         nc.sync.dma_start(tab2_w[:], words(tab2_words[0]))
         nc.sync.dma_start(wang_raw[1][:], wang_v[:, :, BANK // 2 : BANK])
         nc.sync.dma_start(pos_t[:], pos1)
         nc.sync.dma_start(wsub1_raw[0][:], wsub1_v[:, :, 0:BANK])
-        for quad in range(QUADS):
-            nc.sync.dma_start(
-                wsub2_s_raw[32 * quad : 32 * quad + 4, :], wsub2_scales[0][4 * quad : 4 * quad + 4, :].bitcast(I32)
-            )
+        for r in range(4):
+            nc.sync.dma_start(wsub2_s_raw[r:PART:32, :], wsub2_scales[0][r:16:4, :].bitcast(I32))
 
         bias_ps = banks.tile([PART, BANK], F32, name="bank", tag="bank")
         nc.tensor.transpose(bias_ps[:, 0:PART], bias_rows[:], ident[:])
@@ -162,10 +160,8 @@ def tile_list_halo_spin_orientation_kernel(
         wspin_raw = [kept("wspin_raw%d" % a, [PART, 4, N], F32, tag="stage%d" % (a + 1)) for a in range(2)]
         for t in range(4):
             nc.sync.dma_start(wspin_raw[0][:, t, :], wspin_v[0, t])
-        for quad in range(QUADS):
-            nc.sync.dma_start(
-                v2_s[32 * quad : 32 * quad + 4, :].bitcast(I32), v2_sg[4 * quad : 4 * quad + 4, :].bitcast(I32)
-            )
+        for r in range(4):
+            nc.sync.dma_start(v2_s[r:PART:32, :].bitcast(I32), v2_sg[r:16:4, :].bitcast(I32))
         for t in range(4):
             nc.sync.dma_start(wspin_raw[1][:, t, :], wspin_v[1, t])
 

@@ -20,6 +20,7 @@ ALU = mybir.AluOpType
 
 PART = 128
 BANK = 512
+QUADS = 4
 ROW_TILES = H // PART
 BIAS_ROW = PART - ROW_TILES
 PIECES = ([(0, 256), (256, 256)], [(0, 256), (256, 128), (384, 128)])
@@ -98,31 +99,32 @@ def tile_list_halo_spin_orientation_kernel(
         v_sg = kept("v_sg", [PART, S], U8, tag="picked_scales")
         v_s = kept("v_s", [PART, 2, S], U8)
 
-        for g in range(2):
-            nc.sync.dma_start(
-                tab_s[g:32:2, :].bitcast(I32), tab_scales[g].rearrange("(q r) c -> r q c", r=4).bitcast(I32)
-            )
+        nc.sync.dma_start(tab_s[0:32, :].bitcast(I32), tab_scales.rearrange("g r c -> r g c").bitcast(I32))
         nc.sync.dma_start(offs_t[:], offs)
         nc.sync.dma_start(tab_w[0][:], words(tab_words[0]))
-        for r in range(4):
+        for quad in range(QUADS):
             nc.sync.dma_start(
-                wang_s_raw[r:PART:32, :].rearrange("q (g c) -> q g c", g=2),
-                wang_scales[:, r:16:4, :].rearrange("g q c -> q g c").bitcast(I32),
+                wang_s_raw[32 * quad : 32 * quad + 4, :].rearrange("s (g c) -> s g c", g=2),
+                wang_scales[:, 4 * quad : 4 * quad + 4, :].rearrange("g s c -> s g c").bitcast(I32),
             )
         nc.sync.dma_start(wang_raw[0][:], wang_v[:, :, 0 : BANK // 2])
         nc.sync.dma_start(tab_w[1][:], words(tab_words[1]))
         nc.sync.dma_start(offs2_t[:], offs2)
         nc.vector.tensor_copy(v_sg[:], tab_s[:].indirect(offs_t[:]))
-        for r in range(4):
-            nc.sync.dma_start(v_s[r:PART:32].bitcast(I32), v_sg[8 * r : 8 * r + 8, :].bitcast(I32))
+        for quad in range(QUADS):
+            nc.sync.dma_start(
+                v_s[32 * quad : 32 * quad + 4].bitcast(I32), v_sg[8 * quad : 8 * quad + 8, :].bitcast(I32)
+            )
         for a in range(2):
             nc.sync.dma_start(wsub2_raw[a][:], words(wsub2_words[0])[:, BANK * a : BANK * (a + 1)])
         nc.sync.dma_start(tab2_w[:], words(tab2_words[0]))
         nc.sync.dma_start(wang_raw[1][:], wang_v[:, :, BANK // 2 : BANK])
         nc.sync.dma_start(pos_t[:], pos1)
         nc.sync.dma_start(wsub1_raw[0][:], wsub1_v[:, :, 0:BANK])
-        for r in range(4):
-            nc.sync.dma_start(wsub2_s_raw[r:PART:32, :], wsub2_scales[0][r:16:4, :].bitcast(I32))
+        for quad in range(QUADS):
+            nc.sync.dma_start(
+                wsub2_s_raw[32 * quad : 32 * quad + 4, :], wsub2_scales[0][4 * quad : 4 * quad + 4, :].bitcast(I32)
+            )
 
         bias_ps = banks.tile([PART, BANK], F32, name="bank", tag="bank")
         nc.tensor.transpose(bias_ps[:, 0:PART], bias_rows[:], ident[:])
@@ -160,8 +162,10 @@ def tile_list_halo_spin_orientation_kernel(
         wspin_raw = [kept("wspin_raw%d" % a, [PART, 4, N], F32, tag="stage%d" % (a + 1)) for a in range(2)]
         for t in range(4):
             nc.sync.dma_start(wspin_raw[0][:, t, :], wspin_v[0, t])
-        for r in range(4):
-            nc.sync.dma_start(v2_s[r:PART:32, :].bitcast(I32), v2_sg[r:16:4, :].bitcast(I32))
+        for quad in range(QUADS):
+            nc.sync.dma_start(
+                v2_s[32 * quad : 32 * quad + 4, :].bitcast(I32), v2_sg[4 * quad : 4 * quad + 4, :].bitcast(I32)
+            )
         for t in range(4):
             nc.sync.dma_start(wspin_raw[1][:, t, :], wspin_v[1, t])
 
@@ -246,43 +250,41 @@ def tile_list_halo_spin_orientation_kernel(
         def trig(a, c):
             m0, w = PIECES[a][c]
             if (a, c) == last:
-                cos[a, c] = placed("cos_last", [PART, 4, w], F32, at_cos_last)
+                cos[a, c] = placed("cos_last", [PART, 2, w, 2], F32, at_cos_last)
             else:
-                cos[a, c] = kept("cos%d%d" % (a, c), [PART, 4, w], F32)
-            sin[a, c] = kept("sin%d%d" % (a, c), [PART, 4, w], F32)
-            picked = ang[a][:, :, m0 : m0 + w]
+                cos[a, c] = kept("cos%d%d" % (a, c), [PART, 2, w, 2], F32)
+            sin[a, c] = kept("sin%d%d" % (a, c), [PART, 2, w, 2], F32)
+            picked = ang[a][:, :, m0 : m0 + w].rearrange("p (y z) m -> p y m z", z=2)
             nc.scalar.activation(cos[a, c][:], picked, ACT.Abs)
             nc.scalar.activation(sin[a, c][:], picked, ACT.Sin)
             nc.scalar.activation(cos[a, c][:], cos[a, c][:], ACT.Sin, bias=math.pi / 2, scale=-1.0)
 
         def products(a, c, name, codes, scales, factor, dst):
             m0, w = PIECES[a][c]
-            tiles = BANK // w
-            dst[a, c] = kept("%s%d%d" % (name, a, c), [PART, w // 4, 4, 4], F32)
-            for t0 in range(0, 4, tiles):
-                bank = proj.tile([PART, tiles, w], F32, name="projection", tag="projection")
-                for d in range(tiles):
-                    cols = slice(PART * (t0 + d), PART * (t0 + d + 1))
+            dst[a, c] = kept("%s%d%d" % (name, a, c), [PART, w, 4], F32)
+            for u0 in range(0, w, PART):
+                bank = proj.tile([PART, 4, PART], F32, name="projection", tag="projection")
+                picked = slice(m0 + u0, m0 + u0 + PART)
+                for t in range(4):
+                    cols = slice(PART * t, PART * (t + 1))
                     nc.tensor.matmul_mx(
-                        out=bank[:, d, :],
+                        out=bank[:, t, :],
                         lhsT=codes[:, cols].bitcast(FP8X4),
                         lhsT_scale=scales[:, cols],
-                        rhs=v2_w[:, m0 : m0 + w].bitcast(FP8X4),
-                        rhs_scale=v2_s[:, m0 : m0 + w],
+                        rhs=v2_w[:, picked].bitcast(FP8X4),
+                        rhs_scale=v2_s[:, picked],
                         start=True,
                         stop=True,
                     )
                 nc.vector.tensor_tensor(
-                    dst[a, c][:].rearrange("p u t e -> p t u e")[:, t0 : t0 + tiles],
-                    bank[:].rearrange("p t (u e) -> p t u e", e=4),
-                    factor[a, c][:, t0 : t0 + tiles, :].rearrange("p t (u e) -> p t u e", e=4),
+                    dst[a, c][:, u0 : u0 + PART, :].rearrange("p m (y z) -> p m y z", z=2),
+                    bank[:].rearrange("p (y z) m -> p m y z", z=2),
+                    factor[a, c][:, :, u0 : u0 + PART, :].rearrange("p y m z -> p m y z"),
                     ALU.mult,
                 )
 
-        def mix(a, c, engine, dst):
-            engine.tensor_tensor(
-                dst.rearrange("p (u e) t -> p u t e", e=4), cos_b1[a, c][:], sin_b2[a, c][:], ALU.add
-            )
+        def mix(a, c, engine, dst, cols=slice(None)):
+            engine.tensor_tensor(dst[:], cos_b1[a, c][:, cols, :], sin_b2[a, c][:, cols, :], ALU.add)
 
         def project(a, c):
             trig(a, c)
@@ -293,77 +295,92 @@ def tile_list_halo_spin_orientation_kernel(
             project(0, c)
         h0_b = [placed("h0_b%d" % c, [PART, 256, 4], BF16, at_h0_b + 2048 * c) for c in range(2)]
         for c in range(2):
-            mix(0, c, nc.gpsimd, h0_b[c][:])
-        for c in range(len(PIECES[1])):
+            mix(0, c, nc.gpsimd, h0_b[c])
+        project(1, 0)
+        h1_first = kept("h1_first", [PART, PART, 4], BF16)
+        mix(1, 0, nc.gpsimd, h1_first, slice(0, PART))
+        for c in range(1, len(PIECES[1])):
             project(1, c)
 
-        wspin_b1 = placed("wspin_b1", [PART, N, 4], BF16, at_ang1)
-        nc.scalar.copy(
-            wspin_b1[:].rearrange("p (u e) t -> p u t e", e=4), wspin_raw[1][:].rearrange("p t (u e) -> p u t e", e=4)
-        )
+        wspin_b1 = [placed("wspin_b1%d" % b, [PART, 256, 4], BF16, at_ang1 + 2048 * b) for b in range(2)]
+        for b in range(2):
+            nc.scalar.copy(
+                wspin_b1[b][:].rearrange("p (u e) t -> p u t e", e=4),
+                wspin_raw[1][:, :, halves[b]].rearrange("p t (u e) -> p u t e", e=4),
+            )
 
-        wspin_s = [kept("wspin_s%d" % a, [PART, N], U8) for a in range(2)]
-        wspin_w = [placed("wspin_w0", [PART, N], U32, at_cos_last - 1984)]
-        h0_w = placed("h0_w", [PART, P], U32, at_cos_last + 64)
-        h0_s = kept("h0_s", [PART, P], U8)
-        wspin_w.append(placed("wspin_w1", [PART, N], U32, at_h0_b + 2048))
+        wspin_w = [[kept("wspin_w%d%d" % (a, b), [PART, 256], U32) for b in range(2)] for a in range(2)]
+        wspin_s = [
+            [placed("wspin_s0%d" % b, [PART, 256], U8, at_cos_last + 256 * b) for b in range(2)],
+            [kept("wspin_s1%d" % b, [PART, 256], U8) for b in range(2)],
+        ]
+        h0_w = kept("h0_w", [PART, P], U32)
+        h0_s = placed("h0_s", [PART, P], U8, at_cos_last + 512)
         h1_b = [
-            placed("h1_b0", [PART, 256, 4], BF16, at_h0_b),
-            placed("h1_b1", [PART, 128, 4], BF16, at_ang1),
-            placed("h1_b2", [PART, 128, 4], BF16, at_h0_b),
+            placed("h1_b0", [PART, PART, 4], BF16, at_h0_b),
+            placed("h1_b1", [PART, PART, 4], BF16, at_ang1),
+            placed("h1_b2", [PART, PART, 4], BF16, at_h0_b),
         ]
         h1_w = [kept("h1_w%d" % c, [PART, w], U32) for c, (m0, w) in enumerate(PIECES[1])]
-        h1_s = [kept("h1_s%d" % c, [PART, w], U8) for c, (m0, w) in enumerate(PIECES[1])]
+        h1_s = [placed("h1_s0", [PART, 256], U8, at_cos_last + 1024)]
+        h1_s += [kept("h1_s%d" % c, [PART, PART], U8) for c in (1, 2)]
         out_banks = {}
 
-        def spin(a, c):
+        def spin(a, c, b):
             m0, w = PIECES[1][c]
             codes, scales = (h0_w[:, m0 : m0 + w], h0_s[:, m0 : m0 + w]) if a == 0 else (h1_w[c][:], h1_s[c][:])
-            for b in range(2):
-                if a == 0 and c < last[1]:
-                    out_banks[c, b] = banks.tile([PART, 2, w], F32, name="bank", tag="bank")
-                elif a == 0:
-                    out_banks[c, b] = proj.tile([PART, 2, w], F32, name="projection", tag="projection")
-                for d in range(2):
-                    rows = slice(PART * (2 * b + d), PART * (2 * b + d + 1))
-                    nc.tensor.matmul_mx(
-                        out=out_banks[c, b][:, d, :],
-                        lhsT=wspin_w[a][:, rows].bitcast(FP8X4),
-                        lhsT_scale=wspin_s[a][:, rows],
-                        rhs=codes.bitcast(FP8X4),
-                        rhs_scale=scales,
-                        start=(a == 0 and d == 0),
-                        stop=(a == 1 and d == 1),
-                    )
+            if a == 0 and c < last[1]:
+                out_banks[c, b] = banks.tile([PART, 2, w], F32, name="bank", tag="bank")
+            elif a == 0:
+                out_banks[c, b] = proj.tile([PART, 2, w], F32, name="projection", tag="projection")
+            for d in range(2):
+                rows = slice(PART * d, PART * (d + 1))
+                nc.tensor.matmul_mx(
+                    out=out_banks[c, b][:, d, :],
+                    lhsT=wspin_w[a][b][:, rows].bitcast(FP8X4),
+                    lhsT_scale=wspin_s[a][b][:, rows],
+                    rhs=codes.bitcast(FP8X4),
+                    rhs_scale=scales,
+                    start=(a == 0 and d == 0),
+                    stop=(a == 1 and d == 1),
+                )
 
         out_v = out.rearrange("(n p) m -> p n m", p=PART)
 
-        def store(c):
+        def store(c, b):
             m0, w = PIECES[1][c]
-            for b in range(2):
-                res = kept("res%d%d" % (c, b), [PART, 2, w], F32)
-                if b == 0 or c == 0:
-                    nc.scalar.copy(res[:], out_banks[c, b][:])
-                else:
-                    nc.vector.tensor_copy(res[:], out_banks[c, b][:])
-                queue = nc.scalar if (c, b) == (last[1], 0) else nc.sync
-                queue.dma_start(out_v[:, 2 * b : 2 * (b + 1), m0 : m0 + w], res[:])
+            res = kept("res%d%d" % (c, b), [PART, 2, w], F32)
+            if b == 0 or c == 0:
+                nc.scalar.copy(res[:], out_banks[c, b][:])
+            else:
+                nc.vector.tensor_copy(res[:], out_banks[c, b][:])
+            queue = nc.scalar if (c, b) == (last[1], 0) else nc.sync
+            queue.dma_start(out_v[:, 2 * b : 2 * (b + 1), m0 : m0 + w], res[:])
 
-        quantize(wspin_w[0][:], wspin_s[0][:], wspin_b0[:])
-        for half in range(2):
-            quantize(h0_w[:, halves[half]], h0_s[:, halves[half]], h0_b[half][:])
-        spin(0, 0)
-        mix(1, 0, nc.vector, h1_b[0][:])
-        quantize(wspin_w[1][:], wspin_s[1][:], wspin_b1[:])
-        quantize(h1_w[0][:], h1_s[0][:], h1_b[0][:])
-        spin(1, 0)
-        spin(0, 1)
-        spin(0, 2)
-        store(0)
-        mix(1, 1, nc.vector, h1_b[1][:])
-        mix(1, 2, nc.vector, h1_b[2][:])
+        quantize(h0_w[:, halves[0]], h0_s[:, halves[0]], h0_b[0][:])
+        quantize(wspin_w[0][0][:], wspin_s[0][0][:], wspin_b0[:, halves[0], :])
+        spin(0, 0, 0)
+        mix(1, 0, nc.vector, h1_b[0], slice(PART, 2 * PART))
+        quantize(h1_w[0][:, 0:PART], h1_s[0][:, 0:PART], h1_first[:])
+        quantize(wspin_w[1][0][:], wspin_s[1][0][:], wspin_b1[0][:])
+        quantize(h1_w[0][:, PART : 2 * PART], h1_s[0][:, PART : 2 * PART], h1_b[0][:])
+        spin(1, 0, 0)
+        store(0, 0)
+        quantize(wspin_w[0][1][:], wspin_s[0][1][:], wspin_b0[:, halves[1], :])
+        quantize(h0_w[:, halves[1]], h0_s[:, halves[1]], h0_b[1][:])
+        quantize(wspin_w[1][1][:], wspin_s[1][1][:], wspin_b1[1][:])
+        spin(0, 0, 1)
+        spin(1, 0, 1)
+        for c in (1, 2):
+            for b in range(2):
+                spin(0, c, b)
+        store(0, 1)
+        for c in (1, 2):
+            mix(1, c, nc.vector, h1_b[c])
         for c in (1, 2):
             quantize(h1_w[c][:], h1_s[c][:], h1_b[c][:])
-            spin(1, c)
+            for b in range(2):
+                spin(1, c, b)
         for c in (1, 2):
-            store(c)
+            for b in range(2):
+                store(c, b)

@@ -23,6 +23,8 @@ BANK = 512
 QUADS = 4
 ROW_TILES = H // PART
 BIAS_ROW = PART - ROW_TILES
+TAB_ROW = PART - 32
+TAB2_ROW = PART - 16
 PIECES = ([(0, 256), (256, 256)], [(0, 256), (256, 128), (384, 128)])
 
 
@@ -60,7 +62,7 @@ def tile_list_halo_spin_orientation_kernel(
         def quantize(codes, scales, values):
             nc.vector.quantize_mx(out=codes.bitcast(FP8X4), scales=scales, in_=values.rearrange("p c j -> p (c j)"))
 
-        at_th7, at_wspin_b0, at_late_b, at_h0_b, at_ang1, at_cos_last = 0, 2048, 4096, 6144, 10240, 20480
+        at_th7, at_early_b, at_late_b, at_h0_b, at_ang1, at_cos_last = 0, 2048, 4096, 6144, 10240, 20480
 
         offs_t = lists.tile([PART, S // 16], U16, name="offs_t")
         pos_t = lists.tile([PART, P // 16], U16, name="pos_t")
@@ -74,18 +76,16 @@ def tile_list_halo_spin_orientation_kernel(
         ident = kept("ident", [PART, PART], F32)
         nc.vector.memset(wang_s_raw[:], 0)
         make_identity(nc, ident[:])
-        nc.vector.memset(tab2_s[:].bitcast(I32), 0)
-        nc.gpsimd.dma_start(tab2_s[0:16, :].bitcast(I32), tab2_scales[0].bitcast(I32))
-        nc.vector.memset(tab_s[32:64, :].bitcast(I32), 0)
-        nc.vector.memset(tab_s[64:PART, :].bitcast(I32), 0)
+        nc.vector.memset(tab_s[0:TAB_ROW, :].bitcast(I32), 0)
+        nc.vector.memset(tab2_s[0:TAB2_ROW, :].bitcast(I32), 0)
+        nc.gpsimd.dma_start(tab2_s[TAB2_ROW:PART, :].bitcast(I32), tab2_scales[0].bitcast(I32))
         for a in range(2):
             nc.gpsimd.dma_start(
                 bias_rows[BIAS_ROW + 4 * a : BIAS_ROW + 4 * a + 4, :].rearrange("t (q i) -> t q i", i=8),
                 bang[BANK * a : BANK * (a + 1)].rearrange("(q t i) -> t q i", t=4, i=8),
             )
-        nc.vector.memset(wsub2_s_raw[:], 0)
-        nc.vector.memset(bias_rows[0:96, :], 0.0)
-        nc.vector.memset(bias_rows[96:BIAS_ROW, :], 0.0)
+        nc.gpsimd.memset(wsub2_s_raw[:], 0)
+        nc.vector.memset(bias_rows[0:BIAS_ROW, :], 0.0)
         warm = kept("warm", [PART, 16], F32)
         nc.scalar.activation(warm[0:96, 0:1], bias_rows[0:96, 0:1], ACT.Sin)
 
@@ -99,7 +99,7 @@ def tile_list_halo_spin_orientation_kernel(
         v_sg = kept("v_sg", [PART, S], U8, tag="picked_scales")
         v_s = kept("v_s", [PART, 2, S], U8)
 
-        nc.sync.dma_start(tab_s[0:32, :].bitcast(I32), tab_scales.rearrange("g r c -> r g c").bitcast(I32))
+        nc.sync.dma_start(tab_s[TAB_ROW:PART, :].bitcast(I32), tab_scales.rearrange("g r c -> r g c").bitcast(I32))
         nc.sync.dma_start(offs_t[:], offs)
         nc.sync.dma_start(tab_w[0][:], words(tab_words[0]))
         for quad in range(QUADS):
@@ -113,7 +113,8 @@ def tile_list_halo_spin_orientation_kernel(
         nc.vector.tensor_copy(v_sg[:], tab_s[:].indirect(offs_t[:]))
         for quad in range(QUADS):
             nc.sync.dma_start(
-                v_s[32 * quad : 32 * quad + 4].bitcast(I32), v_sg[8 * quad : 8 * quad + 8, :].bitcast(I32)
+                v_s[32 * quad : 32 * quad + 4].bitcast(I32),
+                v_sg[TAB_ROW + 8 * quad : TAB_ROW + 8 * quad + 8, :].bitcast(I32),
             )
         for a in range(2):
             nc.sync.dma_start(wsub2_raw[a][:], words(wsub2_words[0])[:, BANK * a : BANK * (a + 1)])
@@ -164,7 +165,8 @@ def tile_list_halo_spin_orientation_kernel(
             nc.sync.dma_start(wspin_raw[0][:, t, :], wspin_v[0, t])
         for quad in range(QUADS):
             nc.sync.dma_start(
-                v2_s[32 * quad : 32 * quad + 4, :].bitcast(I32), v2_sg[4 * quad : 4 * quad + 4, :].bitcast(I32)
+                v2_s[32 * quad : 32 * quad + 4, :].bitcast(I32),
+                v2_sg[TAB2_ROW + 4 * quad : TAB2_ROW + 4 * quad + 4, :].bitcast(I32),
             )
         for t in range(4):
             nc.sync.dma_start(wspin_raw[1][:, t, :], wspin_v[1, t])
@@ -241,8 +243,10 @@ def tile_list_halo_spin_orientation_kernel(
         pick(6)
         pick(7)
 
-        wspin_b0 = placed("wspin_b0", [PART, N, 4], BF16, at_wspin_b0)
-        nc.gpsimd.tensor_scalar(wspin_b0[:], wspin_raw[0][:].rearrange("p t n -> p n t"), 1.0, 0.0, ALU.mult, ALU.add)
+        early_b = placed("early_b", [PART, 3 * PART, 4], BF16, at_early_b)
+        nc.gpsimd.tensor_scalar(
+            early_b[:], wspin_raw[0][:, :, 0 : 3 * PART].rearrange("p t n -> p n t"), 1.0, 0.0, ALU.mult, ALU.add
+        )
 
         cos, sin, cos_b1, sin_b2 = {}, {}, {}, {}
         last = (1, len(PIECES[1]) - 1)
@@ -302,17 +306,26 @@ def tile_list_halo_spin_orientation_kernel(
         for c in range(1, len(PIECES[1])):
             project(1, c)
 
-        wspin_b1 = [placed("wspin_b1%d" % b, [PART, 256, 4], BF16, at_ang1 + 2048 * b) for b in range(2)]
-        for b in range(2):
+        def round_wspin(dst, a, cols):
             nc.scalar.copy(
-                wspin_b1[b][:].rearrange("p (u e) t -> p u t e", e=4),
-                wspin_raw[1][:, :, halves[b]].rearrange("p t (u e) -> p u t e", e=4),
+                dst.rearrange("p (u e) t -> p u t e", e=4), wspin_raw[a][:, :, cols].rearrange("p t (u e) -> p u t e", e=4)
             )
 
-        wspin_w = [[kept("wspin_w%d%d" % (a, b), [PART, 256], U32) for b in range(2)] for a in range(2)]
-        wspin_s = [
-            [placed("wspin_s0%d" % b, [PART, 256], U8, at_cos_last + 256 * b) for b in range(2)],
-            [kept("wspin_s1%d" % b, [PART, 256], U8) for b in range(2)],
+        middle_b = placed("middle_b", [PART, 2 * PART, 4], BF16, at_ang1)
+        late_b = placed("late_b", [PART, 3 * PART, 4], BF16, at_ang1 + 2048)
+        round_wspin(middle_b[:], 1, halves[0])
+        round_wspin(late_b[:, 0:PART, :], 0, slice(3 * PART, N))
+        round_wspin(late_b[:, PART : 3 * PART, :], 1, halves[1])
+
+        early_w = kept("early_w", [PART, 3 * PART], U32)
+        early_s = placed("early_s", [PART, 3 * PART], U8, at_cos_last)
+        middle_w = kept("middle_w", [PART, 2 * PART], U32)
+        middle_s = kept("middle_s", [PART, 2 * PART], U8)
+        late_w = kept("late_w", [PART, 3 * PART], U32)
+        late_s = kept("late_s", [PART, 3 * PART], U8)
+        wspin_at = [
+            [(early_w, early_s, 0), (early_w, early_s, 1), (early_w, early_s, 2), (late_w, late_s, 0)],
+            [(middle_w, middle_s, 0), (middle_w, middle_s, 1), (late_w, late_s, 1), (late_w, late_s, 2)],
         ]
         h0_w = kept("h0_w", [PART, P], U32)
         h0_s = placed("h0_s", [PART, P], U8, at_cos_last + 512)
@@ -334,11 +347,12 @@ def tile_list_halo_spin_orientation_kernel(
             elif a == 0:
                 out_banks[c, b] = proj.tile([PART, 2, w], F32, name="projection", tag="projection")
             for d in range(2):
-                rows = slice(PART * d, PART * (d + 1))
+                weights, weight_scales, slot = wspin_at[a][2 * b + d]
+                rows = slice(PART * slot, PART * (slot + 1))
                 nc.tensor.matmul_mx(
                     out=out_banks[c, b][:, d, :],
-                    lhsT=wspin_w[a][b][:, rows].bitcast(FP8X4),
-                    lhsT_scale=wspin_s[a][b][:, rows],
+                    lhsT=weights[:, rows].bitcast(FP8X4),
+                    lhsT_scale=weight_scales[:, rows],
                     rhs=codes.bitcast(FP8X4),
                     rhs_scale=scales,
                     start=(a == 0 and d == 0),
@@ -358,25 +372,24 @@ def tile_list_halo_spin_orientation_kernel(
             queue.dma_start(out_v[:, 2 * b : 2 * (b + 1), m0 : m0 + w], res[:])
 
         quantize(h0_w[:, halves[0]], h0_s[:, halves[0]], h0_b[0][:])
-        quantize(wspin_w[0][0][:], wspin_s[0][0][:], wspin_b0[:, halves[0], :])
+        quantize(early_w[:], early_s[:], early_b[:])
         spin(0, 0, 0)
         mix(1, 0, nc.vector, h1_b[0], slice(PART, 2 * PART))
         quantize(h1_w[0][:, 0:PART], h1_s[0][:, 0:PART], h1_first[:])
-        quantize(wspin_w[1][0][:], wspin_s[1][0][:], wspin_b1[0][:])
+        quantize(middle_w[:], middle_s[:], middle_b[:])
         quantize(h1_w[0][:, PART : 2 * PART], h1_s[0][:, PART : 2 * PART], h1_b[0][:])
         spin(1, 0, 0)
         store(0, 0)
-        quantize(wspin_w[0][1][:], wspin_s[0][1][:], wspin_b0[:, halves[1], :])
         quantize(h0_w[:, halves[1]], h0_s[:, halves[1]], h0_b[1][:])
-        quantize(wspin_w[1][1][:], wspin_s[1][1][:], wspin_b1[1][:])
+        mix(1, 1, nc.vector, h1_b[1])
+        quantize(late_w[:], late_s[:], late_b[:])
         spin(0, 0, 1)
         spin(1, 0, 1)
         for c in (1, 2):
             for b in range(2):
                 spin(0, c, b)
         store(0, 1)
-        for c in (1, 2):
-            mix(1, c, nc.vector, h1_b[c])
+        mix(1, 2, nc.vector, h1_b[2])
         for c in (1, 2):
             quantize(h1_w[c][:], h1_s[c][:], h1_b[c][:])
             for b in range(2):

@@ -23,6 +23,7 @@ BANK = 512
 QUADS = 4
 ROW_TILES = H // PART
 BIAS_ROW = PART - ROW_TILES
+WARM_PASSES = 3
 TAB_ROW = PART - 32
 TAB2_ROW = PART - 16
 PIECES = ([(0, 256), (256, 256)], [(0, 256), (256, 128), (384, 128)])
@@ -107,40 +108,35 @@ def tile_list_halo_spin_orientation_kernel(
                 wang_s_raw[32 * quad : 32 * quad + 4, :].rearrange("s (g c) -> s g c", g=2),
                 wang_scales[:, 4 * quad : 4 * quad + 4, :].rearrange("g s c -> s g c").bitcast(I32),
             )
+        nc.sync.dma_start(offs2_t[:], offs2)
         nc.sync.dma_start(wang_raw[0][:], wang_v[:, :, 0 : BANK // 2])
         nc.sync.dma_start(tab_w[1][:], words(tab_words[1]))
-        nc.sync.dma_start(offs2_t[:], offs2)
         nc.vector.tensor_copy(v_sg[:], tab_s[:].indirect(offs_t[:]))
         for quad in range(QUADS):
             nc.sync.dma_start(
                 v_s[32 * quad : 32 * quad + 4].bitcast(I32),
                 v_sg[TAB_ROW + 8 * quad : TAB_ROW + 8 * quad + 8, :].bitcast(I32),
             )
-        for a in range(2):
-            nc.sync.dma_start(wsub2_raw[a][:], words(wsub2_words[0])[:, BANK * a : BANK * (a + 1)])
+        nc.sync.dma_start(wsub2_raw[0][:], words(wsub2_words[0])[:, 0:BANK])
         nc.sync.dma_start(tab2_w[:], words(tab2_words[0]))
         nc.sync.dma_start(wang_raw[1][:], wang_v[:, :, BANK // 2 : BANK])
         nc.sync.dma_start(pos_t[:], pos1)
+        nc.sync.dma_start(wsub2_raw[1][:], words(wsub2_words[0])[:, BANK : 2 * BANK])
         nc.sync.dma_start(wsub1_raw[0][:], wsub1_v[:, :, 0:BANK])
         for quad in range(QUADS):
             nc.sync.dma_start(
                 wsub2_s_raw[32 * quad : 32 * quad + 4, :], wsub2_scales[0][4 * quad : 4 * quad + 4, :].bitcast(I32)
             )
 
-        bias_ps = banks.tile([PART, BANK], F32, name="bank", tag="bank")
-        nc.tensor.transpose(bias_ps[:, 0:PART], bias_rows[:], ident[:])
-        bias = kept("bias", [PART, ROW_TILES], F32)
-        nc.scalar.copy(bias[:], bias_ps[:, BIAS_ROW:PART])
-
         v_w = [[kept("v_w%d%d" % (g, half), [PART, BANK], U32) for half in range(2)] for g in range(2)]
+        v2_sg = [kept("v2_sg0", [PART, P // 2], U8), kept("v2_sg1", [PART, P // 2], U8, tag="picked_scales")]
         for g in range(2):
             for half in range(2):
                 picks = offs_t[:, 32 * half : 32 * (half + 1)]
                 nc.vector.tensor_copy(v_w[g][half][:], tab_w[g][:].bitcast(U32).indirect(picks))
-        v2_sg = kept("v2_sg", [PART, P], U8, tag="picked_scales")
+            nc.vector.tensor_copy(v2_sg[g][:], tab2_s[:].indirect(offs2_t[:, 16 * g : 16 * (g + 1)]))
         v2_s = kept("v2_s", [PART, P], U8)
         v2_w = kept("v2_w", [PART, P], U32)
-        nc.vector.tensor_copy(v2_sg[:], tab2_s[:].indirect(offs2_t[:]))
         nc.vector.tensor_copy(v2_w[:], tab2_w[:].bitcast(U32).indirect(offs2_t[:]))
 
         wang_w = [kept("wang_w%d" % a, [PART, 2, BANK // 2], I32) for a in range(2)]
@@ -153,9 +149,23 @@ def tile_list_halo_spin_orientation_kernel(
 
         order_columns(wang_s[:].rearrange("p g c -> p (g c)"), wang_s_raw[:], 2, scalar_move)
         order_wang(0, scalar_move)
-        for a in range(2):
-            order_columns(wsub2_w[a][:], wsub2_raw[a][:], 8, scalar_move)
+        order_columns(wsub2_w[0][:], wsub2_raw[0][:], 8, scalar_move)
         order_wang(1, nc.vector.tensor_copy)
+
+        bias_ps = banks.tile([PART, BANK], F32, name="bank", tag="bank")
+        for d in range(WARM_PASSES):
+            nc.tensor.matmul_mx(
+                out=bias_ps[:],
+                lhsT=wang_w[0][:, 0, 0:64].bitcast(FP4X4),
+                lhsT_scale=wang_s[:, 0, 0:32].bitcast(U8),
+                rhs=v_w[0][0][:].bitcast(FP8X4),
+                rhs_scale=wang_s[:, 0, 0 : BANK // 4].bitcast(U8),
+                start=True,
+                stop=True,
+            )
+        nc.tensor.transpose(bias_ps[:, 0:PART], bias_rows[:], ident[:])
+        bias = kept("bias", [PART, ROW_TILES], F32)
+        nc.scalar.copy(bias[:], bias_ps[:, BIAS_ROW:PART])
 
         wspin_v = wspin.rearrange("(a q t i) n -> a t q i n", a=2, t=4, i=8)
         wsub1_raw.append(kept("wsub1_raw1", [PART, 4, BANK], F32, tag="stage0"))
@@ -163,11 +173,12 @@ def tile_list_halo_spin_orientation_kernel(
         wspin_raw = [kept("wspin_raw%d" % a, [PART, 4, N], F32, tag="stage%d" % (a + 1)) for a in range(2)]
         for t in range(4):
             nc.sync.dma_start(wspin_raw[0][:, t, :], wspin_v[0, t])
-        for quad in range(QUADS):
-            nc.sync.dma_start(
-                v2_s[32 * quad : 32 * quad + 4, :].bitcast(I32),
-                v2_sg[TAB2_ROW + 4 * quad : TAB2_ROW + 4 * quad + 4, :].bitcast(I32),
-            )
+        for half in range(2):
+            for quad in range(QUADS):
+                nc.sync.dma_start(
+                    v2_s[32 * quad : 32 * quad + 4, 256 * half : 256 * (half + 1)].bitcast(I32),
+                    v2_sg[half][TAB2_ROW + 4 * quad : TAB2_ROW + 4 * quad + 4, :].bitcast(I32),
+                )
         for t in range(4):
             nc.sync.dma_start(wspin_raw[1][:, t, :], wspin_v[1, t])
 
@@ -228,6 +239,7 @@ def tile_list_halo_spin_orientation_kernel(
             )
         pick(2)
         quantize(wsub1_w[0][:], wsub1_s[0][:], wsub1_b0[:])
+        order_columns(wsub2_w[1][:], wsub2_raw[1][:], 8, nc.vector.tensor_copy)
         order_columns(wsub2_s[:], wsub2_s_raw[:], 2, nc.vector.tensor_copy)
         pick(3)
         wsub1_b1 = [placed("wsub1_b10", [PART, 256, 4], BF16, at_late_b), late_by_scalar]
@@ -339,15 +351,16 @@ def tile_list_halo_spin_orientation_kernel(
         h1_s += [kept("h1_s%d" % c, [PART, PART], U8) for c in (1, 2)]
         out_banks = {}
 
-        def spin(a, c, b):
+        def spin(a, c, tiles):
             m0, w = PIECES[1][c]
             codes, scales = (h0_w[:, m0 : m0 + w], h0_s[:, m0 : m0 + w]) if a == 0 else (h1_w[c][:], h1_s[c][:])
-            if a == 0 and c < last[1]:
-                out_banks[c, b] = banks.tile([PART, 2, w], F32, name="bank", tag="bank")
-            elif a == 0:
-                out_banks[c, b] = proj.tile([PART, 2, w], F32, name="projection", tag="projection")
-            for d in range(2):
-                weights, weight_scales, slot = wspin_at[a][2 * b + d]
+            for n in tiles:
+                b, d = divmod(n, 2)
+                if (a, d) == (0, 0) and c < last[1]:
+                    out_banks[c, b] = banks.tile([PART, 2, w], F32, name="bank", tag="bank")
+                elif (a, d) == (0, 0):
+                    out_banks[c, b] = proj.tile([PART, 2, w], F32, name="projection", tag="projection")
+                weights, weight_scales, slot = wspin_at[a][n]
                 rows = slice(PART * slot, PART * (slot + 1))
                 nc.tensor.matmul_mx(
                     out=out_banks[c, b][:, d, :],
@@ -355,8 +368,8 @@ def tile_list_halo_spin_orientation_kernel(
                     lhsT_scale=weight_scales[:, rows],
                     rhs=codes.bitcast(FP8X4),
                     rhs_scale=scales,
-                    start=(a == 0 and d == 0),
-                    stop=(a == 1 and d == 1),
+                    start=(a, d) == (0, 0),
+                    stop=(a, d) == (1, 1),
                 )
 
         out_v = out.rearrange("(n p) m -> p n m", p=PART)
@@ -373,27 +386,27 @@ def tile_list_halo_spin_orientation_kernel(
 
         quantize(h0_w[:, halves[0]], h0_s[:, halves[0]], h0_b[0][:])
         quantize(early_w[:], early_s[:], early_b[:])
-        spin(0, 0, 0)
+        spin(0, 0, [0, 1, 2])
+        quantize(h0_w[:, halves[1]], h0_s[:, halves[1]], h0_b[1][:])
+        for c in (1, 2):
+            spin(0, c, [0, 1, 2])
         mix(1, 0, nc.vector, h1_b[0], slice(PART, 2 * PART))
         quantize(h1_w[0][:, 0:PART], h1_s[0][:, 0:PART], h1_first[:])
         quantize(middle_w[:], middle_s[:], middle_b[:])
         quantize(h1_w[0][:, PART : 2 * PART], h1_s[0][:, PART : 2 * PART], h1_b[0][:])
-        spin(1, 0, 0)
+        spin(1, 0, [0, 1])
         store(0, 0)
-        quantize(h0_w[:, halves[1]], h0_s[:, halves[1]], h0_b[1][:])
-        mix(1, 1, nc.vector, h1_b[1])
         quantize(late_w[:], late_s[:], late_b[:])
-        spin(0, 0, 1)
-        spin(1, 0, 1)
-        for c in (1, 2):
-            for b in range(2):
-                spin(0, c, b)
+        spin(0, 0, [3])
+        spin(1, 0, [2, 3])
         store(0, 1)
-        mix(1, 2, nc.vector, h1_b[2])
+        for c in (1, 2):
+            spin(0, c, [3])
+        for c in (1, 2):
+            mix(1, c, nc.vector, h1_b[c])
         for c in (1, 2):
             quantize(h1_w[c][:], h1_s[c][:], h1_b[c][:])
-            for b in range(2):
-                spin(1, c, b)
+            spin(1, c, [0, 1, 2, 3])
         for c in (1, 2):
             for b in range(2):
                 store(c, b)

@@ -20,7 +20,7 @@ ALU = mybir.AluOpType
 
 PART = 128
 BANK = 512
-QUADS = 4
+QUADS = (0, 2, 1, 3)
 ROW_TILES = H // PART
 BIAS_ROW = PART - ROW_TILES
 WARM_PASSES = 3
@@ -63,7 +63,8 @@ def tile_list_halo_spin_orientation_kernel(
         def quantize(codes, scales, values):
             nc.vector.quantize_mx(out=codes.bitcast(FP8X4), scales=scales, in_=values.rearrange("p c j -> p (c j)"))
 
-        at_th7, at_early_b, at_late_b, at_h0_b, at_ang1, at_cos_last = 0, 2048, 4096, 6144, 10240, 20480
+        at_th7, at_early_b, at_late_b, at_h0_b, at_ang1, at_cos_last = 0, 2048, 4096, 7168, 12288, 20480
+        at_h1_first = at_ang1 - 1024
 
         offs_t = lists.tile([PART, S // 16], U16, name="offs_t")
         pos_t = lists.tile([PART, P // 16], U16, name="pos_t")
@@ -96,14 +97,14 @@ def tile_list_halo_spin_orientation_kernel(
         wang_v = wang_words.rearrange("g p c -> p g c").bitcast(I32)
         wsub2_raw = [kept("wsub2_raw%d" % a, [PART, BANK], I32) for a in range(2)]
         wsub1_v = wsub1.rearrange("(p j) c -> p j c", j=4)
-        wsub1_raw = [kept("wsub1_raw0", [PART, 4, BANK], F32)]
+        wsub1_raw1 = kept("wsub1_raw1", [PART, 4, BANK], F32)
         v_sg = kept("v_sg", [PART, S], U8, tag="picked_scales")
         v_s = kept("v_s", [PART, 2, S], U8)
 
         nc.sync.dma_start(tab_s[TAB_ROW:PART, :].bitcast(I32), tab_scales.rearrange("g r c -> r g c").bitcast(I32))
         nc.sync.dma_start(offs_t[:], offs)
         nc.sync.dma_start(tab_w[0][:], words(tab_words[0]))
-        for quad in range(QUADS):
+        for quad in QUADS:
             nc.sync.dma_start(
                 wang_s_raw[32 * quad : 32 * quad + 4, :].rearrange("s (g c) -> s g c", g=2),
                 wang_scales[:, 4 * quad : 4 * quad + 4, :].rearrange("g s c -> s g c").bitcast(I32),
@@ -112,7 +113,7 @@ def tile_list_halo_spin_orientation_kernel(
         nc.sync.dma_start(wang_raw[0][:], wang_v[:, :, 0 : BANK // 2])
         nc.sync.dma_start(tab_w[1][:], words(tab_words[1]))
         nc.vector.tensor_copy(v_sg[:], tab_s[:].indirect(offs_t[:]))
-        for quad in range(QUADS):
+        for quad in QUADS:
             nc.sync.dma_start(
                 v_s[32 * quad : 32 * quad + 4].bitcast(I32),
                 v_sg[TAB_ROW + 8 * quad : TAB_ROW + 8 * quad + 8, :].bitcast(I32),
@@ -122,8 +123,8 @@ def tile_list_halo_spin_orientation_kernel(
         nc.sync.dma_start(wang_raw[1][:], wang_v[:, :, BANK // 2 : BANK])
         nc.sync.dma_start(pos_t[:], pos1)
         nc.sync.dma_start(wsub2_raw[1][:], words(wsub2_words[0])[:, BANK : 2 * BANK])
-        nc.sync.dma_start(wsub1_raw[0][:], wsub1_v[:, :, 0:BANK])
-        for quad in range(QUADS):
+        nc.sync.dma_start(wsub1_raw1[:], wsub1_v[:, :, BANK : 2 * BANK])
+        for quad in QUADS:
             nc.sync.dma_start(
                 wsub2_s_raw[32 * quad : 32 * quad + 4, :], wsub2_scales[0][4 * quad : 4 * quad + 4, :].bitcast(I32)
             )
@@ -168,13 +169,13 @@ def tile_list_halo_spin_orientation_kernel(
         nc.scalar.copy(bias[:], bias_ps[:, BIAS_ROW:PART])
 
         wspin_v = wspin.rearrange("(a q t i) n -> a t q i n", a=2, t=4, i=8)
-        wsub1_raw.append(kept("wsub1_raw1", [PART, 4, BANK], F32, tag="stage0"))
-        nc.sync.dma_start(wsub1_raw[1][:], wsub1_v[:, :, BANK : 2 * BANK])
+        wsub1_raw = [kept("wsub1_raw0", [PART, 4, BANK], F32, tag="stage0"), wsub1_raw1]
+        nc.sync.dma_start(wsub1_raw[0][:], wsub1_v[:, :, 0:BANK])
         wspin_raw = [kept("wspin_raw%d" % a, [PART, 4, N], F32, tag="stage%d" % (a + 1)) for a in range(2)]
         for t in range(4):
             nc.sync.dma_start(wspin_raw[0][:, t, :], wspin_v[0, t])
         for half in range(2):
-            for quad in range(QUADS):
+            for quad in QUADS:
                 nc.sync.dma_start(
                     v2_s[32 * quad : 32 * quad + 4, 256 * half : 256 * (half + 1)].bitcast(I32),
                     v2_sg[half][TAB2_ROW + 4 * quad : TAB2_ROW + 4 * quad + 4, :].bitcast(I32),
@@ -206,16 +207,19 @@ def tile_list_halo_spin_orientation_kernel(
         def pick(j):
             nc.vector.tensor_copy(ang[j // 4][:, j % 4, :], th[j][:].indirect(pos_t[:]))
 
-        def round_wsub1(dst, a, t0, tiles, copy):
-            for t in range(tiles):
-                copy(
-                    dst[:, PART * t : PART * (t + 1), :].rearrange("p (q h e) j -> p q h j e", h=2, e=4),
-                    wsub1_raw[a][:].rearrange("p j (q t h e) -> p t q h j e", t=4, h=2, e=4)[:, t0 + t],
-                )
+        def round_wsub1(dst, a, t):
+            nc.scalar.copy(
+                dst.rearrange("p (q h e) j -> p q h j e", h=2, e=4),
+                wsub1_raw[a][:].rearrange("p j (q t h e) -> p t q h j e", t=4, h=2, e=4)[:, t],
+            )
 
-        wsub1_b0 = kept("wsub1_b0", [PART, BANK, 4], BF16)
-        wsub1_w = [kept("wsub1_w0", [PART, BANK], U32)]
-        late_by_scalar = kept("wsub1_b11", [PART, 256, 4], BF16)
+        def round_pair(dst, a, t0):
+            nc.vector.tensor_copy(
+                dst.rearrange("p (t q i) j -> p t q j i", t=2, i=8),
+                wsub1_raw[a][:].rearrange("p j (q t i) -> p t q j i", t=4, i=8)[:, t0 : t0 + 2],
+            )
+
+        wsub1_b1 = [kept("wsub1_b1%d" % half, [PART, 256, 4], BF16) for half in range(2)]
         wsub1_s = [kept("wsub1_s%d" % a, [PART, BANK], U8) for a in range(2)]
         halves = [slice(256 * half, 256 * (half + 1)) for half in range(2)]
 
@@ -225,33 +229,30 @@ def tile_list_halo_spin_orientation_kernel(
         for j in range(2, 6):
             for half in range(2):
                 angles([j], half)
-        round_wsub1(late_by_scalar, 1, 2, 2, nc.scalar.copy)
+        for t in (2, 3):
+            round_wsub1(wsub1_b1[1][:, PART * (t - 2) : PART * (t - 1), :], 1, t)
         for j in range(6, ROW_TILES):
             for half in range(2):
                 angles([j], half)
 
+        wsub1_w1 = kept("wsub1_w1", [PART, BANK], U32)
         pick(0)
         pick(1)
-        for h in range(2):
-            nc.vector.tensor_copy(
-                wsub1_b0[:].rearrange("p (t q h e) j -> p h t q j e", t=4, h=2, e=4)[:, h],
-                wsub1_raw[0][:].rearrange("p j (q t h e) -> p h t q j e", t=4, h=2, e=4)[:, h],
-            )
+        round_pair(wsub1_b1[0][:], 1, 0)
         pick(2)
-        quantize(wsub1_w[0][:], wsub1_s[0][:], wsub1_b0[:])
+        quantize(wsub1_w1[:, halves[0]], wsub1_s[1][:, halves[0]], wsub1_b1[0][:])
         order_columns(wsub2_w[1][:], wsub2_raw[1][:], 8, nc.vector.tensor_copy)
         order_columns(wsub2_s[:], wsub2_s_raw[:], 2, nc.vector.tensor_copy)
         pick(3)
-        wsub1_b1 = [placed("wsub1_b10", [PART, 256, 4], BF16, at_late_b), late_by_scalar]
-        nc.vector.tensor_copy(
-            wsub1_b1[0][:].rearrange("p (t q i) j -> p t q j i", t=2, i=8),
-            wsub1_raw[1][:].rearrange("p j (q t i) -> p t q j i", t=4, i=8)[:, 0:2],
-        )
+        wsub1_b0 = [placed("wsub1_b00", [PART, 256, 4], BF16, at_late_b), kept("wsub1_b01", [PART, 256, 4], BF16)]
+        for half in range(2):
+            round_pair(wsub1_b0[half][:], 0, 2 * half)
         pick(4)
-        wsub1_w.append(kept("wsub1_w1", [PART, BANK], U32, tag="wsub1_b0"))
-        quantize(wsub1_w[1][:, halves[0]], wsub1_s[1][:, halves[0]], wsub1_b1[0][:])
+        quantize(wsub1_w1[:, halves[1]], wsub1_s[1][:, halves[1]], wsub1_b1[1][:])
+        wsub1_w = [kept("wsub1_w0", [PART, BANK], U32, tag="wsub1_b11"), wsub1_w1]
         pick(5)
-        quantize(wsub1_w[1][:, halves[1]], wsub1_s[1][:, halves[1]], wsub1_b1[1][:])
+        for half in range(2):
+            quantize(wsub1_w[0][:, halves[half]], wsub1_s[0][:, halves[half]], wsub1_b0[half][:])
         pick(6)
         pick(7)
 
@@ -313,7 +314,7 @@ def tile_list_halo_spin_orientation_kernel(
         for c in range(2):
             mix(0, c, nc.gpsimd, h0_b[c])
         project(1, 0)
-        h1_first = kept("h1_first", [PART, PART, 4], BF16)
+        h1_first = placed("h1_first", [PART, PART, 4], BF16, at_h1_first)
         mix(1, 0, nc.gpsimd, h1_first, slice(0, PART))
         for c in range(1, len(PIECES[1])):
             project(1, c)
@@ -334,7 +335,7 @@ def tile_list_halo_spin_orientation_kernel(
         middle_w = kept("middle_w", [PART, 2 * PART], U32)
         middle_s = kept("middle_s", [PART, 2 * PART], U8)
         late_w = kept("late_w", [PART, 3 * PART], U32)
-        late_s = kept("late_s", [PART, 3 * PART], U8)
+        late_s = placed("late_s", [PART, 3 * PART], U8, at_h1_first)
         wspin_at = [
             [(early_w, early_s, 0), (early_w, early_s, 1), (early_w, early_s, 2), (late_w, late_s, 0)],
             [(middle_w, middle_s, 0), (middle_w, middle_s, 1), (late_w, late_s, 1), (late_w, late_s, 2)],
@@ -343,7 +344,7 @@ def tile_list_halo_spin_orientation_kernel(
         h0_s = placed("h0_s", [PART, P], U8, at_cos_last + 512)
         h1_b = [
             placed("h1_b0", [PART, PART, 4], BF16, at_h0_b),
-            placed("h1_b1", [PART, PART, 4], BF16, at_ang1),
+            placed("h1_b1", [PART, PART, 4], BF16, at_ang1 - 512),
             placed("h1_b2", [PART, PART, 4], BF16, at_h0_b),
         ]
         h1_w = [kept("h1_w%d" % c, [PART, w], U32) for c, (m0, w) in enumerate(PIECES[1])]

@@ -24,6 +24,8 @@ QUADS = (0, 2, 1, 3)
 ROW_TILES = H // PART
 BIAS_ROW = PART - ROW_TILES
 WARM_PASSES = 3
+KEEP_WARM_PASSES = 2
+PROJ_BANKS = 3
 TAB_ROW = PART - 32
 TAB2_ROW = PART - 16
 PIECES = ([(0, 256), (256, 256)], [(0, 256), (256, 128), (384, 128)])
@@ -40,7 +42,12 @@ def tile_list_halo_spin_orientation_kernel(
         keep = ctx.enter_context(tc.tile_pool(name="keep", bufs=1))
         shared = ctx.enter_context(tc.tile_pool(name="shared", bufs=1))
         banks = ctx.enter_context(tc.psum_pool(name="banks", bufs=5))
-        proj = ctx.enter_context(tc.psum_pool(name="proj", bufs=3))
+        proj = ctx.enter_context(tc.psum_pool(name="proj", bufs=1))
+        turns = []
+
+        def next_bank(shape):
+            turns.append(len(turns) % PROJ_BANKS)
+            return proj.tile(shape, F32, name="projection%d" % turns[-1], tag="projection%d" % turns[-1])
 
         def kept(name, shape, dtype, tag=None):
             return keep.tile(shape, dtype, name=name, tag=tag or name, align_bytes=64)
@@ -63,8 +70,7 @@ def tile_list_halo_spin_orientation_kernel(
         def quantize(codes, scales, values):
             nc.vector.quantize_mx(out=codes.bitcast(FP8X4), scales=scales, in_=values.rearrange("p c j -> p (c j)"))
 
-        at_th7, at_early_b, at_late_b, at_h0_b, at_ang1, at_cos_last = 0, 2048, 4096, 7168, 12288, 20480
-        at_h1_first = at_ang1 - 1024
+        at_th7, at_wspin_b0, at_late_b, at_h_b, at_ang1, at_cos_last = 0, 2048, 4096, 7168, 12288, 20480
 
         offs_t = lists.tile([PART, S // 16], U16, name="offs_t")
         pos_t = lists.tile([PART, P // 16], U16, name="pos_t")
@@ -256,10 +262,8 @@ def tile_list_halo_spin_orientation_kernel(
         pick(6)
         pick(7)
 
-        early_b = placed("early_b", [PART, 3 * PART, 4], BF16, at_early_b)
-        nc.gpsimd.tensor_scalar(
-            early_b[:], wspin_raw[0][:, :, 0 : 3 * PART].rearrange("p t n -> p n t"), 1.0, 0.0, ALU.mult, ALU.add
-        )
+        wspin_b0 = placed("wspin_b0", [PART, N, 4], BF16, at_wspin_b0)
+        nc.gpsimd.tensor_scalar(wspin_b0[:], wspin_raw[0][:].rearrange("p t n -> p n t"), 1.0, 0.0, ALU.mult, ALU.add)
 
         cos, sin, cos_b1, sin_b2 = {}, {}, {}, {}
         last = (1, len(PIECES[1]) - 1)
@@ -280,7 +284,7 @@ def tile_list_halo_spin_orientation_kernel(
             m0, w = PIECES[a][c]
             dst[a, c] = kept("%s%d%d" % (name, a, c), [PART, w, 4], F32)
             for u0 in range(0, w, PART):
-                bank = proj.tile([PART, 4, PART], F32, name="projection", tag="projection")
+                bank = next_bank([PART, 4, PART])
                 picked = slice(m0 + u0, m0 + u0 + PART)
                 for t in range(4):
                     cols = slice(PART * t, PART * (t + 1))
@@ -308,67 +312,66 @@ def tile_list_halo_spin_orientation_kernel(
             products(a, c, "sin_b2_", wsub2_w[a][:], wsub2_s[:].bitcast(U8)[:, BANK * a : BANK * (a + 1)], sin, sin_b2)
             products(a, c, "cos_b1_", wsub1_w[a][:], wsub1_s[a][:], cos, cos_b1)
 
-        for c in range(2):
-            project(0, c)
-        h0_b = [placed("h0_b%d" % c, [PART, 256, 4], BF16, at_h0_b + 2048 * c) for c in range(2)]
-        for c in range(2):
-            mix(0, c, nc.gpsimd, h0_b[c])
-        project(1, 0)
-        h1_first = placed("h1_first", [PART, PART, 4], BF16, at_h1_first)
-        mix(1, 0, nc.gpsimd, h1_first, slice(0, PART))
-        for c in range(1, len(PIECES[1])):
+        h_b = {
+            (0, 0): placed("h_b00", [PART, 256, 4], BF16, at_h_b),
+            (1, 0): placed("h_b10", [PART, 256, 4], BF16, at_h_b + 2048),
+            (0, 1): placed("h_b01", [PART, PART, 4], BF16, at_h_b + 4096),
+        }
+        for a in range(2):
+            project(a, 0)
+            mix(a, 0, nc.gpsimd, h_b[a, 0])
+        project(0, 1)
+        mix(0, 1, nc.gpsimd, h_b[0, 1], slice(0, PART))
+        for c in (1, 2):
             project(1, c)
-
-        def round_wspin(dst, a, cols):
-            nc.scalar.copy(
-                dst.rearrange("p (u e) t -> p u t e", e=4), wspin_raw[a][:, :, cols].rearrange("p t (u e) -> p u t e", e=4)
+        out_banks = {(2, 0): next_bank([PART, 2, PART])}
+        for d in range(KEEP_WARM_PASSES):
+            nc.tensor.matmul_mx(
+                out=next_bank([PART, BANK])[:],
+                lhsT=wsub2_w[0][:, 0:PART].bitcast(FP8X4),
+                lhsT_scale=wsub2_s[:].bitcast(U8)[:, 0:PART],
+                rhs=v2_w[:].bitcast(FP8X4),
+                rhs_scale=v2_s[:],
+                start=True,
+                stop=True,
             )
 
-        middle_b = placed("middle_b", [PART, 2 * PART, 4], BF16, at_ang1)
-        late_b = placed("late_b", [PART, 3 * PART, 4], BF16, at_ang1 + 2048)
-        round_wspin(middle_b[:], 1, halves[0])
-        round_wspin(late_b[:, 0:PART, :], 0, slice(3 * PART, N))
-        round_wspin(late_b[:, PART : 3 * PART, :], 1, halves[1])
+        wspin_b1 = [placed("wspin_b1%d" % b, [PART, 256, 4], BF16, at_ang1 + 2048 * b) for b in range(2)]
+        for b in range(2):
+            nc.scalar.copy(
+                wspin_b1[b][:].rearrange("p (u e) t -> p u t e", e=4),
+                wspin_raw[1][:, :, halves[b]].rearrange("p t (u e) -> p u t e", e=4),
+            )
 
-        early_w = kept("early_w", [PART, 3 * PART], U32)
-        early_s = placed("early_s", [PART, 3 * PART], U8, at_cos_last)
-        middle_w = kept("middle_w", [PART, 2 * PART], U32)
-        middle_s = kept("middle_s", [PART, 2 * PART], U8)
-        late_w = kept("late_w", [PART, 3 * PART], U32)
-        late_s = placed("late_s", [PART, 3 * PART], U8, at_h1_first)
-        wspin_at = [
-            [(early_w, early_s, 0), (early_w, early_s, 1), (early_w, early_s, 2), (late_w, late_s, 0)],
-            [(middle_w, middle_s, 0), (middle_w, middle_s, 1), (late_w, late_s, 1), (late_w, late_s, 2)],
-        ]
-        h0_w = kept("h0_w", [PART, P], U32)
-        h0_s = placed("h0_s", [PART, P], U8, at_cos_last + 512)
-        h1_b = [
-            placed("h1_b0", [PART, PART, 4], BF16, at_h0_b),
-            placed("h1_b1", [PART, PART, 4], BF16, at_ang1 - 512),
-            placed("h1_b2", [PART, PART, 4], BF16, at_h0_b),
-        ]
-        h1_w = [kept("h1_w%d" % c, [PART, w], U32) for c, (m0, w) in enumerate(PIECES[1])]
-        h1_s = [placed("h1_s0", [PART, 256], U8, at_cos_last + 1024)]
-        h1_s += [kept("h1_s%d" % c, [PART, PART], U8) for c in (1, 2)]
-        out_banks = {}
+        wspin_w = [kept("wspin_w%d" % a, [PART, N], U32) for a in range(2)]
+        wspin_s = [placed("wspin_s0", [PART, N], U8, at_cos_last), kept("wspin_s1", [PART, N], U8)]
+        h_w, h_s = {}, {}
+        for c, (m0, w) in enumerate(PIECES[1]):
+            for a in range(2):
+                h_w[a, c] = kept("h_w%d%d" % (a, c), [PART, w], U32)
+                if (a, c) in h_b:
+                    h_s[a, c] = placed("h_s%d%d" % (a, c), [PART, w], U8, at_cos_last + 512 * (c + 1) + 256 * a)
+                else:
+                    h_s[a, c] = kept("h_s%d%d" % (a, c), [PART, w], U8)
 
-        def spin(a, c, tiles):
+        def quantize_h(a, c):
+            quantize(h_w[a, c][:], h_s[a, c][:], h_b[a, c][:])
+
+        def spin(a, c, b):
             m0, w = PIECES[1][c]
-            codes, scales = (h0_w[:, m0 : m0 + w], h0_s[:, m0 : m0 + w]) if a == 0 else (h1_w[c][:], h1_s[c][:])
-            for n in tiles:
-                b, d = divmod(n, 2)
-                if (a, d) == (0, 0) and c < last[1]:
-                    out_banks[c, b] = banks.tile([PART, 2, w], F32, name="bank", tag="bank")
-                elif (a, d) == (0, 0):
-                    out_banks[c, b] = proj.tile([PART, 2, w], F32, name="projection", tag="projection")
-                weights, weight_scales, slot = wspin_at[a][n]
-                rows = slice(PART * slot, PART * (slot + 1))
+            if a == 0 and c < last[1]:
+                out_banks[c, b] = banks.tile([PART, 2, w], F32, name="bank", tag="bank")
+            elif a == 0 and b == 1:
+                turns.append(0)
+                out_banks[c, b] = next_bank([PART, 2, w])
+            for d in range(2):
+                rows = slice(PART * (2 * b + d), PART * (2 * b + d + 1))
                 nc.tensor.matmul_mx(
                     out=out_banks[c, b][:, d, :],
-                    lhsT=weights[:, rows].bitcast(FP8X4),
-                    lhsT_scale=weight_scales[:, rows],
-                    rhs=codes.bitcast(FP8X4),
-                    rhs_scale=scales,
+                    lhsT=wspin_w[a][:, rows].bitcast(FP8X4),
+                    lhsT_scale=wspin_s[a][:, rows],
+                    rhs=h_w[a, c][:].bitcast(FP8X4),
+                    rhs_scale=h_s[a, c][:],
                     start=(a, d) == (0, 0),
                     stop=(a, d) == (1, 1),
                 )
@@ -378,36 +381,40 @@ def tile_list_halo_spin_orientation_kernel(
         def store(c, b):
             m0, w = PIECES[1][c]
             res = kept("res%d%d" % (c, b), [PART, 2, w], F32)
-            if b == 0 or c == 0:
-                nc.scalar.copy(res[:], out_banks[c, b][:])
-            else:
+            if (c, b) == (last[1], 1):
                 nc.vector.tensor_copy(res[:], out_banks[c, b][:])
+            else:
+                nc.scalar.copy(res[:], out_banks[c, b][:])
             queue = nc.scalar if (c, b) == (last[1], 0) else nc.sync
             queue.dma_start(out_v[:, 2 * b : 2 * (b + 1), m0 : m0 + w], res[:])
 
-        quantize(h0_w[:, halves[0]], h0_s[:, halves[0]], h0_b[0][:])
-        quantize(early_w[:], early_s[:], early_b[:])
-        spin(0, 0, [0, 1, 2])
-        quantize(h0_w[:, halves[1]], h0_s[:, halves[1]], h0_b[1][:])
-        for c in (1, 2):
-            spin(0, c, [0, 1, 2])
-        mix(1, 0, nc.vector, h1_b[0], slice(PART, 2 * PART))
-        quantize(h1_w[0][:, 0:PART], h1_s[0][:, 0:PART], h1_first[:])
-        quantize(middle_w[:], middle_s[:], middle_b[:])
-        quantize(h1_w[0][:, PART : 2 * PART], h1_s[0][:, PART : 2 * PART], h1_b[0][:])
-        spin(1, 0, [0, 1])
+        quantize_h(0, 0)
+        quantize(wspin_w[0][:], wspin_s[0][:], wspin_b0[:])
+        for b in range(2):
+            spin(0, 0, b)
+        quantize_h(1, 0)
+        quantize(wspin_w[1][:, halves[0]], wspin_s[1][:, halves[0]], wspin_b1[0][:])
+        spin(1, 0, 0)
         store(0, 0)
-        quantize(late_w[:], late_s[:], late_b[:])
-        spin(0, 0, [3])
-        spin(1, 0, [2, 3])
+        h_b[1, 1] = placed("h_b11", [PART, PART, 4], BF16, at_h_b)
+        mix(1, 1, nc.vector, h_b[1, 1])
+        quantize(wspin_w[1][:, halves[1]], wspin_s[1][:, halves[1]], wspin_b1[1][:])
+        spin(1, 0, 1)
         store(0, 1)
-        for c in (1, 2):
-            spin(0, c, [3])
-        for c in (1, 2):
-            mix(1, c, nc.vector, h1_b[c])
-        for c in (1, 2):
-            quantize(h1_w[c][:], h1_s[c][:], h1_b[c][:])
-            spin(1, c, [0, 1, 2, 3])
-        for c in (1, 2):
+        quantize_h(0, 1)
+        quantize_h(1, 1)
+        for a in range(2):
             for b in range(2):
-                store(c, b)
+                spin(a, 1, b)
+        for b in range(2):
+            store(1, b)
+        h_b[0, 2] = placed("h_b02", [PART, PART, 4], BF16, at_h_b + 2048)
+        h_b[1, 2] = placed("h_b12", [PART, PART, 4], BF16, at_h_b + 4096)
+        mix(0, 1, nc.vector, h_b[0, 2], slice(PART, 2 * PART))
+        mix(1, 2, nc.vector, h_b[1, 2])
+        for a in range(2):
+            quantize_h(a, 2)
+            for b in range(2):
+                spin(a, 2, b)
+        for b in range(2):
+            store(2, b)

@@ -139,8 +139,14 @@ def tile_list_halo_spin_orientation_kernel(
         v2_sg = [kept("v2_sg0", [PART, P // 2], U8), kept("v2_sg1", [PART, P // 2], U8, tag="picked_scales")]
         for g in range(2):
             for half in range(2):
-                picks = offs_t[:, 32 * half : 32 * (half + 1)]
-                nc.vector.tensor_copy(v_w[g][half][:], tab_w[g][:].bitcast(U32).indirect(picks))
+                parts = 2 if (g, half) == (1, 0) else 1
+                for part in range(parts):
+                    w = BANK // parts
+                    first = (BANK * half + w * part) // 16
+                    nc.vector.tensor_copy(
+                        v_w[g][half][:, w * part : w * (part + 1)],
+                        tab_w[g][:].bitcast(U32).indirect(offs_t[:, first : first + w // 16]),
+                    )
             nc.vector.tensor_copy(v2_sg[g][:], tab2_s[:].indirect(offs2_t[:, 16 * g : 16 * (g + 1)]))
         v2_s = kept("v2_s", [PART, P], U8)
         v2_w = kept("v2_w", [PART, P], U32)
@@ -210,6 +216,23 @@ def tile_list_halo_spin_orientation_kernel(
             for j, bank in zip(tiles, sums):
                 nc.scalar.activation(th[j][:, cols], bank[:], ACT.Identity, bias=bias[:, j : j + 1])
 
+        def first_angles(quarter):
+            cols = slice(256 * quarter, 256 * (quarter + 1))
+            bank = banks.tile([PART, 2, 256], F32, name="bank", tag="bank")
+            for g in range(2):
+                for j in range(2):
+                    nc.tensor.matmul_mx(
+                        out=bank[:, j, :],
+                        lhsT=wang_w[0][:, g, 64 * j : 64 * (j + 1)].bitcast(FP4X4),
+                        lhsT_scale=wang_s[:, g, 32 * j : 32 * (j + 1)].bitcast(U8),
+                        rhs=v_w[g][0][:, cols].bitcast(FP8X4),
+                        rhs_scale=v_s[:, g, cols],
+                        start=(g, j) == (0, 0),
+                        stop=(g, j) == (1, 1),
+                    )
+            for j in range(2):
+                nc.scalar.activation(th[j][:, cols], bank[:, j, :], ACT.Identity, bias=bias[:, j : j + 1])
+
         def pick(j):
             nc.vector.tensor_copy(ang[j // 4][:, j % 4, :], th[j][:].indirect(pos_t[:]))
 
@@ -229,10 +252,12 @@ def tile_list_halo_spin_orientation_kernel(
         wsub1_s = [kept("wsub1_s%d" % a, [PART, BANK], U8) for a in range(2)]
         halves = [slice(256 * half, 256 * (half + 1)) for half in range(2)]
 
-        angles([0, 1], 0)
-        angles([0], 1)
-        angles([1], 1)
-        for j in range(2, 6):
+        for quarter in range(2):
+            first_angles(quarter)
+        angles([2], 0)
+        for j in range(3):
+            angles([j], 1)
+        for j in range(3, 6):
             for half in range(2):
                 angles([j], half)
         for t in (2, 3):
@@ -398,10 +423,10 @@ def tile_list_halo_spin_orientation_kernel(
         store(0, 0)
         h_b[1, 1] = placed("h_b11", [PART, PART, 4], BF16, at_h_b)
         mix(1, 1, nc.vector, h_b[1, 1])
+        quantize_h(0, 1)
         quantize(wspin_w[1][:, halves[1]], wspin_s[1][:, halves[1]], wspin_b1[1][:])
         spin(1, 0, 1)
         store(0, 1)
-        quantize_h(0, 1)
         quantize_h(1, 1)
         for a in range(2):
             for b in range(2):

@@ -104,7 +104,7 @@ def tile_list_halo_spin_orientation_kernel(
         wsub2_raw = [kept("wsub2_raw%d" % a, [PART, BANK], I32) for a in range(2)]
         wsub1_v = wsub1.rearrange("(p j) c -> p j c", j=4)
         wsub1_raw1 = kept("wsub1_raw1", [PART, 4, BANK], F32)
-        v_sg = kept("v_sg", [PART, S], U8, tag="picked_scales")
+        v_sg = kept("v_sg", [PART, S], U8)
         v_s = kept("v_s", [PART, 2, S], U8)
 
         nc.sync.dma_start(tab_s[TAB_ROW:PART, :].bitcast(I32), tab_scales.rearrange("g r c -> r g c").bitcast(I32))
@@ -136,7 +136,7 @@ def tile_list_halo_spin_orientation_kernel(
             )
 
         v_w = [[kept("v_w%d%d" % (g, half), [PART, BANK], U32) for half in range(2)] for g in range(2)]
-        v2_sg = [kept("v2_sg0", [PART, P // 2], U8), kept("v2_sg1", [PART, P // 2], U8, tag="picked_scales")]
+        v2_sg = kept("v2_sg", [PART, P], U8)
         for g in range(2):
             for half in range(2):
                 parts = 2 if (g, half) == (1, 0) else 1
@@ -147,7 +147,8 @@ def tile_list_halo_spin_orientation_kernel(
                         v_w[g][half][:, w * part : w * (part + 1)],
                         tab_w[g][:].bitcast(U32).indirect(offs_t[:, first : first + w // 16]),
                     )
-            nc.vector.tensor_copy(v2_sg[g][:], tab2_s[:].indirect(offs2_t[:, 16 * g : 16 * (g + 1)]))
+            if g == 0:
+                nc.vector.tensor_copy(v2_sg[:], tab2_s[:].indirect(offs2_t[:]))
         v2_s = kept("v2_s", [PART, P], U8)
         v2_w = kept("v2_w", [PART, P], U32)
         nc.vector.tensor_copy(v2_w[:], tab2_w[:].bitcast(U32).indirect(offs2_t[:]))
@@ -186,12 +187,11 @@ def tile_list_halo_spin_orientation_kernel(
         wspin_raw = [kept("wspin_raw%d" % a, [PART, 4, N], F32, tag="stage%d" % (a + 1)) for a in range(2)]
         for t in range(4):
             nc.sync.dma_start(wspin_raw[0][:, t, :], wspin_v[0, t])
-        for half in range(2):
-            for quad in QUADS:
-                nc.sync.dma_start(
-                    v2_s[32 * quad : 32 * quad + 4, 256 * half : 256 * (half + 1)].bitcast(I32),
-                    v2_sg[half][TAB2_ROW + 4 * quad : TAB2_ROW + 4 * quad + 4, :].bitcast(I32),
-                )
+        for quad in QUADS:
+            nc.sync.dma_start(
+                v2_s[32 * quad : 32 * quad + 4, :].bitcast(I32),
+                v2_sg[TAB2_ROW + 4 * quad : TAB2_ROW + 4 * quad + 4, :].bitcast(I32),
+            )
         for t in range(4):
             nc.sync.dma_start(wspin_raw[1][:, t, :], wspin_v[1, t])
 

@@ -20,15 +20,25 @@ ALU = mybir.AluOpType
 
 PART = 128
 BANK = 512
-QUADS = (0, 2, 1, 3)
+HALF = BANK // 2
 ROW_TILES = H // PART
+QUADS = (0, 2, 1, 3)
 BIAS_ROW = PART - ROW_TILES
-WARM_PASSES = 3
-KEEP_WARM_PASSES = 2
-PROJ_BANKS = 3
 TAB_ROW = PART - 32
 TAB2_ROW = PART - 16
+WARM_PASSES = 3
+KEEP_WARM_PASSES = 2
+TH_BANKS = 5
+PROJ_BANKS = 3
 PIECES = ([(0, 256), (256, 256)], [(0, 256), (256, 128), (384, 128)])
+LAST = len(PIECES[1]) - 1
+
+AT_TH7 = 0
+AT_WSPIN_B0 = 2048
+AT_WSUB1_B00 = 4096
+AT_H_B = 7168
+AT_ANG1 = 12288
+AT_COS_LAST = 20480
 
 
 def tile_list_halo_spin_orientation_kernel(
@@ -41,9 +51,12 @@ def tile_list_halo_spin_orientation_kernel(
         lists = ctx.enter_context(tc.tile_pool(name="lists", bufs=1))
         keep = ctx.enter_context(tc.tile_pool(name="keep", bufs=1))
         shared = ctx.enter_context(tc.tile_pool(name="shared", bufs=1))
-        banks = ctx.enter_context(tc.psum_pool(name="banks", bufs=5))
+        banks = ctx.enter_context(tc.psum_pool(name="banks", bufs=TH_BANKS))
         proj = ctx.enter_context(tc.psum_pool(name="proj", bufs=1))
         turns = []
+
+        def any_bank(shape):
+            return banks.tile(shape, F32, name="bank", tag="bank")
 
         def next_bank(shape):
             turns.append(len(turns) % PROJ_BANKS)
@@ -70,7 +83,7 @@ def tile_list_halo_spin_orientation_kernel(
         def quantize(codes, scales, values):
             nc.vector.quantize_mx(out=codes.bitcast(FP8X4), scales=scales, in_=values.rearrange("p c j -> p (c j)"))
 
-        at_th7, at_wspin_b0, at_late_b, at_h_b, at_ang1, at_cos_last = 0, 2048, 4096, 7168, 12288, 20480
+        halves = [slice(HALF * half, HALF * (half + 1)) for half in range(2)]
 
         offs_t = lists.tile([PART, S // 16], U16, name="offs_t")
         pos_t = lists.tile([PART, P // 16], U16, name="pos_t")
@@ -79,7 +92,7 @@ def tile_list_halo_spin_orientation_kernel(
         tab_s = kept("tab_s", [PART, T], U8)
         tab2_s = kept("tab2_s", [PART, T2], U8)
         wang_s_raw = kept("wang_s_raw", [PART, H // 2], I32)
-        wsub2_s_raw = placed("wsub2_s_raw", [PART, H // 4], I32, at_late_b)
+        wsub2_s_raw = placed("wsub2_s_raw", [PART, H // 4], I32, AT_WSUB1_B00)
         bias_rows = kept("bias_rows", [PART, PART], F32)
         ident = kept("ident", [PART, PART], F32)
         nc.vector.memset(wang_s_raw[:], 0)
@@ -87,19 +100,19 @@ def tile_list_halo_spin_orientation_kernel(
         nc.vector.memset(tab_s[0:TAB_ROW, :].bitcast(I32), 0)
         nc.vector.memset(tab2_s[0:TAB2_ROW, :].bitcast(I32), 0)
         nc.gpsimd.dma_start(tab2_s[TAB2_ROW:PART, :].bitcast(I32), tab2_scales[0].bitcast(I32))
+        nc.gpsimd.memset(wsub2_s_raw[:], 0)
         for a in range(2):
             nc.gpsimd.dma_start(
                 bias_rows[BIAS_ROW + 4 * a : BIAS_ROW + 4 * a + 4, :].rearrange("t (q i) -> t q i", i=8),
                 bang[BANK * a : BANK * (a + 1)].rearrange("(q t i) -> t q i", t=4, i=8),
             )
-        nc.gpsimd.memset(wsub2_s_raw[:], 0)
         nc.vector.memset(bias_rows[0:BIAS_ROW, :], 0.0)
         warm = kept("warm", [PART, 16], F32)
         nc.scalar.activation(warm[0:96, 0:1], bias_rows[0:96, 0:1], ACT.Sin)
 
         tab_w = [kept("tab_w%d" % g, [PART, T], I32, tag="stage%d" % g) for g in range(2)]
         tab2_w = kept("tab2_w", [PART, T2], I32, tag="stage2")
-        wang_raw = [kept("wang_raw%d" % a, [PART, 2, BANK // 2], I32) for a in range(2)]
+        wang_raw = [kept("wang_raw%d" % a, [PART, 2, HALF], I32) for a in range(2)]
         wang_v = wang_words.rearrange("g p c -> p g c").bitcast(I32)
         wsub2_raw = [kept("wsub2_raw%d" % a, [PART, BANK], I32) for a in range(2)]
         wsub1_v = wsub1.rearrange("(p j) c -> p j c", j=4)
@@ -116,7 +129,7 @@ def tile_list_halo_spin_orientation_kernel(
                 wang_scales[:, 4 * quad : 4 * quad + 4, :].rearrange("g s c -> s g c").bitcast(I32),
             )
         nc.sync.dma_start(offs2_t[:], offs2)
-        nc.sync.dma_start(wang_raw[0][:], wang_v[:, :, 0 : BANK // 2])
+        nc.sync.dma_start(wang_raw[0][:], wang_v[:, :, halves[0]])
         nc.sync.dma_start(tab_w[1][:], words(tab_words[1]))
         nc.vector.tensor_copy(v_sg[:], tab_s[:].indirect(offs_t[:]))
         for quad in QUADS:
@@ -126,7 +139,7 @@ def tile_list_halo_spin_orientation_kernel(
             )
         nc.sync.dma_start(wsub2_raw[0][:], words(wsub2_words[0])[:, 0:BANK])
         nc.sync.dma_start(tab2_w[:], words(tab2_words[0]))
-        nc.sync.dma_start(wang_raw[1][:], wang_v[:, :, BANK // 2 : BANK])
+        nc.sync.dma_start(wang_raw[1][:], wang_v[:, :, halves[1]])
         nc.sync.dma_start(pos_t[:], pos1)
         nc.sync.dma_start(wsub2_raw[1][:], words(wsub2_words[0])[:, BANK : 2 * BANK])
         nc.sync.dma_start(wsub1_raw1[:], wsub1_v[:, :, BANK : 2 * BANK])
@@ -137,23 +150,25 @@ def tile_list_halo_spin_orientation_kernel(
 
         v_w = [[kept("v_w%d%d" % (g, half), [PART, BANK], U32) for half in range(2)] for g in range(2)]
         v2_sg = kept("v2_sg", [PART, P], U8)
-        for g in range(2):
-            for half in range(2):
-                parts = 2 if (g, half) == (1, 0) else 1
-                for part in range(parts):
-                    w = BANK // parts
-                    first = (BANK * half + w * part) // 16
-                    nc.vector.tensor_copy(
-                        v_w[g][half][:, w * part : w * (part + 1)],
-                        tab_w[g][:].bitcast(U32).indirect(offs_t[:, first : first + w // 16]),
-                    )
-            if g == 0:
-                nc.vector.tensor_copy(v2_sg[:], tab2_s[:].indirect(offs2_t[:]))
+
+        def gather_v(g, first, count):
+            half, col = divmod(first, BANK)
+            nc.vector.tensor_copy(
+                v_w[g][half][:, col : col + count],
+                tab_w[g][:].bitcast(U32).indirect(offs_t[:, first // 16 : (first + count) // 16]),
+            )
+
+        gather_v(0, 0, BANK)
+        gather_v(0, BANK, BANK)
+        nc.vector.tensor_copy(v2_sg[:], tab2_s[:].indirect(offs2_t[:]))
+        gather_v(1, 0, HALF)
+        gather_v(1, HALF, HALF)
+        gather_v(1, BANK, BANK)
         v2_s = kept("v2_s", [PART, P], U8)
         v2_w = kept("v2_w", [PART, P], U32)
         nc.vector.tensor_copy(v2_w[:], tab2_w[:].bitcast(U32).indirect(offs2_t[:]))
 
-        wang_w = [kept("wang_w%d" % a, [PART, 2, BANK // 2], I32) for a in range(2)]
+        wang_w = [kept("wang_w%d" % a, [PART, 2, HALF], I32) for a in range(2)]
         wang_s = kept("wang_s", [PART, 2, H // 4], I32)
         wsub2_w = [kept("wsub2_w%d" % a, [PART, BANK], I32) for a in range(2)]
         wsub2_s = kept("wsub2_s", [PART, H // 4], I32)
@@ -166,10 +181,10 @@ def tile_list_halo_spin_orientation_kernel(
         order_columns(wsub2_w[0][:], wsub2_raw[0][:], 8, scalar_move)
         order_wang(1, nc.vector.tensor_copy)
 
-        bias_ps = banks.tile([PART, BANK], F32, name="bank", tag="bank")
+        unread = any_bank([PART, BANK])
         for d in range(WARM_PASSES):
             nc.tensor.matmul_mx(
-                out=bias_ps[:],
+                out=unread[:],
                 lhsT=wang_w[0][:, 0, 0:64].bitcast(FP4X4),
                 lhsT_scale=wang_s[:, 0, 0:32].bitcast(U8),
                 rhs=v_w[0][0][:].bitcast(FP8X4),
@@ -177,6 +192,7 @@ def tile_list_halo_spin_orientation_kernel(
                 start=True,
                 stop=True,
             )
+        bias_ps = any_bank([PART, BANK])
         nc.tensor.transpose(bias_ps[:, 0:PART], bias_rows[:], ident[:])
         bias = kept("bias", [PART, ROW_TILES], F32)
         nc.scalar.copy(bias[:], bias_ps[:, BIAS_ROW:PART])
@@ -196,88 +212,75 @@ def tile_list_halo_spin_orientation_kernel(
             nc.sync.dma_start(wspin_raw[1][:, t, :], wspin_v[1, t])
 
         th = [kept("th%d" % j, [PART, S], F32) for j in range(ROW_TILES - 1)]
-        th.append(placed("th7", [PART, S], F32, at_th7))
-        ang = [kept("ang0", [PART, 4, P], F32), placed("ang1", [PART, 4, P], F32, at_ang1)]
+        th.append(placed("th7", [PART, S], F32, AT_TH7))
+        ang = [kept("ang0", [PART, 4, P], F32), placed("ang1", [PART, 4, P], F32, AT_ANG1)]
 
-        def angles(tiles, half):
-            cols = slice(BANK * half, BANK * (half + 1))
-            sums = [banks.tile([PART, BANK], F32, name="bank", tag="bank") for j in tiles]
+        def angles(tiles, first, count):
+            half, col = divmod(first, BANK)
+            bank = any_bank([PART, len(tiles), count])
             for g in range(2):
-                for j, bank in zip(tiles, sums):
+                for d, j in enumerate(tiles):
                     nc.tensor.matmul_mx(
-                        out=bank[:],
+                        out=bank[:, d, :],
                         lhsT=wang_w[j // 4][:, g, 64 * (j % 4) : 64 * (j % 4 + 1)].bitcast(FP4X4),
                         lhsT_scale=wang_s[:, g, 32 * j : 32 * (j + 1)].bitcast(U8),
-                        rhs=v_w[g][half][:].bitcast(FP8X4),
-                        rhs_scale=v_s[:, g, cols],
-                        start=(g == 0),
-                        stop=(g == 1),
+                        rhs=v_w[g][half][:, col : col + count].bitcast(FP8X4),
+                        rhs_scale=v_s[:, g, first : first + count],
+                        start=(g, d) == (0, 0),
+                        stop=(g, d) == (1, len(tiles) - 1),
                     )
-            for j, bank in zip(tiles, sums):
-                nc.scalar.activation(th[j][:, cols], bank[:], ACT.Identity, bias=bias[:, j : j + 1])
-
-        def first_angles(quarter):
-            cols = slice(256 * quarter, 256 * (quarter + 1))
-            bank = banks.tile([PART, 2, 256], F32, name="bank", tag="bank")
-            for g in range(2):
-                for j in range(2):
-                    nc.tensor.matmul_mx(
-                        out=bank[:, j, :],
-                        lhsT=wang_w[0][:, g, 64 * j : 64 * (j + 1)].bitcast(FP4X4),
-                        lhsT_scale=wang_s[:, g, 32 * j : 32 * (j + 1)].bitcast(U8),
-                        rhs=v_w[g][0][:, cols].bitcast(FP8X4),
-                        rhs_scale=v_s[:, g, cols],
-                        start=(g, j) == (0, 0),
-                        stop=(g, j) == (1, 1),
-                    )
-            for j in range(2):
-                nc.scalar.activation(th[j][:, cols], bank[:, j, :], ACT.Identity, bias=bias[:, j : j + 1])
+            for d, j in enumerate(tiles):
+                nc.scalar.activation(
+                    th[j][:, first : first + count], bank[:, d, :], ACT.Identity, bias=bias[:, j : j + 1]
+                )
 
         def pick(j):
             nc.vector.tensor_copy(ang[j // 4][:, j % 4, :], th[j][:].indirect(pos_t[:]))
 
-        def round_wsub1(dst, a, t):
+        def round_tile_on_scalar(dst, a, t):
             nc.scalar.copy(
                 dst.rearrange("p (q h e) j -> p q h j e", h=2, e=4),
                 wsub1_raw[a][:].rearrange("p j (q t h e) -> p t q h j e", t=4, h=2, e=4)[:, t],
             )
 
-        def round_pair(dst, a, t0):
+        def round_pair_on_vector(dst, a, t0):
             nc.vector.tensor_copy(
                 dst.rearrange("p (t q i) j -> p t q j i", t=2, i=8),
                 wsub1_raw[a][:].rearrange("p j (q t i) -> p t q j i", t=4, i=8)[:, t0 : t0 + 2],
             )
 
-        wsub1_b1 = [kept("wsub1_b1%d" % half, [PART, 256, 4], BF16) for half in range(2)]
+        wsub1_b1 = [kept("wsub1_b1%d" % half, [PART, HALF, 4], BF16) for half in range(2)]
         wsub1_s = [kept("wsub1_s%d" % a, [PART, BANK], U8) for a in range(2)]
-        halves = [slice(256 * half, 256 * (half + 1)) for half in range(2)]
 
-        for quarter in range(2):
-            first_angles(quarter)
-        angles([2], 0)
+        for first in (0, HALF):
+            angles([0, 1], first, HALF)
+        angles([2], 0, BANK)
         for j in range(3):
-            angles([j], 1)
+            angles([j], BANK, BANK)
         for j in range(3, 6):
-            for half in range(2):
-                angles([j], half)
+            for first in (0, BANK):
+                angles([j], first, BANK)
         for t in (2, 3):
-            round_wsub1(wsub1_b1[1][:, PART * (t - 2) : PART * (t - 1), :], 1, t)
+            round_tile_on_scalar(wsub1_b1[1][:, PART * (t - 2) : PART * (t - 1), :], 1, t)
         for j in range(6, ROW_TILES):
-            for half in range(2):
-                angles([j], half)
+            for first in (0, BANK):
+                angles([j], first, BANK)
 
         wsub1_w1 = kept("wsub1_w1", [PART, BANK], U32)
         pick(0)
         pick(1)
-        round_pair(wsub1_b1[0][:], 1, 0)
+        round_pair_on_vector(wsub1_b1[0][:], 1, 0)
         pick(2)
         quantize(wsub1_w1[:, halves[0]], wsub1_s[1][:, halves[0]], wsub1_b1[0][:])
         order_columns(wsub2_w[1][:], wsub2_raw[1][:], 8, nc.vector.tensor_copy)
         order_columns(wsub2_s[:], wsub2_s_raw[:], 2, nc.vector.tensor_copy)
         pick(3)
-        wsub1_b0 = [placed("wsub1_b00", [PART, 256, 4], BF16, at_late_b), kept("wsub1_b01", [PART, 256, 4], BF16)]
+        wsub1_b0 = [
+            placed("wsub1_b00", [PART, HALF, 4], BF16, AT_WSUB1_B00),
+            kept("wsub1_b01", [PART, HALF, 4], BF16),
+        ]
         for half in range(2):
-            round_pair(wsub1_b0[half][:], 0, 2 * half)
+            round_pair_on_vector(wsub1_b0[half][:], 0, 2 * half)
         pick(4)
         quantize(wsub1_w1[:, halves[1]], wsub1_s[1][:, halves[1]], wsub1_b1[1][:])
         wsub1_w = [kept("wsub1_w0", [PART, BANK], U32, tag="wsub1_b11"), wsub1_w1]
@@ -287,16 +290,15 @@ def tile_list_halo_spin_orientation_kernel(
         pick(6)
         pick(7)
 
-        wspin_b0 = placed("wspin_b0", [PART, N, 4], BF16, at_wspin_b0)
+        wspin_b0 = placed("wspin_b0", [PART, N, 4], BF16, AT_WSPIN_B0)
         nc.gpsimd.tensor_scalar(wspin_b0[:], wspin_raw[0][:].rearrange("p t n -> p n t"), 1.0, 0.0, ALU.mult, ALU.add)
 
         cos, sin, cos_b1, sin_b2 = {}, {}, {}, {}
-        last = (1, len(PIECES[1]) - 1)
 
         def trig(a, c):
             m0, w = PIECES[a][c]
-            if (a, c) == last:
-                cos[a, c] = placed("cos_last", [PART, 2, w, 2], F32, at_cos_last)
+            if (a, c) == (1, LAST):
+                cos[a, c] = placed("cos_last", [PART, 2, w, 2], F32, AT_COS_LAST)
             else:
                 cos[a, c] = kept("cos%d%d" % (a, c), [PART, 2, w, 2], F32)
             sin[a, c] = kept("sin%d%d" % (a, c), [PART, 2, w, 2], F32)
@@ -310,15 +312,15 @@ def tile_list_halo_spin_orientation_kernel(
             dst[a, c] = kept("%s%d%d" % (name, a, c), [PART, w, 4], F32)
             for u0 in range(0, w, PART):
                 bank = next_bank([PART, 4, PART])
-                picked = slice(m0 + u0, m0 + u0 + PART)
+                subhalos = slice(m0 + u0, m0 + u0 + PART)
                 for t in range(4):
                     cols = slice(PART * t, PART * (t + 1))
                     nc.tensor.matmul_mx(
                         out=bank[:, t, :],
                         lhsT=codes[:, cols].bitcast(FP8X4),
                         lhsT_scale=scales[:, cols],
-                        rhs=v2_w[:, picked].bitcast(FP8X4),
-                        rhs_scale=v2_s[:, picked],
+                        rhs=v2_w[:, subhalos].bitcast(FP8X4),
+                        rhs_scale=v2_s[:, subhalos],
                         start=True,
                         stop=True,
                     )
@@ -338,18 +340,18 @@ def tile_list_halo_spin_orientation_kernel(
             products(a, c, "cos_b1_", wsub1_w[a][:], wsub1_s[a][:], cos, cos_b1)
 
         h_b = {
-            (0, 0): placed("h_b00", [PART, 256, 4], BF16, at_h_b),
-            (1, 0): placed("h_b10", [PART, 256, 4], BF16, at_h_b + 2048),
-            (0, 1): placed("h_b01", [PART, PART, 4], BF16, at_h_b + 4096),
+            (0, 0): placed("h_b00", [PART, HALF, 4], BF16, AT_H_B),
+            (1, 0): placed("h_b10", [PART, HALF, 4], BF16, AT_H_B + 2048),
+            (0, 1): placed("h_b01", [PART, PART, 4], BF16, AT_H_B + 4096),
         }
         for a in range(2):
             project(a, 0)
             mix(a, 0, nc.gpsimd, h_b[a, 0])
         project(0, 1)
         mix(0, 1, nc.gpsimd, h_b[0, 1], slice(0, PART))
-        for c in (1, 2):
+        for c in (1, LAST):
             project(1, c)
-        out_banks = {(2, 0): next_bank([PART, 2, PART])}
+        out_banks = {(LAST, 0): next_bank([PART, 2, PART])}
         for d in range(KEEP_WARM_PASSES):
             nc.tensor.matmul_mx(
                 out=next_bank([PART, BANK])[:],
@@ -361,7 +363,7 @@ def tile_list_halo_spin_orientation_kernel(
                 stop=True,
             )
 
-        wspin_b1 = [placed("wspin_b1%d" % b, [PART, 256, 4], BF16, at_ang1 + 2048 * b) for b in range(2)]
+        wspin_b1 = [placed("wspin_b1%d" % b, [PART, HALF, 4], BF16, AT_ANG1 + 2048 * b) for b in range(2)]
         for b in range(2):
             nc.scalar.copy(
                 wspin_b1[b][:].rearrange("p (u e) t -> p u t e", e=4),
@@ -369,13 +371,13 @@ def tile_list_halo_spin_orientation_kernel(
             )
 
         wspin_w = [kept("wspin_w%d" % a, [PART, N], U32) for a in range(2)]
-        wspin_s = [placed("wspin_s0", [PART, N], U8, at_cos_last), kept("wspin_s1", [PART, N], U8)]
+        wspin_s = [placed("wspin_s0", [PART, N], U8, AT_COS_LAST), kept("wspin_s1", [PART, N], U8)]
         h_w, h_s = {}, {}
         for c, (m0, w) in enumerate(PIECES[1]):
             for a in range(2):
                 h_w[a, c] = kept("h_w%d%d" % (a, c), [PART, w], U32)
                 if (a, c) in h_b:
-                    h_s[a, c] = placed("h_s%d%d" % (a, c), [PART, w], U8, at_cos_last + 512 * (c + 1) + 256 * a)
+                    h_s[a, c] = placed("h_s%d%d" % (a, c), [PART, w], U8, AT_COS_LAST + N * (c + 1) + HALF * a)
                 else:
                     h_s[a, c] = kept("h_s%d%d" % (a, c), [PART, w], U8)
 
@@ -384,11 +386,8 @@ def tile_list_halo_spin_orientation_kernel(
 
         def spin(a, c, b):
             m0, w = PIECES[1][c]
-            if a == 0 and c < last[1]:
-                out_banks[c, b] = banks.tile([PART, 2, w], F32, name="bank", tag="bank")
-            elif a == 0 and b == 1:
-                turns.append(0)
-                out_banks[c, b] = next_bank([PART, 2, w])
+            if (c, b) not in out_banks:
+                out_banks[c, b] = any_bank([PART, 2, w])
             for d in range(2):
                 rows = slice(PART * (2 * b + d), PART * (2 * b + d + 1))
                 nc.tensor.matmul_mx(
@@ -406,11 +405,11 @@ def tile_list_halo_spin_orientation_kernel(
         def store(c, b):
             m0, w = PIECES[1][c]
             res = kept("res%d%d" % (c, b), [PART, 2, w], F32)
-            if (c, b) == (last[1], 1):
+            if (c, b) == (LAST, 1):
                 nc.vector.tensor_copy(res[:], out_banks[c, b][:])
             else:
                 nc.scalar.copy(res[:], out_banks[c, b][:])
-            queue = nc.scalar if (c, b) == (last[1], 0) else nc.sync
+            queue = nc.scalar if (c, b) == (LAST, 0) else nc.sync
             queue.dma_start(out_v[:, 2 * b : 2 * (b + 1), m0 : m0 + w], res[:])
 
         quantize_h(0, 0)
@@ -421,7 +420,7 @@ def tile_list_halo_spin_orientation_kernel(
         quantize(wspin_w[1][:, halves[0]], wspin_s[1][:, halves[0]], wspin_b1[0][:])
         spin(1, 0, 0)
         store(0, 0)
-        h_b[1, 1] = placed("h_b11", [PART, PART, 4], BF16, at_h_b)
+        h_b[1, 1] = placed("h_b11", [PART, PART, 4], BF16, AT_H_B)
         mix(1, 1, nc.vector, h_b[1, 1])
         quantize_h(0, 1)
         quantize(wspin_w[1][:, halves[1]], wspin_s[1][:, halves[1]], wspin_b1[1][:])
@@ -433,13 +432,13 @@ def tile_list_halo_spin_orientation_kernel(
                 spin(a, 1, b)
         for b in range(2):
             store(1, b)
-        h_b[0, 2] = placed("h_b02", [PART, PART, 4], BF16, at_h_b + 2048)
-        h_b[1, 2] = placed("h_b12", [PART, PART, 4], BF16, at_h_b + 4096)
-        mix(0, 1, nc.vector, h_b[0, 2], slice(PART, 2 * PART))
-        mix(1, 2, nc.vector, h_b[1, 2])
+        h_b[0, LAST] = placed("h_b02", [PART, PART, 4], BF16, AT_H_B + 2048)
+        h_b[1, LAST] = placed("h_b12", [PART, PART, 4], BF16, AT_H_B + 4096)
+        mix(0, 1, nc.vector, h_b[0, LAST], slice(PART, 2 * PART))
+        mix(1, LAST, nc.vector, h_b[1, LAST])
         for a in range(2):
-            quantize_h(a, 2)
+            quantize_h(a, LAST)
             for b in range(2):
-                spin(a, 2, b)
+                spin(a, LAST, b)
         for b in range(2):
-            store(2, b)
+            store(LAST, b)

@@ -33,12 +33,14 @@ PROJ_BANKS = 3
 PIECES = ([(0, 256), (256, 256)], [(0, 256), (256, 128), (384, 128)])
 LAST = len(PIECES[1]) - 1
 
-AT_TH7 = 0
-AT_WSPIN_B0 = 2048
-AT_WSUB1_B00 = 4096
-AT_H_B = 7168
-AT_ANG1 = 12288
-AT_COS_LAST = 20480
+AT_WANG1 = 0
+AT_WSPIN0 = 4096
+AT_WSPIN_B = 13312
+AT_SIN0 = 17408
+AT_COS0 = 21504
+AT_ANG1 = 25600
+AT_COS_LAST = 33792
+AT_H_B = 35840
 
 
 def tile_list_halo_spin_orientation_kernel(
@@ -83,6 +85,9 @@ def tile_list_halo_spin_orientation_kernel(
         def quantize(codes, scales, values):
             nc.vector.quantize_mx(out=codes.bitcast(FP8X4), scales=scales, in_=values.rearrange("p c j -> p (c j)"))
 
+        def round_on_gpsimd(dst, src):
+            nc.gpsimd.tensor_scalar(dst, src, 1.0, 0.0, ALU.mult, ALU.add)
+
         halves = [slice(HALF * half, HALF * (half + 1)) for half in range(2)]
 
         offs_t = lists.tile([PART, S // 16], U16, name="offs_t")
@@ -92,7 +97,7 @@ def tile_list_halo_spin_orientation_kernel(
         tab_s = kept("tab_s", [PART, T], U8)
         tab2_s = kept("tab2_s", [PART, T2], U8)
         wang_s_raw = kept("wang_s_raw", [PART, H // 2], I32)
-        wsub2_s_raw = placed("wsub2_s_raw", [PART, H // 4], I32, AT_WSUB1_B00)
+        wsub2_s_raw = kept("wsub2_s_raw", [PART, H // 4], I32)
         bias_rows = kept("bias_rows", [PART, PART], F32)
         ident = kept("ident", [PART, PART], F32)
         nc.vector.memset(wang_s_raw[:], 0)
@@ -111,12 +116,10 @@ def tile_list_halo_spin_orientation_kernel(
         nc.scalar.activation(warm[0:96, 0:1], bias_rows[0:96, 0:1], ACT.Sin)
 
         tab_w = [kept("tab_w%d" % g, [PART, T], I32, tag="stage%d" % g) for g in range(2)]
-        tab2_w = kept("tab2_w", [PART, T2], I32, tag="stage2")
-        wang_raw = [kept("wang_raw%d" % a, [PART, 2, HALF], I32) for a in range(2)]
+        tab2_w = kept("tab2_w", [PART, T2], I32)
+        wang_raw = [kept("wang_raw0", [PART, 2, HALF], I32), placed("wang_raw1", [PART, 2, HALF], I32, AT_WANG1)]
         wang_v = wang_words.rearrange("g p c -> p g c").bitcast(I32)
-        wsub2_raw = [kept("wsub2_raw%d" % a, [PART, BANK], I32) for a in range(2)]
         wsub1_v = wsub1.rearrange("(p j) c -> p j c", j=4)
-        wsub1_raw1 = kept("wsub1_raw1", [PART, 4, BANK], F32)
         v_sg = kept("v_sg", [PART, S], U8)
         v_s = kept("v_s", [PART, 2, S], U8)
 
@@ -137,18 +140,14 @@ def tile_list_halo_spin_orientation_kernel(
                 v_s[32 * quad : 32 * quad + 4].bitcast(I32),
                 v_sg[TAB_ROW + 8 * quad : TAB_ROW + 8 * quad + 8, :].bitcast(I32),
             )
-        nc.sync.dma_start(wsub2_raw[0][:], words(wsub2_words[0])[:, 0:BANK])
         nc.sync.dma_start(tab2_w[:], words(tab2_words[0]))
         nc.sync.dma_start(wang_raw[1][:], wang_v[:, :, halves[1]])
         nc.sync.dma_start(pos_t[:], pos1)
-        nc.sync.dma_start(wsub2_raw[1][:], words(wsub2_words[0])[:, BANK : 2 * BANK])
-        nc.sync.dma_start(wsub1_raw1[:], wsub1_v[:, :, BANK : 2 * BANK])
-        for quad in QUADS:
-            nc.sync.dma_start(
-                wsub2_s_raw[32 * quad : 32 * quad + 4, :], wsub2_scales[0][4 * quad : 4 * quad + 4, :].bitcast(I32)
-            )
 
-        v_w = [[kept("v_w%d%d" % (g, half), [PART, BANK], U32) for half in range(2)] for g in range(2)]
+        v_w = [
+            [kept("v_w%d0" % g, [PART, BANK], U32), placed("v_w%d1" % g, [PART, BANK], U32, (AT_SIN0, AT_COS0)[g])]
+            for g in range(2)
+        ]
         v2_sg = kept("v2_sg", [PART, P], U8)
 
         def gather_v(g, first, count):
@@ -170,15 +169,12 @@ def tile_list_halo_spin_orientation_kernel(
 
         wang_w = [kept("wang_w%d" % a, [PART, 2, HALF], I32) for a in range(2)]
         wang_s = kept("wang_s", [PART, 2, H // 4], I32)
-        wsub2_w = [kept("wsub2_w%d" % a, [PART, BANK], I32) for a in range(2)]
-        wsub2_s = kept("wsub2_s", [PART, H // 4], I32)
 
         def order_wang(a, copy):
             order_columns(wang_w[a][:].rearrange("p g c -> p (g c)"), wang_raw[a][:].rearrange("p g c -> p (g c)"), 4, copy)
 
         order_columns(wang_s[:].rearrange("p g c -> p (g c)"), wang_s_raw[:], 2, scalar_move)
         order_wang(0, scalar_move)
-        order_columns(wsub2_w[0][:], wsub2_raw[0][:], 8, scalar_move)
         order_wang(1, nc.vector.tensor_copy)
 
         unread = any_bank([PART, BANK])
@@ -198,11 +194,21 @@ def tile_list_halo_spin_orientation_kernel(
         nc.scalar.copy(bias[:], bias_ps[:, BIAS_ROW:PART])
 
         wspin_v = wspin.rearrange("(a q t i) n -> a t q i n", a=2, t=4, i=8)
-        wsub1_raw = [kept("wsub1_raw0", [PART, 4, BANK], F32, tag="stage0"), wsub1_raw1]
-        nc.sync.dma_start(wsub1_raw[0][:], wsub1_v[:, :, 0:BANK])
-        wspin_raw = [kept("wspin_raw%d" % a, [PART, 4, N], F32, tag="stage%d" % (a + 1)) for a in range(2)]
+        wsub1_raw = [kept("wsub1_raw0", [PART, 4, BANK], F32, tag="stage0"), kept("wsub1_raw1", [PART, 4, BANK], F32)]
+        for a in range(2):
+            nc.sync.dma_start(wsub1_raw[a][:], wsub1_v[:, :, BANK * a : BANK * (a + 1)])
+        wsub2_raw = kept("wsub2_raw", [PART, H], I32)
+        nc.sync.dma_start(wsub2_raw[:], words(wsub2_words[0]))
+        wspin_raw = [
+            placed("wspin_raw0", [PART, 4, N], F32, AT_WSPIN0),
+            kept("wspin_raw1", [PART, 4, N], F32, tag="stage1"),
+        ]
         for t in range(4):
             nc.sync.dma_start(wspin_raw[0][:, t, :], wspin_v[0, t])
+        for quad in QUADS:
+            nc.sync.dma_start(
+                wsub2_s_raw[32 * quad : 32 * quad + 4, :], wsub2_scales[0][4 * quad : 4 * quad + 4, :].bitcast(I32)
+            )
         for quad in QUADS:
             nc.sync.dma_start(
                 v2_s[32 * quad : 32 * quad + 4, :].bitcast(I32),
@@ -211,8 +217,7 @@ def tile_list_halo_spin_orientation_kernel(
         for t in range(4):
             nc.sync.dma_start(wspin_raw[1][:, t, :], wspin_v[1, t])
 
-        th = [kept("th%d" % j, [PART, S], F32) for j in range(ROW_TILES - 1)]
-        th.append(placed("th7", [PART, S], F32, AT_TH7))
+        th = [kept("th%d" % j, [PART, S], F32) for j in range(ROW_TILES)]
         ang = [kept("ang0", [PART, 4, P], F32), placed("ang1", [PART, 4, P], F32, AT_ANG1)]
 
         def angles(tiles, first, count):
@@ -234,82 +239,63 @@ def tile_list_halo_spin_orientation_kernel(
                     th[j][:, first : first + count], bank[:, d, :], ACT.Identity, bias=bias[:, j : j + 1]
                 )
 
-        def pick(j):
-            nc.vector.tensor_copy(ang[j // 4][:, j % 4, :], th[j][:].indirect(pos_t[:]))
-
-        def round_tile_on_scalar(dst, a, t):
-            nc.scalar.copy(
-                dst.rearrange("p (q h e) j -> p q h j e", h=2, e=4),
-                wsub1_raw[a][:].rearrange("p j (q t h e) -> p t q h j e", t=4, h=2, e=4)[:, t],
-            )
-
-        def round_pair_on_vector(dst, a, t0):
-            nc.vector.tensor_copy(
-                dst.rearrange("p (t q i) j -> p t q j i", t=2, i=8),
-                wsub1_raw[a][:].rearrange("p j (q t i) -> p t q j i", t=4, i=8)[:, t0 : t0 + 2],
-            )
-
-        wsub1_b1 = [kept("wsub1_b1%d" % half, [PART, HALF, 4], BF16) for half in range(2)]
-        wsub1_s = [kept("wsub1_s%d" % a, [PART, BANK], U8) for a in range(2)]
-
         for first in (0, HALF):
             angles([0, 1], first, HALF)
         angles([2], 0, BANK)
         for j in range(3):
             angles([j], BANK, BANK)
-        for j in range(3, 6):
-            for first in (0, BANK):
-                angles([j], first, BANK)
-        for t in (2, 3):
-            round_tile_on_scalar(wsub1_b1[1][:, PART * (t - 2) : PART * (t - 1), :], 1, t)
-        for j in range(6, ROW_TILES):
+        for j in range(3, ROW_TILES):
             for first in (0, BANK):
                 angles([j], first, BANK)
 
-        wsub1_w1 = kept("wsub1_w1", [PART, BANK], U32)
-        pick(0)
-        pick(1)
-        round_pair_on_vector(wsub1_b1[0][:], 1, 0)
-        pick(2)
-        quantize(wsub1_w1[:, halves[0]], wsub1_s[1][:, halves[0]], wsub1_b1[0][:])
-        order_columns(wsub2_w[1][:], wsub2_raw[1][:], 8, nc.vector.tensor_copy)
+        for j in range(ROW_TILES):
+            nc.vector.tensor_copy(ang[j // 4][:, j % 4, :], th[j][:].indirect(pos_t[:]))
+        wsub1_b = [placed("wsub1_b0", [PART, BANK, 4], BF16, AT_WANG1), kept("wsub1_b1", [PART, BANK, 4], BF16)]
+        for a in range(2):
+            round_on_gpsimd(
+                wsub1_b[a][:].rearrange("p (t q i) j -> p q t (i j)", t=4, i=8),
+                wsub1_raw[a][:].rearrange("p j c -> p c j"),
+            )
+        wspin_b0 = placed("wspin_b0", [PART, N, 4], BF16, AT_WSPIN_B)
+        round_on_gpsimd(wspin_b0[:], wspin_raw[0][:].rearrange("p t n -> p n t"))
+
+        wsub2_s = placed("wsub2_s", [PART, H // 4], I32, AT_WSPIN0)
+        wsub2_w = [placed("wsub2_w%d" % a, [PART, BANK], I32, AT_WSPIN0 + 1024 + 2048 * a) for a in range(2)]
+        wsub1_w = [placed("wsub1_w%d" % a, [PART, BANK], U32, AT_WSPIN0 + 5120 + 2048 * a) for a in range(2)]
+        wsub1_s = [kept("wsub1_s%d" % a, [PART, BANK], U8) for a in range(2)]
+        wspin_w = [kept("wspin_w%d" % a, [PART, N], U32) for a in range(2)]
+        wspin_s0 = kept("wspin_s0", [PART, N], U8)
         order_columns(wsub2_s[:], wsub2_s_raw[:], 2, nc.vector.tensor_copy)
-        pick(3)
-        wsub1_b0 = [
-            placed("wsub1_b00", [PART, HALF, 4], BF16, AT_WSUB1_B00),
-            kept("wsub1_b01", [PART, HALF, 4], BF16),
-        ]
-        for half in range(2):
-            round_pair_on_vector(wsub1_b0[half][:], 0, 2 * half)
-        pick(4)
-        quantize(wsub1_w1[:, halves[1]], wsub1_s[1][:, halves[1]], wsub1_b1[1][:])
-        wsub1_w = [kept("wsub1_w0", [PART, BANK], U32, tag="wsub1_b11"), wsub1_w1]
-        pick(5)
-        for half in range(2):
-            quantize(wsub1_w[0][:, halves[half]], wsub1_s[0][:, halves[half]], wsub1_b0[half][:])
-        pick(6)
-        pick(7)
+        for a in range(2):
+            order_columns(wsub2_w[a][:], wsub2_raw[:, BANK * a : BANK * (a + 1)], 8, nc.vector.tensor_copy)
+            quantize(wsub1_w[a][:], wsub1_s[a][:], wsub1_b[a][:])
+        quantize(wspin_w[0][:], wspin_s0[:], wspin_b0[:])
 
-        wspin_b0 = placed("wspin_b0", [PART, N, 4], BF16, AT_WSPIN_B0)
-        nc.gpsimd.tensor_scalar(wspin_b0[:], wspin_raw[0][:].rearrange("p t n -> p n t"), 1.0, 0.0, ALU.mult, ALU.add)
+        wspin_b1 = [placed("wspin_b10", [PART, HALF, 4], BF16, AT_WSPIN_B)]
+        round_on_gpsimd(wspin_b1[0][:], wspin_raw[1][:, :, halves[0]].rearrange("p t n -> p n t"))
 
         cos, sin, cos_b1, sin_b2 = {}, {}, {}, {}
+        held = {("cos", 0, 0): AT_COS0, ("sin", 0, 0): AT_SIN0, ("cos", 1, LAST): AT_COS_LAST}
 
         def trig(a, c):
             m0, w = PIECES[a][c]
-            if (a, c) == (1, LAST):
-                cos[a, c] = placed("cos_last", [PART, 2, w, 2], F32, AT_COS_LAST)
-            else:
-                cos[a, c] = kept("cos%d%d" % (a, c), [PART, 2, w, 2], F32)
-            sin[a, c] = kept("sin%d%d" % (a, c), [PART, 2, w, 2], F32)
+            for name, dst in (("cos", cos), ("sin", sin)):
+                if (name, a, c) in held:
+                    dst[a, c] = placed("%s%d%d" % (name, a, c), [PART, 2, w, 2], F32, held[name, a, c])
+                else:
+                    dst[a, c] = kept("%s%d%d" % (name, a, c), [PART, 2, w, 2], F32)
             picked = ang[a][:, :, m0 : m0 + w].rearrange("p (y z) m -> p y m z", z=2)
             nc.scalar.activation(cos[a, c][:], picked, ACT.Abs)
             nc.scalar.activation(sin[a, c][:], picked, ACT.Sin)
             nc.scalar.activation(cos[a, c][:], cos[a, c][:], ACT.Sin, bias=math.pi / 2, scale=-1.0)
 
+        made = []
+
         def products(a, c, name, codes, scales, factor, dst):
             m0, w = PIECES[a][c]
-            dst[a, c] = kept("%s%d%d" % (name, a, c), [PART, w, 4], F32)
+            tag = "th%d" % len(made) if len(made) < ROW_TILES else None
+            made.append(name)
+            dst[a, c] = kept("%s%d%d" % (name, a, c), [PART, w, 4], F32, tag=tag)
             for u0 in range(0, w, PART):
                 bank = next_bank([PART, 4, PART])
                 subhalos = slice(m0 + u0, m0 + u0 + PART)
@@ -331,24 +317,19 @@ def tile_list_halo_spin_orientation_kernel(
                     ALU.mult,
                 )
 
-        def mix(a, c, engine, dst, cols=slice(None)):
-            engine.tensor_tensor(dst[:], cos_b1[a, c][:, cols, :], sin_b2[a, c][:, cols, :], ALU.add)
+        def mix(a, c, engine, dst):
+            engine.tensor_tensor(dst[:], cos_b1[a, c][:], sin_b2[a, c][:], ALU.add)
 
         def project(a, c):
             trig(a, c)
             products(a, c, "sin_b2_", wsub2_w[a][:], wsub2_s[:].bitcast(U8)[:, BANK * a : BANK * (a + 1)], sin, sin_b2)
             products(a, c, "cos_b1_", wsub1_w[a][:], wsub1_s[a][:], cos, cos_b1)
 
-        h_b = {
-            (0, 0): placed("h_b00", [PART, HALF, 4], BF16, AT_H_B),
-            (1, 0): placed("h_b10", [PART, HALF, 4], BF16, AT_H_B + 2048),
-            (0, 1): placed("h_b01", [PART, PART, 4], BF16, AT_H_B + 4096),
-        }
-        for a in range(2):
-            project(a, 0)
-            mix(a, 0, nc.gpsimd, h_b[a, 0])
-        project(0, 1)
-        mix(0, 1, nc.gpsimd, h_b[0, 1], slice(0, PART))
+        h_b = {}
+        for d, (a, c) in enumerate([(0, 0), (1, 0), (0, 1)]):
+            project(a, c)
+            h_b[a, c] = placed("h_b%d%d" % (a, c), [PART, HALF, 4], BF16, AT_H_B + 2048 * d)
+            mix(a, c, nc.gpsimd, h_b[a, c])
         for c in (1, LAST):
             project(1, c)
         out_banks = {(LAST, 0): next_bank([PART, 2, PART])}
@@ -363,21 +344,19 @@ def tile_list_halo_spin_orientation_kernel(
                 stop=True,
             )
 
-        wspin_b1 = [placed("wspin_b1%d" % b, [PART, HALF, 4], BF16, AT_ANG1 + 2048 * b) for b in range(2)]
-        for b in range(2):
-            nc.scalar.copy(
-                wspin_b1[b][:].rearrange("p (u e) t -> p u t e", e=4),
-                wspin_raw[1][:, :, halves[b]].rearrange("p t (u e) -> p u t e", e=4),
-            )
+        wspin_b1.append(placed("wspin_b11", [PART, HALF, 4], BF16, AT_ANG1))
+        nc.scalar.copy(
+            wspin_b1[1][:].rearrange("p (u e) t -> p u t e", e=4),
+            wspin_raw[1][:, :, halves[1]].rearrange("p t (u e) -> p u t e", e=4),
+        )
 
-        wspin_w = [kept("wspin_w%d" % a, [PART, N], U32) for a in range(2)]
-        wspin_s = [placed("wspin_s0", [PART, N], U8, AT_COS_LAST), kept("wspin_s1", [PART, N], U8)]
+        wspin_s = [wspin_s0, placed("wspin_s1", [PART, N], U8, AT_COS_LAST + 1024)]
         h_w, h_s = {}, {}
-        for c, (m0, w) in enumerate(PIECES[1]):
-            for a in range(2):
+        for a in range(2):
+            for c, (m0, w) in enumerate(PIECES[a]):
                 h_w[a, c] = kept("h_w%d%d" % (a, c), [PART, w], U32)
                 if (a, c) in h_b:
-                    h_s[a, c] = placed("h_s%d%d" % (a, c), [PART, w], U8, AT_COS_LAST + N * (c + 1) + HALF * a)
+                    h_s[a, c] = placed("h_s%d%d" % (a, c), [PART, w], U8, AT_COS_LAST + HALF * (a + 2 * c))
                 else:
                     h_s[a, c] = kept("h_s%d%d" % (a, c), [PART, w], U8)
 
@@ -386,6 +365,8 @@ def tile_list_halo_spin_orientation_kernel(
 
         def spin(a, c, b):
             m0, w = PIECES[1][c]
+            source = min(c, len(PIECES[a]) - 1)
+            cols = slice(m0 - PIECES[a][source][0], m0 - PIECES[a][source][0] + w)
             if (c, b) not in out_banks:
                 out_banks[c, b] = any_bank([PART, 2, w])
             for d in range(2):
@@ -394,8 +375,8 @@ def tile_list_halo_spin_orientation_kernel(
                     out=out_banks[c, b][:, d, :],
                     lhsT=wspin_w[a][:, rows].bitcast(FP8X4),
                     lhsT_scale=wspin_s[a][:, rows],
-                    rhs=h_w[a, c][:].bitcast(FP8X4),
-                    rhs_scale=h_s[a, c][:],
+                    rhs=h_w[a, source][:, cols].bitcast(FP8X4),
+                    rhs_scale=h_s[a, source][:, cols],
                     start=(a, d) == (0, 0),
                     stop=(a, d) == (1, 1),
                 )
@@ -413,32 +394,26 @@ def tile_list_halo_spin_orientation_kernel(
             queue.dma_start(out_v[:, 2 * b : 2 * (b + 1), m0 : m0 + w], res[:])
 
         quantize_h(0, 0)
-        quantize(wspin_w[0][:], wspin_s[0][:], wspin_b0[:])
         for b in range(2):
             spin(0, 0, b)
-        quantize_h(1, 0)
         quantize(wspin_w[1][:, halves[0]], wspin_s[1][:, halves[0]], wspin_b1[0][:])
+        quantize_h(1, 0)
         spin(1, 0, 0)
         store(0, 0)
         h_b[1, 1] = placed("h_b11", [PART, PART, 4], BF16, AT_H_B)
         mix(1, 1, nc.vector, h_b[1, 1])
-        quantize_h(0, 1)
         quantize(wspin_w[1][:, halves[1]], wspin_s[1][:, halves[1]], wspin_b1[1][:])
         spin(1, 0, 1)
         store(0, 1)
-        quantize_h(1, 1)
-        for a in range(2):
+        quantize_h(0, 1)
+        for c in (1, LAST):
             for b in range(2):
-                spin(a, 1, b)
-        for b in range(2):
-            store(1, b)
-        h_b[0, LAST] = placed("h_b02", [PART, PART, 4], BF16, AT_H_B + 2048)
-        h_b[1, LAST] = placed("h_b12", [PART, PART, 4], BF16, AT_H_B + 4096)
-        mix(0, 1, nc.vector, h_b[0, LAST], slice(PART, 2 * PART))
+                spin(0, c, b)
+        h_b[1, LAST] = placed("h_b12", [PART, PART, 4], BF16, AT_H_B + 2048)
         mix(1, LAST, nc.vector, h_b[1, LAST])
-        for a in range(2):
-            quantize_h(a, LAST)
+        for c in (1, LAST):
+            quantize_h(1, c)
             for b in range(2):
-                spin(a, LAST, b)
-        for b in range(2):
-            store(LAST, b)
+                spin(1, c, b)
+            for b in range(2):
+                store(c, b)

@@ -36,8 +36,12 @@ LAST = len(PIECES[1]) - 1
 AT_WANG1 = 0
 AT_WSPIN0 = 4096
 AT_WSPIN_B = 13312
-AT_SIN0 = 17408
-AT_COS0 = 21504
+AT_COS0 = 17408
+AT_SIN0 = 21504
+AT_V_LAST = AT_SIN0 - 1024
+AT_COS1 = 41984
+AT_SIN1 = 46080
+AT_WANG_LAST = AT_SIN1 - 1024
 AT_ANG1 = 25600
 AT_COS_LAST = 33792
 AT_H_B = 35840
@@ -144,10 +148,8 @@ def tile_list_halo_spin_orientation_kernel(
         nc.sync.dma_start(wang_raw[1][:], wang_v[:, :, halves[1]])
         nc.sync.dma_start(pos_t[:], pos1)
 
-        v_w = [
-            [kept("v_w%d0" % g, [PART, BANK], U32), placed("v_w%d1" % g, [PART, BANK], U32, (AT_SIN0, AT_COS0)[g])]
-            for g in range(2)
-        ]
+        v_w = [[kept("v_w%d%d" % (g, half), [PART, BANK], U32) for half in range(2 - g)] for g in range(2)]
+        v_w[1].append(placed("v_w11", [PART, BANK], U32, AT_V_LAST))
         v2_sg = kept("v2_sg", [PART, P], U8)
 
         def gather_v(g, first, count):
@@ -167,7 +169,7 @@ def tile_list_halo_spin_orientation_kernel(
         v2_w = kept("v2_w", [PART, P], U32)
         nc.vector.tensor_copy(v2_w[:], tab2_w[:].bitcast(U32).indirect(offs2_t[:]))
 
-        wang_w = [kept("wang_w%d" % a, [PART, 2, HALF], I32) for a in range(2)]
+        wang_w = [kept("wang_w0", [PART, 2, HALF], I32), placed("wang_w1", [PART, 2, HALF], I32, AT_WANG_LAST)]
         wang_s = kept("wang_s", [PART, 2, H // 4], I32)
 
         def order_wang(a, copy):
@@ -275,19 +277,44 @@ def tile_list_halo_spin_orientation_kernel(
         round_on_gpsimd(wspin_b1[0][:], wspin_raw[1][:, :, halves[0]].rearrange("p t n -> p n t"))
 
         cos, sin, cos_b1, sin_b2 = {}, {}, {}, {}
-        held = {("cos", 0, 0): AT_COS0, ("sin", 0, 0): AT_SIN0, ("cos", 1, LAST): AT_COS_LAST}
+        held = {
+            ("cos", 0, 0): AT_COS0, ("sin", 0, 0): AT_SIN0, ("cos", 0, 1): AT_COS1, ("sin", 0, 1): AT_SIN1,
+            ("cos", 1, LAST): AT_COS_LAST,
+        }
 
-        def trig(a, c):
+        def picked(name, dst, a, c):
             m0, w = PIECES[a][c]
-            for name, dst in (("cos", cos), ("sin", sin)):
-                if (name, a, c) in held:
-                    dst[a, c] = placed("%s%d%d" % (name, a, c), [PART, 2, w, 2], F32, held[name, a, c])
-                else:
-                    dst[a, c] = kept("%s%d%d" % (name, a, c), [PART, 2, w, 2], F32)
-            picked = ang[a][:, :, m0 : m0 + w].rearrange("p (y z) m -> p y m z", z=2)
-            nc.scalar.activation(cos[a, c][:], picked, ACT.Abs)
-            nc.scalar.activation(sin[a, c][:], picked, ACT.Sin)
+            if (name, a, c) in held:
+                dst[a, c] = placed("%s%d%d" % (name, a, c), [PART, 2, w, 2], F32, held[name, a, c])
+            else:
+                dst[a, c] = kept("%s%d%d" % (name, a, c), [PART, 2, w, 2], F32)
+            return ang[a][:, :, m0 : m0 + w].rearrange("p (y z) m -> p y m z", z=2)
+
+        def magnitude(a, c):
+            angles_in = picked("cos", cos, a, c)
+            nc.scalar.activation(cos[a, c][:], angles_in, ACT.Abs)
+
+        def sine(a, c):
+            angles_in = picked("sin", sin, a, c)
+            nc.scalar.activation(sin[a, c][:], angles_in, ACT.Sin)
+
+        def cosine(a, c):
             nc.scalar.activation(cos[a, c][:], cos[a, c][:], ACT.Sin, bias=math.pi / 2, scale=-1.0)
+
+        magnitude(0, 0)
+        sine(0, 0)
+        magnitude(0, 1)
+        cosine(0, 0)
+        magnitude(1, 0)
+        sine(1, 0)
+        magnitude(1, 1)
+        cosine(1, 0)
+        sine(0, 1)
+        cosine(0, 1)
+        magnitude(1, LAST)
+        for c in (1, LAST):
+            sine(1, c)
+            cosine(1, c)
 
         made = []
 
@@ -321,7 +348,6 @@ def tile_list_halo_spin_orientation_kernel(
             engine.tensor_tensor(dst[:], cos_b1[a, c][:], sin_b2[a, c][:], ALU.add)
 
         def project(a, c):
-            trig(a, c)
             products(a, c, "sin_b2_", wsub2_w[a][:], wsub2_s[:].bitcast(U8)[:, BANK * a : BANK * (a + 1)], sin, sin_b2)
             products(a, c, "cos_b1_", wsub1_w[a][:], wsub1_s[a][:], cos, cos_b1)
 

@@ -34,8 +34,8 @@ PIECES = ([(0, 256), (256, 256)], [(0, 256), (256, 128), (384, 128)])
 LAST = len(PIECES[1]) - 1
 
 AT_WANG1 = 0
-AT_WSPIN0 = 4096
-AT_WSPIN_B = 13312
+AT_TH6 = 6144
+AT_WSUB1_B1 = 13312
 AT_COS0 = 17408
 AT_SIN0 = 21504
 AT_V_LAST = AT_SIN0 - 1024
@@ -147,6 +147,10 @@ def tile_list_halo_spin_orientation_kernel(
         nc.sync.dma_start(tab2_w[:], words(tab2_words[0]))
         nc.sync.dma_start(wang_raw[1][:], wang_v[:, :, halves[1]])
         nc.sync.dma_start(pos_t[:], pos1)
+        for quad in QUADS:
+            nc.sync.dma_start(
+                wsub2_s_raw[32 * quad : 32 * quad + 4, :], wsub2_scales[0][4 * quad : 4 * quad + 4, :].bitcast(I32)
+            )
 
         v_w = [[kept("v_w%d%d" % (g, half), [PART, BANK], U32) for half in range(2 - g)] for g in range(2)]
         v_w[1].append(placed("v_w11", [PART, BANK], U32, AT_V_LAST))
@@ -197,29 +201,25 @@ def tile_list_halo_spin_orientation_kernel(
 
         wspin_v = wspin.rearrange("(a q t i) n -> a t q i n", a=2, t=4, i=8)
         wsub1_raw = [kept("wsub1_raw0", [PART, 4, BANK], F32, tag="stage0"), kept("wsub1_raw1", [PART, 4, BANK], F32)]
-        for a in range(2):
-            nc.sync.dma_start(wsub1_raw[a][:], wsub1_v[:, :, BANK * a : BANK * (a + 1)])
         wsub2_raw = kept("wsub2_raw", [PART, H], I32)
+        nc.sync.dma_start(wsub1_raw[0][:], wsub1_v[:, :, 0:BANK])
         nc.sync.dma_start(wsub2_raw[:], words(wsub2_words[0]))
+        nc.sync.dma_start(wsub1_raw[1][:], wsub1_v[:, :, BANK : 2 * BANK])
         wspin_raw = [
-            placed("wspin_raw0", [PART, 4, N], F32, AT_WSPIN0),
+            kept("wspin_raw0", [PART, 4, N], F32),
             kept("wspin_raw1", [PART, 4, N], F32, tag="stage1"),
         ]
-        for t in range(4):
-            nc.sync.dma_start(wspin_raw[0][:, t, :], wspin_v[0, t])
-        for quad in QUADS:
-            nc.sync.dma_start(
-                wsub2_s_raw[32 * quad : 32 * quad + 4, :], wsub2_scales[0][4 * quad : 4 * quad + 4, :].bitcast(I32)
-            )
         for quad in QUADS:
             nc.sync.dma_start(
                 v2_s[32 * quad : 32 * quad + 4, :].bitcast(I32),
                 v2_sg[TAB2_ROW + 4 * quad : TAB2_ROW + 4 * quad + 4, :].bitcast(I32),
             )
-        for t in range(4):
-            nc.sync.dma_start(wspin_raw[1][:, t, :], wspin_v[1, t])
+        for a in range(2):
+            for t in range(4):
+                nc.sync.dma_start(wspin_raw[a][:, t, :], wspin_v[a, t])
 
-        th = [kept("th%d" % j, [PART, S], F32) for j in range(ROW_TILES)]
+        th = [kept("th%d" % j, [PART, S], F32) for j in range(6)]
+        th.extend([placed("th6", [PART, S], F32, AT_TH6), kept("th7", [PART, S], F32)])
         ang = [kept("ang0", [PART, 4, P], F32), placed("ang1", [PART, 4, P], F32, AT_ANG1)]
 
         def angles(tiles, first, count):
@@ -252,29 +252,25 @@ def tile_list_halo_spin_orientation_kernel(
 
         for j in range(ROW_TILES):
             nc.vector.tensor_copy(ang[j // 4][:, j % 4, :], th[j][:].indirect(pos_t[:]))
-        wsub1_b = [placed("wsub1_b0", [PART, BANK, 4], BF16, AT_WANG1), kept("wsub1_b1", [PART, BANK, 4], BF16)]
+        wsub1_b = [placed("wsub1_b0", [PART, BANK, 4], BF16, AT_WANG1), placed("wsub1_b1", [PART, BANK, 4], BF16, AT_WSUB1_B1)]
         for a in range(2):
             round_on_gpsimd(
                 wsub1_b[a][:].rearrange("p (t q i) j -> p q t (i j)", t=4, i=8),
                 wsub1_raw[a][:].rearrange("p j c -> p c j"),
             )
-        wspin_b0 = placed("wspin_b0", [PART, N, 4], BF16, AT_WSPIN_B)
-        round_on_gpsimd(wspin_b0[:], wspin_raw[0][:].rearrange("p t n -> p n t"))
 
-        wsub2_s = placed("wsub2_s", [PART, H // 4], I32, AT_WSPIN0)
-        wsub2_w = [placed("wsub2_w%d" % a, [PART, BANK], I32, AT_WSPIN0 + 1024 + 2048 * a) for a in range(2)]
-        wsub1_w = [placed("wsub1_w%d" % a, [PART, BANK], U32, AT_WSPIN0 + 5120 + 2048 * a) for a in range(2)]
-        wsub1_s = [kept("wsub1_s%d" % a, [PART, BANK], U8) for a in range(2)]
+        wsub2_s = placed("wsub2_s", [PART, H // 4], I32, AT_TH6 + 256)
+        wsub2_w = [placed("wsub2_w%d" % a, [PART, BANK], I32, AT_TH6 + (1280, -1792)[a]) for a in range(2)]
+        wsub1_w = [kept("wsub1_w%d" % a, [PART, BANK], U32) for a in range(2)]
+        wsub1_s = [placed("wsub1_s%d" % a, [PART, BANK], U8, AT_TH6 + 3328 + BANK * a) for a in range(2)]
         wspin_w = [kept("wspin_w%d" % a, [PART, N], U32) for a in range(2)]
-        wspin_s0 = kept("wspin_s0", [PART, N], U8)
         order_columns(wsub2_s[:], wsub2_s_raw[:], 2, nc.vector.tensor_copy)
         for a in range(2):
             order_columns(wsub2_w[a][:], wsub2_raw[:, BANK * a : BANK * (a + 1)], 8, nc.vector.tensor_copy)
             quantize(wsub1_w[a][:], wsub1_s[a][:], wsub1_b[a][:])
-        quantize(wspin_w[0][:], wspin_s0[:], wspin_b0[:])
 
-        wspin_b1 = [placed("wspin_b10", [PART, HALF, 4], BF16, AT_WSPIN_B)]
-        round_on_gpsimd(wspin_b1[0][:], wspin_raw[1][:, :, halves[0]].rearrange("p t n -> p n t"))
+        wspin_b0 = placed("wspin_b0", [PART, N, 4], BF16, AT_WSUB1_B1)
+        round_on_gpsimd(wspin_b0[:], wspin_raw[0][:].rearrange("p t n -> p n t"))
 
         cos, sin, cos_b1, sin_b2 = {}, {}, {}, {}
         held = {
@@ -320,7 +316,7 @@ def tile_list_halo_spin_orientation_kernel(
 
         def products(a, c, name, codes, scales, factor, dst):
             m0, w = PIECES[a][c]
-            tag = "th%d" % len(made) if len(made) < ROW_TILES else None
+            tag = "th%d" % len(made) if len(made) < 6 else None
             made.append(name)
             dst[a, c] = kept("%s%d%d" % (name, a, c), [PART, w, 4], F32, tag=tag)
             for u0 in range(0, w, PART):
@@ -344,8 +340,8 @@ def tile_list_halo_spin_orientation_kernel(
                     ALU.mult,
                 )
 
-        def mix(a, c, engine, dst):
-            engine.tensor_tensor(dst[:], cos_b1[a, c][:], sin_b2[a, c][:], ALU.add)
+        def mix(a, c, engine, dst, cols=slice(None)):
+            engine.tensor_tensor(dst[:], cos_b1[a, c][:, cols, :], sin_b2[a, c][:, cols, :], ALU.add)
 
         def project(a, c):
             products(a, c, "sin_b2_", wsub2_w[a][:], wsub2_s[:].bitcast(U8)[:, BANK * a : BANK * (a + 1)], sin, sin_b2)
@@ -354,8 +350,9 @@ def tile_list_halo_spin_orientation_kernel(
         h_b = {}
         for d, (a, c) in enumerate([(0, 0), (1, 0), (0, 1)]):
             project(a, c)
-            h_b[a, c] = placed("h_b%d%d" % (a, c), [PART, HALF, 4], BF16, AT_H_B + 2048 * d)
-            mix(a, c, nc.gpsimd, h_b[a, c])
+            w = PIECES[1][c][1]
+            h_b[a, c] = placed("h_b%d%d" % (a, c), [PART, w, 4], BF16, AT_H_B + 2048 * d)
+            mix(a, c, nc.gpsimd, h_b[a, c], slice(0, w))
         for c in (1, LAST):
             project(1, c)
         out_banks = {(LAST, 0): next_bank([PART, 2, PART])}
@@ -370,16 +367,17 @@ def tile_list_halo_spin_orientation_kernel(
                 stop=True,
             )
 
-        wspin_b1.append(placed("wspin_b11", [PART, HALF, 4], BF16, AT_ANG1))
-        nc.scalar.copy(
-            wspin_b1[1][:].rearrange("p (u e) t -> p u t e", e=4),
-            wspin_raw[1][:, :, halves[1]].rearrange("p t (u e) -> p u t e", e=4),
-        )
+        wspin_b1 = [placed("wspin_b1%d" % b, [PART, HALF, 4], BF16, AT_ANG1 + 2048 * b) for b in range(2)]
+        for b in range(2):
+            nc.scalar.copy(
+                wspin_b1[b][:].rearrange("p (u e) t -> p u t e", e=4),
+                wspin_raw[1][:, :, halves[b]].rearrange("p t (u e) -> p u t e", e=4),
+            )
 
-        wspin_s = [wspin_s0, placed("wspin_s1", [PART, N], U8, AT_COS_LAST + 1024)]
+        wspin_s = [placed("wspin_s0", [PART, N], U8, AT_COS_LAST + 1024), kept("wspin_s1", [PART, N], U8)]
         h_w, h_s = {}, {}
         for a in range(2):
-            for c, (m0, w) in enumerate(PIECES[a]):
+            for c, (m0, w) in enumerate(PIECES[1]):
                 h_w[a, c] = kept("h_w%d%d" % (a, c), [PART, w], U32)
                 if (a, c) in h_b:
                     h_s[a, c] = placed("h_s%d%d" % (a, c), [PART, w], U8, AT_COS_LAST + HALF * (a + 2 * c))
@@ -391,8 +389,6 @@ def tile_list_halo_spin_orientation_kernel(
 
         def spin(a, c, b):
             m0, w = PIECES[1][c]
-            source = min(c, len(PIECES[a]) - 1)
-            cols = slice(m0 - PIECES[a][source][0], m0 - PIECES[a][source][0] + w)
             if (c, b) not in out_banks:
                 out_banks[c, b] = any_bank([PART, 2, w])
             for d in range(2):
@@ -401,8 +397,8 @@ def tile_list_halo_spin_orientation_kernel(
                     out=out_banks[c, b][:, d, :],
                     lhsT=wspin_w[a][:, rows].bitcast(FP8X4),
                     lhsT_scale=wspin_s[a][:, rows],
-                    rhs=h_w[a, source][:, cols].bitcast(FP8X4),
-                    rhs_scale=h_s[a, source][:, cols],
+                    rhs=h_w[a, c][:].bitcast(FP8X4),
+                    rhs_scale=h_s[a, c][:],
                     start=(a, d) == (0, 0),
                     stop=(a, d) == (1, 1),
                 )
@@ -420,26 +416,32 @@ def tile_list_halo_spin_orientation_kernel(
             queue.dma_start(out_v[:, 2 * b : 2 * (b + 1), m0 : m0 + w], res[:])
 
         quantize_h(0, 0)
+        quantize(wspin_w[0][:], wspin_s[0][:], wspin_b0[:])
         for b in range(2):
             spin(0, 0, b)
-        quantize(wspin_w[1][:, halves[0]], wspin_s[1][:, halves[0]], wspin_b1[0][:])
         quantize_h(1, 0)
+        quantize(wspin_w[1][:, halves[0]], wspin_s[1][:, halves[0]], wspin_b1[0][:])
         spin(1, 0, 0)
         store(0, 0)
         h_b[1, 1] = placed("h_b11", [PART, PART, 4], BF16, AT_H_B)
         mix(1, 1, nc.vector, h_b[1, 1])
+        quantize_h(0, 1)
         quantize(wspin_w[1][:, halves[1]], wspin_s[1][:, halves[1]], wspin_b1[1][:])
         spin(1, 0, 1)
         store(0, 1)
-        quantize_h(0, 1)
-        for c in (1, LAST):
+        quantize_h(1, 1)
+        for a in range(2):
             for b in range(2):
-                spin(0, c, b)
-        h_b[1, LAST] = placed("h_b12", [PART, PART, 4], BF16, AT_H_B + 2048)
+                spin(a, 1, b)
+        for b in range(2):
+            store(1, b)
+        h_b[0, LAST] = placed("h_b02", [PART, PART, 4], BF16, AT_H_B + 2048)
+        h_b[1, LAST] = placed("h_b12", [PART, PART, 4], BF16, AT_H_B + 4096)
+        mix(0, 1, nc.vector, h_b[0, LAST], slice(PART, 2 * PART))
         mix(1, LAST, nc.vector, h_b[1, LAST])
-        for c in (1, LAST):
-            quantize_h(1, c)
+        for a in range(2):
+            quantize_h(a, LAST)
             for b in range(2):
-                spin(1, c, b)
-            for b in range(2):
-                store(c, b)
+                spin(a, LAST, b)
+        for b in range(2):
+            store(LAST, b)

import math
from contextlib import ExitStack

import concourse.mybir as mybir
from concourse.masks import make_identity

K, K2, T, T2, S, P, H, N = 1024, 512, 2048, 1024, 1024, 512, 1024, 512
FLOPS = 2 * K * H * S + 2 * 2 * K2 * H * P + 2 * H * N * P

F32 = mybir.dt.float32
BF16 = mybir.dt.bfloat16
I32 = mybir.dt.int32
U32 = mybir.dt.uint32
U16 = mybir.dt.uint16
U8 = mybir.dt.uint8
FP8X4 = mybir.dt.float8_e4m3fn_x4
FP4X4 = mybir.dt.float4_e2m1fn_x4
ACT = mybir.ActivationFunctionType
ALU = mybir.AluOpType

PART = 128
BANK = 512
HALF = BANK // 2
ROW_TILES = H // PART
QUADS = (0, 2, 1, 3)
BIAS_ROW = PART - ROW_TILES
TAB_ROW = PART - 32
TAB2_ROW = PART - 16
WARM_PASSES = 3
KEEP_WARM_PASSES = 2
TH_BANKS = 5
PROJ_BANKS = 3
PIECES = ([(0, 256), (256, 256)], [(0, 256), (256, 128), (384, 128)])
LAST = len(PIECES[1]) - 1

AT_WANG1 = 0
AT_TH6 = 6144
AT_WSUB1_B1 = 13312
AT_COS0 = 17408
AT_SIN0 = 21504
AT_V_LAST = AT_SIN0 - 1024
AT_COS1 = 41984
AT_SIN1 = 46080
AT_WANG_LAST = AT_SIN1 - 1024
AT_ANG1 = 25600
AT_COS_LAST = 33792
AT_H_B = 35840


def tile_list_halo_spin_orientation_kernel(
    tc, tab_words, tab_scales, offs, pos1, tab2_words, tab2_scales, offs2, wang_words, wang_scales,
    bang, wsub1, wsub2_words, wsub2_scales, wspin, out,
):
    nc = tc.nc

    with ExitStack() as ctx:
        lists = ctx.enter_context(tc.tile_pool(name="lists", bufs=1))
        keep = ctx.enter_context(tc.tile_pool(name="keep", bufs=1))
        shared = ctx.enter_context(tc.tile_pool(name="shared", bufs=1))
        banks = ctx.enter_context(tc.psum_pool(name="banks", bufs=TH_BANKS))
        proj = ctx.enter_context(tc.psum_pool(name="proj", bufs=1))
        turns = []

        def any_bank(shape):
            return banks.tile(shape, F32, name="bank", tag="bank")

        def next_bank(shape):
            turns.append(len(turns) % PROJ_BANKS)
            return proj.tile(shape, F32, name="projection%d" % turns[-1], tag="projection%d" % turns[-1])

        def kept(name, shape, dtype, tag=None):
            return keep.tile(shape, dtype, name=name, tag=tag or name, align_bytes=64)

        def placed(name, shape, dtype, offset):
            return shared.tile(shape, dtype, name=name, offset=offset, align_bytes=64)

        def words(packed):
            return packed.rearrange("p c i -> p (c i)").bitcast(I32)

        def order_columns(dst, src, run, copy):
            copy(
                dst.rearrange("p (a t q w) -> p a t q w", t=4, q=16, w=run),
                src.rearrange("p (a q t w) -> p a t q w", t=4, q=16, w=run),
            )

        def scalar_move(dst, src):
            nc.scalar.copy(dst.bitcast(U32), src.bitcast(U32))

        def quantize(codes, scales, values):
            nc.vector.quantize_mx(out=codes.bitcast(FP8X4), scales=scales, in_=values.rearrange("p c j -> p (c j)"))

        def round_on_gpsimd(dst, src):
            nc.gpsimd.tensor_scalar(dst, src, 1.0, 0.0, ALU.mult, ALU.add)

        halves = [slice(HALF * half, HALF * (half + 1)) for half in range(2)]

        offs_t = lists.tile([PART, S // 16], U16, name="offs_t")
        pos_t = lists.tile([PART, P // 16], U16, name="pos_t")
        offs2_t = lists.tile([PART, P // 16], U16, name="offs2_t")

        tab_s = kept("tab_s", [PART, T], U8)
        tab2_s = kept("tab2_s", [PART, T2], U8)
        wang_s_raw = kept("wang_s_raw", [PART, H // 2], I32)
        wsub2_s_raw = kept("wsub2_s_raw", [PART, H // 4], I32)
        bias_rows = kept("bias_rows", [PART, PART], F32)
        ident = kept("ident", [PART, PART], F32)
        nc.vector.memset(wang_s_raw[:], 0)
        make_identity(nc, ident[:])
        nc.vector.memset(tab_s[0:TAB_ROW, :].bitcast(I32), 0)
        nc.vector.memset(tab2_s[0:TAB2_ROW, :].bitcast(I32), 0)
        nc.gpsimd.dma_start(tab2_s[TAB2_ROW:PART, :].bitcast(I32), tab2_scales[0].bitcast(I32))
        nc.gpsimd.memset(wsub2_s_raw[:], 0)
        for a in range(2):
            nc.gpsimd.dma_start(
                bias_rows[BIAS_ROW + 4 * a : BIAS_ROW + 4 * a + 4, :].rearrange("t (q i) -> t q i", i=8),
                bang[BANK * a : BANK * (a + 1)].rearrange("(q t i) -> t q i", t=4, i=8),
            )
        nc.vector.memset(bias_rows[0:BIAS_ROW, :], 0.0)
        warm = kept("warm", [PART, 16], F32)
        nc.scalar.activation(warm[0:96, 0:1], bias_rows[0:96, 0:1], ACT.Sin)

        tab_w = [kept("tab_w%d" % g, [PART, T], I32, tag="stage%d" % g) for g in range(2)]
        tab2_w = kept("tab2_w", [PART, T2], I32)
        wang_raw = [kept("wang_raw0", [PART, 2, HALF], I32), placed("wang_raw1", [PART, 2, HALF], I32, AT_WANG1)]
        wang_v = wang_words.rearrange("g p c -> p g c").bitcast(I32)
        wsub1_v = wsub1.rearrange("(p j) c -> p j c", j=4)
        v_sg = kept("v_sg", [PART, S], U8)
        v_s = kept("v_s", [PART, 2, S], U8)

        nc.sync.dma_start(tab_s[TAB_ROW:PART, :].bitcast(I32), tab_scales.rearrange("g r c -> r g c").bitcast(I32))
        nc.sync.dma_start(offs_t[:], offs)
        nc.sync.dma_start(tab_w[0][:], words(tab_words[0]))
        for quad in QUADS:
            nc.sync.dma_start(
                wang_s_raw[32 * quad : 32 * quad + 4, :].rearrange("s (g c) -> s g c", g=2),
                wang_scales[:, 4 * quad : 4 * quad + 4, :].rearrange("g s c -> s g c").bitcast(I32),
            )
        nc.sync.dma_start(offs2_t[:], offs2)
        nc.sync.dma_start(wang_raw[0][:], wang_v[:, :, halves[0]])
        nc.sync.dma_start(tab_w[1][:], words(tab_words[1]))
        nc.vector.tensor_copy(v_sg[:], tab_s[:].indirect(offs_t[:]))
        for quad in QUADS:
            nc.sync.dma_start(
                v_s[32 * quad : 32 * quad + 4].bitcast(I32),
                v_sg[TAB_ROW + 8 * quad : TAB_ROW + 8 * quad + 8, :].bitcast(I32),
            )
        nc.sync.dma_start(tab2_w[:], words(tab2_words[0]))
        nc.sync.dma_start(wang_raw[1][:], wang_v[:, :, halves[1]])
        nc.sync.dma_start(pos_t[:], pos1)
        for quad in QUADS:
            nc.sync.dma_start(
                wsub2_s_raw[32 * quad : 32 * quad + 4, :], wsub2_scales[0][4 * quad : 4 * quad + 4, :].bitcast(I32)
            )

        v_w = [[kept("v_w%d%d" % (g, half), [PART, BANK], U32) for half in range(2 - g)] for g in range(2)]
        v_w[1].append(placed("v_w11", [PART, BANK], U32, AT_V_LAST))
        v2_sg = kept("v2_sg", [PART, P], U8)

        def gather_v(g, first, count):
            half, col = divmod(first, BANK)
            nc.vector.tensor_copy(
                v_w[g][half][:, col : col + count],
                tab_w[g][:].bitcast(U32).indirect(offs_t[:, first // 16 : (first + count) // 16]),
            )

        gather_v(0, 0, BANK)
        gather_v(0, BANK, BANK)
        nc.vector.tensor_copy(v2_sg[:], tab2_s[:].indirect(offs2_t[:]))
        gather_v(1, 0, HALF)
        gather_v(1, HALF, HALF)
        gather_v(1, BANK, BANK)
        v2_s = kept("v2_s", [PART, P], U8)
        v2_w = kept("v2_w", [PART, P], U32)
        nc.vector.tensor_copy(v2_w[:], tab2_w[:].bitcast(U32).indirect(offs2_t[:]))

        wang_w = [kept("wang_w0", [PART, 2, HALF], I32), placed("wang_w1", [PART, 2, HALF], I32, AT_WANG_LAST)]
        wang_s = kept("wang_s", [PART, 2, H // 4], I32)

        def order_wang(a, copy):
            order_columns(wang_w[a][:].rearrange("p g c -> p (g c)"), wang_raw[a][:].rearrange("p g c -> p (g c)"), 4, copy)

        order_columns(wang_s[:].rearrange("p g c -> p (g c)"), wang_s_raw[:], 2, scalar_move)
        order_wang(0, scalar_move)
        order_wang(1, nc.vector.tensor_copy)

        unread = any_bank([PART, BANK])
        for d in range(WARM_PASSES):
            nc.tensor.matmul_mx(
                out=unread[:],
                lhsT=wang_w[0][:, 0, 0:64].bitcast(FP4X4),
                lhsT_scale=wang_s[:, 0, 0:32].bitcast(U8),
                rhs=v_w[0][0][:].bitcast(FP8X4),
                rhs_scale=wang_s[:, 0, 0 : BANK // 4].bitcast(U8),
                start=True,
                stop=True,
            )
        bias_ps = any_bank([PART, BANK])
        nc.tensor.transpose(bias_ps[:, 0:PART], bias_rows[:], ident[:])
        bias = kept("bias", [PART, ROW_TILES], F32)
        nc.scalar.copy(bias[:], bias_ps[:, BIAS_ROW:PART])

        wspin_v = wspin.rearrange("(a q t i) n -> a t q i n", a=2, t=4, i=8)
        wsub1_raw = [kept("wsub1_raw0", [PART, 4, BANK], F32, tag="stage0"), kept("wsub1_raw1", [PART, 4, BANK], F32)]
        wsub2_raw = kept("wsub2_raw", [PART, H], I32)
        nc.sync.dma_start(wsub1_raw[0][:], wsub1_v[:, :, 0:BANK])
        nc.sync.dma_start(wsub2_raw[:], words(wsub2_words[0]))
        nc.sync.dma_start(wsub1_raw[1][:], wsub1_v[:, :, BANK : 2 * BANK])
        wspin_raw = [
            kept("wspin_raw0", [PART, 4, N], F32),
            kept("wspin_raw1", [PART, 4, N], F32, tag="stage1"),
        ]
        for quad in QUADS:
            nc.sync.dma_start(
                v2_s[32 * quad : 32 * quad + 4, :].bitcast(I32),
                v2_sg[TAB2_ROW + 4 * quad : TAB2_ROW + 4 * quad + 4, :].bitcast(I32),
            )
        for a in range(2):
            for t in range(4):
                nc.sync.dma_start(wspin_raw[a][:, t, :], wspin_v[a, t])

        th = [kept("th%d" % j, [PART, S], F32) for j in range(6)]
        th.extend([placed("th6", [PART, S], F32, AT_TH6), kept("th7", [PART, S], F32)])
        ang = [kept("ang0", [PART, 4, P], F32), placed("ang1", [PART, 4, P], F32, AT_ANG1)]

        def angles(tiles, first, count):
            half, col = divmod(first, BANK)
            bank = any_bank([PART, len(tiles), count])
            for g in range(2):
                for d, j in enumerate(tiles):
                    nc.tensor.matmul_mx(
                        out=bank[:, d, :],
                        lhsT=wang_w[j // 4][:, g, 64 * (j % 4) : 64 * (j % 4 + 1)].bitcast(FP4X4),
                        lhsT_scale=wang_s[:, g, 32 * j : 32 * (j + 1)].bitcast(U8),
                        rhs=v_w[g][half][:, col : col + count].bitcast(FP8X4),
                        rhs_scale=v_s[:, g, first : first + count],
                        start=(g, d) == (0, 0),
                        stop=(g, d) == (1, len(tiles) - 1),
                    )
            for d, j in enumerate(tiles):
                nc.scalar.activation(
                    th[j][:, first : first + count], bank[:, d, :], ACT.Identity, bias=bias[:, j : j + 1]
                )

        for first in (0, HALF):
            angles([0, 1], first, HALF)
        angles([2], 0, BANK)
        for j in range(3):
            angles([j], BANK, BANK)
        for j in range(3, ROW_TILES):
            for first in (0, BANK):
                angles([j], first, BANK)

        for j in range(ROW_TILES):
            nc.vector.tensor_copy(ang[j // 4][:, j % 4, :], th[j][:].indirect(pos_t[:]))
        wsub1_b = [placed("wsub1_b0", [PART, BANK, 4], BF16, AT_WANG1), placed("wsub1_b1", [PART, BANK, 4], BF16, AT_WSUB1_B1)]
        for a in range(2):
            round_on_gpsimd(
                wsub1_b[a][:].rearrange("p (t q i) j -> p q t (i j)", t=4, i=8),
                wsub1_raw[a][:].rearrange("p j c -> p c j"),
            )

        wsub2_s = placed("wsub2_s", [PART, H // 4], I32, AT_TH6 + 256)
        wsub2_w = [placed("wsub2_w%d" % a, [PART, BANK], I32, AT_TH6 + (1280, -1792)[a]) for a in range(2)]
        wsub1_w = [kept("wsub1_w%d" % a, [PART, BANK], U32) for a in range(2)]
        wsub1_s = [placed("wsub1_s%d" % a, [PART, BANK], U8, AT_TH6 + 3328 + BANK * a) for a in range(2)]
        wspin_w = [kept("wspin_w%d" % a, [PART, N], U32) for a in range(2)]
        order_columns(wsub2_s[:], wsub2_s_raw[:], 2, nc.vector.tensor_copy)
        for a in range(2):
            order_columns(wsub2_w[a][:], wsub2_raw[:, BANK * a : BANK * (a + 1)], 8, nc.vector.tensor_copy)
            quantize(wsub1_w[a][:], wsub1_s[a][:], wsub1_b[a][:])

        wspin_b0 = placed("wspin_b0", [PART, N, 4], BF16, AT_WSUB1_B1)
        round_on_gpsimd(wspin_b0[:], wspin_raw[0][:].rearrange("p t n -> p n t"))

        cos, sin, cos_b1, sin_b2 = {}, {}, {}, {}
        held = {
            ("cos", 0, 0): AT_COS0, ("sin", 0, 0): AT_SIN0, ("cos", 0, 1): AT_COS1, ("sin", 0, 1): AT_SIN1,
            ("cos", 1, LAST): AT_COS_LAST,
        }

        def picked(name, dst, a, c):
            m0, w = PIECES[a][c]
            if (name, a, c) in held:
                dst[a, c] = placed("%s%d%d" % (name, a, c), [PART, 2, w, 2], F32, held[name, a, c])
            else:
                dst[a, c] = kept("%s%d%d" % (name, a, c), [PART, 2, w, 2], F32)
            return ang[a][:, :, m0 : m0 + w].rearrange("p (y z) m -> p y m z", z=2)

        def magnitude(a, c):
            angles_in = picked("cos", cos, a, c)
            nc.scalar.activation(cos[a, c][:], angles_in, ACT.Abs)

        def sine(a, c):
            angles_in = picked("sin", sin, a, c)
            nc.scalar.activation(sin[a, c][:], angles_in, ACT.Sin)

        def cosine(a, c):
            nc.scalar.activation(cos[a, c][:], cos[a, c][:], ACT.Sin, bias=math.pi / 2, scale=-1.0)

        magnitude(0, 0)
        sine(0, 0)
        magnitude(0, 1)
        cosine(0, 0)
        magnitude(1, 0)
        sine(1, 0)
        magnitude(1, 1)
        cosine(1, 0)
        sine(0, 1)
        cosine(0, 1)
        magnitude(1, LAST)
        for c in (1, LAST):
            sine(1, c)
            cosine(1, c)

        made = []

        def products(a, c, name, codes, scales, factor, dst):
            m0, w = PIECES[a][c]
            tag = "th%d" % len(made) if len(made) < 6 else None
            made.append(name)
            dst[a, c] = kept("%s%d%d" % (name, a, c), [PART, w, 4], F32, tag=tag)
            for u0 in range(0, w, PART):
                bank = next_bank([PART, 4, PART])
                subhalos = slice(m0 + u0, m0 + u0 + PART)
                for t in range(4):
                    cols = slice(PART * t, PART * (t + 1))
                    nc.tensor.matmul_mx(
                        out=bank[:, t, :],
                        lhsT=codes[:, cols].bitcast(FP8X4),
                        lhsT_scale=scales[:, cols],
                        rhs=v2_w[:, subhalos].bitcast(FP8X4),
                        rhs_scale=v2_s[:, subhalos],
                        start=True,
                        stop=True,
                    )
                nc.vector.tensor_tensor(
                    dst[a, c][:, u0 : u0 + PART, :].rearrange("p m (y z) -> p m y z", z=2),
                    bank[:].rearrange("p (y z) m -> p m y z", z=2),
                    factor[a, c][:, :, u0 : u0 + PART, :].rearrange("p y m z -> p m y z"),
                    ALU.mult,
                )

        def mix(a, c, engine, dst, cols=slice(None)):
            engine.tensor_tensor(dst[:], cos_b1[a, c][:, cols, :], sin_b2[a, c][:, cols, :], ALU.add)

        def project(a, c):
            products(a, c, "sin_b2_", wsub2_w[a][:], wsub2_s[:].bitcast(U8)[:, BANK * a : BANK * (a + 1)], sin, sin_b2)
            products(a, c, "cos_b1_", wsub1_w[a][:], wsub1_s[a][:], cos, cos_b1)

        h_b = {}
        for d, (a, c) in enumerate([(0, 0), (1, 0), (0, 1)]):
            project(a, c)
            w = PIECES[1][c][1]
            h_b[a, c] = placed("h_b%d%d" % (a, c), [PART, w, 4], BF16, AT_H_B + 2048 * d)
            mix(a, c, nc.gpsimd, h_b[a, c], slice(0, w))
        for c in (1, LAST):
            project(1, c)
        out_banks = {(LAST, 0): next_bank([PART, 2, PART])}
        for d in range(KEEP_WARM_PASSES):
            nc.tensor.matmul_mx(
                out=next_bank([PART, BANK])[:],
                lhsT=wsub2_w[0][:, 0:PART].bitcast(FP8X4),
                lhsT_scale=wsub2_s[:].bitcast(U8)[:, 0:PART],
                rhs=v2_w[:].bitcast(FP8X4),
                rhs_scale=v2_s[:],
                start=True,
                stop=True,
            )

        wspin_b1 = [placed("wspin_b1%d" % b, [PART, HALF, 4], BF16, AT_ANG1 + 2048 * b) for b in range(2)]
        for b in range(2):
            nc.scalar.copy(
                wspin_b1[b][:].rearrange("p (u e) t -> p u t e", e=4),
                wspin_raw[1][:, :, halves[b]].rearrange("p t (u e) -> p u t e", e=4),
            )

        wspin_s = [placed("wspin_s0", [PART, N], U8, AT_COS_LAST + 1024), kept("wspin_s1", [PART, N], U8)]
        h_w, h_s = {}, {}
        for a in range(2):
            for c, (m0, w) in enumerate(PIECES[1]):
                h_w[a, c] = kept("h_w%d%d" % (a, c), [PART, w], U32)
                if (a, c) in h_b:
                    h_s[a, c] = placed("h_s%d%d" % (a, c), [PART, w], U8, AT_COS_LAST + HALF * (a + 2 * c))
                else:
                    h_s[a, c] = kept("h_s%d%d" % (a, c), [PART, w], U8)

        def quantize_h(a, c):
            quantize(h_w[a, c][:], h_s[a, c][:], h_b[a, c][:])

        def spin(a, c, b):
            m0, w = PIECES[1][c]
            if (c, b) not in out_banks:
                out_banks[c, b] = any_bank([PART, 2, w])
            for d in range(2):
                rows = slice(PART * (2 * b + d), PART * (2 * b + d + 1))
                nc.tensor.matmul_mx(
                    out=out_banks[c, b][:, d, :],
                    lhsT=wspin_w[a][:, rows].bitcast(FP8X4),
                    lhsT_scale=wspin_s[a][:, rows],
                    rhs=h_w[a, c][:].bitcast(FP8X4),
                    rhs_scale=h_s[a, c][:],
                    start=(a, d) == (0, 0),
                    stop=(a, d) == (1, 1),
                )

        out_v = out.rearrange("(n p) m -> p n m", p=PART)

        def store(c, b):
            m0, w = PIECES[1][c]
            res = kept("res%d%d" % (c, b), [PART, 2, w], F32)
            if (c, b) == (LAST, 1):
                nc.vector.tensor_copy(res[:], out_banks[c, b][:])
            else:
                nc.scalar.copy(res[:], out_banks[c, b][:])
            queue = nc.scalar if (c, b) == (LAST, 0) else nc.sync
            queue.dma_start(out_v[:, 2 * b : 2 * (b + 1), m0 : m0 + w], res[:])

        quantize_h(0, 0)
        quantize(wspin_w[0][:], wspin_s[0][:], wspin_b0[:])
        for b in range(2):
            spin(0, 0, b)
        quantize_h(1, 0)
        quantize(wspin_w[1][:, halves[0]], wspin_s[1][:, halves[0]], wspin_b1[0][:])
        spin(1, 0, 0)
        store(0, 0)
        h_b[1, 1] = placed("h_b11", [PART, PART, 4], BF16, AT_H_B)
        mix(1, 1, nc.vector, h_b[1, 1])
        quantize_h(0, 1)
        quantize(wspin_w[1][:, halves[1]], wspin_s[1][:, halves[1]], wspin_b1[1][:])
        spin(1, 0, 1)
        store(0, 1)
        quantize_h(1, 1)
        for a in range(2):
            for b in range(2):
                spin(a, 1, b)
        for b in range(2):
            store(1, b)
        h_b[0, LAST] = placed("h_b02", [PART, PART, 4], BF16, AT_H_B + 2048)
        h_b[1, LAST] = placed("h_b12", [PART, PART, 4], BF16, AT_H_B + 4096)
        mix(0, 1, nc.vector, h_b[0, LAST], slice(PART, 2 * PART))
        mix(1, LAST, nc.vector, h_b[1, LAST])
        for a in range(2):
            quantize_h(a, LAST)
            for b in range(2):
                spin(a, LAST, b)
        for b in range(2):
            store(LAST, b)
